import numpy as np, ml_dtypes
CORES = [113,118,241,246]
N = 4
BF = ml_dtypes.bfloat16
def gentries(a):
    return np.ascontiguousarray(a.reshape(8, 16, -1).transpose(0, 2, 1)).reshape(8, -1)
def gtable(e):
    e = np.asarray(e); return np.ascontiguousarray(e.reshape(8, -1, 16).transpose(0, 2, 1)).reshape(128, -1).astype(np.int32)
T, C, R, S, VI = 4096, 1024, 48, 20, 6
def parts(rng):
    book = rng.integers(0, T, (N, 8, 16, C)); mix = rng.choice(np.array([0.2, 0.5, 0.8, 1.0]), (N, 8, 1, 1))
    W = np.minimum((256 * ((1 - mix) * rng.random((N, 8, 1, T)) + mix * rng.random((N, 8, 16, T)))).astype(np.int64), 255)
    wt = rng.integers(0, 256, (N, 8, 16)); sg = rng.integers(0, T, (N, 8, T)); sg[:, ::2] = np.argsort(rng.random((N, 4, T)), axis=-1)
    return book, W, wt, sg, rng.integers(0, C, (N, 8, S, R))
def pack(book, W, wt, sg, km):
    return {"book": np.ascontiguousarray(book.reshape(N, 128, C)).astype(np.int32), "tru": np.ascontiguousarray(W.reshape(N, 128, T)).astype(np.float32).astype(BF),
            "wt": np.ascontiguousarray(wt.reshape(N, 128, 1)).astype(np.int32), "sg0": np.stack([gtable(v) for v in sg]), "km0": np.stack([gtable(v.reshape(8, -1)) for v in km])}
def setup_inputs(rng):
    book, W, wt, sg, km = parts(rng)
    km[:, :, :, 3] = km[:, :, :1, 3]; km[:, :, :, 7] = km[:, :, :, 5]; km[:, :, :, 9] = km[:, :, :, 5]
    return pack(book, W, wt, sg, km)
def setup_inputs_spread(rng):
    book, W, wt, sg, km = parts(rng)
    W = np.minimum((np.exp2(8 * rng.random((N, 8, 1, T))) * rng.random((N, 8, 16, T)) * (rng.random((N, 8, 1, T)) > 0.0625)).astype(np.int64), 255)
    W[:, 1::2] = 255 - W[:, 1::2]; wt = np.minimum(np.exp2(8 * rng.random((N, 8, 16))).astype(np.int64), 255)
    book[:, :, ::2] = np.minimum((T * rng.random((N, 8, 8, C)) ** 3).astype(np.int64), T - 1)
    sg[:, ::3] = np.minimum((T * rng.random((N, 3, T)) ** 2).astype(np.int64), T - 1)
    km = np.minimum((C * rng.random((N, 8, S, R)) ** 2).astype(np.int64), C - 1)
    return pack(book, W, wt, sg, km)
def setup_inputs_ends(rng):
    book, W, wt, sg, km = parts(rng)
    kind = rng.random((N, 8, 1, T)); one = (np.arange(16)[:, None] == rng.integers(0, 16, (N, 8, 1, T))).astype(np.int64)
    bits = 255 * rng.integers(0, 2, (N, 8, 16, T))
    W = np.where(kind < 0.2, 255, np.where(kind < 0.32, 255 - one, np.where(kind < 0.44, 0, np.where(kind < 0.5, one, np.where(kind < 0.75, bits, W)))))
    sg = np.where(rng.random((N, 8, T)) < 0.65, (T - 1) * rng.integers(0, 2, (N, 8, T)), sg); sg[..., 0] = 0; sg[..., T - 1] = T - 1
    kc = rng.random((N, 8, 1, C)); two = (T - 1) * rng.integers(0, 2, (N, 8, 16, C))
    book = np.where(kc < 0.22, T - 1, np.where(kc < 0.33, 0, np.where(kc < 0.58, two, np.where((kc < 0.72) & (rng.random(book.shape) < 0.5), two, book))))
    book[..., 0] = (T - 1) * ((np.arange(16) + rng.integers(0, 2, (N, 8, 1))) % 2); book[..., C - 1] = T - 1
    km = np.where(rng.random(km.shape) < 0.65, (C - 1) * rng.integers(0, 2, km.shape), km)
    wt = 255 * rng.integers(0, 2, (N, 8, 16)); wt[:, :, :5] = rng.integers(0, 256, (N, 8, 5)); wt[:, 0] = 255; wt[:, 7] = 255; wt[:, 4] = 0
    for q in range(N):
        for g in range(8):
            kd = (g + q) % 4
            if q == N - 2 or (q == 0 and kd == 2) or (q == N - 1 and g == 7): kd = 0
            P = np.where(rng.permutation(16) < int(rng.integers(8, 10)), 255, 0)
            W[q, g, :, 0] = (0, 255, 255, 255 - P)[kd]; W[q, g, :, T - 1] = (255, 0, 255, P)[kd]
    km[0, :, 0, :] = 0
    km[N - 2, :, 0, :] = C - 1; km[N - 2, :, S - 1, :] = 0; km[N - 2, :, 1:S - 1, R - 1] = C - 1
    km[N - 1, 7, :, R - 1] = C - 1
    W[N - 1, 7, :, 7] = 255 * (np.arange(16) % 2); sg[N - 1, 7, 1] = 0; sg[N - 1, 7, 2] = 7; sg[N - 1, 7, T - 2] = T - 1
    e = np.full(16, 2); e[2] = T - 2; e[15] = T - 1; e[5] = 1; e[14] = 0; book[N - 1, 7, :, 600] = e
    return pack(book, W, wt, sg, km)
def setup_inputs_corners(rng):
    book, W, wt, sg, km = parts(rng); h = C // 2
    km[:, 0] = rng.integers(0, C, (N, 1, R))
    W[:, 1:3, :, :T // 2] = rng.integers(0, 100, (N, 2, 16, T // 2)); W[:, 1:3, :, T // 2:] = rng.integers(156, 256, (N, 2, 16, T - T // 2)); sg[:, 1:3] = np.arange(T)
    book[:, 1:3, :, :h] = rng.integers(T // 2, T, (N, 2, 16, h)); book[:, 1:3, :, h:] = rng.integers(0, T // 2, (N, 2, 16, C - h))
    km[:, 1] = rng.integers(0, h, (N, 1, R)); km[:, 1, S - 1] = rng.integers(h, C, (N, R))
    km[:, 2, 0] = rng.integers(0, h, (N, R)); km[:, 2, 1:] = rng.integers(h, C, (N, S - 1, R))
    book[:, 3, :, ::2] = rng.integers(0, T, (N, 1, h))
    sg[:, 4] = np.where(np.arange(T) % 2 == 0, 0, T - 1); book[:, 4] = (book[:, 4] // 2) * 2 + np.arange(C) % 2
    for q in range(N):
        m = 9 if q % 2 == 0 else 8
        W[q, 4, :, 0] = np.where(np.arange(16) < m, 10, 200); W[q, 4, :, T - 1] = np.where(np.arange(16) < m, 20, 100)
    wt[:, 5] = 0; wt[:, 7] = 255; wt[:, 6] = 255 * rng.integers(0, 2, (N, 16)); wt[:, 6, :4] = rng.integers(1, 256, (N, 4))
    few = np.concatenate([np.array([0, T - 1, 1, T - 2]), rng.permutation(T - 8)[:20] + 4]); book[:, 6] = few[book[:, 6] % 24]
    book[:, 7, 0] = T - 1; sg[:, 7, T - 1] = T - 1; W[:, 7, :, T - 1] = 255
    return pack(book, W, wt, sg, km)
def aim(rng, w, taken, m):
    V = rng.integers(0, 255, (16, 2048)); u = np.add.reduce(w[:, None] * V, axis=0) & 4095; n = ((u * u >> 5) + 37 * u) & (C - 1)
    v, i = np.unique(n, return_index=True); i = rng.permutation(i[~np.isin(v, taken)])[:m]
    return V[:, i], n[i]
def plant(rng, bk, Wg, s, cols, a, b, zero, top, rest, g):
    for j in range(R):
        kind = (j + g) % 3; one = (np.arange(16) == int(rng.integers(0, 16))).astype(np.int64); p, o = rng.permutation(16)[:2]
        pool = (rest, zero, top)[kind]; col = pool[rng.integers(0, len(pool), 16)]
        if kind == 1: p, o = int(rng.integers(1, 16)), 0
        if kind == 2: p, o = 0, int(rng.integers(1, 16))
        col[p] = a[j]; col[o] = b[j]; bk[:, cols[j]] = col
        Wg[:, s[a[j]]] = one if kind == 1 else 255
        Wg[:, s[b[j]]] = 255 - one if kind == 2 else 0
def setup_inputs_full(rng):
    book, W, wt, sg, km = parts(rng); W = np.clip(W, 1, 254); sg = np.argsort(rng.random((N, 8, T)), axis=-1); wt[:, :, 0] = 255
    for r in range(0, N - 1, 2):
        q = r + 1
        for g in range(8):
            x = rng.permutation(T); a0, b0, a1, b1 = np.array(x[:4 * R]).reshape(4, R)
            z, zero, top, rest = x[4 * R:5 * R + 1], x[5 * R + 1:5 * R + 17], x[5 * R + 17:5 * R + 33], x[5 * R + 33:]
            if g == 3: a1[7] = b0[7]; b1[9] = a0[9]
            if g == 5: a1[5] = a0[0]
            y = rng.permutation(C); O, P, X1, X = int(y[0]), int(y[1]), int(y[2]), y[3:3 + R]
            V0, n0 = aim(rng, wt[r, g], y[:3 + R], R); V1, n1 = aim(rng, wt[q, g], np.concatenate([y[:3], n0]), R + 1)
            for c in (r, q):
                W[c, g][:, sg[c, g][zero]] = 0; W[c, g][:, sg[c, g][top]] = 255
            W[r, g][:, sg[r, g][z[:R]]] = V0; book[r, g][:, X] = z[:R]; book[r, g][:, O] = zero[0]
            plant(rng, book[r, g], W[r, g], sg[r, g], n0, a0, b0, zero, top, rest, g)
            km[r, g, 0] = O; km[r, g, 1] = X
            W[q, g][:, sg[q, g][z]] = V1; book[q, g][:, n0] = z[:R]; book[q, g][:, X1] = z[R]
            book[q, g][:, O] = top[0]; book[q, g][:, P] = zero[0]; book[q, g][:, n1[R]] = top[1]
            plant(rng, book[q, g], W[q, g], sg[q, g], n1, a1, b1, zero, top, rest, g + 1)
            if g == 5: book[q, g][:, n1[0]] = a1[0]
            km[q, g, 0] = P; km[q, g, 1] = X1
    return pack(book, W, wt, sg, km)
def setup_inputs_hush(rng):
    book, W, wt, sg, km = parts(rng); q0 = int(rng.integers(0, N))
    for q in (q0, (q0 + 2) % N):
        for g in range(8):
            x = rng.permutation(T)[:3]; m = rng.permutation(T)[:3]; y = rng.permutation(C)[:3]
            hi = rng.integers(160, 255, 16) if g < 7 else np.where(rng.permutation(16) < 9, 254, 255)
            sg[q, g, x] = m; W[q, g, :, m[0]] = 0; W[q, g, :, m[1]] = 255; W[q, g, :, m[2]] = hi
            book[q, g] = np.where(book[q, g] == x[0], x[1], book[q, g]); book[q, g][:, y] = x
            wt[q, g] = rng.integers(224, 256, 16) if g < 7 else 255
            km[q, g, :, ::2] = y[1]; km[q, g, S - 1, ::2] = y[2]; km[(q - 1) % N, g, 0] = y[0]
    return pack(book, W, wt, sg, km)
def check_inputs(d):
    bad = []
    for k, lo, hi in (("book", 0, T - 1), ("tru", 0, 255), ("wt", 0, 255), ("sg0", 0, T - 1), ("km0", 0, C - 1)):
        v = np.asarray(d[k]).astype(np.float64)
        if not (np.min(v) >= lo and np.max(v) <= hi): bad.append("range of " + k)
        elif np.any(np.floor(v) != v): bad.append("whole numbers in " + k)
    return bad
def reference(book, tru, wt, sg0, km0):
    B = np.ascontiguousarray(book.astype(np.int64).reshape(N, 8, 16, C).transpose(0, 1, 3, 2))
    W = np.ascontiguousarray(tru.astype(np.float32).astype(np.int64).reshape(N, 8, 16, T).transpose(0, 1, 3, 2))
    w = wt.astype(np.int64).reshape(N, 8, 16)
    s = np.stack([gentries(v) for v in sg0]).astype(np.int64)
    K = np.stack([gentries(v) for v in km0]).astype(np.int64).reshape(N, 8, S, R)
    a = np.full((N, 8, S, R), -1, np.int64); b = np.full((N, 8, S, R), -1, np.int64)
    last = np.zeros(N, np.int64); ar = np.arange(R)
    for t in range(VI):
        new = np.zeros(N, np.int64)
        for r in range(N):
            q = (r + t) % N
            for g in range(8):
                Z = W[q, g][s[q, g]]
                y = np.min(Z[B[q, g][K[r, g].reshape(-1)]], axis=1).reshape(S, R, 16)
                con = np.add.reduce((y[1:] < y[:1]).astype(np.int64), axis=2) >= 9
                hit = np.any(con, axis=0); ks = np.where(hit, 1 + np.argmax(con, axis=0), 1 + t)
                u = np.add.reduce(y[ks, ar] * w[q, g], axis=1) & 4095
                n = ((u * u >> 5) + 37 * u + last[q]) & (C - 1)
                e = B[q, g][n]; sc = np.add.reduce(Z[e], axis=2)
                na = e[ar, np.argmax(sc, axis=1)]; nb = e[ar, np.argmin(sc, axis=1)]
                oa = np.where(hit, a[r, g, ks, ar], -1); ob = np.where(hit, b[r, g, ks, ar], -1)
                nm = np.stack([na, nb, oa, ob]); nm = np.where(nm < 0, T, nm)
                own = np.full(T + 1, R, np.int64); np.minimum.at(own, nm, np.broadcast_to(ar, (4, R))); own[T] = R
                ok = (na != nb) & (na != oa) & (na != ob) & (nb != oa) & (nb != ob) & ~np.any(own[nm] < ar, axis=0)
                old = np.array(s[q, g]); i = np.nonzero(ok)[0]; h = np.nonzero(ok & (oa >= 0))[0]
                s[q, g, na[i]] = old[nb[i]]; s[q, g, nb[i]] = old[na[i]]
                s[q, g, oa[h]] = old[ob[h]]; s[q, g, ob[h]] = old[oa[h]]
                K[r, g, ks, ar] = n; a[r, g, ks, ar] = np.where(ok, na, -1); b[r, g, ks, ar] = np.where(ok, nb, -1)
                new[q] += np.add.reduce(hit.astype(np.int64))
        last = new
    return {"yk": np.stack([gtable(v.reshape(8, -1)) for v in K]).astype(np.float32), "ya": np.stack([gtable(v.reshape(8, -1)) for v in a]).astype(np.float32),
            "yb": np.stack([gtable(v.reshape(8, -1)) for v in b]).astype(np.float32), "ys": s.astype(np.float32)}

@@ -1,0 +1,523 @@
+from concourse.bass import DstId, RemoteDMATransfer
+from concourse.mybir import dt, AluOpType, AxisListType, ActivationFunctionType
+
+VI = 6
+PADC = 4288
+PH = 344
+P_CH = [96, 120, 128]
+S_CH = [128, 104, 68, 28, 8]
+S0_CH = [128, 128, 128, 128, 128, 80, 48, 16]
+V0_CH = [128, 112]
+YW = 1 + 16 * 1024
+B1, B2 = float(2 ** 23), float(2 ** 21)
+
+_sb = {
+    "truv": (4096, "bfloat16"), "Z": (PADC, "bfloat16"), "S": (PADC, "float32"), "iot": (4096, "float32"),
+    "booki": (1408, "int32"), "blist": (1024 - 2 * PH, "uint16"), "sgi": (256, "int32"), "sgl": (256, "uint16"),
+    "kmi": (64, "int32"),
+    "G": (16384, "bfloat16"), "blist0": (1024, "uint16"), "H": (16 * PH, "bfloat16"), "ysc": (YW, "bfloat16"), "rst": (2048, "bfloat16"), "rst8": (2048, "bfloat16"),
+    "lai": (PH, "int32"), "lbi": (PH, "int32"), "la": (PH, "uint16"), "lb": (PH, "uint16"),
+    "lzz": (240, "float32"), "pad8": (24, "float32"),
+    "pi": (1, "int32"), "pj": (1, "int32"), "pg": (1, "int32"), "colf": (16, "float32"),
+    "iof": (128, "float32"), "iog": (128, "float32"), "ioj": (192, "float32"),
+    "idf": (128, "float32"), "idb": (128, "bfloat16"), "bof": (128, "float32"), "bob": (128, "bfloat16"),
+    "thr": (128, "bfloat16"), "thf": (128, "float32"), "onb": (128, "bfloat16"), "dm": (192, "float32"),
+    "selc": (96, "float32"), "selt": (96, "float32"), "selc2": (96, "float32"), "sel8": (8, "float32"), "cntw": (8, "bfloat16"), "usel": (8, "bfloat16"),
+    "scw": (16, "bfloat16"), "pmx": (192, "bfloat16"), "e0": (128, "float32"), "e1": (128, "float32"), "e8": (128, "bfloat16"),
+    "srst": (256, "float32"), "kd1": (160, "float32"), "padf": (12, "float32"), "sumr": (120, "float32"),
+    "kl": (58, "uint16"), "kl2": (6, "uint16"), "y00": (96, "bfloat16"), "y": (912, "bfloat16"), "lt": (912, "bfloat16"),
+    "xx": (160, "float32"), "d1u": (160, "float32"), "su": (320, "float32"), "xt": (48, "float32"), "selo": (96, "float32"),
+    "uint": (28, "int32"), "nK": (3, "float32"), "nl": (4, "uint16"), "nl6": (6, "uint16"), "bkl": (48, "uint16"), "bk2": (96, "float32"),
+    "zc": (768, "bfloat16"), "ko": (3, "float32"), "kz": (3, "float32"), "kst": (3, "float32"), "hitb": (3, "bfloat16"),
+    "eqo": (60, "float32"), "pr": (120, "float32"), "osm": (120, "float32"), "owno": (6, "float32"), "owno2": (6, "float32"), "ownn": (6, "float32"),
+    "zz": (6, "float32"), "f6": (6, "float32"), "dn": (12, "float32"), "dd": (96, "float32"),
+    "sk": (256, "float32"), "ki": (16, "int32"), "kia": (16, "int32"), "kb": (16, "bfloat16"), "xp": (96, "bfloat16"),
+    "em": (96, "float32"), "mb": (96, "float32"), "nsel": (96, "float32"), "fn": (192, "uint16"),
+    "eqb": (2304, "bfloat16"), "cm": (192, "float32"), "m3": (3, "float32"), "acc": (12, "float32"),
+    "of1": (12, "float32"), "of2": (12, "float32"), "offs": (12, "uint16"), "pl": (12, "uint16"),
+    "zp": (192, "bfloat16"), "sp": (192, "float32"), "neq": (60, "float32"), "ab6": (6, "float32"), "val6": (6, "float32"),
+    "xs": (180, "float32"), "ts3": (180, "float32"), "cc": (1, "float32"), "sf": (180, "float32"),
+}
+SCRATCH = {}
+for _k in _sb:
+    SCRATCH[_k] = ("sbuf", [128, _sb[_k][0]], _sb[_k][1])
+for _t in range(VI + 1):
+    SCRATCH["st%d" % _t] = ("sbuf", [128, 180], "float32")
+for _t in range(VI - 1):
+    SCRATCH["so%d" % _t] = ("sbuf", [128, 180], "float32")
+for _t in range(8):
+    SCRATCH["ps%d" % _t] = ("psum", [128, 512], "float32")
+SEMAPHORES = ["sv", "ss", "sp_", "sg_", "lsg", "ltr", "lbk", "lbw", "lkm", "lwt", "lhf", "lhg", "dout", "lsem"] + ["arr%d" % _t for _t in range(1, VI + 1)]
+
+
+def rank_program(g, core, T, topo):
+    rank = T.rank_of(core)
+    if rank is None:
+        return
+    A, AX, AF = AluOpType, AxisListType, ActivationFunctionType
+    cores = T.cores
+    nxt, prv = cores[(rank + 1) % 4], cores[(rank + 3) % 4]
+
+    eng = {"v": g.vector, "s": g.scalar, "p": g.tensor, "g": g, "y": g.sync}
+    semn = {"v": "sv", "s": "ss", "p": "sp_", "g": "sg_"}
+    cnt = {"v": 0, "s": 0, "p": 0, "g": 0}
+    waited = {}
+    wr, rd = {}, {}
+
+    def need(q, sem, n):
+        if waited.get((q, sem), 0) < n:
+            waited[(q, sem)] = n
+            eng[q].wait_ge(T.sem[sem], n)
+
+    def deps(q, r, w):
+        lst = {}
+        for k in r:
+            if k in wr:
+                sem, n, q2 = wr[k]
+                if not (q == "p" and q2 == "p"):
+                    lst[sem] = max(lst.get(sem, 0), n)
+        for k in w:
+            if k in wr and wr[k][2] != q:
+                lst[wr[k][0]] = max(lst.get(wr[k][0], 0), wr[k][1])
+            for (sem, n, q2) in rd.get(k, {}).values():
+                if q2 != q or q == "v":
+                    lst[sem] = max(lst.get(sem, 0), n)
+        for sem in lst:
+            need(q, sem, lst[sem])
+
+    def note(q, r, w, tag):
+        for k in r:
+            rd.setdefault(k, {})[q] = tag
+        for k in w:
+            wr[k] = tag
+            rd[k] = {}
+
+    def E(q, f, r, w):
+        deps(q, r, w)
+        i = f(eng[q])
+        cnt[q] += 1
+        i.then_inc(T.sem[semn[q]], 1)
+        note(q, r, w, (semn[q], cnt[q], q))
+
+    def dma(q, out, in_, sem, r, w):
+        deps(q, r, w)
+        eng[q].dma_start(out=out, in_=in_).then_inc(T.sem[sem], 16)
+        note(q, r, w, (sem, 16, "dma"))
+
+    def ts(out, in0, s1, op0, r, w, s2=None, op1=None):
+        if op1 is None:
+            E("v", lambda e: e.tensor_scalar(out=out, in0=in0, scalar1=s1, scalar2=None, op0=op0), r, w)
+        else:
+            E("v", lambda e: e.tensor_scalar(out=out, in0=in0, scalar1=s1, scalar2=s2, op0=op0, op1=op1), r, w)
+
+    def tt(out, a, b, op, r, w):
+        E("v", lambda e: e.tensor_tensor(out=out, in0=a, in1=b, op=op), r, w)
+
+    def cp(out, a, r, w):
+        E("v", lambda e: e.tensor_copy(out=out, in_=a), r, w)
+
+    def scan(out, d0, d1, op0, op1, r, w):
+        E("v", lambda e: e.tensor_tensor_scan(out=out, data0=d0, data1=d1, initial=0.0, op0=op0, op1=op1), r, w)
+
+    def red(out, a, op, r, w):
+        E("v", lambda e: e.tensor_reduce(out=out, in_=a, axis=AX.X, op=op), r, w)
+
+    def ms(ap, c, w, r=()):
+        E("v", lambda e: e.memset(ap, c), r, w)
+
+    def act(out, a, r, w, **kw):
+        E("s", lambda e: e.activation(out=out, in_=a, func=AF.Copy, **kw), r, w)
+
+    def mm(out, lhsT, rhs, r, w, start=True, stop=True):
+        E("p", lambda e: e.matmul(out, lhsT, rhs, start, stop), r, w)
+
+    def iota(out, pattern, base, cm, w):
+        E("g", lambda e: e.iota(out, pattern, base, cm, allow_small_or_imprecise_dtypes=True), [], w)
+
+    dma("y", T.sgi[:, :], T.sg0[:, :], "lsg", [], ["sgi"])
+    dma("y", T.truv[:, :], T.tru[:, :], "ltr", [], ["truv"])
+    dma("s", T.booki[:, 0:1024], T.book[:, :], "lbk", [], ["bookA"])
+    dma("y", T.kmi[:, 60:61], T.wt[:, :], "lwt", [], ["wti"])
+    dma("y", T.kmi[:, 0:60], T.km0[:, :], "lkm", [], ["kmi"])
+    dma("y", T.booki[:, 1024:1408], T.book[:, 0:384], "lbw", [], ["bookB"])
+
+    def halves(q, buf, o, key, sem):
+        for p in range(8):
+            for h in range(2):
+                eng[q].dma_start(out=buf[p + 8 * h:128:16, :], in_=T.book[p + o:128:16, 512 * h:512 * h + PH]).then_inc(T.sem[sem], 16)
+        note(q, [], [key], (sem, 256, "dma"))
+
+    halves("y", T.lbi, 8, "lbi", "lhf")
+
+    cp(T.sgl[:, :], T.sgi[:, :], ["sgi"], ["sgl"])
+    ms(T.Z[:, 4096:PADC], 0.0, ["Zpad"])
+    ms(T.rst[:, :], 0.0, ["rst"])
+    ms(T.rst8[:, :], 0.0, ["rst8"])
+    ms(T.rst[:, 0:2048:16], 512.0, ["rst"], ["rst"])
+    ms(T.rst8[:, 0:2048:8], 512.0, ["rst8"], ["rst8"])
+    ms(T.ysc[:, 0:1], 0.0, ["Y0"])
+    iota(T.pi[:, :], [[0, 1]], 0, 1, ["pi"])
+    iota(T.iof[:, :], [[1, 128]], 0, 0, ["iof"])
+    iota(T.iog[:, :], [[1, 8], [0, 16]], 0, 0, ["iog"])
+    iota(T.ioj[:, :], [[0, 12], [1, 16]], 0, 0, ["ioj"])
+    iota(T.kd1[:, :], [[0, 8], [1, 20]], 256, 0, ["kd1"])
+    iota(T.padf[:, :], [[16, 12]], 4096, 0, ["padf"])
+    iota(T.iot[:, :], [[1, 4096]], 0, 0, ["iot"])
+    halves("g", T.lai, 0, "lai", "lhg")
+    act(T.Z[:, 0:2048], T.truv[:, :].indirect(T.sgl[:, 0:128]), ["truv", "sgl"], ["ZA"])
+    Zk = ["ZA", "ZB", "Zpad"]
+    Zall = T.Z[:, :]
+
+    def yphase(before_tail):
+        c, pits, sits = 0, [], []
+        for i in range(len(P_CH)):
+            pits.append((c, P_CH[i], "G%d" % i, "H%d" % i))
+            c += P_CH[i]
+        for i in range(len(S_CH)):
+            sits.append((c, S_CH[i], "J%d" % i))
+            c += S_CH[i]
+        for (c, n, k, k2) in pits:
+            act(T.G[:, 16 * c:16 * (c + n)], Zall.indirect(T.lb[:, c:c + n]), Zk + ["lb"], [k])
+        for (c, n, k) in sits:
+            act(T.G[:, 16 * c:16 * (c + n)], Zall.indirect(T.blist[:, c - PH:c - PH + n]), Zk + ["blist"], [k])
+        for (c, n, k, k2) in pits:
+            tt(T.H[:, 16 * c:16 * (c + n)], Zall.indirect(T.la[:, c:c + n]), T.G[:, 16 * c:16 * (c + n)], A.min, Zk + ["la", k], [k2])
+        for (c, n, k, k2) in pits:
+            scan(T.ysc[:, 1 + 16 * c:1 + 16 * (c + n)], T.rst8[:, 0:16 * n], T.H[:, 16 * c:16 * (c + n)], A.max, A.min, ["rst8", k2], ["Y"])
+        for i in range(len(sits)):
+            (c, n, k) = sits[i]
+            before_tail(i)
+            scan(T.ysc[:, 1 + 16 * c:1 + 16 * (c + n)], T.rst[:, 0:16 * n], T.G[:, 16 * c:16 * (c + n)], A.max, A.min, ["rst", k], ["Y"])
+
+    def lists(t, i):
+        st = T["st%d" % t]
+        sk_ = "st%d" % t
+        lz, lz2, lw = T.lzz[:, 0:60], T.lzz[:, 60:120], T.lzz[:, 120:180]
+        if i == 0:
+            ts(lz, st[:, 0:60], 511.5, A.is_ge, [sk_], ["lz"], -511.5, A.mult)
+        if i == 1:
+            tt(lz2, st[:, 0:60], lz, A.add, [sk_, "lz"], ["lz2"])
+        if i == 2:
+            ts(lw, lz2, -(PH - 0.5), A.add, ["lz2"], ["lw"], 0.0, A.max)
+        if i == 3:
+            tt(T.lzz[:, 180:240], lz2, lw, A.add, ["lz2", "lw"], ["lz3"])
+        if i < 4:
+            return
+        ts(T.kl2[:, 0:3], T.lzz[:, 180:240:20], 16.0, A.mult, ["lz3"], ["kl2"], 8.0, A.add)
+        ts(T.kl2[:, 3:6], T.lzz[:, 180:240:20], 16.0, A.mult, ["lz3"], ["kl2"], 8.0, A.add)
+        for jb in range(3):
+            ts(T.kl[:, jb:57:3], T.lzz[:, 181 + 20 * jb:200 + 20 * jb], 16.0, A.mult, ["lz3"], ["kl"], 8.0, A.add)
+
+    def consts():
+        C = T.colf
+        ts(T.pj[:, :], T.pi[:, :], 15, A.bitwise_and, ["pi"], ["pj"])
+        ts(T.pg[:, :], T.pi[:, :], 4, A.arith_shift_right, ["pi"], ["pg"])
+        cp(C[:, 0:1], T.pi[:, :], ["pi"], ["c0"])
+        cp(C[:, 1:2], T.pj[:, :], ["pj"], ["c1"])
+        cp(C[:, 2:3], T.pg[:, :], ["pg"], ["c2"])
+        cp(C[:, 9:10], T.kmi[:, 60:61], ["wti"], ["c9"])
+        ts(C[:, 3:4], C[:, 1:2], 14.5, A.is_lt, ["c1"], ["c3"], B2, A.mult)
+        ts(C[:, 4:5], C[:, 1:2], -1.0, A.mult, ["c1"], ["c4"], 15.0, A.add)
+        ts(C[:, 5:6], C[:, 2:3], 16.0, A.mult, ["c2"], ["c5"], C[:, 0:1], A.add)
+        ts(C[:, 6:7], C[:, 5:6], 16.0, A.add, ["c5"], ["c6"])
+        ts(C[:, 7:8], C[:, 0:1], -8.0, A.add, ["c0"], ["c7"])
+        ts(C[:, 8:9], C[:, 3:4], 276.0, A.add, ["c3"], ["c8"])
+        ts(T.sel8[:, :], T.iof[:, 0:8], C[:, 2:3], A.is_equal, ["iof", "c2"], ["sel8"])
+        ts(T.cntw[:, :], T.sel8[:, :], 32.0, A.mult, ["sel8"], ["cntw"])
+        ts(T.usel[:, :], T.sel8[:, :], C[:, 9:10], A.mult, ["sel8", "c9"], ["usel"])
+        ts(T.scw[:, 0:8], T.sel8[:, :], 16.0, A.mult, ["sel8"], ["scw"])
+        ts(T.scw[:, 8:16], T.sel8[:, :], -16.0, A.mult, ["sel8"], ["scw"])
+        ts(T.idf[:, :], T.iof[:, :], C[:, 0:1], A.is_equal, ["iof", "c0"], ["idf"])
+        ts(T.idb[:, :], T.iof[:, :], C[:, 0:1], A.is_equal, ["iof", "c0"], ["idb"])
+        ts(T.bof[:, :], T.iog[:, :], C[:, 2:3], A.is_equal, ["iog", "c2"], ["bof"])
+        ts(T.bob[:, :], T.iog[:, :], C[:, 2:3], A.is_equal, ["iog", "c2"], ["bob"], 8192.0, A.mult)
+        ts(T.thf[:, :], T.ioj[:, 0:128], C[:, 1:2], A.is_ge, ["ioj", "c1"], ["thf"], 8192.0, A.mult)
+        tt(T.thr[:, :], T.thf[:, :], T.bof[:, :], A.mult, ["thf", "bof"], ["thr"])
+        ms(T.onb[:, :], 1.0, ["onb"])
+        ts(T.dm[:, :], T.ioj[:, :], C[:, 1:2], A.is_equal, ["ioj", "c1"], ["dm"])
+        ts(T.selt[:, :], T.ioj[:, 0:96], C[:, 1:2], A.is_le, ["ioj", "c1"], ["selt"], -B1, A.mult)
+        ts(T.selc[:, :], T.ioj[:, 0:96], C[:, 1:2], A.subtract, ["ioj", "c1"], ["selc"], 1.0, A.is_equal)
+        ts(T.selc[:, :], T.selc[:, :], B2, A.mult, ["selc"], ["selc"])
+        tt(T.selc[:, :], T.selc[:, :], T.selt[:, :], A.add, ["selc", "selt"], ["selc"])
+        ts(C[:, 10:11], C[:, 1:2], 14.5, A.is_lt, ["c1"], ["c10"], 8192.0, A.mult)
+        ts(T.selt[:, :], T.ioj[:, 0:96], C[:, 1:2], A.is_le, ["ioj", "c1"], ["selt"], -131072.0, A.mult)
+        ts(T.selc2[:, :], T.ioj[:, 0:96], C[:, 1:2], A.subtract, ["ioj", "c1"], ["selc2"], 1.0, A.is_equal)
+        ts(T.selc2[:, :], T.selc2[:, :], 8192.0, A.mult, ["selc2"], ["selc2"])
+        tt(T.selc2[:, :], T.selc2[:, :], T.selt[:, :], A.add, ["selc2", "selt"], ["selc2"])
+        ts(T.pmx[0:48, 0:96], T.iof[0:48, 0:96], C[0:48, 5:6], A.is_equal, ["iof", "c5"], ["pmx"])
+        ts(T.pmx[0:48, 96:192], T.iof[0:48, 0:96], C[0:48, 6:7], A.is_equal, ["iof", "c6"], ["pmx"])
+        ts(T.e0[0:16, :], T.iog[0:16, :], C[0:16, 0:1], A.is_equal, ["iog", "c0"], ["e0"])
+        ts(T.e1[0:16, :], T.iog[0:16, :], C[0:16, 7:8], A.is_equal, ["iog", "c7"], ["e1"])
+        ts(T.e8[0:8, :], T.iog[0:8, :], C[0:8, 0:1], A.is_equal, ["iog", "c0"], ["e8"])
+        ms(T.srst[:, :], 1.0, ["srst"])
+        ms(T.srst[:, 0:256:16], -1048576.0, ["srst"], ["srst"])
+        ms(T.sumr[:, :], 1.0, ["sumr"])
+        ms(T.sumr[:, 0:120:20], 0.0, ["sumr"], ["sumr"])
+        ts(T.pad8[:, 0:12], T.padf[:, :], C[:, 1:2], A.add, ["padf", "c1"], ["pad8"])
+        ts(T.pad8[:, 12:24], T.padf[:, :], C[:, 1:2], A.add, ["padf", "c1"], ["pad8"], 8192.0, A.add)
+        ms(T.S[:, 4096:PADC], 0.0, ["Spad"])
+        ms(T.ps3[:, 0:160], 512.0, ["B3"])
+        ms(T.st0[:, 60:180], 0.0, ["st0n"])
+        for jb in range(3):
+            cp(T.st0[:, 20 * jb:20 * jb + 20], T.kmi[:, jb:60:3], ["kmi"], ["st0"])
+
+    cp(T.blist0[:, :], T.booki[:, 0:1024], ["bookA"], ["blist0"])
+    cp(T.Z[:, 2048:4096], T.truv[:, :].indirect(T.sgl[:, 128:256]), ["truv", "sgl"], ["ZB"])
+    c, its = 0, []
+    for (chs, nm) in ((S0_CH, "J"), (V0_CH, "V")):
+        for i in range(len(chs)):
+            its.append((c, chs[i], nm + "0%d" % i, nm))
+            c += chs[i]
+    for (c, n, k, nm) in its:
+        (act if nm == "J" else cp)(T.G[:, 16 * c:16 * (c + n)], Zall.indirect(T.blist0[:, c:c + n]), Zk + ["blist0"], [k])
+    consts()
+    for jb in range(3):
+        ts(T.kl[:, jb:57:3], T.st0[:, 20 * jb + 1:20 * jb + 20], 16.0, A.mult, ["st0"], ["kl"], 16.0, A.add)
+    for i in range(2):
+        ts(T.kl2[:, 3 * i:3 * i + 3], T.st0[:, 0:60:20], 16.0, A.mult, ["st0"], ["kl2"], 16.0, A.add)
+    for (c, n, k, nm) in its[len(S0_CH):] + its[:len(S0_CH)]:
+        scan(T.ysc[:, 1 + 16 * c:1 + 16 * (c + n)], T.rst[:, 0:16 * n], T.G[:, 16 * c:16 * (c + n)], A.max, A.min, ["rst", k], ["Y"])
+    for k in ("J", "V"):
+        for i in range(8):
+            wr.pop(k + "0%d" % i, None)
+    Sk = ["S0", "S1", "Spad"]
+    C = T.colf
+    ywin = T.ysc[:, :]
+
+    def sinit(a, b, key):
+        act(T.S[:, a:b], T.iot[:, :].indirect(T.sgl[:, a // 16:b // 16]), ["iot", "sgl"], [key])
+
+    for t in range(VI):
+        st, stk = T["st%d" % t], "st%d" % t
+        last = t == VI - 1
+        M = 2 if t == 0 else 4
+        cp(T.y00[:, :], ywin.indirect(T.kl2[:, 0:6]), ["Y", "kl2"], ["y00"])
+        act(T.y[:, 384:480], ywin.indirect(T.kl[:, 24:30]), ["Y", "kl"], ["yS1"])
+        cp(T.y[:, 0:384], ywin.indirect(T.kl[:, 0:24]), ["Y", "kl"], ["yV"])
+        act(T.y[:, 480:912], ywin.indirect(T.kl[:, 30:57]), ["Y", "kl"], ["yS2"])
+        if t == 0:
+            sinit(0, 2048, "S0")
+        for i in range(5):
+            mm(T.ps0[:, 96 * i:96 * i + 96], T.idb[:, :], T.y00[:, :], ["idb", "y00"], ["B0"])
+        for i in range(5):
+            n = 96 if i < 4 else 48
+            mm(T.ps1[:, 96 * i:96 * i + n], T.idb[:, :], T.y00[:, 0:n], ["idb", "y00"], ["B1"])
+
+        def yslot(k):
+            return T.y[:, 48 * (k - 1):48 * k], ("yV" if k <= 8 else ("yS1" if k <= 10 else "yS2"))
+
+        def usum(k, p):
+            ap, key = yslot(k)
+            mm(T.ps2[0:48, p:160:20], ap, T.usel[:, :], [key, "usel"], ["B2"])
+
+        def csum(k):
+            mm(T.ps3[0:48, 20 - k:160:20], T.lt[:, 48 * (k - 1):48 * k], T.cntw[:, :], ["lt1" if k <= 10 else "lt2", "cntw"], ["B3"])
+
+        usum(1 + t, 0)
+        for k in range(1, 11):
+            usum(k, 20 - k)
+        tt(T.lt[:, 0:480], T.y[:, 0:480], T.ps0[:, 0:480], A.is_lt, ["yV", "yS1", "B0"], ["lt1"])
+        for k in range(1, 11):
+            csum(k)
+        tt(T.lt[:, 480:912], T.y[:, 480:912], T.ps1[:, 0:432], A.is_lt, ["yS2", "B1"], ["lt2"])
+        for k in range(11, 20):
+            csum(k)
+        for k in range(11, 20):
+            usum(k, 20 - k)
+        if t == 0:
+            cp(T.lb[:, :], T.lbi[:, :], ["lbi"], ["lb"])
+        ts(T.xx[0:48, :], T.ps3[0:48, 0:160], 272.0, A.is_lt, ["B3"], ["xx"], B2, A.mult)
+        scan(T.su[0:48, 160:320], T.ps3[0:48, 0:160], T.kd1[0:48, :], A.max, A.min, ["B3", "kd1"], ["suk"])
+        tt(T.d1u[0:48, :], T.ps2[0:48, 0:160], T.xx[0:48, :], A.subtract, ["B2", "xx"], ["d1u"])
+        scan(T.su[0:48, 0:160], T.xx[0:48, :], T.d1u[0:48, :], A.min, A.max, ["xx", "d1u"], ["suu"])
+        mm(T.ps5[0:16, 0:48], T.su[0:48, 19:320:20], T.idf[0:48, 0:48], ["suk", "suu", "idf"], ["B5"])
+        cp(T.xt[0:16, :], T.ps5[0:16, 0:48], ["B5"], ["xt"])
+        mm(T.ps5[:, 64:112], T.e0[0:16, :], T.xt[0:16, :], ["e0", "xt"], ["B5"])
+        mm(T.ps5[:, 112:160], T.e1[0:16, :], T.xt[0:16, :], ["e1", "xt"], ["B5"])
+        scan(T.selo[:, :], T.selc[:, :], T.ps5[:, 64:160], A.add, A.max, ["selc", "B5"], ["selo"])
+        uI, uU, uV, uQ, uF, uN, uM = [T.uint[:, 4 * i:4 * i + 3] for i in range(7)]
+        def eqold(jb):
+            if M == 4:
+                ts(T.eqo[:, 20 * jb:20 * jb + 20], T.iof[:, 0:20], T.ko[:, jb:jb + 1], A.is_equal, ["iof", "ko"], ["eqo"])
+
+        def prold(a):
+            if M == 4:
+                tt(T.pr[:, 60 * a - 60:60 * a], st[:, 60 * a:60 * a + 60], T.eqo[:, :], A.mult, [stk, "eqo"], ["pr"])
+
+        cp(uI, T.selo[:, 15:48:16], ["selo"], ["uI"])
+        ts(T.ko[:, :], T.selo[:, 63:96:16], C[:, 8:9], A.subtract, ["selo", "c8"], ["ko"], -1.0, A.mult)
+        ts(uU, uI, 4095, A.bitwise_and, ["uI"], ["uU"])
+        eqold(0)
+        eqold(1)
+        ts(uV, uU, 1184.0, A.add, ["uU"], ["uV"])
+        eqold(2)
+        tt(uQ, uU, uV, A.mult, ["uU", "uV"], ["uQ"])
+        prold(1)
+        ts(uF, uQ, 5, A.arith_shift_right, ["uQ"], ["uF"], 1023, A.bitwise_and)
+        prold(2)
+        cadd = 0.0 if t == 0 else T.cc[:, 0:1]
+        ck = [] if t == 0 else ["cc"]
+        ts(T.nl[:, 0:3], uF, cadd, A.add, ["uF"] + ck, ["nl"])
+        bwin = T.booki[:, :]
+        if M == 4:
+            scan(T.osm[:, :], T.sumr[:, :], T.pr[:, :], A.mult, A.add, ["sumr", "pr"], ["osm"])
+        cp(T.bkl[:, :], bwin.indirect(T.nl[:, 0:3]), ["bookA", "bookB", "nl"], ["bkl"])
+        if M == 4:
+            ts(T.owno[:, :], T.osm[:, 19:120:20], -1.0, A.add, ["osm"], ["owno"])
+            ts(T.zz[:, :], T.osm[:, 19:120:20], 0.0, A.is_equal, ["osm"], ["zz"], 16387.0, A.mult)
+        act(T.zc[:, 384:768], Zall.indirect(T.bkl[:, 24:48]), Zk + ["bkl"], ["zcS"])
+        cp(T.zc[:, 0:384], Zall.indirect(T.bkl[:, 0:24]), Zk + ["bkl"], ["zcV"])
+        if t == 0:
+            cp(T.blist[:, 0:1024 - 2 * PH:2], T.booki[:, PH:512], ["bookA"], ["blist"])
+            cp(T.blist[:, 1:1024 - 2 * PH:2], T.booki[:, 512 + PH:1024], ["bookA"], ["blist"])
+            sinit(2048, 4096, "S1")
+        for p in range(16):
+            mm(T.ps4[0:48, p:256:16], T.zc[:, p:768:16], T.scw[:, :], ["zcS", "zcV", "scw"], ["B4"])
+        if M == 4:
+            tt(T.f6[:, :], T.owno[:, :], T.zz[:, :], A.add, ["owno", "zz"], ["f6"])
+            for jb in range(3):
+                E("s", lambda e, jb=jb: e.activation(out=T.dd[:, 32 * jb:32 * jb + 16], in_=T.dm[:, 0:16], func=AF.Copy, scale=T.f6[:, jb:jb + 1]), ["dm", "f6"], ["ddS"])
+            for jb in range(3):
+                ts(T.dd[:, 32 * jb + 16:32 * jb + 32], T.dm[:, 0:16], T.f6[:, 3 + jb:4 + jb], A.mult, ["dm", "f6"], ["ddV"])
+        scan(T.sk[0:48, :], T.srst[0:48, :], T.ps4[0:48, 0:256], A.add, A.max, ["srst", "B4"], ["sk"])
+        cp(T.ki[0:48, :], T.sk[0:48, 15:256:16], ["sk"], ["ki"])
+        ts(T.nl6[:, 0:6:2], uF, cadd, A.add, ["uF"] + ck, ["nl6"])
+        if M == 4:
+            ts(T.owno2[:, :], T.owno[:, :], C[:, 10:11], A.add, ["owno", "c10"], ["owno2"])
+        ts(T.kia[0:48, :], T.ki[0:48, :], 15, A.bitwise_and, ["ki"], ["kia"])
+        ts(T.nl6[:, 1:6:2], uF, cadd, A.add, ["uF"] + ck, ["nl6"])
+        cp(T.kb[0:48, :], T.kia[0:48, :], ["kia"], ["kb"])
+        cp(T.bk2[:, :], bwin.indirect(T.nl6[:, :]), ["bookA", "bookB", "nl6"], ["bk2"])
+        mm(T.ps6[0:8, 0:96], T.kb[0:48, 0:8], T.pmx[0:48, 0:96], ["kb", "pmx"], ["B6"], True, False)
+        mm(T.ps6[0:8, 0:96], T.kb[0:48, 8:16], T.pmx[0:48, 96:192], ["kb", "pmx"], ["B6"], False, True)
+        cp(T.xp[0:8, :], T.ps6[0:8, 0:96], ["B6"], ["xp"])
+        mm(T.ps6[:, 96:192], T.e8[0:8, :], T.xp[0:8, :], ["e8", "xp"], ["B6"])
+        if M == 4:
+            mm(T.ps7[:, 0:96], T.bof[:, :], T.dd[:, :], ["bof", "ddS", "ddV"], ["B7"])
+        ts(T.em[:, :], T.ps6[:, 96:192], C[:, 4:5], A.is_equal, ["B6", "c4"], ["em"])
+        tt(T.mb[:, :], T.em[:, :], T.bk2[:, :], A.mult, ["em", "bk2"], ["mb"])
+        mm(T.ps6[:, 192:288], T.bof[:, :], T.mb[:, :], ["bof", "mb"], ["B6"])
+        if M == 4:
+            for jb in range(3):
+                ts(T.fn[:, 64 * jb + 32:64 * jb + 64], T.ps7[:, 32 * jb:32 * jb + 32], C[:, 10:11], A.add, ["B7", "c10"], ["fn"])
+            for o in range(2):
+                tt(T.dn[:, 2 + o:12:4], T.f6[:, 3 * o:3 * o + 3], T.pad8[:, 14 + o:24:4], A.subtract, ["f6", "pad8"], ["dnO"])
+        scan(T.nsel[:, :], T.selc2[:, :], T.ps6[:, 192:288], A.add, A.max, ["selc2", "B6"], ["nsel"])
+        R = 16 * M
+        if M == 2:
+            ts(T.fn[:, 0:96], T.ps6[:, 192:288], C[:, 10:11], A.add, ["B6", "c10"], ["fn"])
+        else:
+            for jb in range(3):
+                ts(T.fn[:, 64 * jb:64 * jb + 32], T.ps6[:, 192 + 32 * jb:224 + 32 * jb], C[:, 10:11], A.add, ["B6", "c10"], ["fn"])
+        def early(now):
+            if not now:
+                return
+            ts(uN, uF, cadd, A.add, ["uF"] + ck, ["uN"])
+            ts(T.kz[:, :], T.ko[:, :], 20.0, A.is_equal, ["ko"], ["kz"], float(t + 1 - 20), A.mult)
+            ts(T.val6[:, :], T.ownn[:, :], 1.0, A.add, ["ownn"], ["val6"])
+            ts(uM, uN, 1023, A.bitwise_and, ["uN"], ["uM"])
+            tt(T.kst[:, :], T.kz[:, :], T.ko[:, :], A.add, ["kz", "ko"], ["kst"])
+            cp(T.nK[:, :], uM, ["uM"], ["nK"])
+            for jb in range(3):
+                ts(T.neq[:, 20 * jb:20 * jb + 20], T.iof[:, 0:20], T.kst[:, jb:jb + 1], A.not_equal, ["iof", "kst"], ["neq"])
+            for jb in range(3):
+                ts(T.xs[:, 20 * jb:20 * jb + 20], T.iof[:, 0:20], T.kst[:, jb:jb + 1], A.is_equal, ["iof", "kst", "nK"], ["xs"], T.nK[:, jb:jb + 1], A.mult)
+            if last:
+                ts(T.lzz[:, 0:120], st[:, 60:180], -1.0, A.add, [stk], ["lz"])
+            for a in range(3):
+                old = st[:, 60 * a:60 * a + 60] if a == 0 or not last else T.lzz[:, 60 * a - 60:60 * a]
+                tt(T.ts3[:, 60 * a:60 * a + 60], old, T.neq[:, :], A.mult, [stk, "neq", "lz"] + (["st0n"] if t == 0 else []), ["ts3"])
+            if last:
+                fin_part(0)
+
+        def fin_part(a):
+            for jb in range(3):
+                c = 60 * a + 20 * jb
+                tt(T.sf[:, 60 * a + jb:60 * a + 60:3], T.ts3[:, c:c + 20], T.xs[:, c:c + 20], A.add, ["ts3", "xs"], ["sf"])
+
+        tiles = []
+        for jb in range(3):
+            for m in range(M):
+                e = 15 + 16 * (2 * jb + m)
+                col = T.nsel[:, e:e + 1] if m < 2 else T.owno2[:, 3 * (m - 2) + jb:3 * (m - 2) + jb + 1]
+                b = 192 * len(tiles)
+                key = "e_%d" % len(tiles)
+                ts(T.eqb[:, b:b + R * (3 - jb)], T.fn[:, R * jb:3 * R], col, A.is_equal, ["fn", "nsel", "owno2"] if m >= 2 else ["fn", "nsel"], [key])
+                tiles.append((jb, b, key))
+            if jb == 0:
+                ts(T.ownn[:, :], T.nsel[:, 15:96:16], C[:, 10:11], A.subtract, ["nsel", "c10"], ["ownn"])
+        for jb in range(3):
+            todo = [(T.bob, "bob", b + R * (jb - j2), key) for (j2, b, key) in tiles if j2 < jb] + [(T.thr, "thr", b, key) for (j2, b, key) in tiles if j2 == jb]
+            for i in range(len(todo)):
+                wm, wk, b, key = todo[i]
+                mm(T.ps7[:, 128 + R * jb:128 + R * jb + R], wm[:, :], T.eqb[:, b:b + R], [wk, key], ["B7"], i == 0, i == len(todo) - 1)
+        LW = 3 * M
+        cp(T.pl[:, 0:LW:M], T.ownn[:, 1:6:2], ["ownn"], ["pl"])
+        cp(T.pl[:, 1:LW:M], T.ownn[:, 0:6:2], ["ownn"], ["pl"])
+        if M == 4:
+            cp(T.pl[:, 2:12:4], T.owno[:, 3:6], ["owno"], ["pl"])
+            cp(T.pl[:, 3:12:4], T.owno[:, 0:3], ["owno"], ["pl"])
+        if not last:
+            act(T.zp[:, 0:16 * LW], Zall.indirect(T.pl[:, 0:LW]), Zk + ["pl"], ["zp"])
+        act(T.sp[:, 0:16 * LW], T.S[:, :].indirect(T.pl[:, 0:LW]), Sk + ["pl"], ["sp"])
+        for s_ in range(2):
+            tt(T.dn[:, s_:LW:M], T.ownn[:, s_:6:2], T.pad8[:, 12 + s_:12 + LW:M], A.subtract, ["ownn", "pad8"], ["dnN"])
+        early(last)
+        tt(T.cm[:, 0:3 * R], T.ps7[:, 128:128 + 3 * R], T.dm[:, 0:3 * R], A.mult, ["B7", "dm"], ["cm"])
+        for jb in range(3):
+            red(T.m3[:, jb:jb + 1], T.cm[:, R * jb:R * jb + R], A.max, ["cm"], ["m3"])
+        dk = ["dnN", "dnO"] if M == 4 else ["dnN"]
+        for jb in range(3):
+            ts(T.of1[:, M * jb:M * jb + M], T.dn[:, M * jb:M * jb + M], T.m3[:, jb:jb + 1], A.add, dk + ["m3"], ["of1"], 0.0, A.min)
+        tt(T.of2[:, 0:LW], T.of1[:, 0:LW], T.pad8[:, 0:LW], A.add, ["of1", "pad8"], ["of2"])
+        cp(T.offs[:, 0:LW], T.of2[:, 0:LW], ["of2"], ["offs"])
+        if not last:
+            cp(Zall.indirect(T.offs[:, 0:LW]), T.zp[:, 0:16 * LW], ["offs", "zp"], Zk)
+        if not last:
+            ts(T.hitb[:, :], T.ko[:, :], 19.5, A.is_lt, ["ko"], ["hitb"])
+            mm(T.ps7[:, 384:387], T.onb[:, :], T.hitb[:, :], ["onb", "hitb"], ["B7"])
+        early(not last)
+        for q in range(2):
+            ts(T.acc[:, q:6:2], T.m3[:, :], 12288.0, A.is_lt, ["m3"], ["acc"])
+        tt(T.ab6[:, :], T.val6[:, :], T.acc[:, 0:6], A.mult, ["val6", "acc"], ["ab6"])
+        if last:
+            ts(T.ab6[:, :], T.ab6[:, :], -1.0, A.add, ["ab6"], ["ab6"])
+        for jb in range(3):
+            for a in range(1, 3):
+                c = 60 * a + 20 * jb
+                ts(T.xs[:, c:c + 20], T.iof[:, 0:20], T.kst[:, jb:jb + 1], A.is_equal, ["iof", "kst", "ab6"], ["xs"], T.ab6[:, 2 * jb + a - 1:2 * jb + a], A.mult)
+        if not last:
+            sok = "so%d" % t
+            tt(T[sok][:, :], T.ts3[:, :], T.xs[:, :], A.add, ["ts3", "xs"], [sok])
+            dst, src_ap = nxt, T[sok][:, :]
+        else:
+            fin_part(1)
+            fin_part(2)
+            sok = "sf"
+            dst, src_ap = prv, T.sf[:, :]
+        deps("g", [sok], [])
+        rid, pid = topo.addr(dst, core)
+        en = topo.engines(core, dst)[:8]
+        g.remote_dma(out_ap=T["st%d" % (t + 1)][:, :], in_ap=src_ap, remote_sem=T.sem["arr%d" % (t + 1)], local_sem=T.sem.lsem,
+                     pid=pid, routing_id=rid, dma_engine_mask=sum(1 << e for e in en))
+        cnt["sent"] = cnt.get("sent", 0) + len(en)
+        frm = prv if not last else nxt
+        wr["st%d" % (t + 1)] = ("arr%d" % (t + 1), len(topo.engines(frm, core)[:8]), "remote")
+        cp(T.S[:, :].indirect(T.offs[:, 0:LW]), T.sp[:, 0:16 * LW], ["offs", "sp"], Sk)
+        if last:
+            dma("y", T.ys[:, :], T.S[0:128:16, 0:4096], "dout", Sk, [])
+            break
+        red(T.cc[:, :], T.ps7[:, 384:387], A.add, ["B7"], ["cc"])
+        if t == 0:
+            cp(T.la[:, :], T.lai[:, :], ["lai"], ["la"])
+        yphase(lambda i, t=t: lists(t + 1, i))
+
+    fin = T["st%d" % VI]
+    k = "st%d" % VI
+    dma("y", T.yk[:, :], fin[:, 0:60], "dout", [k], [])
+    dma("s", T.ya[:, :], fin[:, 60:120], "dout", [k], [])
+    dma("y", T.yb[:, :], fin[:, 120:180], "dout", [k], [])
+    need("y", "dout", 64)
+    need("g", "lsem", cnt["sent"])
+    for q in ("v", "s", "p", "g"):
+        need("g", semn[q], cnt[q])

@@ -2,49 +2,48 @@ from concourse.bass import DstId, RemoteDMATransfer
 from concourse.mybir import dt, AluOpType, AxisListType, ActivationFunctionType
 
 VI = 6
-PADC = 4288
-PH = 344
-P_CH = [96, 120, 128]
-S_CH = [128, 104, 68, 28, 8]
-S0_CH = [128, 128, 128, 128, 128, 80, 48, 16]
-V0_CH = [128, 112]
+PADC = 4480
+P_CH = [24, 64, 80, 96, 104]
+PH = sum(P_CH)
+S_CH = [128, 96, 48, 16]
+S0_CH = [128, 128, 128, 128, 96, 64, 32, 16]
+V0_CH = [128, 128, 48]
 YW = 1 + 16 * 1024
-B1, B2 = float(2 ** 23), float(2 ** 21)
+OFF = 2048.0
+BIG = 30000.0
+SW = 208
 
 _sb = {
     "truv": (4096, "bfloat16"), "Z": (PADC, "bfloat16"), "S": (PADC, "float32"), "iot": (4096, "float32"),
-    "booki": (1408, "int32"), "blist": (1024 - 2 * PH, "uint16"), "sgi": (256, "int32"), "sgl": (256, "uint16"),
-    "kmi": (64, "int32"),
-    "G": (16384, "bfloat16"), "blist0": (1024, "uint16"), "H": (16 * PH, "bfloat16"), "ysc": (YW, "bfloat16"), "rst": (2048, "bfloat16"), "rst8": (2048, "bfloat16"),
-    "lai": (PH, "int32"), "lbi": (PH, "int32"), "la": (PH, "uint16"), "lb": (PH, "uint16"),
-    "lzz": (240, "float32"), "pad8": (24, "float32"),
+    "booki": (2048, "int32"), "sgi": (256, "int32"), "sgl": (256, "uint16"), "kmi": (64, "int32"),
+    "G": (16384, "bfloat16"), "blist": (1024, "uint16"), "H": (16 * PH, "bfloat16"), "ysc": (YW, "bfloat16"),
+    "rst": (2048, "bfloat16"), "rst8": (2048, "bfloat16"),
+    "lai": (2 * PH, "int32"), "lbi": (2 * PH, "int32"), "la": (PH, "uint16"), "lb": (PH, "uint16"),
     "pi": (1, "int32"), "pj": (1, "int32"), "pg": (1, "int32"), "colf": (16, "float32"),
-    "iof": (128, "float32"), "iog": (128, "float32"), "ioj": (192, "float32"),
-    "idf": (128, "float32"), "idb": (128, "bfloat16"), "bof": (128, "float32"), "bob": (128, "bfloat16"),
-    "thr": (128, "bfloat16"), "thf": (128, "float32"), "onb": (128, "bfloat16"), "dm": (192, "float32"),
-    "selc": (96, "float32"), "selt": (96, "float32"), "selc2": (96, "float32"), "sel8": (8, "float32"), "cntw": (8, "bfloat16"), "usel": (8, "bfloat16"),
-    "scw": (16, "bfloat16"), "pmx": (192, "bfloat16"), "e0": (128, "float32"), "e1": (128, "float32"), "e8": (128, "bfloat16"),
-    "srst": (256, "float32"), "kd1": (160, "float32"), "padf": (12, "float32"), "sumr": (120, "float32"),
-    "kl": (58, "uint16"), "kl2": (6, "uint16"), "y00": (96, "bfloat16"), "y": (912, "bfloat16"), "lt": (912, "bfloat16"),
-    "xx": (160, "float32"), "d1u": (160, "float32"), "su": (320, "float32"), "xt": (48, "float32"), "selo": (96, "float32"),
-    "uint": (28, "int32"), "nK": (3, "float32"), "nl": (4, "uint16"), "nl6": (6, "uint16"), "bkl": (48, "uint16"), "bk2": (96, "float32"),
-    "zc": (768, "bfloat16"), "ko": (3, "float32"), "kz": (3, "float32"), "kst": (3, "float32"), "hitb": (3, "bfloat16"),
-    "eqo": (60, "float32"), "pr": (120, "float32"), "osm": (120, "float32"), "owno": (6, "float32"), "owno2": (6, "float32"), "ownn": (6, "float32"),
-    "zz": (6, "float32"), "f6": (6, "float32"), "dn": (12, "float32"), "dd": (96, "float32"),
-    "sk": (256, "float32"), "ki": (16, "int32"), "kia": (16, "int32"), "kb": (16, "bfloat16"), "xp": (96, "bfloat16"),
-    "em": (96, "float32"), "mb": (96, "float32"), "nsel": (96, "float32"), "fn": (192, "uint16"),
-    "eqb": (2304, "bfloat16"), "cm": (192, "float32"), "m3": (3, "float32"), "acc": (12, "float32"),
-    "of1": (12, "float32"), "of2": (12, "float32"), "offs": (12, "uint16"), "pl": (12, "uint16"),
-    "zp": (192, "bfloat16"), "sp": (192, "float32"), "neq": (60, "float32"), "ab6": (6, "float32"), "val6": (6, "float32"),
-    "xs": (180, "float32"), "ts3": (180, "float32"), "cc": (1, "float32"), "sf": (180, "float32"),
+    "iof": (128, "float32"), "iog": (128, "float32"), "ioj": (128, "float32"), "io8": (48, "float32"), "iob": (48, "float32"),
+    "idb": (128, "bfloat16"), "idh": (128, "float16"), "bof": (128, "float32"), "onb": (128, "bfloat16"),
+    "dm": (16, "float32"), "sel8": (8, "float32"), "cntw": (8, "bfloat16"), "usel": (8, "bfloat16"), "scw": (16, "bfloat16"),
+    "selj": (384, "float16"), "mk5": (48, "float16"), "mk6": (48, "float16"), "pst": (48, "float32"), "tmp": (192, "float32"),
+    "msk": (96, "float32"), "msk2": (64, "float32"), "pns": (64, "float32"), "hrow": (160, "bfloat16"), "crow": (160, "bfloat16"), "hrf": (160, "float32"),
+    "srst": (256, "float32"), "padf": (12, "float32"), "pado": (12, "float32"), "sumr": (126, "float32"),
+    "kl": (64, "uint16"), "y": (1008, "bfloat16"), "lt": (912, "bfloat16"),
+    "hi": (160, "float32"), "su": (160, "float32"), "uint": (64, "int32"), "nk": (16, "float16"), "pk": (48, "float32"),
+    "nl": (4, "uint16"), "bkl": (48, "uint16"), "zc": (768, "bfloat16"), "tf": (768, "float32"),
+    "sm": (32, "float32"), "hitb": (4, "bfloat16"), "eqo": (63, "float32"), "pr": (126, "float32"), "osm": (126, "float32"),
+    "dd": (96, "float32"), "sk": (256, "float32"), "kr": (16, "float32"), "qh": (16, "float16"), "pk2": (48, "float32"),
+    "fl": (10, "uint16"), "fn": (320, "float16"), "ns": (96, "float32"),
+    "eqb": (1536, "bfloat16"), "cn": (768, "bfloat16"), "dn": (12, "float32"), "of1": (12, "float32"),
+    "offs": (12, "uint16"), "pl": (12, "uint16"), "zp": (192, "bfloat16"), "sp": (192, "float32"),
+    "neq": (63, "float32"), "xs": (192, "float32"), "ts3": (192, "float32"), "cc": (1, "float32"), "sf": (180, "float32"),
+    "cur": (126, "float32"), "xn": (126, "float32"),
+    "fa": (128, "float32"), "fb": (128, "float32"), "v6": (8, "float32"), "home": (180, "float32"),
 }
 SCRATCH = {}
 for _k in _sb:
     SCRATCH[_k] = ("sbuf", [128, _sb[_k][0]], _sb[_k][1])
-for _t in range(VI + 1):
-    SCRATCH["st%d" % _t] = ("sbuf", [128, 180], "float32")
-for _t in range(VI - 1):
-    SCRATCH["so%d" % _t] = ("sbuf", [128, 180], "float32")
+for _t in range(VI):
+    SCRATCH["st%d" % _t] = ("sbuf", [128, SW], "float32")
+    SCRATCH["so%d" % _t] = ("sbuf", [128, SW], "float32")
 for _t in range(8):
     SCRATCH["ps%d" % _t] = ("psum", [128, 512], "float32")
 SEMAPHORES = ["sv", "ss", "sp_", "sg_", "lsg", "ltr", "lbk", "lbw", "lkm", "lwt", "lhf", "lhg", "dout", "lsem"] + ["arr%d" % _t for _t in range(1, VI + 1)]
@@ -116,8 +115,8 @@ def rank_program(g, core, T, topo):
     def cp(out, a, r, w):
         E("v", lambda e: e.tensor_copy(out=out, in_=a), r, w)
 
-    def scan(out, d0, d1, op0, op1, r, w):
-        E("v", lambda e: e.tensor_tensor_scan(out=out, data0=d0, data1=d1, initial=0.0, op0=op0, op1=op1), r, w)
+    def scan(out, d0, d1, op0, op1, r, w, init=0.0):
+        E("v", lambda e: e.tensor_tensor_scan(out=out, data0=d0, data1=d1, initial=init, op0=op0, op1=op1), r, w)
 
     def red(out, a, op, r, w):
         E("v", lambda e: e.tensor_reduce(out=out, in_=a, axis=AX.X, op=op), r, w)
@@ -125,8 +124,8 @@ def rank_program(g, core, T, topo):
     def ms(ap, c, w, r=()):
         E("v", lambda e: e.memset(ap, c), r, w)
 
-    def act(out, a, r, w, **kw):
-        E("s", lambda e: e.activation(out=out, in_=a, func=AF.Copy, **kw), r, w)
+    def act(out, a, r, w, func=None, **kw):
+        E("s", lambda e: e.activation(out=out, in_=a, func=AF.Copy if func is None else func, **kw), r, w)
 
     def mm(out, lhsT, rhs, r, w, start=True, stop=True):
         E("p", lambda e: e.matmul(out, lhsT, rhs, start, stop), r, w)
@@ -135,40 +134,113 @@ def rank_program(g, core, T, topo):
         E("g", lambda e: e.iota(out, pattern, base, cm, allow_small_or_imprecise_dtypes=True), [], w)
 
     dma("y", T.sgi[:, :], T.sg0[:, :], "lsg", [], ["sgi"])
-    dma("y", T.truv[:, :], T.tru[:, :], "ltr", [], ["truv"])
-    dma("s", T.booki[:, 0:1024], T.book[:, :], "lbk", [], ["bookA"])
+    dma("s", T.truv[:, :], T.tru[:, :], "ltr", [], ["truv"])
     dma("y", T.kmi[:, 60:61], T.wt[:, :], "lwt", [], ["wti"])
+    dma("y", T.booki[:, 0:1024], T.book[:, :], "lbk", [], ["bookA"])
     dma("y", T.kmi[:, 0:60], T.km0[:, :], "lkm", [], ["kmi"])
-    dma("y", T.booki[:, 1024:1408], T.book[:, 0:384], "lbw", [], ["bookB"])
+    dma("y", T.booki[:, 1024:2048], T.book[:, :], "lbw", [], ["bookB"])
 
     def halves(q, buf, o, key, sem):
         for p in range(8):
             for h in range(2):
-                eng[q].dma_start(out=buf[p + 8 * h:128:16, :], in_=T.book[p + o:128:16, 512 * h:512 * h + PH]).then_inc(T.sem[sem], 16)
+                eng[q].dma_start(out=buf[p + 8 * h:128:16, :], in_=T.book[p + o:128:16, h:h + 2 * PH]).then_inc(T.sem[sem], 16)
         note(q, [], [key], (sem, 256, "dma"))
 
     halves("y", T.lbi, 8, "lbi", "lhf")
 
-    cp(T.sgl[:, :], T.sgi[:, :], ["sgi"], ["sgl"])
-    ms(T.Z[:, 4096:PADC], 0.0, ["Zpad"])
-    ms(T.rst[:, :], 0.0, ["rst"])
-    ms(T.rst8[:, :], 0.0, ["rst8"])
-    ms(T.rst[:, 0:2048:16], 512.0, ["rst"], ["rst"])
-    ms(T.rst8[:, 0:2048:8], 512.0, ["rst8"], ["rst8"])
-    ms(T.ysc[:, 0:1], 0.0, ["Y0"])
     iota(T.pi[:, :], [[0, 1]], 0, 1, ["pi"])
     iota(T.iof[:, :], [[1, 128]], 0, 0, ["iof"])
     iota(T.iog[:, :], [[1, 8], [0, 16]], 0, 0, ["iog"])
-    iota(T.ioj[:, :], [[0, 12], [1, 16]], 0, 0, ["ioj"])
-    iota(T.kd1[:, :], [[0, 8], [1, 20]], 256, 0, ["kd1"])
-    iota(T.padf[:, :], [[16, 12]], 4096, 0, ["padf"])
-    iota(T.iot[:, :], [[1, 4096]], 0, 0, ["iot"])
+    iota(T.ioj[:, :], [[0, 8], [1, 16]], 0, 0, ["ioj"])
+    iota(T.io8[:, :], [[0, 6], [1, 8]], 0, 0, ["io8"])
+    iota(T.iob[:, :], [[256, 3], [0, 16]], 15, 0, ["iob"])
+    iota(T.hrf[:, :], [[0, 8], [1, 20]], -10, 0, ["hrf"])
+    iota(T.padf[:, :], [[32, 12]], 4096 - int(OFF), 0, ["padf"])
+    iota(T.iot[:, :], [[1, 4096]], -int(OFF), 0, ["iot"])
     halves("g", T.lai, 0, "lai", "lhg")
+    C = T.colf
+    ms(T.Z[:, 4096:PADC], 0.0, ["Zpad"])
+    ms(T.rst[:, :], 0.0, ["rst"])
+    ms(T.rst8[:, :], 0.0, ["rst8"])
+    ms(T.ysc[:, 0:1], 0.0, ["Y0"])
+    ms(T.srst[:, :], 1.0, ["srst"])
+    ms(T.sumr[:, :], 1.0, ["sumr"])
+    ms(T.crow[:, :], -17.0 * 2 ** 24, ["crow"])
+    ms(T.onb[:, :], 1.0, ["onb"])
+    ms(T.S[:, 4096:PADC], 0.0, ["Spad"])
+    ms(T.fn[:, :], BIG, ["fnO", "fnA", "fnB"])
+    for t in range(VI):
+        ms(T["so%d" % t][:, 186:SW], 0.0, ["soz%d" % t])
+    ms(T.msk[:, :], 0.0, ["msk"])
+    ms(T.msk2[:, :], 0.0, ["msk2"])
+    ms(T.rst[:, 0:2048:16], 512.0, ["rst"], ["rst"])
+    ms(T.rst8[:, 0:2048:8], 512.0, ["rst8"], ["rst8"])
+    ms(T.srst[:, 0:256:16], -1048576.0, ["srst"], ["srst"])
+    ms(T.sumr[:, 0:126:21], 0.0, ["sumr"], ["sumr"])
+    ms(T.crow[:, 0:160:20], 2.0 ** 26, ["crow"], ["crow"])
+    ts(T.pj[:, :], T.pi[:, :], 15, A.bitwise_and, ["pi"], ["pj"])
+    ts(T.pg[:, :], T.pi[:, :], 4, A.arith_shift_right, ["pi"], ["pg"])
+    cp(C[:, 0:1], T.pi[:, :], ["pi"], ["c0"])
+    cp(C[:, 1:2], T.pj[:, :], ["pj"], ["c1"])
+    cp(C[:, 2:3], T.pg[:, :], ["pg"], ["c2"])
+    ts(T.idb[:, :], T.iof[:, :], C[:, 0:1], A.is_equal, ["iof", "c0"], ["idb"])
+    ts(T.idh[:, :], T.iof[:, :], C[:, 0:1], A.is_equal, ["iof", "c0"], ["idh"])
+    ts(C[:, 3:4], C[:, 1:2], 16.0, A.mult, ["c1"], ["c3"])
+    ts(C[:, 4:5], C[:, 1:2], 2.0, A.mult, ["c1"], ["c4"])
+    for jb in range(3):
+        ts(C[:, 5 + jb:6 + jb], C[:, 0:1], -16.0 * jb, A.add, ["c0"], ["c5"])
+    ts(T.sel8[:, :], T.iof[:, 0:8], C[:, 2:3], A.is_equal, ["iof", "c2"], ["sel8"])
+    ts(T.bof[:, :], T.iog[:, :], C[:, 2:3], A.is_equal, ["iog", "c2"], ["bof"])
+    ts(T.dm[:, :], T.ioj[:, 0:16], C[:, 1:2], A.is_equal, ["ioj", "c1"], ["dm"])
+    ts(T.cntw[:, :], T.sel8[:, :], 2.0 ** 25, A.mult, ["sel8"], ["cntw"])
+    ts(T.scw[:, 0:8], T.sel8[:, :], 32.0, A.mult, ["sel8"], ["scw"])
+    ts(T.scw[:, 8:16], T.sel8[:, :], -32.0, A.mult, ["sel8"], ["scw"])
+    ts(T.hrow[:, :], T.hrf[:, :], 2.0 ** 20, A.mult, ["hrf"], ["hrow"])
+    for jb in range(3):
+        ts(T.selj[0:48, 128 * jb:128 * jb + 128], T.ioj[0:48, 0:128], C[0:48, 5 + jb:6 + jb], A.is_equal, ["ioj", "c5"], ["selj"])
+    ts(T.tmp[:, 0:48], T.io8[:, :], C[:, 2:3], A.is_gt, ["io8", "c2"], ["tmpA"], BIG, A.mult)
+    ts(T.tmp[:, 64:128], T.ioj[:, 0:64], C[:, 1:2], A.is_gt, ["ioj", "c1"], ["tmpB"], BIG, A.mult)
+    ts(T.tmp[:, 128:176], T.iob[:, :], C[:, 3:4], A.add, ["iob", "c3"], ["tmpC"])
+    ts(T.pado[:, :], T.padf[:, :], C[:, 4:5], A.add, ["padf", "c4"], ["pado"])
+    ts(T.pst[:, :], T.tmp[:, 0:48], -4.0, A.mult, ["tmpA"], ["pst"], 2 * BIG, A.add)
+    ts(T.pns[:, :], T.tmp[:, 64:128], -4.0, A.mult, ["tmpB"], ["pns"], 2 * BIG, A.add)
+    tt(T.mk6[:, :], T.tmp[:, 0:48], T.tmp[:, 128:176], A.add, ["tmpA", "tmpC"], ["mk6"])
+    for i in range(6):
+        ts(T.mk5[:, 8 * i:8 * i + 8], T.tmp[:, 8 * i:8 * i + 8], -1536.0 * (i % 2), A.add, ["tmpA"], ["mk5"])
+    cp(T.msk[:, 64:96], T.tmp[:, 64:96], ["tmpB", "msk"], ["msk"])
+    cp(T.msk2[:, 32:64], T.tmp[:, 64:96], ["tmpB", "msk2"], ["msk2"])
+    for a in range(2):
+        for jb in range(3):
+            c = 63 * a + 21 * jb
+            ts(T.cur[:, c:c + 21], T.iof[:, 0:21], 0.0, A.mult, ["iof", "pado"], ["cur"], T.pado[:, 3 * a + jb:3 * a + jb + 1], A.add)
+    cp(T.sgl[:, :], T.sgi[:, :], ["sgi"], ["sgl"])
+    cp(C[:, 9:10], T.kmi[:, 60:61], ["wti"], ["c9"])
+    ts(T.usel[:, :], T.sel8[:, :], C[:, 9:10], A.mult, ["sel8", "c9"], ["usel"])
+
     act(T.Z[:, 0:2048], T.truv[:, :].indirect(T.sgl[:, 0:128]), ["truv", "sgl"], ["ZA"])
+    cp(T.Z[:, 2048:4096], T.truv[:, :].indirect(T.sgl[:, 128:256]), ["truv", "sgl"], ["ZB"])
+    cp(T.blist[:, :], T.booki[:, 0:1024], ["bookA"], ["blist"])
     Zk = ["ZA", "ZB", "Zpad"]
     Zall = T.Z[:, :]
+    c, its = 0, []
+    for (chs, nm) in ((S0_CH, "J"), (V0_CH, "V")):
+        for i in range(len(chs)):
+            its.append((c, chs[i], nm + "0%d" % i, nm))
+            c += chs[i]
+    for (c, n, k, nm) in its:
+        (act if nm == "J" else cp)(T.G[:, 16 * c:16 * (c + n)], Zall.indirect(T.blist[:, c:c + n]), Zk + ["blist"], [k])
+    ts(T.kl[:, 0:3], T.kmi[:, 0:3], 16.0, A.mult, ["kmi"], ["kl"], 16.0, A.add)
+    ts(T.kl[:, 3:63], T.kmi[:, 0:60], 16.0, A.mult, ["kmi"], ["kl"], 16.0, A.add)
+    ts(T.fa[:, 0:60], T.kmi[:, 0:60], 2.0, A.mult, ["kmi"], ["fa"], 1.0 - 2 * PH, A.add)
+    for (c, n, k, nm) in its[len(S0_CH):] + its[:len(S0_CH)]:
+        scan(T.ysc[:, 1 + 16 * c:1 + 16 * (c + n)], T.rst[:, 0:16 * n], T.G[:, 16 * c:16 * (c + n)], A.max, A.min, ["rst", k], ["Y"])
+        if k == "V00":
+            tt(T.st0[:, 0:60], T.fa[:, 0:60], T.kmi[:, 0:60], A.max, ["fa", "kmi"], ["st0"])
+    for k in ("J", "V"):
+        for i in range(8):
+            wr.pop(k + "0%d" % i, None)
 
-    def yphase(before_tail):
+    def yphase(lists):
         c, pits, sits = 0, [], []
         for i in range(len(P_CH)):
             pits.append((c, P_CH[i], "G%d" % i, "H%d" % i))
@@ -177,346 +249,285 @@ def rank_program(g, core, T, topo):
             sits.append((c, S_CH[i], "J%d" % i))
             c += S_CH[i]
         for (c, n, k, k2) in pits:
-            act(T.G[:, 16 * c:16 * (c + n)], Zall.indirect(T.lb[:, c:c + n]), Zk + ["lb"], [k])
+            (cp if c == 0 else act)(T.G[:, 16 * c:16 * (c + n)], Zall.indirect(T.lb[:, c:c + n]), Zk + ["lb"], [k])
         for (c, n, k) in sits:
-            act(T.G[:, 16 * c:16 * (c + n)], Zall.indirect(T.blist[:, c - PH:c - PH + n]), Zk + ["blist"], [k])
-        for (c, n, k, k2) in pits:
-            tt(T.H[:, 16 * c:16 * (c + n)], Zall.indirect(T.la[:, c:c + n]), T.G[:, 16 * c:16 * (c + n)], A.min, Zk + ["la", k], [k2])
-        for (c, n, k, k2) in pits:
-            scan(T.ysc[:, 1 + 16 * c:1 + 16 * (c + n)], T.rst8[:, 0:16 * n], T.H[:, 16 * c:16 * (c + n)], A.max, A.min, ["rst8", k2], ["Y"])
-        for i in range(len(sits)):
-            (c, n, k) = sits[i]
-            before_tail(i)
+            act(T.G[:, 16 * c:16 * (c + n)], Zall.indirect(T.blist[:, c + PH:c + PH + n]), Zk + ["blist"], [k])
+        for i in range(len(pits) + 1):
+            if i < len(pits):
+                (c, n, k, k2) = pits[i]
+                tt(T.H[:, 16 * c:16 * (c + n)], Zall.indirect(T.la[:, c:c + n]), T.G[:, 16 * c:16 * (c + n)], A.min, Zk + ["la", k], [k2])
+            if i > 0:
+                (c, n, k, k2) = pits[i - 1]
+                scan(T.ysc[:, 1 + 16 * c:1 + 16 * (c + n)], T.rst8[:, 0:16 * n], T.H[:, 16 * c:16 * (c + n)], A.max, A.min, ["rst8", k2], ["Y"])
+            if i == len(pits) - 1:
+                lists()
+        for (c, n, k) in sits:
             scan(T.ysc[:, 1 + 16 * c:1 + 16 * (c + n)], T.rst[:, 0:16 * n], T.G[:, 16 * c:16 * (c + n)], A.max, A.min, ["rst", k], ["Y"])
 
-    def lists(t, i):
-        st = T["st%d" % t]
-        sk_ = "st%d" % t
-        lz, lz2, lw = T.lzz[:, 0:60], T.lzz[:, 60:120], T.lzz[:, 120:180]
-        if i == 0:
-            ts(lz, st[:, 0:60], 511.5, A.is_ge, [sk_], ["lz"], -511.5, A.mult)
-        if i == 1:
-            tt(lz2, st[:, 0:60], lz, A.add, [sk_, "lz"], ["lz2"])
-        if i == 2:
-            ts(lw, lz2, -(PH - 0.5), A.add, ["lz2"], ["lw"], 0.0, A.max)
-        if i == 3:
-            tt(T.lzz[:, 180:240], lz2, lw, A.add, ["lz2", "lw"], ["lz3"])
-        if i < 4:
-            return
-        ts(T.kl2[:, 0:3], T.lzz[:, 180:240:20], 16.0, A.mult, ["lz3"], ["kl2"], 8.0, A.add)
-        ts(T.kl2[:, 3:6], T.lzz[:, 180:240:20], 16.0, A.mult, ["lz3"], ["kl2"], 8.0, A.add)
-        for jb in range(3):
-            ts(T.kl[:, jb:57:3], T.lzz[:, 181 + 20 * jb:200 + 20 * jb], 16.0, A.mult, ["lz3"], ["kl"], 8.0, A.add)
-
-    def consts():
-        C = T.colf
-        ts(T.pj[:, :], T.pi[:, :], 15, A.bitwise_and, ["pi"], ["pj"])
-        ts(T.pg[:, :], T.pi[:, :], 4, A.arith_shift_right, ["pi"], ["pg"])
-        cp(C[:, 0:1], T.pi[:, :], ["pi"], ["c0"])
-        cp(C[:, 1:2], T.pj[:, :], ["pj"], ["c1"])
-        cp(C[:, 2:3], T.pg[:, :], ["pg"], ["c2"])
-        cp(C[:, 9:10], T.kmi[:, 60:61], ["wti"], ["c9"])
-        ts(C[:, 3:4], C[:, 1:2], 14.5, A.is_lt, ["c1"], ["c3"], B2, A.mult)
-        ts(C[:, 4:5], C[:, 1:2], -1.0, A.mult, ["c1"], ["c4"], 15.0, A.add)
-        ts(C[:, 5:6], C[:, 2:3], 16.0, A.mult, ["c2"], ["c5"], C[:, 0:1], A.add)
-        ts(C[:, 6:7], C[:, 5:6], 16.0, A.add, ["c5"], ["c6"])
-        ts(C[:, 7:8], C[:, 0:1], -8.0, A.add, ["c0"], ["c7"])
-        ts(C[:, 8:9], C[:, 3:4], 276.0, A.add, ["c3"], ["c8"])
-        ts(T.sel8[:, :], T.iof[:, 0:8], C[:, 2:3], A.is_equal, ["iof", "c2"], ["sel8"])
-        ts(T.cntw[:, :], T.sel8[:, :], 32.0, A.mult, ["sel8"], ["cntw"])
-        ts(T.usel[:, :], T.sel8[:, :], C[:, 9:10], A.mult, ["sel8", "c9"], ["usel"])
-        ts(T.scw[:, 0:8], T.sel8[:, :], 16.0, A.mult, ["sel8"], ["scw"])
-        ts(T.scw[:, 8:16], T.sel8[:, :], -16.0, A.mult, ["sel8"], ["scw"])
-        ts(T.idf[:, :], T.iof[:, :], C[:, 0:1], A.is_equal, ["iof", "c0"], ["idf"])
-        ts(T.idb[:, :], T.iof[:, :], C[:, 0:1], A.is_equal, ["iof", "c0"], ["idb"])
-        ts(T.bof[:, :], T.iog[:, :], C[:, 2:3], A.is_equal, ["iog", "c2"], ["bof"])
-        ts(T.bob[:, :], T.iog[:, :], C[:, 2:3], A.is_equal, ["iog", "c2"], ["bob"], 8192.0, A.mult)
-        ts(T.thf[:, :], T.ioj[:, 0:128], C[:, 1:2], A.is_ge, ["ioj", "c1"], ["thf"], 8192.0, A.mult)
-        tt(T.thr[:, :], T.thf[:, :], T.bof[:, :], A.mult, ["thf", "bof"], ["thr"])
-        ms(T.onb[:, :], 1.0, ["onb"])
-        ts(T.dm[:, :], T.ioj[:, :], C[:, 1:2], A.is_equal, ["ioj", "c1"], ["dm"])
-        ts(T.selt[:, :], T.ioj[:, 0:96], C[:, 1:2], A.is_le, ["ioj", "c1"], ["selt"], -B1, A.mult)
-        ts(T.selc[:, :], T.ioj[:, 0:96], C[:, 1:2], A.subtract, ["ioj", "c1"], ["selc"], 1.0, A.is_equal)
-        ts(T.selc[:, :], T.selc[:, :], B2, A.mult, ["selc"], ["selc"])
-        tt(T.selc[:, :], T.selc[:, :], T.selt[:, :], A.add, ["selc", "selt"], ["selc"])
-        ts(C[:, 10:11], C[:, 1:2], 14.5, A.is_lt, ["c1"], ["c10"], 8192.0, A.mult)
-        ts(T.selt[:, :], T.ioj[:, 0:96], C[:, 1:2], A.is_le, ["ioj", "c1"], ["selt"], -131072.0, A.mult)
-        ts(T.selc2[:, :], T.ioj[:, 0:96], C[:, 1:2], A.subtract, ["ioj", "c1"], ["selc2"], 1.0, A.is_equal)
-        ts(T.selc2[:, :], T.selc2[:, :], 8192.0, A.mult, ["selc2"], ["selc2"])
-        tt(T.selc2[:, :], T.selc2[:, :], T.selt[:, :], A.add, ["selc2", "selt"], ["selc2"])
-        ts(T.pmx[0:48, 0:96], T.iof[0:48, 0:96], C[0:48, 5:6], A.is_equal, ["iof", "c5"], ["pmx"])
-        ts(T.pmx[0:48, 96:192], T.iof[0:48, 0:96], C[0:48, 6:7], A.is_equal, ["iof", "c6"], ["pmx"])
-        ts(T.e0[0:16, :], T.iog[0:16, :], C[0:16, 0:1], A.is_equal, ["iog", "c0"], ["e0"])
-        ts(T.e1[0:16, :], T.iog[0:16, :], C[0:16, 7:8], A.is_equal, ["iog", "c7"], ["e1"])
-        ts(T.e8[0:8, :], T.iog[0:8, :], C[0:8, 0:1], A.is_equal, ["iog", "c0"], ["e8"])
-        ms(T.srst[:, :], 1.0, ["srst"])
-        ms(T.srst[:, 0:256:16], -1048576.0, ["srst"], ["srst"])
-        ms(T.sumr[:, :], 1.0, ["sumr"])
-        ms(T.sumr[:, 0:120:20], 0.0, ["sumr"], ["sumr"])
-        ts(T.pad8[:, 0:12], T.padf[:, :], C[:, 1:2], A.add, ["padf", "c1"], ["pad8"])
-        ts(T.pad8[:, 12:24], T.padf[:, :], C[:, 1:2], A.add, ["padf", "c1"], ["pad8"], 8192.0, A.add)
-        ms(T.S[:, 4096:PADC], 0.0, ["Spad"])
-        ms(T.ps3[:, 0:160], 512.0, ["B3"])
-        ms(T.st0[:, 60:180], 0.0, ["st0n"])
-        for jb in range(3):
-            cp(T.st0[:, 20 * jb:20 * jb + 20], T.kmi[:, jb:60:3], ["kmi"], ["st0"])
-
-    cp(T.blist0[:, :], T.booki[:, 0:1024], ["bookA"], ["blist0"])
-    cp(T.Z[:, 2048:4096], T.truv[:, :].indirect(T.sgl[:, 128:256]), ["truv", "sgl"], ["ZB"])
-    c, its = 0, []
-    for (chs, nm) in ((S0_CH, "J"), (V0_CH, "V")):
-        for i in range(len(chs)):
-            its.append((c, chs[i], nm + "0%d" % i, nm))
-            c += chs[i]
-    for (c, n, k, nm) in its:
-        (act if nm == "J" else cp)(T.G[:, 16 * c:16 * (c + n)], Zall.indirect(T.blist0[:, c:c + n]), Zk + ["blist0"], [k])
-    consts()
-    for jb in range(3):
-        ts(T.kl[:, jb:57:3], T.st0[:, 20 * jb + 1:20 * jb + 20], 16.0, A.mult, ["st0"], ["kl"], 16.0, A.add)
-    for i in range(2):
-        ts(T.kl2[:, 3 * i:3 * i + 3], T.st0[:, 0:60:20], 16.0, A.mult, ["st0"], ["kl2"], 16.0, A.add)
-    for (c, n, k, nm) in its[len(S0_CH):] + its[:len(S0_CH)]:
-        scan(T.ysc[:, 1 + 16 * c:1 + 16 * (c + n)], T.rst[:, 0:16 * n], T.G[:, 16 * c:16 * (c + n)], A.max, A.min, ["rst", k], ["Y"])
-    for k in ("J", "V"):
-        for i in range(8):
-            wr.pop(k + "0%d" % i, None)
     Sk = ["S0", "S1", "Spad"]
-    C = T.colf
     ywin = T.ysc[:, :]
+    bwin = T.booki[:, :]
+    twin = T.tf[:, :]
 
     def sinit(a, b, key):
-        act(T.S[:, a:b], T.iot[:, :].indirect(T.sgl[:, a // 16:b // 16]), ["iot", "sgl"], [key])
+        act(T.S[:, a:b], T.iot[:, :].indirect(T.sgl[:, a // 16:b // 16]), ["iot", "sgl"], [key], bias=OFF)
+
+    def statics():
+        mm(T.ps2[0:48, 0:160], T.onb[0:1, 0:48], T.hrow[0:1, :], ["onb", "hrow"], ["B2"], True, False)
+        mm(T.ps3[0:48, 0:160], T.onb[0:1, 0:48], T.crow[0:1, :], ["onb", "crow"], ["B3"], True, False)
+        mm(T.ps5[:, 0:48], T.idh[:, :], T.mk5[:, :], ["idh", "mk5"], ["B5"], True, False)
+        mm(T.ps6[:, 0:48], T.idh[:, :], T.mk6[:, :], ["idh", "mk6"], ["B6"], True, False)
 
     for t in range(VI):
         st, stk = T["st%d" % t], "st%d" % t
+        so, soz = T["so%d" % t], "soz%d" % t
         last = t == VI - 1
-        M = 2 if t == 0 else 4
-        cp(T.y00[:, :], ywin.indirect(T.kl2[:, 0:6]), ["Y", "kl2"], ["y00"])
-        act(T.y[:, 384:480], ywin.indirect(T.kl[:, 24:30]), ["Y", "kl"], ["yS1"])
-        cp(T.y[:, 0:384], ywin.indirect(T.kl[:, 0:24]), ["Y", "kl"], ["yV"])
-        act(T.y[:, 480:912], ywin.indirect(T.kl[:, 30:57]), ["Y", "kl"], ["yS2"])
-        if t == 0:
+        old = t > 0
+        LW = 12 if old else 6
+        statics()
+        act(T.y[:, 0:96], ywin.indirect(T.kl[:, 0:6]), ["Y", "kl"], ["y00"])
+        cp(T.y[:, 96:416], ywin.indirect(T.kl[:, 6:26]), ["Y", "kl"], ["yA"])
+        act(T.y[:, 416:768], ywin.indirect(T.kl[:, 26:48]), ["Y", "kl"], ["yB"])
+        act(T.y[:, 768:1008], ywin.indirect(T.kl[:, 48:63]), ["Y", "kl"], ["yC"])
+        for i in range(4):
+            n = 96 if i < 3 else 48
+            mm(T.ps0[:, 96 * i:96 * i + n], T.idb[:, :], T.y[:, 0:n], ["idb", "y00"], ["B0"])
+        chunks = [(1, 6, ["yA"]), (7, 13, ["yA", "yB"]), (14, 19, ["yB", "yC"])]
+
+        def usum(k, p, keys, stop=False):
+            mm(T.ps2[0:48, p:160:20], T.y[:, 48 * k + 48:48 * k + 96], T.usel[:, :], keys + ["usel"], ["B2"], False, stop)
+
+        def csum(k, key):
+            mm(T.ps3[0:48, 20 - k:160:20], T.lt[:, 48 * (k - 1):48 * k], T.cntw[:, :], [key, "cntw"], ["B3"], False, k == 19)
+
+        def less(i):
+            k0, k1, keys = chunks[i]
+            tt(T.lt[:, 48 * (k0 - 1):48 * k1], T.y[:, 48 * k0 + 48:48 * k1 + 96], T.ps0[:, 0:48 * (k1 - k0 + 1)], A.is_lt, keys + ["B0"], ["lt%d" % i])
+
+        def arrived(a):
+            for jb in range(3):
+                c = 63 * a + 21 * jb
+                ts(T.xn[:, c:c + 21], T.iof[:, 0:21], st[:, 198 + jb:199 + jb], A.is_equal, ["iof", stk], ["xn"], st[:, 186 + 3 * a + jb:187 + 3 * a + jb], A.mult)
+
+        usum(1 + t, 0, ["yA"])
+        for k in range(1, 7):
+            usum(k, 20 - k, ["yA"])
+        less(0)
+        less(1)
+        less(2)
+        for k in range(1, 7):
+            csum(k, "lt0")
+        for k in range(7, 20):
+            usum(k, 20 - k, ["yA", "yB"] if k < 14 else ["yB", "yC"], k == 19)
+        act(T.hi[0:48, :], T.ps2[0:48, 0:160], ["B2"], ["hi"])
+        for k in range(7, 20):
+            csum(k, "lt1" if k < 14 else "lt2")
+        if old:
+            lw0 = 12 if t > 1 else 6
+            cp(T.S[:, :].indirect(T.offs[:, 0:lw0]), T.sp[:, 0:16 * lw0], ["offs", "sp"], Sk)
+            red(T.cc[:, :], T.ps1[:, 0:3], A.add, ["B1"], ["cc"])
+        else:
             sinit(0, 2048, "S0")
-        for i in range(5):
-            mm(T.ps0[:, 96 * i:96 * i + 96], T.idb[:, :], T.y00[:, :], ["idb", "y00"], ["B0"])
-        for i in range(5):
-            n = 96 if i < 4 else 48
-            mm(T.ps1[:, 96 * i:96 * i + n], T.idb[:, :], T.y00[:, 0:n], ["idb", "y00"], ["B1"])
-
-        def yslot(k):
-            return T.y[:, 48 * (k - 1):48 * k], ("yV" if k <= 8 else ("yS1" if k <= 10 else "yS2"))
-
-        def usum(k, p):
-            ap, key = yslot(k)
-            mm(T.ps2[0:48, p:160:20], ap, T.usel[:, :], [key, "usel"], ["B2"])
-
-        def csum(k):
-            mm(T.ps3[0:48, 20 - k:160:20], T.lt[:, 48 * (k - 1):48 * k], T.cntw[:, :], ["lt1" if k <= 10 else "lt2", "cntw"], ["B3"])
-
-        usum(1 + t, 0)
-        for k in range(1, 11):
-            usum(k, 20 - k)
-        tt(T.lt[:, 0:480], T.y[:, 0:480], T.ps0[:, 0:480], A.is_lt, ["yV", "yS1", "B0"], ["lt1"])
-        for k in range(1, 11):
-            csum(k)
-        tt(T.lt[:, 480:912], T.y[:, 480:912], T.ps1[:, 0:432], A.is_lt, ["yS2", "B1"], ["lt2"])
-        for k in range(11, 20):
-            csum(k)
-        for k in range(11, 20):
-            usum(k, 20 - k)
-        if t == 0:
-            cp(T.lb[:, :], T.lbi[:, :], ["lbi"], ["lb"])
-        ts(T.xx[0:48, :], T.ps3[0:48, 0:160], 272.0, A.is_lt, ["B3"], ["xx"], B2, A.mult)
-        scan(T.su[0:48, 160:320], T.ps3[0:48, 0:160], T.kd1[0:48, :], A.max, A.min, ["B3", "kd1"], ["suk"])
-        tt(T.d1u[0:48, :], T.ps2[0:48, 0:160], T.xx[0:48, :], A.subtract, ["B2", "xx"], ["d1u"])
-        scan(T.su[0:48, 0:160], T.xx[0:48, :], T.d1u[0:48, :], A.min, A.max, ["xx", "d1u"], ["suu"])
-        mm(T.ps5[0:16, 0:48], T.su[0:48, 19:320:20], T.idf[0:48, 0:48], ["suk", "suu", "idf"], ["B5"])
-        cp(T.xt[0:16, :], T.ps5[0:16, 0:48], ["B5"], ["xt"])
-        mm(T.ps5[:, 64:112], T.e0[0:16, :], T.xt[0:16, :], ["e0", "xt"], ["B5"])
-        mm(T.ps5[:, 112:160], T.e1[0:16, :], T.xt[0:16, :], ["e1", "xt"], ["B5"])
-        scan(T.selo[:, :], T.selc[:, :], T.ps5[:, 64:160], A.add, A.max, ["selc", "B5"], ["selo"])
-        uI, uU, uV, uQ, uF, uN, uM = [T.uint[:, 4 * i:4 * i + 3] for i in range(7)]
-        def eqold(jb):
-            if M == 4:
-                ts(T.eqo[:, 20 * jb:20 * jb + 20], T.iof[:, 0:20], T.ko[:, jb:jb + 1], A.is_equal, ["iof", "ko"], ["eqo"])
-
-        def prold(a):
-            if M == 4:
-                tt(T.pr[:, 60 * a - 60:60 * a], st[:, 60 * a:60 * a + 60], T.eqo[:, :], A.mult, [stk, "eqo"], ["pr"])
-
-        cp(uI, T.selo[:, 15:48:16], ["selo"], ["uI"])
-        ts(T.ko[:, :], T.selo[:, 63:96:16], C[:, 8:9], A.subtract, ["selo", "c8"], ["ko"], -1.0, A.mult)
+            cp(T.lb[:, :], T.lbi[:, 0:2 * PH:2], ["lbi"], ["lb"])
+        scan(T.su[0:48, :], T.ps3[0:48, 0:160], T.hi[0:48, :], A.max, A.min, ["B3", "hi"], ["su"])
+        x = T.su[0:48, 19:160:20]
+        uI, uU, uQ, uA, uF, uB = [T.uint[0:48, 8 * i:8 * i + 8] for i in range(6)]
+        cp(uI, x, ["su"], ["uI"])
+        ts(T.nk[0:48, 8:16], x, -2.0 ** -20, A.mult, ["su"], ["nkk"], 1546.49609375, A.add)
         ts(uU, uI, 4095, A.bitwise_and, ["uI"], ["uU"])
-        eqold(0)
-        eqold(1)
-        ts(uV, uU, 1184.0, A.add, ["uU"], ["uV"])
-        eqold(2)
-        tt(uQ, uU, uV, A.mult, ["uU", "uV"], ["uQ"])
-        prold(1)
+        tt(uQ, uU, uU, A.mult, ["uU"], ["uQ"])
+        ts(uA, uU, 37.0, A.mult, ["uU"] + (["cc"] if old else []), ["uA"], T.cc[0:48, 0:1] if old else 0.0, A.add)
         ts(uF, uQ, 5, A.arith_shift_right, ["uQ"], ["uF"], 1023, A.bitwise_and)
-        prold(2)
-        cadd = 0.0 if t == 0 else T.cc[:, 0:1]
-        ck = [] if t == 0 else ["cc"]
-        ts(T.nl[:, 0:3], uF, cadd, A.add, ["uF"] + ck, ["nl"])
-        bwin = T.booki[:, :]
-        if M == 4:
-            scan(T.osm[:, :], T.sumr[:, :], T.pr[:, :], A.mult, A.add, ["sumr", "pr"], ["osm"])
+        ts(uB, uA, 1023, A.bitwise_and, ["uA"], ["uB"])
+        tt(T.nk[0:48, 0:8], uF, uB, A.add, ["uF", "uB"], ["nkn"])
+        for jb in range(3):
+            mm(T.ps5[:, 16 * jb:16 * jb + 16], T.selj[0:48, 128 * jb:128 * jb + 128], T.nk[0:48, :], ["selj", "nkn", "nkk"], ["B5"], False, jb == 2)
+        if old:
+            arrived(0)
+            arrived(1)
+        scan(T.pk[:, :], T.pst[:, :], T.ps5[:, 0:48], A.max, A.min, ["pst", "B5"], ["pk"])
+        n0, ko = T.pk[:, 7:48:16], T.pk[:, 15:48:16]
+
+        def kcol(jb):
+            return T.pk[:, 15 + 16 * jb:16 + 16 * jb]
+
+        def kstc(jb):
+            return so[:, 198 + jb:199 + jb]
+
+        kz, nw, nK, z2, lz, lzn = [T.sm[:, 4 * i:4 * i + 3] for i in range(6)]
+        if old:
+            tt(T.cur[:, :], st[:, 60:186], T.xn[:, :], A.add, [stk, "xn"], ["cur"])
+        cp(T.nl[:, 0:3], n0, ["pk"], ["nl"])
+        if old:
+            for jb in range(2):
+                ts(T.eqo[:, 21 * jb:21 * jb + 21], T.iof[:, 0:21], kcol(jb), A.is_equal, ["iof", "pk"], ["eqo"])
         cp(T.bkl[:, :], bwin.indirect(T.nl[:, 0:3]), ["bookA", "bookB", "nl"], ["bkl"])
-        if M == 4:
-            ts(T.owno[:, :], T.osm[:, 19:120:20], -1.0, A.add, ["osm"], ["owno"])
-            ts(T.zz[:, :], T.osm[:, 19:120:20], 0.0, A.is_equal, ["osm"], ["zz"], 16387.0, A.mult)
+        if old:
+            ts(T.eqo[:, 42:63], T.iof[:, 0:21], kcol(2), A.is_equal, ["iof", "pk"], ["eqo"])
+        ts(kz, ko, 20.0, A.is_equal, ["pk"], ["kz"], float(t + 1 - 20), A.mult)
         act(T.zc[:, 384:768], Zall.indirect(T.bkl[:, 24:48]), Zk + ["bkl"], ["zcS"])
         cp(T.zc[:, 0:384], Zall.indirect(T.bkl[:, 0:24]), Zk + ["bkl"], ["zcV"])
-        if t == 0:
-            cp(T.blist[:, 0:1024 - 2 * PH:2], T.booki[:, PH:512], ["bookA"], ["blist"])
-            cp(T.blist[:, 1:1024 - 2 * PH:2], T.booki[:, 512 + PH:1024], ["bookA"], ["blist"])
-            sinit(2048, 4096, "S1")
+        act(T.tf[:, :], T.iot[:, :].indirect(T.bkl[:, :]), ["iot", "bkl"], ["tf"])
         for p in range(16):
             mm(T.ps4[0:48, p:256:16], T.zc[:, p:768:16], T.scw[:, :], ["zcS", "zcV", "scw"], ["B4"])
-        if M == 4:
-            tt(T.f6[:, :], T.owno[:, :], T.zz[:, :], A.add, ["owno", "zz"], ["f6"])
+        if old:
+            for a in range(2):
+                tt(T.pr[:, 63 * a:63 * a + 63], T.cur[:, 63 * a:63 * a + 63], T.eqo[:, :], A.mult, ["cur", "eqo"], ["pr"])
+        tt(so[:, 198:201], kz, ko, A.add, ["kz", "pk", soz], ["kst"])
+        ts(nw, n0, 1023.5, A.is_ge, ["pk"], ["nw"], -1024.0, A.mult)
+        if old:
+            scan(T.osm[:, :], T.sumr[:, :], T.pr[:, :], A.mult, A.add, ["sumr", "pr"], ["osm"])
             for jb in range(3):
-                E("s", lambda e, jb=jb: e.activation(out=T.dd[:, 32 * jb:32 * jb + 16], in_=T.dm[:, 0:16], func=AF.Copy, scale=T.f6[:, jb:jb + 1]), ["dm", "f6"], ["ddS"])
-            for jb in range(3):
-                ts(T.dd[:, 32 * jb + 16:32 * jb + 32], T.dm[:, 0:16], T.f6[:, 3 + jb:4 + jb], A.mult, ["dm", "f6"], ["ddV"])
-        scan(T.sk[0:48, :], T.srst[0:48, :], T.ps4[0:48, 0:256], A.add, A.max, ["srst", "B4"], ["sk"])
-        cp(T.ki[0:48, :], T.sk[0:48, 15:256:16], ["sk"], ["ki"])
-        ts(T.nl6[:, 0:6:2], uF, cadd, A.add, ["uF"] + ck, ["nl6"])
-        if M == 4:
-            ts(T.owno2[:, :], T.owno[:, :], C[:, 10:11], A.add, ["owno", "c10"], ["owno2"])
-        ts(T.kia[0:48, :], T.ki[0:48, :], 15, A.bitwise_and, ["ki"], ["kia"])
-        ts(T.nl6[:, 1:6:2], uF, cadd, A.add, ["uF"] + ck, ["nl6"])
-        cp(T.kb[0:48, :], T.kia[0:48, :], ["kia"], ["kb"])
-        cp(T.bk2[:, :], bwin.indirect(T.nl6[:, :]), ["bookA", "bookB", "nl6"], ["bk2"])
-        mm(T.ps6[0:8, 0:96], T.kb[0:48, 0:8], T.pmx[0:48, 0:96], ["kb", "pmx"], ["B6"], True, False)
-        mm(T.ps6[0:8, 0:96], T.kb[0:48, 8:16], T.pmx[0:48, 96:192], ["kb", "pmx"], ["B6"], False, True)
-        cp(T.xp[0:8, :], T.ps6[0:8, 0:96], ["B6"], ["xp"])
-        mm(T.ps6[:, 96:192], T.e8[0:8, :], T.xp[0:8, :], ["e8", "xp"], ["B6"])
-        if M == 4:
-            mm(T.ps7[:, 0:96], T.bof[:, :], T.dd[:, :], ["bof", "ddS", "ddV"], ["B7"])
-        ts(T.em[:, :], T.ps6[:, 96:192], C[:, 4:5], A.is_equal, ["B6", "c4"], ["em"])
-        tt(T.mb[:, :], T.em[:, :], T.bk2[:, :], A.mult, ["em", "bk2"], ["mb"])
-        mm(T.ps6[:, 192:288], T.bof[:, :], T.mb[:, :], ["bof", "mb"], ["B6"])
-        if M == 4:
-            for jb in range(3):
-                ts(T.fn[:, 64 * jb + 32:64 * jb + 64], T.ps7[:, 32 * jb:32 * jb + 32], C[:, 10:11], A.add, ["B7", "c10"], ["fn"])
-            for o in range(2):
-                tt(T.dn[:, 2 + o:12:4], T.f6[:, 3 * o:3 * o + 3], T.pad8[:, 14 + o:24:4], A.subtract, ["f6", "pad8"], ["dnO"])
-        scan(T.nsel[:, :], T.selc2[:, :], T.ps6[:, 192:288], A.add, A.max, ["selc2", "B6"], ["nsel"])
-        R = 16 * M
-        if M == 2:
-            ts(T.fn[:, 0:96], T.ps6[:, 192:288], C[:, 10:11], A.add, ["B6", "c10"], ["fn"])
+                for o in range(2):
+                    e = 63 * o + 21 * jb + 20
+                    act(T.dd[:, 32 * jb + 16 * o:32 * jb + 16 * o + 16], T.dm[:, :], ["dm", "osm"], ["dd"], scale=T.osm[:, e:e + 1])
         else:
-            for jb in range(3):
-                ts(T.fn[:, 64 * jb:64 * jb + 32], T.ps6[:, 192 + 32 * jb:224 + 32 * jb], C[:, 10:11], A.add, ["B6", "c10"], ["fn"])
-        def early(now):
-            if not now:
-                return
-            ts(uN, uF, cadd, A.add, ["uF"] + ck, ["uN"])
-            ts(T.kz[:, :], T.ko[:, :], 20.0, A.is_equal, ["ko"], ["kz"], float(t + 1 - 20), A.mult)
-            ts(T.val6[:, :], T.ownn[:, :], 1.0, A.add, ["ownn"], ["val6"])
-            ts(uM, uN, 1023, A.bitwise_and, ["uN"], ["uM"])
-            tt(T.kst[:, :], T.kz[:, :], T.ko[:, :], A.add, ["kz", "ko"], ["kst"])
-            cp(T.nK[:, :], uM, ["uM"], ["nK"])
-            for jb in range(3):
-                ts(T.neq[:, 20 * jb:20 * jb + 20], T.iof[:, 0:20], T.kst[:, jb:jb + 1], A.not_equal, ["iof", "kst"], ["neq"])
-            for jb in range(3):
-                ts(T.xs[:, 20 * jb:20 * jb + 20], T.iof[:, 0:20], T.kst[:, jb:jb + 1], A.is_equal, ["iof", "kst", "nK"], ["xs"], T.nK[:, jb:jb + 1], A.mult)
-            if last:
-                ts(T.lzz[:, 0:120], st[:, 60:180], -1.0, A.add, [stk], ["lz"])
-            for a in range(3):
-                old = st[:, 60 * a:60 * a + 60] if a == 0 or not last else T.lzz[:, 60 * a - 60:60 * a]
-                tt(T.ts3[:, 60 * a:60 * a + 60], old, T.neq[:, :], A.mult, [stk, "neq", "lz"] + (["st0n"] if t == 0 else []), ["ts3"])
-            if last:
-                fin_part(0)
-
-        def fin_part(a):
-            for jb in range(3):
-                c = 60 * a + 20 * jb
-                tt(T.sf[:, 60 * a + jb:60 * a + 60:3], T.ts3[:, c:c + 20], T.xs[:, c:c + 20], A.add, ["ts3", "xs"], ["sf"])
-
-        tiles = []
+            sinit(2048, 4096, "S1")
+        tt(nK, n0, nw, A.add, ["pk", "nw"], ["nK"])
         for jb in range(3):
-            for m in range(M):
-                e = 15 + 16 * (2 * jb + m)
-                col = T.nsel[:, e:e + 1] if m < 2 else T.owno2[:, 3 * (m - 2) + jb:3 * (m - 2) + jb + 1]
-                b = 192 * len(tiles)
-                key = "e_%d" % len(tiles)
-                ts(T.eqb[:, b:b + R * (3 - jb)], T.fn[:, R * jb:3 * R], col, A.is_equal, ["fn", "nsel", "owno2"] if m >= 2 else ["fn", "nsel"], [key])
-                tiles.append((jb, b, key))
-            if jb == 0:
-                ts(T.ownn[:, :], T.nsel[:, 15:96:16], C[:, 10:11], A.subtract, ["nsel", "c10"], ["ownn"])
+            ts(T.neq[:, 21 * jb:21 * jb + 21], T.iof[:, 0:21], kstc(jb), A.not_equal, ["iof", "kst"], ["neq"])
+        if not last:
+            ts(z2, nK, 2.0, A.mult, ["nK"], ["z2"], 1.0 - 2 * PH, A.add)
+            ts(T.hitb[:, 0:3], ko, 19.5, A.is_lt, ["pk"], ["hitb"])
+            tt(lz, z2, nK, A.max, ["z2", "nK"], ["lz"])
+        else:
+            ts(T.fb[:, 0:60], st[:, 0:60], 0.5, A.mult, [stk], ["fb"], PH - 0.5, A.add)
+            ts(T.fa[:, 0:126], T.cur[:, :], OFF - 0.5, A.is_ge, ["cur"], ["fa"], -8192.0, A.mult)
+            tt(T.fb[:, 64:124], T.fb[:, 0:60], st[:, 0:60], A.min, [stk, "fb"], ["fb2"])
+        scan(T.sk[0:48, :], T.srst[0:48, :], T.ps4[0:48, 0:256], A.add, A.max, ["srst", "B4"], ["sk"])
+        key = T.sk[0:48, 15:256:16]
+        if not last:
+            ts(lzn, lz, -1.0, A.mult, ["lz"], ["lzn"])
+            for jb in range(3):
+                act(T.xs[:, jb:60:3], T.neq[:, 21 * jb:21 * jb + 20], ["neq", "lz", "lzn"], ["xsP"], func=AF.Identity,
+                    scale=T.sm[:, 20 + jb:21 + jb], bias=T.sm[:, 16 + jb:17 + jb])
+        MG = 1.5 * 2 ** 28
+        ts(T.kr[0:48, :], key, MG, A.add, ["sk"], ["kr"], MG, A.subtract)
+        if old:
+            tt(T.dn[:, 6:12], T.osm[:, 20:126:21], T.pado[:, 6:12], A.subtract, ["osm", "pado"], ["dnO"])
+        tt(T.qh[0:48, :], T.kr[0:48, :], key, A.subtract, ["kr", "sk"], ["qh"])
         for jb in range(3):
-            todo = [(T.bob, "bob", b + R * (jb - j2), key) for (j2, b, key) in tiles if j2 < jb] + [(T.thr, "thr", b, key) for (j2, b, key) in tiles if j2 == jb]
-            for i in range(len(todo)):
-                wm, wk, b, key = todo[i]
-                mm(T.ps7[:, 128 + R * jb:128 + R * jb + R], wm[:, :], T.eqb[:, b:b + R], [wk, key], ["B7"], i == 0, i == len(todo) - 1)
-        LW = 3 * M
-        cp(T.pl[:, 0:LW:M], T.ownn[:, 1:6:2], ["ownn"], ["pl"])
-        cp(T.pl[:, 1:LW:M], T.ownn[:, 0:6:2], ["ownn"], ["pl"])
-        if M == 4:
-            cp(T.pl[:, 2:12:4], T.owno[:, 3:6], ["owno"], ["pl"])
-            cp(T.pl[:, 3:12:4], T.owno[:, 0:3], ["owno"], ["pl"])
+            mm(T.ps6[:, 16 * jb:16 * jb + 16], T.selj[0:48, 128 * jb:128 * jb + 128], T.qh[0:48, :], ["selj", "qh"], ["B6"], False, jb == 2)
+        if old:
+            mm(T.ps7[:, 0:96], T.bof[:, :], T.dd[:, :], ["bof", "dd"], ["B7"])
+            for m in range(2):
+                ts(T.pl[:, 6 + 3 * m:9 + 3 * m], T.osm[:, 83 - 63 * m:126 - 63 * m:21], OFF, A.add, ["osm"], ["pl"])
+        if not last:
+            mm(T.ps1[:, 0:3], T.onb[:, :], T.hitb[:, 0:3], ["onb", "hitb"], ["B1"])
+            for jb in range(3):
+                tt(T.ts3[:, jb:60:3], st[:, jb:60:3], T.neq[:, 21 * jb:21 * jb + 20], A.mult, [stk, "neq"], ["ts3P"])
+        else:
+            tt(T.pr[:, :], T.cur[:, :], T.fa[:, 0:126], A.add, ["cur", "fa"], ["pr"])
+        scan(T.pk2[:, :], T.pst[:, :], T.ps6[:, 0:48], A.max, A.min, ["pst", "B6"], ["pk2"])
+        if not last:
+            tt(so[:, 60:123], T.cur[:, 0:63], T.neq[:, :], A.mult, ["cur", "neq"], ["soA"])
+        else:
+            ts(T.fa[:, 0:126], T.pr[:, :], OFF, A.add, ["pr"], ["fa"], -1.0, A.max)
+        cp(T.fl[:, 0:4], T.pk2[:, 7:32:8], ["pk2"], ["flA"])
+        cp(T.fl[:, 4:10], T.pk2[:, 7:48:8], ["pk2"], ["flB"])
+        if old:
+            cp(T.fn[:, 128:160], T.ps7[:, 0:32], ["B7"], ["fnO"])
+        tt(T.fn[:, 32:96], twin.indirect(T.fl[:, 0:4]), T.tmp[:, 64:128], A.add, ["tf", "flA", "tmpB"], ["fnA"])
+        tt(T.fn[:, 160:256], twin.indirect(T.fl[:, 4:10]), T.msk[:, :], A.add, ["tf", "flB", "msk"], ["fnB"])
+        scan(T.ns[:, 0:64], T.pns[:, :], T.fn[:, 32:96], A.max, A.min, ["pns", "fnA"], ["nsA"])
+        if old:
+            tt(T.fn[:, 256:320], T.ps7[:, 32:96], T.msk2[:, :], A.add, ["B7", "msk2"], ["fnO"])
+        scan(T.ns[:, 64:96], T.pns[:, 0:32], T.fn[:, 224:256], A.max, A.min, ["pns", "fnB"], ["nsB"])
+        reg = [(0, 64), (64, 192), (128, 320)]
+        eo = [0, 256, 768]
+        nsk = ["nsA", "nsB"]
+        M = 4 if old else 2
+
+        def eq(jb, m):
+            a, b = reg[jb]
+            w = b - a
+            col = T.ns[:, 32 * jb + 16 * m + 15:32 * jb + 16 * m + 16] if m < 2 else T.osm[:, 63 * (m - 2) + 21 * jb + 20:63 * (m - 2) + 21 * jb + 21]
+            pos = eo[jb] + w * m
+            ts(T.eqb[:, pos:pos + w], T.fn[:, a:b], col, A.is_equal, ["fnO", "fnA", "fnB"] + (["fnP"] if jb < 2 else []) + [("nsB" if jb == 2 else "nsA") if m < 2 else "osm"], ["e%d" % jb], 8192.0, A.mult)
+
+        def count(jb):
+            w = (reg[jb][1] - reg[jb][0]) * M // 2
+            o = eo[jb] // 2
+            scan(T.cn[:, o:o + w], T.eqb[:, eo[jb]:eo[jb] + w], T.eqb[:, eo[jb] + w:eo[jb] + 2 * w], A.add, A.add, ["e%d" % jb], ["cn%d" % jb], -8192.0 * M)
+            return T.cn[:, o + w - 1:o + w]
+
+        def place(jb, col):
+            ts(T.of1[:, jb:LW:3], T.dn[:, jb:LW:3], col, A.add, ["dn", "dnO", "cn%d" % jb], ["of1"], 0.0, A.min)
+
+        if old:
+            tt(T.fn[:, 0:32], T.ps7[:, 0:32], T.msk2[:, 32:64], A.add, ["B7", "msk2"], ["fnP"])
+            tt(T.fn[:, 96:128], T.ps7[:, 32:64], T.msk2[:, 32:64], A.add, ["B7", "msk2"], ["fnP"])
+        for m in list(range(2, M)) + [0, 1]:
+            eq(2, m)
+        for m in range(2):
+            ts(T.pl[:, 3 * m:3 * m + 3], T.ns[:, 31 - 16 * m:96:32], OFF, A.add, nsk, ["pl"])
         if not last:
             act(T.zp[:, 0:16 * LW], Zall.indirect(T.pl[:, 0:LW]), Zk + ["pl"], ["zp"])
         act(T.sp[:, 0:16 * LW], T.S[:, :].indirect(T.pl[:, 0:LW]), Sk + ["pl"], ["sp"])
-        for s_ in range(2):
-            tt(T.dn[:, s_:LW:M], T.ownn[:, s_:6:2], T.pad8[:, 12 + s_:12 + LW:M], A.subtract, ["ownn", "pad8"], ["dnN"])
-        early(last)
-        tt(T.cm[:, 0:3 * R], T.ps7[:, 128:128 + 3 * R], T.dm[:, 0:3 * R], A.mult, ["B7", "dm"], ["cm"])
-        for jb in range(3):
-            red(T.m3[:, jb:jb + 1], T.cm[:, R * jb:R * jb + R], A.max, ["cm"], ["m3"])
-        dk = ["dnN", "dnO"] if M == 4 else ["dnN"]
-        for jb in range(3):
-            ts(T.of1[:, M * jb:M * jb + M], T.dn[:, M * jb:M * jb + M], T.m3[:, jb:jb + 1], A.add, dk + ["m3"], ["of1"], 0.0, A.min)
-        tt(T.of2[:, 0:LW], T.of1[:, 0:LW], T.pad8[:, 0:LW], A.add, ["of1", "pad8"], ["of2"])
-        cp(T.offs[:, 0:LW], T.of2[:, 0:LW], ["of2"], ["offs"])
-        if not last:
-            cp(Zall.indirect(T.offs[:, 0:LW]), T.zp[:, 0:16 * LW], ["offs", "zp"], Zk)
-        if not last:
-            ts(T.hitb[:, :], T.ko[:, :], 19.5, A.is_lt, ["ko"], ["hitb"])
-            mm(T.ps7[:, 384:387], T.onb[:, :], T.hitb[:, :], ["onb", "hitb"], ["B7"])
-        early(not last)
-        for q in range(2):
-            ts(T.acc[:, q:6:2], T.m3[:, :], 12288.0, A.is_lt, ["m3"], ["acc"])
-        tt(T.ab6[:, :], T.val6[:, :], T.acc[:, 0:6], A.mult, ["val6", "acc"], ["ab6"])
-        if last:
-            ts(T.ab6[:, :], T.ab6[:, :], -1.0, A.add, ["ab6"], ["ab6"])
-        for jb in range(3):
-            for a in range(1, 3):
-                c = 60 * a + 20 * jb
-                ts(T.xs[:, c:c + 20], T.iof[:, 0:20], T.kst[:, jb:jb + 1], A.is_equal, ["iof", "kst", "ab6"], ["xs"], T.ab6[:, 2 * jb + a - 1:2 * jb + a], A.mult)
-        if not last:
-            sok = "so%d" % t
-            tt(T[sok][:, :], T.ts3[:, :], T.xs[:, :], A.add, ["ts3", "xs"], [sok])
-            dst, src_ap = nxt, T[sok][:, :]
-        else:
-            fin_part(1)
-            fin_part(2)
-            sok = "sf"
-            dst, src_ap = prv, T.sf[:, :]
-        deps("g", [sok], [])
-        rid, pid = topo.addr(dst, core)
-        en = topo.engines(core, dst)[:8]
-        g.remote_dma(out_ap=T["st%d" % (t + 1)][:, :], in_ap=src_ap, remote_sem=T.sem["arr%d" % (t + 1)], local_sem=T.sem.lsem,
-                     pid=pid, routing_id=rid, dma_engine_mask=sum(1 << e for e in en))
-        cnt["sent"] = cnt.get("sent", 0) + len(en)
-        frm = prv if not last else nxt
-        wr["st%d" % (t + 1)] = ("arr%d" % (t + 1), len(topo.engines(frm, core)[:8]), "remote")
-        cp(T.S[:, :].indirect(T.offs[:, 0:LW]), T.sp[:, 0:16 * LW], ["offs", "sp"], Sk)
-        if last:
-            dma("y", T.ys[:, :], T.S[0:128:16, 0:4096], "dout", Sk, [])
-            break
-        red(T.cc[:, :], T.ps7[:, 384:387], A.add, ["B7"], ["cc"])
-        if t == 0:
-            cp(T.la[:, :], T.lai[:, :], ["lai"], ["la"])
-        yphase(lambda i, t=t: lists(t + 1, i))
+        c2 = count(2)
+        for m in range(M):
+            eq(1, m)
+        for m in range(2):
+            tt(T.dn[:, 3 * m:3 * m + 3], T.ns[:, 15 + 16 * m:96:32], T.pado[:, 3 * m:3 * m + 3], A.subtract, nsk + ["pado"], ["dn"])
+        c1 = count(1)
+        for m in range(M):
+            eq(0, m)
+        place(2, c2)
+        place(1, c1)
+        c0 = count(0)
+        dst, frm = (nxt, prv) if not last else (prv, nxt)
 
-    fin = T["st%d" % VI]
-    k = "st%d" % VI
-    dma("y", T.yk[:, :], fin[:, 0:60], "dout", [k], [])
-    dma("s", T.ya[:, :], fin[:, 60:120], "dout", [k], [])
-    dma("y", T.yb[:, :], fin[:, 120:180], "dout", [k], [])
+        def send(src_ap, keys, land):
+            deps("g", keys, [])
+            rid, pid = topo.addr(dst, core)
+            en = topo.engines(core, dst)[:8]
+            g.remote_dma(out_ap=T[land][:, :], in_ap=src_ap, remote_sem=T.sem["arr%d" % (t + 1)], local_sem=T.sem.lsem,
+                         pid=pid, routing_id=rid, dma_engine_mask=sum(1 << e for e in en))
+            cnt["sent"] = cnt.get("sent", 0) + len(en)
+            wr[land] = ("arr%d" % (t + 1), len(topo.engines(frm, core)[:8]), "remote")
+
+        if last:
+            break
+        tt(so[:, 123:186], T.cur[:, 63:126], T.neq[:, :], A.mult, ["cur", "neq"], ["soB"])
+        place(0, c0)
+        tt(so[:, 0:60], T.ts3[:, 0:60], T.xs[:, 0:60], A.add, ["ts3P", "xsP"], ["soP"])
+        tt(so[:, 186:186 + LW], T.of1[:, 0:LW], T.pado[:, 0:LW], A.add, ["of1", "pado", soz], ["of2"])
+        ts(T.offs[:, 0:LW], so[:, 186:186 + LW], OFF, A.add, ["of2"], ["offs"])
+        if t == 0:
+            cp(T.la[:, :], T.lai[:, 0:2 * PH:2], ["lai"], ["la"])
+        cp(Zall.indirect(T.offs[:, 0:LW]), T.zp[:, 0:16 * LW], ["offs", "zp"], Zk)
+        send(so[:, :], ["soP", "soA", "soB", "of2", "kst", soz], "st%d" % (t + 1))
+
+        def lists():
+            s2, k2 = T["st%d" % (t + 1)], "st%d" % (t + 1)
+            ts(T.kl[:, 0:3], s2[:, 0:3], 8.0, A.mult, [k2], ["kl"], 8.0, A.add)
+            ts(T.kl[:, 3:63], s2[:, 0:60], 8.0, A.mult, [k2], ["kl"], 8.0, A.add)
+
+        yphase(lists)
+
+    cols = [c0, c1, c2]
+    ts(T.v6[:, 0:6], T.ns[:, 15:96:16], OFF, A.add, nsk, ["v6a"])
+    place(0, c0)
+    for jb in range(3):
+        tt(T.ts3[:, jb:60:3], T.fb[:, 64 + jb:124:3], T.neq[:, 21 * jb:21 * jb + 20], A.mult, ["fb2", "neq"], ["ts3P"])
+    for jb in range(3):
+        ts(T.v6[:, 2 * jb:2 * jb + 2], T.v6[:, 2 * jb:2 * jb + 2], cols[jb], A.subtract, ["v6a", "cn%d" % jb], ["v6"], -1.0, A.max)
+    for jb in range(3):
+        ts(T.xs[:, jb:60:3], T.iof[:, 0:20], kstc(jb), A.is_equal, ["iof", "kst", "nK"], ["xsP"], T.sm[:, 8 + jb:9 + jb], A.mult)
+    for a in range(2):
+        for jb in range(3):
+            c = 63 * a + 21 * jb
+            tt(T.ts3[:, 60 + 60 * a + jb:120 + 60 * a:3], T.fa[:, c:c + 20], T.neq[:, 21 * jb:21 * jb + 20], A.mult, ["fa", "neq"], ["ts3N"])
+            ts(T.xs[:, 60 + 60 * a + jb:120 + 60 * a:3], T.iof[:, 0:20], kstc(jb), A.is_equal, ["iof", "kst", "v6"], ["xsN"], T.v6[:, 2 * jb + a:2 * jb + a + 1], A.mult)
+    tt(so[:, 186:198], T.of1[:, :], T.pado[:, :], A.add, ["of1", "pado", soz], ["of2"])
+    tt(T.sf[:, :], T.ts3[:, 0:180], T.xs[:, 0:180], A.add, ["ts3P", "ts3N", "xsP", "xsN"], ["sf"])
+    send(T.sf[:, :], ["sf"], "home")
+    ts(T.offs[:, :], so[:, 186:198], OFF, A.add, ["of2"], ["offs"])
+    cp(T.S[:, :].indirect(T.offs[:, :]), T.sp[:, :], ["offs", "sp"], Sk)
+    dma("y", T.ys[:, :], T.S[0:128:16, 0:4096], "dout", Sk, [])
+    dma("y", T.yk[:, :], T.home[:, 0:60], "dout", ["home"], [])
+    dma("s", T.ya[:, :], T.home[:, 60:120], "dout", ["home"], [])
+    dma("y", T.yb[:, :], T.home[:, 120:180], "dout", ["home"], [])
     need("y", "dout", 64)
     need("g", "lsem", cnt["sent"])
     for q in ("v", "s", "p", "g"):

@@ -3,22 +3,26 @@ from concourse.mybir import dt, AluOpType, AxisListType, ActivationFunctionType
 
 VI = 6
 PADC = 4480
-P_CH = [24, 64, 80, 96, 104]
+P_CH = [48, 72, 72, 72]
 PH = sum(P_CH)
-S_CH = [128, 96, 48, 16]
-S0_CH = [128, 128, 128, 128, 96, 64, 32, 16]
-V0_CH = [128, 128, 48]
-YW = 1 + 16 * 1024
+NP = PH // 24
+N_CH = [96, 144, 96, 32, 16]
+NN = sum(N_CH)
+KN = 3 * NP + NP % 2
+K0 = KN + NN // 16 + (NN // 16) % 2
+ZS = 168
+YP, YN, YW = 768, 768 + 16 * PH, 768 + 16 * (PH + NN)
 OFF = 2048.0
 BIG = 30000.0
-SW = 208
+SW = 264
 
 _sb = {
     "truv": (4096, "bfloat16"), "Z": (PADC, "bfloat16"), "S": (PADC, "float32"), "iot": (4096, "float32"),
     "booki": (2048, "int32"), "sgi": (256, "int32"), "sgl": (256, "uint16"), "kmi": (64, "int32"),
-    "G": (16384, "bfloat16"), "blist": (1024, "uint16"), "H": (16 * PH, "bfloat16"), "ysc": (YW, "bfloat16"),
-    "rst": (2048, "bfloat16"), "rst8": (2048, "bfloat16"),
-    "lai": (2 * PH, "int32"), "lbi": (2 * PH, "int32"), "la": (PH, "uint16"), "lb": (PH, "uint16"),
+    "G": (YW, "bfloat16"), "nat": (48 + NN, "uint16"), "H": (16 * PH, "bfloat16"), "ysc": (YW, "bfloat16"),
+    "rst": (16 * max(N_CH), "bfloat16"), "rst8": (16 * max(P_CH), "bfloat16"),
+    "bhi": (1024, "int32"), "blo": (1024, "int32"), "thi": (2 * PH, "bfloat16"), "tlo": (2 * PH, "bfloat16"),
+    "hsel": (1024, "bfloat16"), "la": (PH, "uint16"), "lb": (PH, "uint16"), "ab": (63, "float32"),
     "pi": (1, "int32"), "pj": (1, "int32"), "pg": (1, "int32"), "colf": (16, "float32"),
     "iof": (128, "float32"), "iog": (128, "float32"), "ioj": (128, "float32"), "io8": (48, "float32"), "iob": (48, "float32"),
     "idb": (128, "bfloat16"), "idh": (128, "float16"), "bof": (128, "float32"), "onb": (128, "bfloat16"),
@@ -26,16 +30,15 @@ _sb = {
     "selj": (384, "float16"), "mk5": (48, "float16"), "mk6": (48, "float16"), "pst": (48, "float32"), "tmp": (192, "float32"),
     "msk": (96, "float32"), "msk2": (64, "float32"), "pns": (64, "float32"), "hrow": (160, "bfloat16"), "crow": (160, "bfloat16"), "hrf": (160, "float32"),
     "srst": (256, "float32"), "padf": (12, "float32"), "pado": (12, "float32"), "sumr": (126, "float32"),
-    "kl": (64, "uint16"), "y": (1008, "bfloat16"), "lt": (912, "bfloat16"),
+    "lt": (912, "bfloat16"),
     "hi": (160, "float32"), "su": (160, "float32"), "uint": (64, "int32"), "nk": (16, "float16"), "pk": (48, "float32"),
     "nl": (4, "uint16"), "bkl": (48, "uint16"), "zc": (768, "bfloat16"), "tf": (768, "float32"),
-    "sm": (32, "float32"), "hitb": (4, "bfloat16"), "eqo": (63, "float32"), "pr": (126, "float32"), "osm": (126, "float32"),
-    "dd": (96, "float32"), "sk": (256, "float32"), "kr": (16, "float32"), "qh": (16, "float16"), "pk2": (48, "float32"),
+    "sm": (32, "float32"), "hitb": (4, "bfloat16"), "pr": (126, "float32"), "osm": (126, "float32"),
+    "dd": (96, "float16"), "sk": (256, "float32"), "kr": (16, "float32"), "qh": (16, "float16"), "pk2": (48, "float32"),
     "fl": (10, "uint16"), "fn": (320, "float16"), "ns": (96, "float32"),
     "eqb": (1536, "bfloat16"), "cn": (768, "bfloat16"), "dn": (12, "float32"), "of1": (12, "float32"),
-    "offs": (12, "uint16"), "pl": (12, "uint16"), "zp": (192, "bfloat16"), "sp": (192, "float32"),
-    "neq": (63, "float32"), "xs": (192, "float32"), "ts3": (192, "float32"), "cc": (1, "float32"), "sf": (180, "float32"),
-    "cur": (126, "float32"), "xn": (126, "float32"),
+    "offs": (12 * VI, "uint16"), "pl": (12 * VI, "uint16"), "zp": (192, "bfloat16"), "sp": (192, "float32"),
+    "ts3": (192, "float32"), "cc": (1, "float32"), "sf": (180, "float32"), "cur": (126, "float32"), "boh": (128, "float16"),
     "fa": (128, "float32"), "fb": (128, "float32"), "v6": (8, "float32"), "home": (180, "float32"),
 }
 SCRATCH = {}
@@ -44,9 +47,12 @@ for _k in _sb:
 for _t in range(VI):
     SCRATCH["st%d" % _t] = ("sbuf", [128, SW], "float32")
     SCRATCH["so%d" % _t] = ("sbuf", [128, SW], "float32")
+    SCRATCH["kl%d" % _t] = ("sbuf", [128, 64], "uint16")
+    SCRATCH["ko%d" % _t] = ("sbuf", [128, 64], "uint16")
 for _t in range(8):
     SCRATCH["ps%d" % _t] = ("psum", [128, 512], "float32")
-SEMAPHORES = ["sv", "ss", "sp_", "sg_", "lsg", "ltr", "lbk", "lbw", "lkm", "lwt", "lhf", "lhg", "dout", "lsem"] + ["arr%d" % _t for _t in range(1, VI + 1)]
+SEMAPHORES = (["sv", "ss", "sp_", "sg_", "lsg", "ltr", "lbk", "lbw", "lkm", "lwt", "dout", "lsem"]
+              + ["a_st%d" % _t for _t in range(1, VI)] + ["a_kl%d" % _t for _t in range(1, VI)] + ["a_home"])
 
 
 def rank_program(g, core, T, topo):
@@ -75,11 +81,15 @@ def rank_program(g, core, T, topo):
                 sem, n, q2 = wr[k]
                 if not (q == "p" and q2 == "p"):
                     lst[sem] = max(lst.get(sem, 0), n)
+            if k[0] == "B":
+                for (sem, n, q2) in rd.get(k, {}).values():
+                    if q2 != q:
+                        lst[sem] = max(lst.get(sem, 0), n)
         for k in w:
             if k in wr and wr[k][2] != q:
                 lst[wr[k][0]] = max(lst.get(wr[k][0], 0), wr[k][1])
             for (sem, n, q2) in rd.get(k, {}).values():
-                if q2 != q or q == "v":
+                if q2 != q or q != "p":
                     lst[sem] = max(lst.get(sem, 0), n)
         for sem in lst:
             need(q, sem, lst[sem])
@@ -134,19 +144,11 @@ def rank_program(g, core, T, topo):
         E("g", lambda e: e.iota(out, pattern, base, cm, allow_small_or_imprecise_dtypes=True), [], w)
 
     dma("y", T.sgi[:, :], T.sg0[:, :], "lsg", [], ["sgi"])
-    dma("s", T.truv[:, :], T.tru[:, :], "ltr", [], ["truv"])
-    dma("y", T.kmi[:, 60:61], T.wt[:, :], "lwt", [], ["wti"])
+    dma("y", T.truv[:, :], T.tru[:, :], "ltr", [], ["truv"])
     dma("y", T.booki[:, 0:1024], T.book[:, :], "lbk", [], ["bookA"])
     dma("y", T.kmi[:, 0:60], T.km0[:, :], "lkm", [], ["kmi"])
+    dma("y", T.kmi[:, 60:61], T.wt[:, :], "lwt", [], ["wti"])
     dma("y", T.booki[:, 1024:2048], T.book[:, :], "lbw", [], ["bookB"])
-
-    def halves(q, buf, o, key, sem):
-        for p in range(8):
-            for h in range(2):
-                eng[q].dma_start(out=buf[p + 8 * h:128:16, :], in_=T.book[p + o:128:16, h:h + 2 * PH]).then_inc(T.sem[sem], 16)
-        note(q, [], [key], (sem, 256, "dma"))
-
-    halves("y", T.lbi, 8, "lbi", "lhf")
 
     iota(T.pi[:, :], [[0, 1]], 0, 1, ["pi"])
     iota(T.iof[:, :], [[1, 128]], 0, 0, ["iof"])
@@ -156,121 +158,216 @@ def rank_program(g, core, T, topo):
     iota(T.iob[:, :], [[256, 3], [0, 16]], 15, 0, ["iob"])
     iota(T.hrf[:, :], [[0, 8], [1, 20]], -10, 0, ["hrf"])
     iota(T.padf[:, :], [[32, 12]], 4096 - int(OFF), 0, ["padf"])
+    iota(T.rst[:, :], [[0, max(N_CH)], [-512, 16]], 512, 0, ["rst"])
+    iota(T.rst8[:, :], [[0, max(P_CH) * 2], [-512, 8]], 512, 0, ["rst8"])
     iota(T.iot[:, :], [[1, 4096]], -int(OFF), 0, ["iot"])
-    halves("g", T.lai, 0, "lai", "lhg")
     C = T.colf
+    ID = AF.Identity
     ms(T.Z[:, 4096:PADC], 0.0, ["Zpad"])
-    ms(T.rst[:, :], 0.0, ["rst"])
-    ms(T.rst8[:, :], 0.0, ["rst8"])
-    ms(T.ysc[:, 0:1], 0.0, ["Y0"])
+    ts(T.pj[:, :], T.pi[:, :], 15, A.bitwise_and, ["pi"], ["pj"])
+    ts(T.pg[:, :], T.pi[:, :], 4, A.arith_shift_right, ["pi"], ["pg"])
+    ts(T.uint[:, 0:1], T.pi[:, :], 7, A.bitwise_and, ["pi"], ["uI"])
+    cp(C[:, 0:1], T.pi[:, :], ["pi"], ["c0"])
+    cp(C[:, 1:2], T.pj[:, :], ["pj"], ["c1"])
+    cp(C[:, 2:3], T.pg[:, :], ["pg"], ["c2"])
+    cp(C[:, 10:11], T.uint[:, 0:1], ["uI"], ["c10"])
+    for t in range(VI - 1):
+        ms(T["ko%d" % t][:, :], 0, ["ko%d" % t])
+    ms(T.kl0[:, :], 0, ["kl0"])
     ms(T.srst[:, :], 1.0, ["srst"])
     ms(T.sumr[:, :], 1.0, ["sumr"])
     ms(T.crow[:, :], -17.0 * 2 ** 24, ["crow"])
     ms(T.onb[:, :], 1.0, ["onb"])
     ms(T.S[:, 4096:PADC], 0.0, ["Spad"])
     ms(T.fn[:, :], BIG, ["fnO", "fnA", "fnB"])
-    for t in range(VI):
-        ms(T["so%d" % t][:, 186:SW], 0.0, ["soz%d" % t])
-    ms(T.msk[:, :], 0.0, ["msk"])
-    ms(T.msk2[:, :], 0.0, ["msk2"])
-    ms(T.rst[:, 0:2048:16], 512.0, ["rst"], ["rst"])
-    ms(T.rst8[:, 0:2048:8], 512.0, ["rst8"], ["rst8"])
     ms(T.srst[:, 0:256:16], -1048576.0, ["srst"], ["srst"])
     ms(T.sumr[:, 0:126:21], 0.0, ["sumr"], ["sumr"])
     ms(T.crow[:, 0:160:20], 2.0 ** 26, ["crow"], ["crow"])
-    ts(T.pj[:, :], T.pi[:, :], 15, A.bitwise_and, ["pi"], ["pj"])
-    ts(T.pg[:, :], T.pi[:, :], 4, A.arith_shift_right, ["pi"], ["pg"])
-    cp(C[:, 0:1], T.pi[:, :], ["pi"], ["c0"])
-    cp(C[:, 1:2], T.pj[:, :], ["pj"], ["c1"])
-    cp(C[:, 2:3], T.pg[:, :], ["pg"], ["c2"])
-    ts(T.idb[:, :], T.iof[:, :], C[:, 0:1], A.is_equal, ["iof", "c0"], ["idb"])
-    ts(T.idh[:, :], T.iof[:, :], C[:, 0:1], A.is_equal, ["iof", "c0"], ["idh"])
-    ts(C[:, 3:4], C[:, 1:2], 16.0, A.mult, ["c1"], ["c3"])
-    ts(C[:, 4:5], C[:, 1:2], 2.0, A.mult, ["c1"], ["c4"])
+    act(C[:, 3:4], C[:, 1:2], ["c1"], ["c3"], scale=16.0)
+    act(C[:, 4:5], C[:, 1:2], ["c1"], ["c4"], scale=2.0)
     for jb in range(3):
-        ts(C[:, 5 + jb:6 + jb], C[:, 0:1], -16.0 * jb, A.add, ["c0"], ["c5"])
-    ts(T.sel8[:, :], T.iof[:, 0:8], C[:, 2:3], A.is_equal, ["iof", "c2"], ["sel8"])
+        act(C[:, 5 + jb:6 + jb], C[:, 0:1], ["c0"], ["c5"], bias=-16.0 * jb)
+    for t in range(VI):
+        act(T["so%d" % t][:, 186:SW], T.iof[:, 0:SW - 186], ["iof"], ["soz%d" % t], scale=0.0)
+    act(T.msk[:, 0:64], T.iof[:, 0:64], ["iof"], ["msk"], scale=0.0)
+    act(T.msk2[:, 0:32], T.iof[:, 0:32], ["iof"], ["msk2"], scale=0.0)
+    act(T.pado[:, :], T.padf[:, :], ["padf", "c4"], ["pado"], func=ID, bias=C[:, 4:5])
+    act(T.tmp[:, 128:176], T.iob[:, :], ["iob", "c3"], ["tmpC"], func=ID, bias=C[:, 3:4])
+    act(T.hrow[:, :], T.hrf[:, :], ["hrf"], ["hrow"], scale=2.0 ** 20)
+    ts(C[:, 11:12], C[:, 1:2], 7.5, A.is_lt, ["c1"], ["c11"])
+    ts(C[:, 12:13], C[:, 1:2], 7.5, A.is_gt, ["c1"], ["c11"])
     ts(T.bof[:, :], T.iog[:, :], C[:, 2:3], A.is_equal, ["iog", "c2"], ["bof"])
-    ts(T.dm[:, :], T.ioj[:, 0:16], C[:, 1:2], A.is_equal, ["ioj", "c1"], ["dm"])
-    ts(T.cntw[:, :], T.sel8[:, :], 2.0 ** 25, A.mult, ["sel8"], ["cntw"])
-    ts(T.scw[:, 0:8], T.sel8[:, :], 32.0, A.mult, ["sel8"], ["scw"])
-    ts(T.scw[:, 8:16], T.sel8[:, :], -32.0, A.mult, ["sel8"], ["scw"])
-    ts(T.hrow[:, :], T.hrf[:, :], 2.0 ** 20, A.mult, ["hrf"], ["hrow"])
-    for jb in range(3):
-        ts(T.selj[0:48, 128 * jb:128 * jb + 128], T.ioj[0:48, 0:128], C[0:48, 5 + jb:6 + jb], A.is_equal, ["ioj", "c5"], ["selj"])
+    for h in range(2):
+        ts(T["f" + "ab"[h]][:, :], T.ioj[:, :], -8.0 * h, A.add, ["ioj", "c10"], ["f" + "ab"[h]], C[:, 10:11], A.is_equal)
+    ts(T.sel8[:, :], T.iof[:, 0:8], C[:, 2:3], A.is_equal, ["iof", "c2"], ["sel8"])
+    for h in range(2):
+        tt(T["f" + "ab"[h]][:, :], T["f" + "ab"[h]][:, :], T.bof[:, :], A.mult, ["f" + "ab"[h], "bof"], ["f" + "ab"[h]])
+    cp(T.sgl[:, :], T.sgi[:, :], ["sgi"], ["sgl"])
+    for h in range(2):
+        for o in range(2):
+            c = 256 * o + 128 * h
+            act(T.hsel[:, c:c + 128], T["f" + "ab"[h]][:, :], ["f" + "ab"[h], "c11"], ["hsel"], scale=C[:, 11 + o:12 + o])
+    act(T.hsel[:, 512:1024], T.hsel[:, 0:512], ["hsel"], ["hsel"], scale=64.0)
+    cp(T.boh[:, :], T.bof[:, :], ["bof"], ["boh"])
     ts(T.tmp[:, 0:48], T.io8[:, :], C[:, 2:3], A.is_gt, ["io8", "c2"], ["tmpA"], BIG, A.mult)
     ts(T.tmp[:, 64:128], T.ioj[:, 0:64], C[:, 1:2], A.is_gt, ["ioj", "c1"], ["tmpB"], BIG, A.mult)
-    ts(T.tmp[:, 128:176], T.iob[:, :], C[:, 3:4], A.add, ["iob", "c3"], ["tmpC"])
-    ts(T.pado[:, :], T.padf[:, :], C[:, 4:5], A.add, ["padf", "c4"], ["pado"])
-    ts(T.pst[:, :], T.tmp[:, 0:48], -4.0, A.mult, ["tmpA"], ["pst"], 2 * BIG, A.add)
-    ts(T.pns[:, :], T.tmp[:, 64:128], -4.0, A.mult, ["tmpB"], ["pns"], 2 * BIG, A.add)
+    ts(T.idb[:, :], T.iof[:, :], C[:, 0:1], A.is_equal, ["iof", "c0"], ["idb"])
+    ts(T.idh[:, :], T.iof[:, :], C[:, 0:1], A.is_equal, ["iof", "c0"], ["idh"])
+    ts(T.dm[:, :], T.ioj[:, 0:16], C[:, 1:2], A.is_equal, ["ioj", "c1"], ["dm"])
+    for jb in range(3):
+        ts(T.selj[0:48, 128 * jb:128 * jb + 128], T.ioj[0:48, 0:128], C[0:48, 5 + jb:6 + jb], A.is_equal, ["ioj", "c5"], ["selj"])
     tt(T.mk6[:, :], T.tmp[:, 0:48], T.tmp[:, 128:176], A.add, ["tmpA", "tmpC"], ["mk6"])
     for i in range(6):
         ts(T.mk5[:, 8 * i:8 * i + 8], T.tmp[:, 8 * i:8 * i + 8], -1536.0 * (i % 2), A.add, ["tmpA"], ["mk5"])
-    cp(T.msk[:, 64:96], T.tmp[:, 64:96], ["tmpB", "msk"], ["msk"])
-    cp(T.msk2[:, 32:64], T.tmp[:, 64:96], ["tmpB", "msk2"], ["msk2"])
+    act(T.padf[:, :], T.pado[:, :], ["pado"], ["padn", "padf"], scale=-1.0)
     for a in range(2):
         for jb in range(3):
             c = 63 * a + 21 * jb
-            ts(T.cur[:, c:c + 21], T.iof[:, 0:21], 0.0, A.mult, ["iof", "pado"], ["cur"], T.pado[:, 3 * a + jb:3 * a + jb + 1], A.add)
-    cp(T.sgl[:, :], T.sgi[:, :], ["sgi"], ["sgl"])
-    cp(C[:, 9:10], T.kmi[:, 60:61], ["wti"], ["c9"])
-    ts(T.usel[:, :], T.sel8[:, :], C[:, 9:10], A.mult, ["sel8", "c9"], ["usel"])
+            act(T.cur[:, c:c + 21], T.iof[:, 0:21], ["iof", "pado"], ["cur"], func=ID, scale=0.0, bias=T.pado[:, 4 * jb + a:4 * jb + a + 1])
+    act(T.dn[:, :], T.iof[:, 0:12], ["iof"], ["dn", "dnO"], scale=0.0)
+    ms(T.pl[:, 0:12], 4096, ["pl0"])
+    act(T.cntw[:, :], T.sel8[:, :], ["sel8"], ["cntw"], scale=2.0 ** 25)
+    act(T.scw[:, 0:8], T.sel8[:, :], ["sel8"], ["scw"], scale=32.0)
+    act(T.scw[:, 8:16], T.sel8[:, :], ["sel8"], ["scw"], scale=-32.0)
+    act(T.pst[:, :], T.tmp[:, 0:48], ["tmpA"], ["pst"], scale=-4.0, bias=2 * BIG)
+    act(T.pns[:, :], T.tmp[:, 64:128], ["tmpB"], ["pns"], scale=-4.0, bias=2 * BIG)
+    act(T.msk[:, 64:96], T.tmp[:, 64:96], ["tmpB"], ["msk"])
+    act(T.msk2[:, 32:64], T.tmp[:, 64:96], ["tmpB"], ["msk2"])
 
-    act(T.Z[:, 0:2048], T.truv[:, :].indirect(T.sgl[:, 0:128]), ["truv", "sgl"], ["ZA"])
-    cp(T.Z[:, 2048:4096], T.truv[:, :].indirect(T.sgl[:, 128:256]), ["truv", "sgl"], ["ZB"])
-    cp(T.blist[:, :], T.booki[:, 0:1024], ["bookA"], ["blist"])
+    act(T.Z[:, 0:16 * ZS], T.truv[:, :].indirect(T.sgl[:, 0:ZS]), ["truv", "sgl"], ["ZA"])
+    cp(T.Z[:, 16 * ZS:4096], T.truv[:, :].indirect(T.sgl[:, ZS:256]), ["truv", "sgl"], ["ZB"])
+    ts(T.bhi[:, :], T.booki[:, 0:1024], 6, A.arith_shift_right, ["bookA"], ["bhi"])
     Zk = ["ZA", "ZB", "Zpad"]
     Zall = T.Z[:, :]
-    c, its = 0, []
-    for (chs, nm) in ((S0_CH, "J"), (V0_CH, "V")):
-        for i in range(len(chs)):
-            its.append((c, chs[i], nm + "0%d" % i, nm))
-            c += chs[i]
-    for (c, n, k, nm) in its:
-        (act if nm == "J" else cp)(T.G[:, 16 * c:16 * (c + n)], Zall.indirect(T.blist[:, c:c + n]), Zk + ["blist"], [k])
-    ts(T.kl[:, 0:3], T.kmi[:, 0:3], 16.0, A.mult, ["kmi"], ["kl"], 16.0, A.add)
-    ts(T.kl[:, 3:63], T.kmi[:, 0:60], 16.0, A.mult, ["kmi"], ["kl"], 16.0, A.add)
-    ts(T.fa[:, 0:60], T.kmi[:, 0:60], 2.0, A.mult, ["kmi"], ["fa"], 1.0 - 2 * PH, A.add)
-    for (c, n, k, nm) in its[len(S0_CH):] + its[:len(S0_CH)]:
-        scan(T.ysc[:, 1 + 16 * c:1 + 16 * (c + n)], T.rst[:, 0:16 * n], T.G[:, 16 * c:16 * (c + n)], A.max, A.min, ["rst", k], ["Y"])
-        if k == "V00":
-            tt(T.st0[:, 0:60], T.fa[:, 0:60], T.kmi[:, 0:60], A.max, ["fa", "kmi"], ["st0"])
-    for k in ("J", "V"):
-        for i in range(8):
-            wr.pop(k + "0%d" % i, None)
-
-    def yphase(lists):
-        c, pits, sits = 0, [], []
-        for i in range(len(P_CH)):
-            pits.append((c, P_CH[i], "G%d" % i, "H%d" % i))
-            c += P_CH[i]
-        for i in range(len(S_CH)):
-            sits.append((c, S_CH[i], "J%d" % i))
-            c += S_CH[i]
-        for (c, n, k, k2) in pits:
-            (cp if c == 0 else act)(T.G[:, 16 * c:16 * (c + n)], Zall.indirect(T.lb[:, c:c + n]), Zk + ["lb"], [k])
-        for (c, n, k) in sits:
-            act(T.G[:, 16 * c:16 * (c + n)], Zall.indirect(T.blist[:, c + PH:c + PH + n]), Zk + ["blist"], [k])
-        for i in range(len(pits) + 1):
-            if i < len(pits):
-                (c, n, k, k2) = pits[i]
-                tt(T.H[:, 16 * c:16 * (c + n)], Zall.indirect(T.la[:, c:c + n]), T.G[:, 16 * c:16 * (c + n)], A.min, Zk + ["la", k], [k2])
-            if i > 0:
-                (c, n, k, k2) = pits[i - 1]
-                scan(T.ysc[:, 1 + 16 * c:1 + 16 * (c + n)], T.rst8[:, 0:16 * n], T.H[:, 16 * c:16 * (c + n)], A.max, A.min, ["rst8", k2], ["Y"])
-            if i == len(pits) - 1:
-                lists()
-        for (c, n, k) in sits:
-            scan(T.ysc[:, 1 + 16 * c:1 + 16 * (c + n)], T.rst[:, 0:16 * n], T.G[:, 16 * c:16 * (c + n)], A.max, A.min, ["rst", k], ["Y"])
-
-    Sk = ["S0", "S1", "Spad"]
-    ywin = T.ysc[:, :]
+    Sk = ["S0", "Spad"]
     bwin = T.booki[:, :]
     twin = T.tf[:, :]
 
-    def sinit(a, b, key):
-        act(T.S[:, a:b], T.iot[:, :].indirect(T.sgl[:, a // 16:b // 16]), ["iot", "sgl"], [key], bias=OFF)
+    def klist(buf, key, src, skey):
+        cp(buf[:, 0:3 * NP], src[:, 3:3 + 3 * NP], [skey, key], [key + "a"])
+        cp(buf[:, KN:KN + NN // 16], src[:, 3 + 3 * NP:60], [skey, key], [key + "b"])
+        cp(buf[:, K0:K0 + 3], src[:, 0:3], [skey, key], [key + "c"])
+
+    klist(T.kl0, "kl0", T.kmi, "kmi")
+    ts(T.blo[:, :], T.booki[:, 0:1024], 63, A.bitwise_and, ["bookA"], ["blo"])
+    cp(C[:, 9:10], T.kmi[:, 60:61], ["wti"], ["c9"])
+    cp(T.st0[:, 0:60], T.kmi[:, 0:60], ["kmi"], ["st0"])
+    ts(T.usel[:, :], T.sel8[:, :], C[:, 9:10], A.mult, ["sel8", "c9"], ["usel"])
+
+    def klk(t):
+        return ["kl0a", "kl0b", "kl0c"] if t == 0 else ["kl%d" % t]
+
+    def halves(t):
+        kl = T["kl%d" % t]
+        act(T.thi[:, :], T.bhi[:, :].indirect(kl[:, 0:3 * NP]), ["bhi"] + klk(t), ["thi"])
+        act(T.tlo[:, :], T.blo[:, :].indirect(kl[:, 0:3 * NP]), ["blo"] + klk(t), ["tlo"])
+        for (src, key, c0) in ((T.thi, "thi", 512), (T.tlo, "tlo", 0)):
+            for o in (1, 0):
+                for h in range(2):
+                    c = c0 + 256 * o + 128 * h
+                    mm(T["ps%d" % (4 + 3 * o)][:, 0:PH], T.hsel[:, c:c + 128], src[:, h:2 * PH:2], ["hsel", key], ["B%d" % (4 + 3 * o)], c0 > 0 and h == 0, c0 == 0 and h == 1)
+
+    def wholes(t):
+        cp(T.nat[:, 48:48 + N_CH[0]], bwin.indirect(T["kl%d" % t][:, KN:KN + N_CH[0] // 16]), ["bookA", "bookB"] + klk(t), ["natA"])
+
+    def sinit(a, b):
+        act(T.S[:, a:b], T.iot[:, :].indirect(T.sgl[:, a // 16:b // 16]), ["iot", "sgl"], ["S0"], bias=OFF)
+
+    def sread(v):
+        act(T.sp[:, :], T.S[:, :].indirect(T.pl[:, 12 * v:12 * v + 12]), Sk + ["pl%d" % v], ["sp"])
+
+    def swrite(v):
+        cp(T.S[:, :].indirect(T.offs[:, 12 * v:12 * v + 12]), T.sp[:, :], ["offsA", "offsB", "sp"] + Sk, Sk)
+
+    def yslot(k, n=1):
+        if k == 0:
+            return T.ysc[:, 15:768:16]
+        if k <= NP:
+            return T.ysc[:, YP + 384 * (k - 1) + 7:YP + 384 * (k - 1 + n):8]
+        return T.ysc[:, YN + 768 * (k - 1 - NP) + 15:YN + 768 * (k - 1 - NP + n):16]
+
+    def answers(t, swaps):
+        kl = T["kl%d" % t]
+        pits, nits = [], []
+        for (chs, its) in ((P_CH, pits), (N_CH, nits)):
+            c = 0
+            for n in chs:
+                its.append((c, n))
+                c += n
+        done = [0, NP]
+
+        def sums(cls, upto, key):
+            k0, k1 = done[cls] + 1, upto
+            done[cls] = max(done[cls], upto)
+            if k1 < k0:
+                return
+            tt(T.lt[:, 48 * (k0 - 1):48 * k1], yslot(k0, k1 - k0 + 1), T.ps0[:, 0:48 * (k1 - k0 + 1)], A.is_lt, [key, "B0"], ["lt" + key])
+            for k in range(k0, k1 + 1):
+                for p in ([0] if k == 1 + t else []) + [20 - k]:
+                    mm(T.ps2[0:48, p:160:20], yslot(k), T.usel[:, :], [key, "usel"], ["B2"], False, k == 19)
+            for k in range(k0, k1 + 1):
+                mm(T.ps3[0:48, 20 - k:160:20], T.lt[:, 48 * (k - 1):48 * k], T.cntw[:, :], ["lt" + key, "cntw"], ["B3"], False, k == 19)
+
+        def ngather(i):
+            c, n = nits[i]
+            act(T.G[:, YN + 16 * c:YN + 16 * (c + n)], Zall.indirect(T.nat[:, 48 + c:48 + c + n]), Zk + ["natA" if i == 0 else "natB"], ["J%d" % i])
+
+        def nscan(i):
+            c, n = nits[i]
+            scan(T.ysc[:, YN + 16 * c:YN + 16 * (c + n)], T.rst[:, 0:16 * n], T.G[:, YN + 16 * c:YN + 16 * (c + n)], A.max, A.min, ["rst", "J%d" % i], ["YN%d" % i])
+
+        def pgather(i, f):
+            c, n = pits[i]
+            f(T.G[:, YP + 16 * c:YP + 16 * (c + n)], Zall.indirect(T.lb[:, c:c + n]), Zk + ["lb"], ["G%d" % i])
+
+        def pfold(i):
+            c, n = pits[i]
+            tt(T.H[:, 16 * c:16 * (c + n)], Zall.indirect(T.la[:, c:c + n]), T.G[:, YP + 16 * c:YP + 16 * (c + n)], A.min, Zk + ["la", "G%d" % i], ["H%d" % i])
+
+        def pscan(i):
+            c, n = pits[i]
+            scan(T.ysc[:, YP + 16 * c:YP + 16 * (c + n)], T.rst8[:, 0:16 * n], T.H[:, 16 * c:16 * (c + n)], A.max, A.min, ["rst8", "H%d" % i], ["YP%d" % i])
+
+        n1 = N_CH[0] // 16
+        ngather(0)
+        cp(T.nat[:, 0:48], bwin.indirect(kl[:, K0:K0 + 3]), ["bookA", "bookB"] + klk(t), ["nat0"])
+        cp(T.nat[:, 48 + N_CH[0]:48 + NN], bwin.indirect(kl[:, KN + n1:KN + NN // 16]), ["bookA", "bookB"] + klk(t), ["natB"])
+        cp(T.G[:, 0:768], Zall.indirect(T.nat[:, 0:48]), Zk + ["nat0"], ["G00"])
+        cp(T.lb[:, :], T.ps7[:, 0:PH], ["B7"], ["lb"])
+        scan(T.ysc[:, 0:768], T.rst[:, 0:768], T.G[:, 0:768], A.max, A.min, ["rst", "G00"], ["Y0"])
+        cp(T.la[:, :], T.ps4[:, 0:PH], ["B4"], ["la"])
+        statics()
+        for i in range(3):
+            mm(T.ps0[:, 48 * i:48 * i + 48], T.idb[:, :], yslot(0), ["idb", "Y0"], ["B0"])
+        if len(swaps) > 0:
+            swrite(swaps[0])
+        pgather(0, act if swaps else cp)
+        pgather(1, act)
+        if len(swaps) > 1:
+            sread(swaps[1])
+        for i in range(2, len(pits)):
+            pgather(i, act)
+        for i in range(1, len(nits)):
+            ngather(i)
+        nscan(0)
+        pfold(0)
+        sums(1, NP + N_CH[0] // 48, "YN0")
+        for i in range(1, len(pits)):
+            pfold(i)
+            if i == 2 and len(swaps) > 1:
+                swrite(swaps[1])
+            if i > 1:
+                sums(0, sum(pits[i - 2]) // 24, "YP%d" % (i - 2))
+            pscan(i - 1)
+        pscan(len(pits) - 1)
+        sums(0, sum(pits[-2]) // 24, "YP%d" % (len(pits) - 2))
+        for i in range(1, len(nits)):
+            nscan(i)
+            if i == 1:
+                sums(0, NP, "YP%d" % (len(pits) - 1))
+            else:
+                sums(1, NP + sum(nits[i - 1]) // 48, "YN%d" % (i - 1))
+        sums(1, 19, "YN%d" % (len(nits) - 1))
 
     def statics():
         mm(T.ps2[0:48, 0:160], T.onb[0:1, 0:48], T.hrow[0:1, :], ["onb", "hrow"], ["B2"], True, False)
@@ -278,57 +375,39 @@ def rank_program(g, core, T, topo):
         mm(T.ps5[:, 0:48], T.idh[:, :], T.mk5[:, :], ["idh", "mk5"], ["B5"], True, False)
         mm(T.ps6[:, 0:48], T.idh[:, :], T.mk6[:, :], ["idh", "mk6"], ["B6"], True, False)
 
+    halves(0)
+    wholes(0)
+    answers(0, [])
+    SPIECE = [(0, 1280, 1792), (1792, 2816, 3328), (3328, 4096, 4096)]
+    SWAPS = [[], [], [0, 1], [2, 3], [4]]
+
     for t in range(VI):
         st, stk = T["st%d" % t], "st%d" % t
         so, soz = T["so%d" % t], "soz%d" % t
         last = t == VI - 1
         old = t > 0
-        LW = 12 if old else 6
-        statics()
-        act(T.y[:, 0:96], ywin.indirect(T.kl[:, 0:6]), ["Y", "kl"], ["y00"])
-        cp(T.y[:, 96:416], ywin.indirect(T.kl[:, 6:26]), ["Y", "kl"], ["yA"])
-        act(T.y[:, 416:768], ywin.indirect(T.kl[:, 26:48]), ["Y", "kl"], ["yB"])
-        act(T.y[:, 768:1008], ywin.indirect(T.kl[:, 48:63]), ["Y", "kl"], ["yC"])
-        for i in range(4):
-            n = 96 if i < 3 else 48
-            mm(T.ps0[:, 96 * i:96 * i + n], T.idb[:, :], T.y[:, 0:n], ["idb", "y00"], ["B0"])
-        chunks = [(1, 6, ["yA"]), (7, 13, ["yA", "yB"]), (14, 19, ["yB", "yC"])]
+        plk = "pl%d" % t
+        dst, frm = (nxt, prv) if not last else (prv, nxt)
 
-        def usum(k, p, keys, stop=False):
-            mm(T.ps2[0:48, p:160:20], T.y[:, 48 * k + 48:48 * k + 96], T.usel[:, :], keys + ["usel"], ["B2"], False, stop)
+        def send(src_ap, keys, land):
+            deps("g", keys, [])
+            rid, pid = topo.addr(dst, core)
+            en = topo.engines(core, dst)[:8]
+            g.remote_dma(out_ap=T[land][:, :], in_ap=src_ap, remote_sem=T.sem["a_" + land], local_sem=T.sem.lsem,
+                         pid=pid, routing_id=rid, dma_engine_mask=sum(1 << e for e in en))
+            cnt["sent"] = cnt.get("sent", 0) + len(en)
+            wr[land] = ("a_" + land, len(topo.engines(frm, core)[:8]), "remote")
 
-        def csum(k, key):
-            mm(T.ps3[0:48, 20 - k:160:20], T.lt[:, 48 * (k - 1):48 * k], T.cntw[:, :], [key, "cntw"], ["B3"], False, k == 19)
-
-        def less(i):
-            k0, k1, keys = chunks[i]
-            tt(T.lt[:, 48 * (k0 - 1):48 * k1], T.y[:, 48 * k0 + 48:48 * k1 + 96], T.ps0[:, 0:48 * (k1 - k0 + 1)], A.is_lt, keys + ["B0"], ["lt%d" % i])
-
-        def arrived(a):
-            for jb in range(3):
-                c = 63 * a + 21 * jb
-                ts(T.xn[:, c:c + 21], T.iof[:, 0:21], st[:, 198 + jb:199 + jb], A.is_equal, ["iof", stk], ["xn"], st[:, 186 + 3 * a + jb:187 + 3 * a + jb], A.mult)
-
-        usum(1 + t, 0, ["yA"])
-        for k in range(1, 7):
-            usum(k, 20 - k, ["yA"])
-        less(0)
-        less(1)
-        less(2)
-        for k in range(1, 7):
-            csum(k, "lt0")
-        for k in range(7, 20):
-            usum(k, 20 - k, ["yA", "yB"] if k < 14 else ["yB", "yC"], k == 19)
-        act(T.hi[0:48, :], T.ps2[0:48, 0:160], ["B2"], ["hi"])
-        for k in range(7, 20):
-            csum(k, "lt1" if k < 14 else "lt2")
         if old:
-            lw0 = 12 if t > 1 else 6
-            cp(T.S[:, :].indirect(T.offs[:, 0:lw0]), T.sp[:, 0:16 * lw0], ["offs", "sp"], Sk)
-            red(T.cc[:, :], T.ps1[:, 0:3], A.add, ["B1"], ["cc"])
-        else:
-            sinit(0, 2048, "S0")
-            cp(T.lb[:, :], T.lbi[:, 0:2 * PH:2], ["lbi"], ["lb"])
+            act(T.sm[:, 28:31], T.ps1[:, 0:3], ["B1"], ["cc"], accum_out=T.cc[:, :])
+        act(T.hi[0:48, :], T.ps2[0:48, 0:160], ["B2"], ["hi"])
+        if old:
+            for a in range(2):
+                for jb in range(3):
+                    c = 64 + 63 * a + 21 * jb
+                    act(T.ps1[:, c:c + 21], st[:, 198 + 21 * jb:219 + 21 * jb], [stk], ["B1"], scale=st[:, 186 + 4 * jb + a:187 + 4 * jb + a])
+        if t < 3:
+            sinit(SPIECE[t][0], SPIECE[t][1])
         scan(T.su[0:48, :], T.ps3[0:48, 0:160], T.hi[0:48, :], A.max, A.min, ["B3", "hi"], ["su"])
         x = T.su[0:48, 19:160:20]
         uI, uU, uQ, uA, uF, uB = [T.uint[0:48, 8 * i:8 * i + 8] for i in range(6)]
@@ -343,89 +422,86 @@ def rank_program(g, core, T, topo):
         for jb in range(3):
             mm(T.ps5[:, 16 * jb:16 * jb + 16], T.selj[0:48, 128 * jb:128 * jb + 128], T.nk[0:48, :], ["selj", "nkn", "nkk"], ["B5"], False, jb == 2)
         if old:
-            arrived(0)
-            arrived(1)
+            tt(T.cur[:, :], st[:, 60:186], T.ps1[:, 64:190], A.add, [stk, "B1"], ["cur"])
         scan(T.pk[:, :], T.pst[:, :], T.ps5[:, 0:48], A.max, A.min, ["pst", "B5"], ["pk"])
-        n0, ko = T.pk[:, 7:48:16], T.pk[:, 15:48:16]
-
-        def kcol(jb):
-            return T.pk[:, 15 + 16 * jb:16 + 16 * jb]
-
-        def kstc(jb):
-            return so[:, 198 + jb:199 + jb]
-
-        kz, nw, nK, z2, lz, lzn = [T.sm[:, 4 * i:4 * i + 3] for i in range(6)]
-        if old:
-            tt(T.cur[:, :], st[:, 60:186], T.xn[:, :], A.add, [stk, "xn"], ["cur"])
+        n0 = T.pk[:, 7:48:16]
+        nw, nK, kz, kst = [T.sm[:, 4 * i:4 * i + 3] for i in range(4)]
+        eqo, neq = T.ps0[:, 0:63], T.ps3[:, 0:63]
         cp(T.nl[:, 0:3], n0, ["pk"], ["nl"])
-        if old:
-            for jb in range(2):
-                ts(T.eqo[:, 21 * jb:21 * jb + 21], T.iof[:, 0:21], kcol(jb), A.is_equal, ["iof", "pk"], ["eqo"])
+        ts(nw, n0, 1023.5, A.is_ge, ["pk"], ["nw"], -1024.0, A.mult)
+        ts(kz, T.pk[:, 15:48:16], 20.0, A.is_equal, ["pk"], ["kz"], float(t + 1 - 20), A.mult)
+        for jb in range(3):
+            act(T.ab[:, 21 * jb:21 * jb + 21], T.iof[:, 0:21], ["iof", "pk"], ["ab"], func=AF.Abs, scale=-1.0, bias=T.pk[:, 15 + 16 * jb:16 + 16 * jb])
         cp(T.bkl[:, :], bwin.indirect(T.nl[:, 0:3]), ["bookA", "bookB", "nl"], ["bkl"])
         if old:
-            ts(T.eqo[:, 42:63], T.iof[:, 0:21], kcol(2), A.is_equal, ["iof", "pk"], ["eqo"])
-        ts(kz, ko, 20.0, A.is_equal, ["pk"], ["kz"], float(t + 1 - 20), A.mult)
+            act(eqo, T.ab[:, :], ["ab"], ["B0"], func=AF.Relu, scale=-1.0, bias=1.0)
+        tt(nK, n0, nw, A.add, ["pk", "nw"], ["nK"])
+        tt(kst, kz, T.pk[:, 15:48:16], A.add, ["pk", "kz"], ["kst"])
         act(T.zc[:, 384:768], Zall.indirect(T.bkl[:, 24:48]), Zk + ["bkl"], ["zcS"])
         cp(T.zc[:, 0:384], Zall.indirect(T.bkl[:, 0:24]), Zk + ["bkl"], ["zcV"])
-        act(T.tf[:, :], T.iot[:, :].indirect(T.bkl[:, :]), ["iot", "bkl"], ["tf"])
         for p in range(16):
             mm(T.ps4[0:48, p:256:16], T.zc[:, p:768:16], T.scw[:, :], ["zcS", "zcV", "scw"], ["B4"])
+        act(T.tf[:, :], T.iot[:, :].indirect(T.bkl[:, :]), ["iot", "bkl"], ["tf"])
+        if not last:
+            act(T.hitb[:, 0:3], T.ab[:, 20:63:21], ["ab"], ["hitb"], func=AF.Sign)
+        for jb in range(3):
+            act(T.ab[:, 21 * jb:21 * jb + 21], T.iof[:, 0:21], ["iof", "kst"], ["ab"], func=AF.Abs, scale=-1.0, bias=T.sm[:, 12 + jb:13 + jb])
+        act(so[:, 198:261], T.ab[:, :], ["ab", soz], ["eqk"], func=AF.Relu, scale=-1.0, bias=1.0)
+        act(neq, T.ab[:, :], ["ab"], ["B3"], func=AF.Sign)
+        if t < 2:
+            sinit(SPIECE[t][1], SPIECE[t][2])
+        for jb in range(3):
+            ts(T.ps2[:, 64 + jb:124:3], T.iof[:, 0:20], T.sm[:, 12 + jb:13 + jb], A.not_equal, ["iof", "kst"], ["B2"])
+        for jb in range(3):
+            ts(T.ps2[:, jb:60:3], T.iof[:, 0:20], T.sm[:, 12 + jb:13 + jb], A.is_equal, ["iof", "kst", "nK"], ["B2"], T.sm[:, 4 + jb:5 + jb], A.mult)
         if old:
             for a in range(2):
-                tt(T.pr[:, 63 * a:63 * a + 63], T.cur[:, 63 * a:63 * a + 63], T.eqo[:, :], A.mult, ["cur", "eqo"], ["pr"])
-        tt(so[:, 198:201], kz, ko, A.add, ["kz", "pk", soz], ["kst"])
-        ts(nw, n0, 1023.5, A.is_ge, ["pk"], ["nw"], -1024.0, A.mult)
+                tt(T.pr[:, 63 * a:63 * a + 63], T.cur[:, 63 * a:63 * a + 63], eqo, A.mult, ["cur", "B0"], ["pr"])
+        tt(T.ts3[:, 0:60], st[:, 0:60], T.ps2[:, 64:124], A.mult, [stk, "B2"], ["ts3P"])
         if old:
             scan(T.osm[:, :], T.sumr[:, :], T.pr[:, :], A.mult, A.add, ["sumr", "pr"], ["osm"])
-            for jb in range(3):
-                for o in range(2):
-                    e = 63 * o + 21 * jb + 20
-                    act(T.dd[:, 32 * jb + 16 * o:32 * jb + 16 * o + 16], T.dm[:, :], ["dm", "osm"], ["dd"], scale=T.osm[:, e:e + 1])
-        else:
-            sinit(2048, 4096, "S1")
-        tt(nK, n0, nw, A.add, ["pk", "nw"], ["nK"])
-        for jb in range(3):
-            ts(T.neq[:, 21 * jb:21 * jb + 21], T.iof[:, 0:21], kstc(jb), A.not_equal, ["iof", "kst"], ["neq"])
+
+        def spread(jb):
+            for o in range(2 if old else 0):
+                e = 63 * o + 21 * jb + 20
+                ts(T.dd[:, 32 * jb + 16 * o:32 * jb + 16 * o + 16], T.dm[:, :], T.osm[:, e:e + 1], A.mult, ["dm", "osm"], ["dd"])
+
         if not last:
-            ts(z2, nK, 2.0, A.mult, ["nK"], ["z2"], 1.0 - 2 * PH, A.add)
-            ts(T.hitb[:, 0:3], ko, 19.5, A.is_lt, ["pk"], ["hitb"])
-            tt(lz, z2, nK, A.max, ["z2", "nK"], ["lz"])
+            tt(so[:, 0:60], T.ts3[:, 0:60], T.ps2[:, 0:60], A.add, ["ts3P", "B2"], ["soP"])
         else:
-            ts(T.fb[:, 0:60], st[:, 0:60], 0.5, A.mult, [stk], ["fb"], PH - 0.5, A.add)
             ts(T.fa[:, 0:126], T.cur[:, :], OFF - 0.5, A.is_ge, ["cur"], ["fa"], -8192.0, A.mult)
-            tt(T.fb[:, 64:124], T.fb[:, 0:60], st[:, 0:60], A.min, [stk, "fb"], ["fb2"])
         scan(T.sk[0:48, :], T.srst[0:48, :], T.ps4[0:48, 0:256], A.add, A.max, ["srst", "B4"], ["sk"])
-        key = T.sk[0:48, 15:256:16]
         if not last:
-            ts(lzn, lz, -1.0, A.mult, ["lz"], ["lzn"])
-            for jb in range(3):
-                act(T.xs[:, jb:60:3], T.neq[:, 21 * jb:21 * jb + 20], ["neq", "lz", "lzn"], ["xsP"], func=AF.Identity,
-                    scale=T.sm[:, 20 + jb:21 + jb], bias=T.sm[:, 16 + jb:17 + jb])
+            kok = "ko%d" % t
+            klist(T[kok], kok, so, "soP")
+            send(T[kok][:, :], [kok + "a", kok + "b", kok + "c"], "kl%d" % (t + 1))
+        key = T.sk[0:48, 15:256:16]
         MG = 1.5 * 2 ** 28
         ts(T.kr[0:48, :], key, MG, A.add, ["sk"], ["kr"], MG, A.subtract)
-        if old:
-            tt(T.dn[:, 6:12], T.osm[:, 20:126:21], T.pado[:, 6:12], A.subtract, ["osm", "pado"], ["dnO"])
+        spread(0)
         tt(T.qh[0:48, :], T.kr[0:48, :], key, A.subtract, ["kr", "sk"], ["qh"])
         for jb in range(3):
             mm(T.ps6[:, 16 * jb:16 * jb + 16], T.selj[0:48, 128 * jb:128 * jb + 128], T.qh[0:48, :], ["selj", "qh"], ["B6"], False, jb == 2)
+        spread(1)
+        spread(2)
         if old:
-            mm(T.ps7[:, 0:96], T.bof[:, :], T.dd[:, :], ["bof", "dd"], ["B7"])
+            mm(T.ps7[:, 0:96], T.boh[:, :], T.dd[:, :], ["boh", "dd"], ["B7"])
             for m in range(2):
-                ts(T.pl[:, 6 + 3 * m:9 + 3 * m], T.osm[:, 83 - 63 * m:126 - 63 * m:21], OFF, A.add, ["osm"], ["pl"])
+                ts(T.pl[:, 12 * t + 2 + m:12 * t + 12:4], T.osm[:, 83 - 63 * m:126 - 63 * m:21], OFF, A.add, ["osm"], [plk])
         if not last:
             mm(T.ps1[:, 0:3], T.onb[:, :], T.hitb[:, 0:3], ["onb", "hitb"], ["B1"])
-            for jb in range(3):
-                tt(T.ts3[:, jb:60:3], st[:, jb:60:3], T.neq[:, 21 * jb:21 * jb + 20], A.mult, [stk, "neq"], ["ts3P"])
         else:
             tt(T.pr[:, :], T.cur[:, :], T.fa[:, 0:126], A.add, ["cur", "fa"], ["pr"])
         scan(T.pk2[:, :], T.pst[:, :], T.ps6[:, 0:48], A.max, A.min, ["pst", "B6"], ["pk2"])
-        if not last:
-            tt(so[:, 60:123], T.cur[:, 0:63], T.neq[:, :], A.mult, ["cur", "neq"], ["soA"])
-        else:
+        if last:
             ts(T.fa[:, 0:126], T.pr[:, :], OFF, A.add, ["pr"], ["fa"], -1.0, A.max)
         cp(T.fl[:, 0:4], T.pk2[:, 7:32:8], ["pk2"], ["flA"])
         cp(T.fl[:, 4:10], T.pk2[:, 7:48:8], ["pk2"], ["flB"])
         if old:
+            for jb in (2, 1, 0):
+                for o in range(2):
+                    e, c = 4 * jb + 2 + o, 63 * o + 21 * jb + 20
+                    act(T.dn[:, e:e + 1], T.osm[:, c:c + 1], ["osm", "padn"], ["dnO"], func=AF.Identity, bias=T.padf[:, e:e + 1])
             cp(T.fn[:, 128:160], T.ps7[:, 0:32], ["B7"], ["fnO"])
         tt(T.fn[:, 32:96], twin.indirect(T.fl[:, 0:4]), T.tmp[:, 64:128], A.add, ["tf", "flA", "tmpB"], ["fnA"])
         tt(T.fn[:, 160:256], twin.indirect(T.fl[:, 4:10]), T.msk[:, :], A.add, ["tf", "flB", "msk"], ["fnB"])
@@ -452,78 +528,70 @@ def rank_program(g, core, T, topo):
             return T.cn[:, o + w - 1:o + w]
 
         def place(jb, col):
-            ts(T.of1[:, jb:LW:3], T.dn[:, jb:LW:3], col, A.add, ["dn", "dnO", "cn%d" % jb], ["of1"], 0.0, A.min)
+            ts(T.of1[:, 4 * jb:4 * jb + 4], T.dn[:, 4 * jb:4 * jb + 4], col, A.add, ["dn", "dnO", "cn%d" % jb], ["of1%d" % jb], 0.0, A.min)
 
         if old:
             tt(T.fn[:, 0:32], T.ps7[:, 0:32], T.msk2[:, 32:64], A.add, ["B7", "msk2"], ["fnP"])
             tt(T.fn[:, 96:128], T.ps7[:, 32:64], T.msk2[:, 32:64], A.add, ["B7", "msk2"], ["fnP"])
+        for jb in (2, 1, 0):
+            for m in range(2):
+                e, c = 4 * jb + m, 32 * jb + 16 * m + 15
+                act(T.dn[:, e:e + 1], T.ns[:, c:c + 1], nsk + ["padn"], ["dn"], func=AF.Identity, bias=T.padf[:, e:e + 1])
         for m in list(range(2, M)) + [0, 1]:
             eq(2, m)
         for m in range(2):
-            ts(T.pl[:, 3 * m:3 * m + 3], T.ns[:, 31 - 16 * m:96:32], OFF, A.add, nsk, ["pl"])
+            ts(T.pl[:, 12 * t + m:12 * t + 12:4], T.ns[:, 31 - 16 * m:96:32], OFF, A.add, nsk, [plk])
         if not last:
-            act(T.zp[:, 0:16 * LW], Zall.indirect(T.pl[:, 0:LW]), Zk + ["pl"], ["zp"])
-        act(T.sp[:, 0:16 * LW], T.S[:, :].indirect(T.pl[:, 0:LW]), Sk + ["pl"], ["sp"])
+            act(T.zp[:, :], Zall.indirect(T.pl[:, 12 * t:12 * t + 12]), Zk + [plk], ["zp"])
+            halves(t + 1)
+            if SWAPS[t]:
+                sread(SWAPS[t][0])
+        else:
+            sread(t)
         c2 = count(2)
         for m in range(M):
             eq(1, m)
-        for m in range(2):
-            tt(T.dn[:, 3 * m:3 * m + 3], T.ns[:, 15 + 16 * m:96:32], T.pado[:, 3 * m:3 * m + 3], A.subtract, nsk + ["pado"], ["dn"])
+        place(2, c2)
+        if not last:
+            tt(so[:, 123:186], T.cur[:, 63:126], neq, A.mult, ["cur", "B3"], ["soB"])
         c1 = count(1)
         for m in range(M):
             eq(0, m)
-        place(2, c2)
         place(1, c1)
+        if not last:
+            tt(so[:, 60:123], T.cur[:, 0:63], neq, A.mult, ["cur", "B3"], ["soA"])
         c0 = count(0)
-        dst, frm = (nxt, prv) if not last else (prv, nxt)
-
-        def send(src_ap, keys, land):
-            deps("g", keys, [])
-            rid, pid = topo.addr(dst, core)
-            en = topo.engines(core, dst)[:8]
-            g.remote_dma(out_ap=T[land][:, :], in_ap=src_ap, remote_sem=T.sem["arr%d" % (t + 1)], local_sem=T.sem.lsem,
-                         pid=pid, routing_id=rid, dma_engine_mask=sum(1 << e for e in en))
-            cnt["sent"] = cnt.get("sent", 0) + len(en)
-            wr[land] = ("arr%d" % (t + 1), len(topo.engines(frm, core)[:8]), "remote")
-
         if last:
             break
-        tt(so[:, 123:186], T.cur[:, 63:126], T.neq[:, :], A.mult, ["cur", "neq"], ["soB"])
+        o = 12 * t
+        tt(so[:, 190:198], T.of1[:, 4:12], T.pado[:, 4:12], A.add, ["of11", "of12", "pado", soz], ["of2A"])
         place(0, c0)
-        tt(so[:, 0:60], T.ts3[:, 0:60], T.xs[:, 0:60], A.add, ["ts3P", "xsP"], ["soP"])
-        tt(so[:, 186:186 + LW], T.of1[:, 0:LW], T.pado[:, 0:LW], A.add, ["of1", "pado", soz], ["of2"])
-        ts(T.offs[:, 0:LW], so[:, 186:186 + LW], OFF, A.add, ["of2"], ["offs"])
-        if t == 0:
-            cp(T.la[:, :], T.lai[:, 0:2 * PH:2], ["lai"], ["la"])
-        cp(Zall.indirect(T.offs[:, 0:LW]), T.zp[:, 0:16 * LW], ["offs", "zp"], Zk)
-        send(so[:, :], ["soP", "soA", "soB", "of2", "kst", soz], "st%d" % (t + 1))
-
-        def lists():
-            s2, k2 = T["st%d" % (t + 1)], "st%d" % (t + 1)
-            ts(T.kl[:, 0:3], s2[:, 0:3], 8.0, A.mult, [k2], ["kl"], 8.0, A.add)
-            ts(T.kl[:, 3:63], s2[:, 0:60], 8.0, A.mult, [k2], ["kl"], 8.0, A.add)
-
-        yphase(lists)
+        ts(T.offs[:, o + 4:o + 12], so[:, 190:198], OFF, A.add, ["of2A"], ["offsA"])
+        tt(so[:, 186:190], T.of1[:, 0:4], T.pado[:, 0:4], A.add, ["of10", "pado", soz], ["of2B"])
+        cp(Zall.indirect(T.offs[:, o + 4:o + 12]), T.zp[:, 64:192], ["offsA", "zp"], Zk)
+        ts(T.offs[:, o:o + 4], so[:, 186:190], OFF, A.add, ["of2B"], ["offsB"])
+        send(so[:, :], ["soP", "soA", "soB", "of2A", "of2B", "eqk", soz], "st%d" % (t + 1))
+        wholes(t + 1)
+        cp(Zall.indirect(T.offs[:, o:o + 4]), T.zp[:, 0:64], ["offsB", "zp"] + Zk, Zk)
+        answers(t + 1, SWAPS[t])
 
     cols = [c0, c1, c2]
     ts(T.v6[:, 0:6], T.ns[:, 15:96:16], OFF, A.add, nsk, ["v6a"])
-    place(0, c0)
-    for jb in range(3):
-        tt(T.ts3[:, jb:60:3], T.fb[:, 64 + jb:124:3], T.neq[:, 21 * jb:21 * jb + 20], A.mult, ["fb2", "neq"], ["ts3P"])
-    for jb in range(3):
-        ts(T.v6[:, 2 * jb:2 * jb + 2], T.v6[:, 2 * jb:2 * jb + 2], cols[jb], A.subtract, ["v6a", "cn%d" % jb], ["v6"], -1.0, A.max)
-    for jb in range(3):
-        ts(T.xs[:, jb:60:3], T.iof[:, 0:20], kstc(jb), A.is_equal, ["iof", "kst", "nK"], ["xsP"], T.sm[:, 8 + jb:9 + jb], A.mult)
+    for jb in (2, 1, 0):
+        ts(T.v6[:, 2 * jb:2 * jb + 2], T.v6[:, 2 * jb:2 * jb + 2], cols[jb], A.subtract, ["v6a", "cn%d" % jb], ["v6%d" % jb], -1.0, A.max)
+    for jb in (2, 1, 0):
+        for a in range(2):
+            act(T.ps2[:, 60 + 60 * a + jb:120 + 60 * a:3], so[:, 198 + 21 * jb:218 + 21 * jb], ["eqk", "v6%d" % jb], ["B2"], scale=T.v6[:, 2 * jb + a:2 * jb + a + 1])
     for a in range(2):
         for jb in range(3):
             c = 63 * a + 21 * jb
-            tt(T.ts3[:, 60 + 60 * a + jb:120 + 60 * a:3], T.fa[:, c:c + 20], T.neq[:, 21 * jb:21 * jb + 20], A.mult, ["fa", "neq"], ["ts3N"])
-            ts(T.xs[:, 60 + 60 * a + jb:120 + 60 * a:3], T.iof[:, 0:20], kstc(jb), A.is_equal, ["iof", "kst", "v6"], ["xsN"], T.v6[:, 2 * jb + a:2 * jb + a + 1], A.mult)
-    tt(so[:, 186:198], T.of1[:, :], T.pado[:, :], A.add, ["of1", "pado", soz], ["of2"])
-    tt(T.sf[:, :], T.ts3[:, 0:180], T.xs[:, 0:180], A.add, ["ts3P", "ts3N", "xsP", "xsN"], ["sf"])
+            tt(T.ts3[:, 60 + 60 * a + jb:120 + 60 * a:3], T.fa[:, c:c + 20], T.ps3[:, 21 * jb:21 * jb + 20], A.mult, ["fa", "B3"], ["ts3N"])
+    place(0, c0)
+    tt(T.sf[:, :], T.ts3[:, 0:180], T.ps2[:, 0:180], A.add, ["ts3P", "ts3N", "B2"], ["sf"])
     send(T.sf[:, :], ["sf"], "home")
-    ts(T.offs[:, :], so[:, 186:198], OFF, A.add, ["of2"], ["offs"])
-    cp(T.S[:, :].indirect(T.offs[:, :]), T.sp[:, :], ["offs", "sp"], Sk)
+    tt(so[:, 186:198], T.of1[:, :], T.pado[:, :], A.add, ["of10", "of11", "of12", "pado", soz], ["of2A"])
+    ts(T.offs[:, 12 * t:12 * t + 12], so[:, 186:198], OFF, A.add, ["of2A"], ["offsA", "offsB"])
+    swrite(t)
     dma("y", T.ys[:, :], T.S[0:128:16, 0:4096], "dout", Sk, [])
     dma("y", T.yk[:, :], T.home[:, 0:60], "dout", ["home"], [])
     dma("s", T.ya[:, :], T.home[:, 60:120], "dout", ["home"], [])

@@ -3,26 +3,27 @@ from concourse.mybir import dt, AluOpType, AxisListType, ActivationFunctionType
 
 VI = 6
 PADC = 4480
-P_CH = [48, 72, 72, 72]
+P_CH = [56, 40, 72, 72, 48]
+P0_CH = [72, 72, 72, 72]
 PH = sum(P_CH)
 NP = PH // 24
-N_CH = [96, 144, 96, 32, 16]
+N_CH = [96, 128, 96, 48, 16]
 NN = sum(N_CH)
-KN = 3 * NP + NP % 2
-K0 = KN + NN // 16 + (NN // 16) % 2
-ZS = 168
-YP, YN, YW = 768, 768 + 16 * PH, 768 + 16 * (PH + NN)
+KN = 3 * NP
+ZS = 128
+YN, YW = 16 * PH, 16 * (PH + NN)
 OFF = 2048.0
 BIG = 30000.0
+HI = 8256.0
 SW = 264
 
 _sb = {
     "truv": (4096, "bfloat16"), "Z": (PADC, "bfloat16"), "S": (PADC, "float32"), "iot": (4096, "float32"),
-    "booki": (2048, "int32"), "sgi": (256, "int32"), "sgl": (256, "uint16"), "kmi": (64, "int32"),
-    "G": (YW, "bfloat16"), "nat": (48 + NN, "uint16"), "H": (16 * PH, "bfloat16"), "ysc": (YW, "bfloat16"),
-    "rst": (16 * max(N_CH), "bfloat16"), "rst8": (16 * max(P_CH), "bfloat16"),
-    "bhi": (1024, "int32"), "blo": (1024, "int32"), "thi": (2 * PH, "bfloat16"), "tlo": (2 * PH, "bfloat16"),
-    "hsel": (1024, "bfloat16"), "la": (PH, "uint16"), "lb": (PH, "uint16"), "ab": (63, "float32"),
+    "booki": (3072, "int32"), "kc": (120, "int32"), "sgi": (256, "int32"), "sgl": (256, "uint16"), "kmi": (64, "int32"),
+    "G": (YW, "bfloat16"), "nat": (NN, "uint16"), "H": (16 * PH, "bfloat16"), "ysc": (YW, "bfloat16"),
+    "rst": (16 * max(N_CH), "bfloat16"), "rst8": (16 * max(P_CH + P0_CH), "bfloat16"),
+    "blo": (3072, "int32"), "thi": (2 * PH, "bfloat16"), "tlo": (2 * PH, "bfloat16"),
+    "hsel": (512, "bfloat16"), "la": (PH, "uint16"), "lb": (PH, "uint16"), "ab": (63, "float32"),
     "pi": (1, "int32"), "pj": (1, "int32"), "pg": (1, "int32"), "colf": (16, "float32"),
     "iof": (128, "float32"), "iog": (128, "float32"), "ioj": (128, "float32"), "io8": (48, "float32"), "iob": (48, "float32"),
     "idb": (128, "bfloat16"), "idh": (128, "float16"), "bof": (128, "float32"), "onb": (128, "bfloat16"),
@@ -39,7 +40,7 @@ _sb = {
     "eqb": (1536, "bfloat16"), "cn": (768, "bfloat16"), "dn": (12, "float32"), "of1": (12, "float32"),
     "offs": (12 * VI, "uint16"), "pl": (12 * VI, "uint16"), "zp": (192, "bfloat16"), "sp": (192, "float32"),
     "ts3": (192, "float32"), "cc": (1, "float32"), "sf": (180, "float32"), "cur": (126, "float32"), "boh": (128, "float16"),
-    "fa": (128, "float32"), "fb": (128, "float32"), "v6": (8, "float32"), "home": (180, "float32"),
+    "fa": (128, "float32"), "fb": (128, "float32"), "v6": (8, "float32"), "home": (120, "float32"), "homek": (60, "float32"),
 }
 SCRATCH = {}
 for _k in _sb:
@@ -51,8 +52,8 @@ for _t in range(VI):
     SCRATCH["ko%d" % _t] = ("sbuf", [128, 64], "uint16")
 for _t in range(8):
     SCRATCH["ps%d" % _t] = ("psum", [128, 512], "float32")
-SEMAPHORES = (["sv", "ss", "sp_", "sg_", "lsg", "ltr", "lbk", "lbw", "lkm", "lwt", "dout", "lsem"]
-              + ["a_st%d" % _t for _t in range(1, VI)] + ["a_kl%d" % _t for _t in range(1, VI)] + ["a_home"])
+SEMAPHORES = (["sv", "ss", "sp_", "sg_", "lsg", "ltr", "lbk", "lbw", "lkm", "lwt", "lrp", "dout", "lsem"]
+              + ["a_st%d" % _t for _t in range(1, VI)] + ["a_kl%d" % _t for _t in range(1, VI)] + ["a_home", "a_homek"])
 
 
 def rank_program(g, core, T, topo):
@@ -143,12 +144,14 @@ def rank_program(g, core, T, topo):
     def iota(out, pattern, base, cm, w):
         E("g", lambda e: e.iota(out, pattern, base, cm, allow_small_or_imprecise_dtypes=True), [], w)
 
+    dma("y", T.booki[:, 0:1024], T.book[:, :], "lbk", [], ["bookA"])
+    dma("s", T.kmi[:, 0:60], T.km0[:, :], "lkm", [], ["kmi"])
     dma("y", T.sgi[:, :], T.sg0[:, :], "lsg", [], ["sgi"])
     dma("y", T.truv[:, :], T.tru[:, :], "ltr", [], ["truv"])
-    dma("y", T.booki[:, 0:1024], T.book[:, :], "lbk", [], ["bookA"])
-    dma("y", T.kmi[:, 0:60], T.km0[:, :], "lkm", [], ["kmi"])
     dma("y", T.kmi[:, 60:61], T.wt[:, :], "lwt", [], ["wti"])
-    dma("y", T.booki[:, 1024:2048], T.book[:, :], "lbw", [], ["bookB"])
+    for i in (1, 2):
+        g.sync.dma_start(out=T.booki[:, 1024 * i:1024 * i + 1024], in_=T.book[:, :]).then_inc(T.sem.lbw, 16)
+    note("y", [], ["bookB"], ("lbw", 32, "dma"))
 
     iota(T.pi[:, :], [[0, 1]], 0, 1, ["pi"])
     iota(T.iof[:, :], [[1, 128]], 0, 0, ["iof"])
@@ -158,8 +161,8 @@ def rank_program(g, core, T, topo):
     iota(T.iob[:, :], [[256, 3], [0, 16]], 15, 0, ["iob"])
     iota(T.hrf[:, :], [[0, 8], [1, 20]], -10, 0, ["hrf"])
     iota(T.padf[:, :], [[32, 12]], 4096 - int(OFF), 0, ["padf"])
+    iota(T.rst8[:, :], [[0, max(P_CH + P0_CH) * 2], [-512, 8]], 512, 0, ["rst8"])
     iota(T.rst[:, :], [[0, max(N_CH)], [-512, 16]], 512, 0, ["rst"])
-    iota(T.rst8[:, :], [[0, max(P_CH) * 2], [-512, 8]], 512, 0, ["rst8"])
     iota(T.iot[:, :], [[1, 4096]], -int(OFF), 0, ["iot"])
     C = T.colf
     ID = AF.Identity
@@ -172,8 +175,7 @@ def rank_program(g, core, T, topo):
     cp(C[:, 2:3], T.pg[:, :], ["pg"], ["c2"])
     cp(C[:, 10:11], T.uint[:, 0:1], ["uI"], ["c10"])
     for t in range(VI - 1):
-        ms(T["ko%d" % t][:, :], 0, ["ko%d" % t])
-    ms(T.kl0[:, :], 0, ["kl0"])
+        ms(T["ko%d" % t][:, 60:64], 0, ["koz%d" % t])
     ms(T.srst[:, :], 1.0, ["srst"])
     ms(T.sumr[:, :], 1.0, ["sumr"])
     ms(T.crow[:, :], -17.0 * 2 ** 24, ["crow"])
@@ -202,73 +204,77 @@ def rank_program(g, core, T, topo):
     ts(T.sel8[:, :], T.iof[:, 0:8], C[:, 2:3], A.is_equal, ["iof", "c2"], ["sel8"])
     for h in range(2):
         tt(T["f" + "ab"[h]][:, :], T["f" + "ab"[h]][:, :], T.bof[:, :], A.mult, ["f" + "ab"[h], "bof"], ["f" + "ab"[h]])
-    cp(T.sgl[:, :], T.sgi[:, :], ["sgi"], ["sgl"])
     for h in range(2):
         for o in range(2):
             c = 256 * o + 128 * h
             act(T.hsel[:, c:c + 128], T["f" + "ab"[h]][:, :], ["f" + "ab"[h], "c11"], ["hsel"], scale=C[:, 11 + o:12 + o])
-    act(T.hsel[:, 512:1024], T.hsel[:, 0:512], ["hsel"], ["hsel"], scale=64.0)
-    cp(T.boh[:, :], T.bof[:, :], ["bof"], ["boh"])
     ts(T.tmp[:, 0:48], T.io8[:, :], C[:, 2:3], A.is_gt, ["io8", "c2"], ["tmpA"], BIG, A.mult)
     ts(T.tmp[:, 64:128], T.ioj[:, 0:64], C[:, 1:2], A.is_gt, ["ioj", "c1"], ["tmpB"], BIG, A.mult)
-    ts(T.idb[:, :], T.iof[:, :], C[:, 0:1], A.is_equal, ["iof", "c0"], ["idb"])
-    ts(T.idh[:, :], T.iof[:, :], C[:, 0:1], A.is_equal, ["iof", "c0"], ["idh"])
-    ts(T.dm[:, :], T.ioj[:, 0:16], C[:, 1:2], A.is_equal, ["ioj", "c1"], ["dm"])
-    for jb in range(3):
-        ts(T.selj[0:48, 128 * jb:128 * jb + 128], T.ioj[0:48, 0:128], C[0:48, 5 + jb:6 + jb], A.is_equal, ["ioj", "c5"], ["selj"])
-    tt(T.mk6[:, :], T.tmp[:, 0:48], T.tmp[:, 128:176], A.add, ["tmpA", "tmpC"], ["mk6"])
-    for i in range(6):
-        ts(T.mk5[:, 8 * i:8 * i + 8], T.tmp[:, 8 * i:8 * i + 8], -1536.0 * (i % 2), A.add, ["tmpA"], ["mk5"])
-    act(T.padf[:, :], T.pado[:, :], ["pado"], ["padn", "padf"], scale=-1.0)
-    for a in range(2):
-        for jb in range(3):
-            c = 63 * a + 21 * jb
-            act(T.cur[:, c:c + 21], T.iof[:, 0:21], ["iof", "pado"], ["cur"], func=ID, scale=0.0, bias=T.pado[:, 4 * jb + a:4 * jb + a + 1])
-    act(T.dn[:, :], T.iof[:, 0:12], ["iof"], ["dn", "dnO"], scale=0.0)
-    ms(T.pl[:, 0:12], 4096, ["pl0"])
-    act(T.cntw[:, :], T.sel8[:, :], ["sel8"], ["cntw"], scale=2.0 ** 25)
-    act(T.scw[:, 0:8], T.sel8[:, :], ["sel8"], ["scw"], scale=32.0)
-    act(T.scw[:, 8:16], T.sel8[:, :], ["sel8"], ["scw"], scale=-32.0)
-    act(T.pst[:, :], T.tmp[:, 0:48], ["tmpA"], ["pst"], scale=-4.0, bias=2 * BIG)
-    act(T.pns[:, :], T.tmp[:, 64:128], ["tmpB"], ["pns"], scale=-4.0, bias=2 * BIG)
-    act(T.msk[:, 64:96], T.tmp[:, 64:96], ["tmpB"], ["msk"])
-    act(T.msk2[:, 32:64], T.tmp[:, 64:96], ["tmpB"], ["msk2"])
 
-    act(T.Z[:, 0:16 * ZS], T.truv[:, :].indirect(T.sgl[:, 0:ZS]), ["truv", "sgl"], ["ZA"])
-    cp(T.Z[:, 16 * ZS:4096], T.truv[:, :].indirect(T.sgl[:, ZS:256]), ["truv", "sgl"], ["ZB"])
-    ts(T.bhi[:, :], T.booki[:, 0:1024], 6, A.arith_shift_right, ["bookA"], ["bhi"])
+    def later_constants():
+        cp(T.boh[:, :], T.bof[:, :], ["bof"], ["boh"])
+        ts(T.idb[:, :], T.iof[:, :], C[:, 0:1], A.is_equal, ["iof", "c0"], ["idb"])
+        ts(T.idh[:, :], T.iof[:, :], C[:, 0:1], A.is_equal, ["iof", "c0"], ["idh"])
+        ts(T.dm[:, :], T.ioj[:, 0:16], C[:, 1:2], A.is_equal, ["ioj", "c1"], ["dm"])
+        for jb in range(3):
+            ts(T.selj[0:48, 128 * jb:128 * jb + 128], T.ioj[0:48, 0:128], C[0:48, 5 + jb:6 + jb], A.is_equal, ["ioj", "c5"], ["selj"])
+        tt(T.mk6[:, :], T.tmp[:, 0:48], T.tmp[:, 128:176], A.add, ["tmpA", "tmpC"], ["mk6"])
+        for i in range(6):
+            ts(T.mk5[:, 8 * i:8 * i + 8], T.tmp[:, 8 * i:8 * i + 8], -1536.0 * (i % 2), A.add, ["tmpA"], ["mk5"])
+        cp(T.offs[:, 0:12], T.padf[:, :], ["padu"], ["offs0", "offs1", "offs2"])
+        ms(T.pl[:, 0:12], 4096, ["pl0"])
+        for a in range(2):
+            for jb in range(3):
+                c = 63 * a + 21 * jb
+                act(T.cur[:, c:c + 21], T.iof[:, 0:21], ["iof", "pado"], ["cur"], func=ID, scale=0.0, bias=T.pado[:, 4 * jb + a:4 * jb + a + 1])
+        act(T.cntw[:, :], T.sel8[:, :], ["sel8"], ["cntw"], scale=2.0 ** 25)
+        act(T.scw[:, 0:8], T.sel8[:, :], ["sel8"], ["scw"], scale=32.0)
+        act(T.scw[:, 8:16], T.sel8[:, :], ["sel8"], ["scw"], scale=-32.0)
+        act(T.pst[:, :], T.tmp[:, 0:48], ["tmpA"], ["pst"], scale=-4.0, bias=2 * BIG)
+        act(T.pns[:, :], T.tmp[:, 64:128], ["tmpB"], ["pns"], scale=-4.0, bias=2 * BIG)
+        act(T.msk[:, 64:96], T.tmp[:, 64:96], ["tmpB"], ["msk"])
+        act(T.msk2[:, 32:64], T.tmp[:, 64:96], ["tmpB"], ["msk2"])
+
+    act(T.padf[:, :], T.pado[:, :], ["pado"], ["padu", "padf"], bias=OFF)
+
+    cp(T.kl0[:, 0:60], T.kmi[:, 0:60], ["kmi"], ["kl0"])
+    ts(T.blo[:, 0:1024], T.booki[:, 0:1024], 63, A.bitwise_and, ["bookA"], ["blo"])
+    deps("y", ["blo"], [])
+    for i in (1, 2):
+        g.sync.dma_start(out=T.blo[:, 1024 * i:1024 * i + 1024], in_=T.blo[:, 0:1024]).then_inc(T.sem.lrp, 16)
+    note("y", [], ["brep"], ("lrp", 32, "dma"))
+    cp(T.sgl[:, :], T.sgi[:, :], ["sgi"], ["sgl"])
     Zk = ["ZA", "ZB", "Zpad"]
     Zall = T.Z[:, :]
     Sk = ["S0", "Spad"]
     bwin = T.booki[:, :]
     twin = T.tf[:, :]
 
-    def klist(buf, key, src, skey):
-        cp(buf[:, 0:3 * NP], src[:, 3:3 + 3 * NP], [skey, key], [key + "a"])
-        cp(buf[:, KN:KN + NN // 16], src[:, 3 + 3 * NP:60], [skey, key], [key + "b"])
-        cp(buf[:, K0:K0 + 3], src[:, 0:3], [skey, key], [key + "c"])
+    BLOCKS = [(0, 96, (4, 7)), (96, PH, (0, 5))]
 
-    klist(T.kl0, "kl0", T.kmi, "kmi")
-    ts(T.blo[:, :], T.booki[:, 0:1024], 63, A.bitwise_and, ["bookA"], ["blo"])
-    cp(C[:, 9:10], T.kmi[:, 60:61], ["wti"], ["c9"])
-    cp(T.st0[:, 0:60], T.kmi[:, 0:60], ["kmi"], ["st0"])
-    ts(T.usel[:, :], T.sel8[:, :], C[:, 9:10], A.mult, ["sel8", "c9"], ["usel"])
+    def bwide(t):
+        return 1024 if t == 0 else 3072
 
-    def klk(t):
-        return ["kl0a", "kl0b", "kl0c"] if t == 0 else ["kl%d" % t]
+    def halves(t, between=None):
+        kl, keys = T["kl%d" % t], ["kl%d" % t] + (["brep"] if t > 0 else [])
+        act(T.thi[:, :], T.booki[:, 0:bwide(t)].indirect(kl[:, 0:KN]), ["bookA", "kl%d" % t] + (["bookB"] if t > 0 else []), ["thi"], bias=HI - 31.5)
+        if between:
+            between()
+        for (a, b, banks) in BLOCKS:
+            act(T.tlo[:, 2 * a:2 * b], T.blo[:, 0:bwide(t)].indirect(kl[:, a // 8:b // 8]), ["blo"] + keys, ["tlo%d" % a])
+            for (src, key, c0) in ((T.thi, "thi", 512), (T.tlo, "tlo%d" % a, 0)):
+                for o in (1, 0):
+                    for h in range(2):
+                        c = 256 * o + 128 * h
+                        mm(T["ps%d" % banks[o]][:, 0:b - a], T.hsel[:, c:c + 128], src[:, 2 * a + h:2 * b:2], ["hsel", key], ["B%d" % banks[o]], c0 > 0 and h == 0, c0 == 0 and h == 1)
 
-    def halves(t):
-        kl = T["kl%d" % t]
-        act(T.thi[:, :], T.bhi[:, :].indirect(kl[:, 0:3 * NP]), ["bhi"] + klk(t), ["thi"])
-        act(T.tlo[:, :], T.blo[:, :].indirect(kl[:, 0:3 * NP]), ["blo"] + klk(t), ["tlo"])
-        for (src, key, c0) in ((T.thi, "thi", 512), (T.tlo, "tlo", 0)):
-            for o in (1, 0):
-                for h in range(2):
-                    c = c0 + 256 * o + 128 * h
-                    mm(T["ps%d" % (4 + 3 * o)][:, 0:PH], T.hsel[:, c:c + 128], src[:, h:2 * PH:2], ["hsel", key], ["B%d" % (4 + 3 * o)], c0 > 0 and h == 0, c0 == 0 and h == 1)
+    def wholes(t, a, b, key):
+        cp(T.nat[:, a:b], T.booki[:, 0:bwide(t)].indirect(T["kl%d" % t][:, KN + a // 16:KN + b // 16]), ["bookA", "kl%d" % t] + (["bookB"] if t > 0 else []), [key])
 
-    def wholes(t):
-        cp(T.nat[:, 48:48 + N_CH[0]], bwin.indirect(T["kl%d" % t][:, KN:KN + N_CH[0] // 16]), ["bookA", "bookB"] + klk(t), ["natA"])
+    def turned(i):
+        a, b, banks = BLOCKS[i]
+        ts(T.lb[:, a:b], T["ps%d" % banks[1]][:, 0:b - a], -HI, A.add, ["B%d" % banks[1]], ["lb%d" % i])
+        ts(T.la[:, a:b], T["ps%d" % banks[0]][:, 0:b - a], -HI, A.add, ["B%d" % banks[0]], ["la%d" % i])
 
     def sinit(a, b):
         act(T.S[:, a:b], T.iot[:, :].indirect(T.sgl[:, a // 16:b // 16]), ["iot", "sgl"], ["S0"], bias=OFF)
@@ -276,25 +282,23 @@ def rank_program(g, core, T, topo):
     def sread(v):
         act(T.sp[:, :], T.S[:, :].indirect(T.pl[:, 12 * v:12 * v + 12]), Sk + ["pl%d" % v], ["sp"])
 
-    def swrite(v):
-        cp(T.S[:, :].indirect(T.offs[:, 12 * v:12 * v + 12]), T.sp[:, :], ["offsA", "offsB", "sp"] + Sk, Sk)
+    def swrite(v, a=0, b=12):
+        cp(T.S[:, :].indirect(T.offs[:, 12 * v + a:12 * v + b]), T.sp[:, 16 * a:16 * b], ["offs0", "offs1", "offs2", "sp"] + Sk, Sk)
 
     def yslot(k, n=1):
-        if k == 0:
-            return T.ysc[:, 15:768:16]
-        if k <= NP:
-            return T.ysc[:, YP + 384 * (k - 1) + 7:YP + 384 * (k - 1 + n):8]
-        return T.ysc[:, YN + 768 * (k - 1 - NP) + 15:YN + 768 * (k - 1 - NP + n):16]
+        if k < NP:
+            return T.ysc[:, 384 * k + 7:384 * (k + n):8]
+        return T.ysc[:, YN + 768 * (k - NP) + 15:YN + 768 * (k - NP + n):16]
 
-    def answers(t, swaps):
+    def answers(t, head=None):
         kl = T["kl%d" % t]
         pits, nits = [], []
-        for (chs, its) in ((P_CH, pits), (N_CH, nits)):
+        for (chs, its) in ((P0_CH if t == 0 else P_CH, pits), (N_CH, nits)):
             c = 0
             for n in chs:
                 its.append((c, n))
                 c += n
-        done = [0, NP]
+        done = [0, NP - 1]
 
         def sums(cls, upto, key):
             k0, k1 = done[cls] + 1, upto
@@ -310,7 +314,7 @@ def rank_program(g, core, T, topo):
 
         def ngather(i):
             c, n = nits[i]
-            act(T.G[:, YN + 16 * c:YN + 16 * (c + n)], Zall.indirect(T.nat[:, 48 + c:48 + c + n]), Zk + ["natA" if i == 0 else "natB"], ["J%d" % i])
+            act(T.G[:, YN + 16 * c:YN + 16 * (c + n)], Zall.indirect(T.nat[:, c:c + n]), Zk + ["natA" if i == 0 else "natB"], ["J%d" % i])
 
         def nscan(i):
             c, n = nits[i]
@@ -318,55 +322,61 @@ def rank_program(g, core, T, topo):
 
         def pgather(i, f):
             c, n = pits[i]
-            f(T.G[:, YP + 16 * c:YP + 16 * (c + n)], Zall.indirect(T.lb[:, c:c + n]), Zk + ["lb"], ["G%d" % i])
+            f(T.G[:, 16 * c:16 * (c + n)], Zall.indirect(T.lb[:, c:c + n]), Zk + ["lb0"] + (["lb1"] if c + n > BLOCKS[0][1] else []), ["G%d" % i])
 
         def pfold(i):
             c, n = pits[i]
-            tt(T.H[:, 16 * c:16 * (c + n)], Zall.indirect(T.la[:, c:c + n]), T.G[:, YP + 16 * c:YP + 16 * (c + n)], A.min, Zk + ["la", "G%d" % i], ["H%d" % i])
+            tt(T.H[:, 16 * c:16 * (c + n)], Zall.indirect(T.la[:, c:c + n]), T.G[:, 16 * c:16 * (c + n)], A.min, Zk + ["la0", "G%d" % i] + (["la1"] if c + n > BLOCKS[0][1] else []), ["H%d" % i])
 
         def pscan(i):
             c, n = pits[i]
-            scan(T.ysc[:, YP + 16 * c:YP + 16 * (c + n)], T.rst8[:, 0:16 * n], T.H[:, 16 * c:16 * (c + n)], A.max, A.min, ["rst8", "H%d" % i], ["YP%d" % i])
+            scan(T.ysc[:, 16 * c:16 * (c + n)], T.rst8[:, 0:16 * n], T.H[:, 16 * c:16 * (c + n)], A.max, A.min, ["rst8", "H%d" % i], ["YP%d" % i])
 
-        n1 = N_CH[0] // 16
-        ngather(0)
-        cp(T.nat[:, 0:48], bwin.indirect(kl[:, K0:K0 + 3]), ["bookA", "bookB"] + klk(t), ["nat0"])
-        cp(T.nat[:, 48 + N_CH[0]:48 + NN], bwin.indirect(kl[:, KN + n1:KN + NN // 16]), ["bookA", "bookB"] + klk(t), ["natB"])
-        cp(T.G[:, 0:768], Zall.indirect(T.nat[:, 0:48]), Zk + ["nat0"], ["G00"])
-        cp(T.lb[:, :], T.ps7[:, 0:PH], ["B7"], ["lb"])
-        scan(T.ysc[:, 0:768], T.rst[:, 0:768], T.G[:, 0:768], A.max, A.min, ["rst", "G00"], ["Y0"])
-        cp(T.la[:, :], T.ps4[:, 0:PH], ["B4"], ["la"])
+        late = t == 0
+        if not late:
+            ngather(0)
+            turned(0)
+            head()
+        pgather(0, cp)
+        if not late:
+            turned(1)
         statics()
-        for i in range(3):
-            mm(T.ps0[:, 48 * i:48 * i + 48], T.idb[:, :], yslot(0), ["idb", "Y0"], ["B0"])
-        if len(swaps) > 0:
-            swrite(swaps[0])
-        pgather(0, act if swaps else cp)
         pgather(1, act)
-        if len(swaps) > 1:
-            sread(swaps[1])
         for i in range(2, len(pits)):
             pgather(i, act)
-        for i in range(1, len(nits)):
-            ngather(i)
-        nscan(0)
+        if t > 0:
+            cp(T.kc[:, 60:120], kl[:, 0:60], ["kl%d" % t], ["kraw"])
+        else:
+            cp(C[:, 9:10], T.kmi[:, 60:61], ["wti"], ["c9"])
         pfold(0)
-        sums(1, NP + N_CH[0] // 48, "YN0")
+        if t > 0:
+            wholes(t, N_CH[0], NN, "natB")
+            ts(T.kc[:, 0:60], T.kc[:, 60:120], 1023, A.bitwise_and, ["kraw"], ["kc"])
+            nscan(0)
+        else:
+            ts(T.usel[:, :], T.sel8[:, :], C[:, 9:10], A.mult, ["sel8", "c9"], ["usel"])
+        for i in range(0 if late else 1, len(nits)):
+            ngather(i)
+        pscan(0)
+        for i in range(6):
+            mm(T.ps0[:, 48 * i:48 * i + 48], T.idb[:, :], yslot(0), ["idb", "YP0"], ["B0"])
         for i in range(1, len(pits)):
             pfold(i)
-            if i == 2 and len(swaps) > 1:
-                swrite(swaps[1])
+            if i == 1 and not late:
+                sums(1, NP - 1 + N_CH[0] // 48, "YN0")
+            if i > 2:
+                sums(0, sum(pits[i - 2]) // 24 - 1, "YP%d" % (i - 2))
             if i > 1:
-                sums(0, sum(pits[i - 2]) // 24, "YP%d" % (i - 2))
-            pscan(i - 1)
+                pscan(i - 1)
         pscan(len(pits) - 1)
-        sums(0, sum(pits[-2]) // 24, "YP%d" % (len(pits) - 2))
-        for i in range(1, len(nits)):
+        sums(0, sum(pits[-2]) // 24 - 1, "YP%d" % (len(pits) - 2))
+        first = 0 if late else 1
+        for i in range(first, len(nits)):
             nscan(i)
-            if i == 1:
-                sums(0, NP, "YP%d" % (len(pits) - 1))
+            if i == first:
+                sums(0, NP - 1, "YP%d" % (len(pits) - 1))
             else:
-                sums(1, NP + sum(nits[i - 1]) // 48, "YN%d" % (i - 1))
+                sums(1, NP - 1 + sum(nits[i - 1]) // 48, "YN%d" % (i - 1))
         sums(1, 19, "YN%d" % (len(nits) - 1))
 
     def statics():
@@ -376,8 +386,15 @@ def rank_program(g, core, T, topo):
         mm(T.ps6[:, 0:48], T.idh[:, :], T.mk6[:, :], ["idh", "mk6"], ["B6"], True, False)
 
     halves(0)
-    wholes(0)
-    answers(0, [])
+    wholes(0, 0, N_CH[0], "natA")
+    wholes(0, N_CH[0], NN, "natB")
+    cp(T.kc[:, 0:60], T.kmi[:, 0:60], ["kmi"], ["kc"])
+    later_constants()
+    turned(0)
+    act(T.Z[:, 0:16 * ZS], T.truv[:, :].indirect(T.sgl[:, 0:ZS]), ["truv", "sgl"], ["ZA"])
+    cp(T.Z[:, 16 * ZS:4096], T.truv[:, :].indirect(T.sgl[:, ZS:256]), ["truv", "sgl"], ["ZB"])
+    turned(1)
+    answers(0)
     SPIECE = [(0, 1280, 1792), (1792, 2816, 3328), (3328, 4096, 4096)]
     SWAPS = [[], [], [0, 1], [2, 3], [4]]
 
@@ -389,11 +406,11 @@ def rank_program(g, core, T, topo):
         plk = "pl%d" % t
         dst, frm = (nxt, prv) if not last else (prv, nxt)
 
-        def send(src_ap, keys, land):
+        def send(src_ap, keys, land, c=0):
             deps("g", keys, [])
             rid, pid = topo.addr(dst, core)
             en = topo.engines(core, dst)[:8]
-            g.remote_dma(out_ap=T[land][:, :], in_ap=src_ap, remote_sem=T.sem["a_" + land], local_sem=T.sem.lsem,
+            g.remote_dma(out_ap=T[land][:, c:], in_ap=src_ap, remote_sem=T.sem["a_" + land], local_sem=T.sem.lsem,
                          pid=pid, routing_id=rid, dma_engine_mask=sum(1 << e for e in en))
             cnt["sent"] = cnt.get("sent", 0) + len(en)
             wr[land] = ("a_" + land, len(topo.engines(frm, core)[:8]), "remote")
@@ -408,12 +425,17 @@ def rank_program(g, core, T, topo):
                     act(T.ps1[:, c:c + 21], st[:, 198 + 21 * jb:219 + 21 * jb], [stk], ["B1"], scale=st[:, 186 + 4 * jb + a:187 + 4 * jb + a])
         if t < 3:
             sinit(SPIECE[t][0], SPIECE[t][1])
+        swap = SWAPS[t - 1] if old else []
+        for v in swap[:1]:
+            swrite(v, 0, 6)
         scan(T.su[0:48, :], T.ps3[0:48, 0:160], T.hi[0:48, :], A.max, A.min, ["B3", "hi"], ["su"])
         x = T.su[0:48, 19:160:20]
         uI, uU, uQ, uA, uF, uB = [T.uint[0:48, 8 * i:8 * i + 8] for i in range(6)]
         cp(uI, x, ["su"], ["uI"])
         ts(T.nk[0:48, 8:16], x, -2.0 ** -20, A.mult, ["su"], ["nkk"], 1546.49609375, A.add)
         ts(uU, uI, 4095, A.bitwise_and, ["uI"], ["uU"])
+        if old:
+            tt(T.cur[:, :], st[:, 60:186], T.ps1[:, 64:190], A.add, [stk, "B1"], ["cur"])
         tt(uQ, uU, uU, A.mult, ["uU"], ["uQ"])
         ts(uA, uU, 37.0, A.mult, ["uU"] + (["cc"] if old else []), ["uA"], T.cc[0:48, 0:1] if old else 0.0, A.add)
         ts(uF, uQ, 5, A.arith_shift_right, ["uQ"], ["uF"], 1023, A.bitwise_and)
@@ -421,21 +443,22 @@ def rank_program(g, core, T, topo):
         tt(T.nk[0:48, 0:8], uF, uB, A.add, ["uF", "uB"], ["nkn"])
         for jb in range(3):
             mm(T.ps5[:, 16 * jb:16 * jb + 16], T.selj[0:48, 128 * jb:128 * jb + 128], T.nk[0:48, :], ["selj", "nkn", "nkk"], ["B5"], False, jb == 2)
-        if old:
-            tt(T.cur[:, :], st[:, 60:186], T.ps1[:, 64:190], A.add, [stk, "B1"], ["cur"])
+        for v in swap[:1]:
+            swrite(v, 6, 12)
+        for v in swap[1:]:
+            sread(v)
         scan(T.pk[:, :], T.pst[:, :], T.ps5[:, 0:48], A.max, A.min, ["pst", "B5"], ["pk"])
         n0 = T.pk[:, 7:48:16]
         nw, nK, kz, kst = [T.sm[:, 4 * i:4 * i + 3] for i in range(4)]
         eqo, neq = T.ps0[:, 0:63], T.ps3[:, 0:63]
         cp(T.nl[:, 0:3], n0, ["pk"], ["nl"])
-        ts(nw, n0, 1023.5, A.is_ge, ["pk"], ["nw"], -1024.0, A.mult)
         ts(kz, T.pk[:, 15:48:16], 20.0, A.is_equal, ["pk"], ["kz"], float(t + 1 - 20), A.mult)
         for jb in range(3):
             act(T.ab[:, 21 * jb:21 * jb + 21], T.iof[:, 0:21], ["iof", "pk"], ["ab"], func=AF.Abs, scale=-1.0, bias=T.pk[:, 15 + 16 * jb:16 + 16 * jb])
         cp(T.bkl[:, :], bwin.indirect(T.nl[:, 0:3]), ["bookA", "bookB", "nl"], ["bkl"])
         if old:
             act(eqo, T.ab[:, :], ["ab"], ["B0"], func=AF.Relu, scale=-1.0, bias=1.0)
-        tt(nK, n0, nw, A.add, ["pk", "nw"], ["nK"])
+        ts(nK, n0, 1024.0, A.add, ["pk"], ["nK"])
         tt(kst, kz, T.pk[:, 15:48:16], A.add, ["pk", "kz"], ["kst"])
         act(T.zc[:, 384:768], Zall.indirect(T.bkl[:, 24:48]), Zk + ["bkl"], ["zcS"])
         cp(T.zc[:, 0:384], Zall.indirect(T.bkl[:, 0:24]), Zk + ["bkl"], ["zcV"])
@@ -451,13 +474,11 @@ def rank_program(g, core, T, topo):
         if t < 2:
             sinit(SPIECE[t][1], SPIECE[t][2])
         for jb in range(3):
-            ts(T.ps2[:, 64 + jb:124:3], T.iof[:, 0:20], T.sm[:, 12 + jb:13 + jb], A.not_equal, ["iof", "kst"], ["B2"])
-        for jb in range(3):
             ts(T.ps2[:, jb:60:3], T.iof[:, 0:20], T.sm[:, 12 + jb:13 + jb], A.is_equal, ["iof", "kst", "nK"], ["B2"], T.sm[:, 4 + jb:5 + jb], A.mult)
         if old:
             for a in range(2):
                 tt(T.pr[:, 63 * a:63 * a + 63], T.cur[:, 63 * a:63 * a + 63], eqo, A.mult, ["cur", "B0"], ["pr"])
-        tt(T.ts3[:, 0:60], st[:, 0:60], T.ps2[:, 64:124], A.mult, [stk, "B2"], ["ts3P"])
+        tt(T.kc[:, 60:120], T.kc[:, 0:60], T.ps2[:, 0:60], A.max, ["kc", "B2"], ["kraw"])
         if old:
             scan(T.osm[:, :], T.sumr[:, :], T.pr[:, :], A.mult, A.add, ["sumr", "pr"], ["osm"])
 
@@ -467,14 +488,18 @@ def rank_program(g, core, T, topo):
                 ts(T.dd[:, 32 * jb + 16 * o:32 * jb + 16 * o + 16], T.dm[:, :], T.osm[:, e:e + 1], A.mult, ["dm", "osm"], ["dd"])
 
         if not last:
-            tt(so[:, 0:60], T.ts3[:, 0:60], T.ps2[:, 0:60], A.add, ["ts3P", "B2"], ["soP"])
-        else:
-            ts(T.fa[:, 0:126], T.cur[:, :], OFF - 0.5, A.is_ge, ["cur"], ["fa"], -8192.0, A.mult)
-        scan(T.sk[0:48, :], T.srst[0:48, :], T.ps4[0:48, 0:256], A.add, A.max, ["srst", "B4"], ["sk"])
-        if not last:
             kok = "ko%d" % t
-            klist(T[kok], kok, so, "soP")
-            send(T[kok][:, :], [kok + "a", kok + "b", kok + "c"], "kl%d" % (t + 1))
+            cp(T[kok][:, 0:60], T.kc[:, 60:120], ["kraw"], [kok])
+            send(T[kok][:, :], [kok, "koz%d" % t], "kl%d" % (t + 1))
+        else:
+            ts(T.kc[:, 0:60], T.kc[:, 60:120], 1023, A.bitwise_and, ["kraw"], ["kc"])
+        for v in swap[1:]:
+            swrite(v, 0, 6)
+        scan(T.sk[0:48, :], T.srst[0:48, :], T.ps4[0:48, 0:256], A.add, A.max, ["srst", "B4"], ["sk"])
+        if last:
+            cp(T.sf[:, 120:180], T.kc[:, 0:60], ["kc"], ["sfk"])
+            send(T.sf[:, 120:180], ["sfk"], "homek")
+            ts(T.fa[:, 0:126], T.cur[:, :], OFF - 0.5, A.is_ge, ["cur"], ["fa"], -8192.0, A.mult)
         key = T.sk[0:48, 15:256:16]
         MG = 1.5 * 2 ** 28
         ts(T.kr[0:48, :], key, MG, A.add, ["sk"], ["kr"], MG, A.subtract)
@@ -492,110 +517,114 @@ def rank_program(g, core, T, topo):
             mm(T.ps1[:, 0:3], T.onb[:, :], T.hitb[:, 0:3], ["onb", "hitb"], ["B1"])
         else:
             tt(T.pr[:, :], T.cur[:, :], T.fa[:, 0:126], A.add, ["cur", "fa"], ["pr"])
+        for v in swap[1:]:
+            swrite(v, 6, 12)
         scan(T.pk2[:, :], T.pst[:, :], T.ps6[:, 0:48], A.max, A.min, ["pst", "B6"], ["pk2"])
         if last:
             ts(T.fa[:, 0:126], T.pr[:, :], OFF, A.add, ["pr"], ["fa"], -1.0, A.max)
+        if old:
+            tt(T.fn[:, 0:32], T.ps7[:, 0:32], T.msk2[:, 32:64], A.add, ["B7", "msk2"], ["fnO"])
+            tt(T.fn[:, 96:128], T.ps7[:, 32:64], T.msk2[:, 32:64], A.add, ["B7", "msk2"], ["fnO"])
+            cp(T.fn[:, 128:160], T.ps7[:, 0:32], ["B7"], ["fnO"])
         cp(T.fl[:, 0:4], T.pk2[:, 7:32:8], ["pk2"], ["flA"])
         cp(T.fl[:, 4:10], T.pk2[:, 7:48:8], ["pk2"], ["flB"])
         if old:
-            for jb in (2, 1, 0):
-                for o in range(2):
-                    e, c = 4 * jb + 2 + o, 63 * o + 21 * jb + 20
-                    act(T.dn[:, e:e + 1], T.osm[:, c:c + 1], ["osm", "padn"], ["dnO"], func=AF.Identity, bias=T.padf[:, e:e + 1])
-            cp(T.fn[:, 128:160], T.ps7[:, 0:32], ["B7"], ["fnO"])
+            tt(T.fn[:, 256:320], T.ps7[:, 32:96], T.msk2[:, :], A.add, ["B7", "msk2"], ["fnO"])
         tt(T.fn[:, 32:96], twin.indirect(T.fl[:, 0:4]), T.tmp[:, 64:128], A.add, ["tf", "flA", "tmpB"], ["fnA"])
         tt(T.fn[:, 160:256], twin.indirect(T.fl[:, 4:10]), T.msk[:, :], A.add, ["tf", "flB", "msk"], ["fnB"])
         scan(T.ns[:, 0:64], T.pns[:, :], T.fn[:, 32:96], A.max, A.min, ["pns", "fnA"], ["nsA"])
-        if old:
-            tt(T.fn[:, 256:320], T.ps7[:, 32:96], T.msk2[:, :], A.add, ["B7", "msk2"], ["fnO"])
-        scan(T.ns[:, 64:96], T.pns[:, 0:32], T.fn[:, 224:256], A.max, A.min, ["pns", "fnB"], ["nsB"])
         reg = [(0, 64), (64, 192), (128, 320)]
         eo = [0, 256, 768]
         nsk = ["nsA", "nsB"]
         M = 4 if old else 2
 
+        def name(jb, m):
+            return T.ns[:, 32 * jb + 16 * m + 15:32 * jb + 16 * m + 16] if m < 2 else T.osm[:, 63 * (m - 2) + 21 * jb + 20:63 * (m - 2) + 21 * jb + 21]
+
         def eq(jb, m):
             a, b = reg[jb]
             w = b - a
-            col = T.ns[:, 32 * jb + 16 * m + 15:32 * jb + 16 * m + 16] if m < 2 else T.osm[:, 63 * (m - 2) + 21 * jb + 20:63 * (m - 2) + 21 * jb + 21]
+            col = name(jb, m)
             pos = eo[jb] + w * m
-            ts(T.eqb[:, pos:pos + w], T.fn[:, a:b], col, A.is_equal, ["fnO", "fnA", "fnB"] + (["fnP"] if jb < 2 else []) + [("nsB" if jb == 2 else "nsA") if m < 2 else "osm"], ["e%d" % jb], 8192.0, A.mult)
+            ts(T.eqb[:, pos:pos + w], T.fn[:, a:b], col, A.is_equal, ["fnO", "fnA"] + (["fnB"] if jb > 0 else []) + [("nsB" if jb == 2 else "nsA") if m < 2 else "osm"], ["e%d" % jb], 8192.0, A.mult)
 
         def count(jb):
             w = (reg[jb][1] - reg[jb][0]) * M // 2
             o = eo[jb] // 2
-            scan(T.cn[:, o:o + w], T.eqb[:, eo[jb]:eo[jb] + w], T.eqb[:, eo[jb] + w:eo[jb] + 2 * w], A.add, A.add, ["e%d" % jb], ["cn%d" % jb], -8192.0 * M)
+            scan(T.cn[:, o:o + w], T.eqb[:, eo[jb]:eo[jb] + w], T.eqb[:, eo[jb] + w:eo[jb] + 2 * w], A.add, A.add, ["e%d" % jb], ["cn%d" % jb], OFF - 8192.0 * M)
             return T.cn[:, o + w - 1:o + w]
 
-        def place(jb, col):
-            ts(T.of1[:, 4 * jb:4 * jb + 4], T.dn[:, 4 * jb:4 * jb + 4], col, A.add, ["dn", "dnO", "cn%d" % jb], ["of1%d" % jb], 0.0, A.min)
+        def place(jb, col, ms_=range(4)):
+            for m in ms_:
+                if m < M:
+                    e = 4 * jb + m
+                    ts(T.offs[:, 12 * t + e:12 * t + e + 1], col, name(jb, m), A.add, nsk + ["osm", "padu", "cn%d" % jb], ["offs%d" % jb], T.padf[:, e:e + 1], A.min)
 
-        if old:
-            tt(T.fn[:, 0:32], T.ps7[:, 0:32], T.msk2[:, 32:64], A.add, ["B7", "msk2"], ["fnP"])
-            tt(T.fn[:, 96:128], T.ps7[:, 32:64], T.msk2[:, 32:64], A.add, ["B7", "msk2"], ["fnP"])
-        for jb in (2, 1, 0):
-            for m in range(2):
-                e, c = 4 * jb + m, 32 * jb + 16 * m + 15
-                act(T.dn[:, e:e + 1], T.ns[:, c:c + 1], nsk + ["padn"], ["dn"], func=AF.Identity, bias=T.padf[:, e:e + 1])
+        for m in range(2, M):
+            eq(0, m)
+        scan(T.ns[:, 64:96], T.pns[:, 0:32], T.fn[:, 224:256], A.max, A.min, ["pns", "fnB"], ["nsB"])
         for m in list(range(2, M)) + [0, 1]:
             eq(2, m)
+        for m in range(2, M):
+            eq(1, m)
         for m in range(2):
             ts(T.pl[:, 12 * t + m:12 * t + 12:4], T.ns[:, 31 - 16 * m:96:32], OFF, A.add, nsk, [plk])
         if not last:
-            act(T.zp[:, :], Zall.indirect(T.pl[:, 12 * t:12 * t + 12]), Zk + [plk], ["zp"])
-            halves(t + 1)
+            halves(t + 1, lambda: act(T.zp[:, :], Zall.indirect(T.pl[:, 12 * t:12 * t + 12]), Zk + [plk], ["zp"]))
             if SWAPS[t]:
                 sread(SWAPS[t][0])
         else:
             sread(t)
+
+        def named(jb, col):
+            ts(T.v6[:, 2 * jb:2 * jb + 2], T.v6[:, 2 * jb:2 * jb + 2], col, A.subtract, ["v6a", "cn%d" % jb], ["v6%d" % jb], -1.0, A.max)
+            for a in range(2):
+                act(T.ps2[:, 60 * a + jb:60 + 60 * a:3], so[:, 198 + 21 * jb:218 + 21 * jb], ["eqk", "v6%d" % jb], ["B2"], scale=T.v6[:, 2 * jb + a:2 * jb + a + 1])
+                c = 63 * a + 21 * jb
+                tt(T.ts3[:, 60 * a + jb:60 + 60 * a:3], T.fa[:, c:c + 20], T.ps3[:, 21 * jb:21 * jb + 20], A.mult, ["fa", "B3"], ["ts3N"])
+
         c2 = count(2)
-        for m in range(M):
-            eq(1, m)
-        place(2, c2)
-        if not last:
-            tt(so[:, 123:186], T.cur[:, 63:126], neq, A.mult, ["cur", "B3"], ["soB"])
-        c1 = count(1)
-        for m in range(M):
-            eq(0, m)
-        place(1, c1)
-        if not last:
-            tt(so[:, 60:123], T.cur[:, 0:63], neq, A.mult, ["cur", "B3"], ["soA"])
-        c0 = count(0)
         if last:
+            ts(T.v6[:, 0:6], T.ns[:, 15:96:16], 2 * OFF, A.add, nsk, ["v6a"])
+        for m in range(2):
+            eq(1, m)
+        for m in range(2):
+            eq(0, m)
+        if last:
+            named(2, c2)
+            c1 = count(1)
+            c0 = count(0)
+            place(2, c2)
+            named(1, c1)
+            named(0, c0)
             break
         o = 12 * t
-        tt(so[:, 190:198], T.of1[:, 4:12], T.pado[:, 4:12], A.add, ["of11", "of12", "pado", soz], ["of2A"])
+        place(2, c2, range(2))
+        c1 = count(1)
+        c0 = count(0)
+        place(2, c2, range(2, 4))
+        place(1, c1)
         place(0, c0)
-        ts(T.offs[:, o + 4:o + 12], so[:, 190:198], OFF, A.add, ["of2A"], ["offsA"])
-        tt(so[:, 186:190], T.of1[:, 0:4], T.pado[:, 0:4], A.add, ["of10", "pado", soz], ["of2B"])
-        cp(Zall.indirect(T.offs[:, o + 4:o + 12]), T.zp[:, 64:192], ["offsA", "zp"], Zk)
-        ts(T.offs[:, o:o + 4], so[:, 186:190], OFF, A.add, ["of2B"], ["offsB"])
-        send(so[:, :], ["soP", "soA", "soB", "of2A", "of2B", "eqk", soz], "st%d" % (t + 1))
-        wholes(t + 1)
-        cp(Zall.indirect(T.offs[:, o:o + 4]), T.zp[:, 0:64], ["offsB", "zp"] + Zk, Zk)
-        answers(t + 1, SWAPS[t])
+        wholes(t + 1, 0, N_CH[0], "natA")
+        cp(Zall.indirect(T.offs[:, o:o + 12]), T.zp[:, :], ["offs0", "offs1", "offs2", "zp"], Zk)
 
-    cols = [c0, c1, c2]
-    ts(T.v6[:, 0:6], T.ns[:, 15:96:16], OFF, A.add, nsk, ["v6a"])
-    for jb in (2, 1, 0):
-        ts(T.v6[:, 2 * jb:2 * jb + 2], T.v6[:, 2 * jb:2 * jb + 2], cols[jb], A.subtract, ["v6a", "cn%d" % jb], ["v6%d" % jb], -1.0, A.max)
-    for jb in (2, 1, 0):
-        for a in range(2):
-            act(T.ps2[:, 60 + 60 * a + jb:120 + 60 * a:3], so[:, 198 + 21 * jb:218 + 21 * jb], ["eqk", "v6%d" % jb], ["B2"], scale=T.v6[:, 2 * jb + a:2 * jb + a + 1])
-    for a in range(2):
-        for jb in range(3):
-            c = 63 * a + 21 * jb
-            tt(T.ts3[:, 60 + 60 * a + jb:120 + 60 * a:3], T.fa[:, c:c + 20], T.ps3[:, 21 * jb:21 * jb + 20], A.mult, ["fa", "B3"], ["ts3N"])
+        def names_go():
+            tt(so[:, 123:186], T.cur[:, 63:126], neq, A.mult, ["cur", "B3"], ["soB"])
+            tt(so[:, 60:123], T.cur[:, 0:63], neq, A.mult, ["cur", "B3"], ["soA"])
+            ts(so[:, 186:198], T.offs[:, o:o + 12], -OFF, A.add, ["offs0", "offs1", "offs2", soz], ["of2"])
+            send(so[:, 60:SW], ["soA", "soB", "of2", "eqk", soz], "st%d" % (t + 1), 60)
+
+        answers(t + 1, names_go)
+
+    place(1, c1)
     place(0, c0)
-    tt(T.sf[:, :], T.ts3[:, 0:180], T.ps2[:, 0:180], A.add, ["ts3P", "ts3N", "B2"], ["sf"])
-    send(T.sf[:, :], ["sf"], "home")
-    tt(so[:, 186:198], T.of1[:, :], T.pado[:, :], A.add, ["of10", "of11", "of12", "pado", soz], ["of2A"])
-    ts(T.offs[:, 12 * t:12 * t + 12], so[:, 186:198], OFF, A.add, ["of2A"], ["offsA", "offsB"])
+    tt(T.sf[:, 0:120], T.ts3[:, 0:120], T.ps2[:, 0:120], A.add, ["ts3N", "B2"], ["sf"])
+    send(T.sf[:, 0:120], ["sf"], "home")
     swrite(t)
+    dma("y", T.yk[:, :], T.homek[:, :], "dout", ["homek"], [])
     dma("y", T.ys[:, :], T.S[0:128:16, 0:4096], "dout", Sk, [])
-    dma("y", T.yk[:, :], T.home[:, 0:60], "dout", ["home"], [])
-    dma("s", T.ya[:, :], T.home[:, 60:120], "dout", ["home"], [])
-    dma("y", T.yb[:, :], T.home[:, 120:180], "dout", ["home"], [])
+    dma("s", T.ya[:, :], T.home[:, 0:60], "dout", ["home"], [])
+    dma("y", T.yb[:, :], T.home[:, 60:120], "dout", ["home"], [])
     need("y", "dout", 64)
     need("g", "lsem", cnt["sent"])
     for q in ("v", "s", "p", "g"):

@@ -3,44 +3,43 @@ from concourse.mybir import dt, AluOpType, AxisListType, ActivationFunctionType
 
 VI = 6
 PADC = 4480
-P_CH = [56, 40, 72, 72, 48]
-P0_CH = [72, 72, 72, 72]
+P_CH = [64, 32, 48, 96, 96]
 PH = sum(P_CH)
 NP = PH // 24
-N_CH = [96, 128, 96, 48, 16]
+N_CH = [144, 96, 32, 16]
 NN = sum(N_CH)
 KN = 3 * NP
-ZS = 128
+B0 = 96
+ZS = 96
 YN, YW = 16 * PH, 16 * (PH + NN)
 OFF = 2048.0
 BIG = 30000.0
-HI = 8256.0
-SW = 264
+SW = 261
 
 _sb = {
-    "truv": (4096, "bfloat16"), "Z": (PADC, "bfloat16"), "S": (PADC, "float32"), "iot": (4096, "float32"),
-    "booki": (3072, "int32"), "kc": (120, "int32"), "sgi": (256, "int32"), "sgl": (256, "uint16"), "kmi": (64, "int32"),
+    "truv": (4096, "bfloat16"), "Z": (PADC, "bfloat16"), "S": (PADC, "float32"), "iot": (PADC, "float32"),
+    "booki": (3072, "int32"), "kc": (120, "int32"), "sgi": (256, "int32"), "sgl": (256, "uint16"), "sgh": (256, "float16"), "kmi": (64, "int32"),
     "G": (YW, "bfloat16"), "nat": (NN, "uint16"), "H": (16 * PH, "bfloat16"), "ysc": (YW, "bfloat16"),
-    "rst": (16 * max(N_CH), "bfloat16"), "rst8": (16 * max(P_CH + P0_CH), "bfloat16"),
-    "blo": (3072, "int32"), "thi": (2 * PH, "bfloat16"), "tlo": (2 * PH, "bfloat16"),
-    "hsel": (512, "bfloat16"), "la": (PH, "uint16"), "lb": (PH, "uint16"), "ab": (63, "float32"),
-    "pi": (1, "int32"), "pj": (1, "int32"), "pg": (1, "int32"), "colf": (16, "float32"),
-    "iof": (128, "float32"), "iog": (128, "float32"), "ioj": (128, "float32"), "io8": (48, "float32"), "iob": (48, "float32"),
-    "idb": (128, "bfloat16"), "idh": (128, "float16"), "bof": (128, "float32"), "onb": (128, "bfloat16"),
-    "dm": (16, "float32"), "sel8": (8, "float32"), "cntw": (8, "bfloat16"), "usel": (8, "bfloat16"), "scw": (16, "bfloat16"),
-    "selj": (384, "float16"), "mk5": (48, "float16"), "mk6": (48, "float16"), "pst": (48, "float32"), "tmp": (192, "float32"),
-    "msk": (96, "float32"), "msk2": (64, "float32"), "pns": (64, "float32"), "hrow": (160, "bfloat16"), "crow": (160, "bfloat16"), "hrf": (160, "float32"),
-    "srst": (256, "float32"), "padf": (12, "float32"), "pado": (12, "float32"), "sumr": (126, "float32"),
+    "rst": (16 * max(N_CH), "bfloat16"), "rst8": (16 * max(P_CH), "bfloat16"), "thi": (2 * PH, "float16"),
+    "hsel": (512, "float16"), "ll": (2 * PH, "uint16"), "ab": (63, "float32"),
+    "pi": (1, "int32"), "pj": (1, "int32"), "pg": (1, "int32"), "cjl": (1, "int32"), "colf": (16, "float32"),
+    "iof": (144, "float32"), "iog": (128, "float32"), "ioj": (128, "float32"), "io8": (72, "float32"), "iom": (96, "float32"), "ion": (160, "float32"),
+    "sgn": (128, "float32"), "scw": (128, "bfloat16"), "id2": (128, "float16"), "mk7": (128, "float16"),
+    "pos": (512, "bfloat16"), "mkn": (160, "float32"),
+    "idb": (128, "bfloat16"), "idh": (144, "float16"), "bof": (128, "float32"), "onb": (256, "bfloat16"), "on2": (48, "bfloat16"),
+    "cntw": (8, "bfloat16"), "usel": (8, "bfloat16"),
+    "selj": (384, "float16"), "mk5": (72, "float16"), "pst": (72, "float32"), "tmp": (144, "float32"),
+    "msk": (96, "float32"), "pns": (32, "float32"), "hrow": (160, "bfloat16"), "crow": (160, "bfloat16"),
+    "padf": (18, "float32"), "padh": (18, "float32"), "curh": (126, "float32"), "sumr": (126, "float32"),
     "lt": (912, "bfloat16"),
-    "hi": (160, "float32"), "su": (160, "float32"), "uint": (64, "int32"), "nk": (16, "float16"), "pk": (48, "float32"),
+    "hi": (160, "float32"), "su": (160, "int32"), "uint": (64, "int32"), "nk": (24, "float16"), "kz": (8, "float16"), "pk": (72, "float32"),
     "nl": (4, "uint16"), "bkl": (48, "uint16"), "zc": (768, "bfloat16"), "tf": (768, "float32"),
-    "sm": (32, "float32"), "hitb": (4, "bfloat16"), "pr": (126, "float32"), "osm": (126, "float32"),
-    "dd": (96, "float16"), "sk": (256, "float32"), "kr": (16, "float32"), "qh": (16, "float16"), "pk2": (48, "float32"),
-    "fl": (10, "uint16"), "fn": (320, "float16"), "ns": (96, "float32"),
-    "eqb": (1536, "bfloat16"), "cn": (768, "bfloat16"), "dn": (12, "float32"), "of1": (12, "float32"),
+    "sm": (4, "float32"), "hitb": (4, "bfloat16"), "pr": (126, "float32"), "osm": (126, "float32"), "sk": (12, "int32"),
+    "fl": (6, "uint16"), "fo": (6, "uint16"), "fn": (320, "float16"), "ns": (96, "float32"),
+    "eqb": (1536, "bfloat16"), "cn": (768, "bfloat16"), "xo": (12, "float32"),
     "offs": (12 * VI, "uint16"), "pl": (12 * VI, "uint16"), "zp": (192, "bfloat16"), "sp": (192, "float32"),
-    "ts3": (192, "float32"), "cc": (1, "float32"), "sf": (180, "float32"), "cur": (126, "float32"), "boh": (128, "float16"),
-    "fa": (128, "float32"), "fb": (128, "float32"), "v6": (8, "float32"), "home": (120, "float32"), "homek": (60, "float32"),
+    "ts3": (120, "float32"), "q1": (120, "float32"), "x1": (120, "float32"), "cc": (1, "float32"), "sf": (180, "float32"), "cur": (126, "float32"),
+    "fa": (128, "float32"), "fb": (128, "float32"), "home": (120, "float32"), "homek": (60, "float32"),
 }
 SCRATCH = {}
 for _k in _sb:
@@ -48,11 +47,11 @@ for _k in _sb:
 for _t in range(VI):
     SCRATCH["st%d" % _t] = ("sbuf", [128, SW], "float32")
     SCRATCH["so%d" % _t] = ("sbuf", [128, SW], "float32")
-    SCRATCH["kl%d" % _t] = ("sbuf", [128, 64], "uint16")
-    SCRATCH["ko%d" % _t] = ("sbuf", [128, 64], "uint16")
+    SCRATCH["kl%d" % _t] = ("sbuf", [128, 60], "uint16")
+    SCRATCH["ko%d" % _t] = ("sbuf", [128, 60], "uint16")
 for _t in range(8):
     SCRATCH["ps%d" % _t] = ("psum", [128, 512], "float32")
-SEMAPHORES = (["sv", "ss", "sp_", "sg_", "lsg", "ltr", "lbk", "lbw", "lkm", "lwt", "lrp", "dout", "lsem"]
+SEMAPHORES = (["sv", "ss", "sp_", "sg_", "lsg", "ltr", "lbk", "lbw", "lkm", "lwt", "dout", "lsem"]
               + ["a_st%d" % _t for _t in range(1, VI)] + ["a_kl%d" % _t for _t in range(1, VI)] + ["a_home", "a_homek"])
 
 
@@ -144,156 +143,160 @@ def rank_program(g, core, T, topo):
     def iota(out, pattern, base, cm, w):
         E("g", lambda e: e.iota(out, pattern, base, cm, allow_small_or_imprecise_dtypes=True), [], w)
 
-    dma("y", T.booki[:, 0:1024], T.book[:, :], "lbk", [], ["bookA"])
-    dma("s", T.kmi[:, 0:60], T.km0[:, :], "lkm", [], ["kmi"])
     dma("y", T.sgi[:, :], T.sg0[:, :], "lsg", [], ["sgi"])
+    dma("s", T.kmi[:, 0:60], T.km0[:, :], "lkm", [], ["kmi"])
     dma("y", T.truv[:, :], T.tru[:, :], "ltr", [], ["truv"])
+    dma("y", T.booki[:, 0:1024], T.book[:, :], "lbk", [], ["bookA"])
     dma("y", T.kmi[:, 60:61], T.wt[:, :], "lwt", [], ["wti"])
+    deps("y", ["bookA"], [])
     for i in (1, 2):
         g.sync.dma_start(out=T.booki[:, 1024 * i:1024 * i + 1024], in_=T.book[:, :]).then_inc(T.sem.lbw, 16)
     note("y", [], ["bookB"], ("lbw", 32, "dma"))
 
     iota(T.pi[:, :], [[0, 1]], 0, 1, ["pi"])
-    iota(T.iof[:, :], [[1, 128]], 0, 0, ["iof"])
+    iota(T.iof[:, :], [[1, 144]], 0, 0, ["iof"])
     iota(T.iog[:, :], [[1, 8], [0, 16]], 0, 0, ["iog"])
     iota(T.ioj[:, :], [[0, 8], [1, 16]], 0, 0, ["ioj"])
-    iota(T.io8[:, :], [[0, 6], [1, 8]], 0, 0, ["io8"])
-    iota(T.iob[:, :], [[256, 3], [0, 16]], 15, 0, ["iob"])
-    iota(T.hrf[:, :], [[0, 8], [1, 20]], -10, 0, ["hrf"])
-    iota(T.padf[:, :], [[32, 12]], 4096 - int(OFF), 0, ["padf"])
-    iota(T.rst8[:, :], [[0, max(P_CH + P0_CH) * 2], [-512, 8]], 512, 0, ["rst8"])
+    iota(T.io8[:, :], [[0, 9], [1, 8]], 0, 0, ["io8"])
+    iota(T.sgn[:, :], [[0, 64], [2048, 2]], -1024, 0, ["sgn"])
+    iota(T.ion[:, 0:64], [[0, 2], [1, 16], [0, 2]], 0, 0, ["ion"])
+    iota(T.ion[:, 64:160], [[50, 3], [1, 16], [0, 2]], -100, 0, ["ion"])
+    iota(T.iom[:, :], [[50, 3], [0, 2], [1, 16]], -100, 0, ["iom"])
+    iota(T.padh[:, 0:12], [[64, 3], [-16, 4]], 2048 + 48, 0, ["padh"])
+    iota(T.padh[:, 12:18], [[64, 3], [-16, 2]], 2048 + 16, 0, ["padh"])
+    iota(T.curh[:, :], [[16, 2], [64, 3], [0, 21]], 2048 - int(OFF) // 2, 0, ["curh"])
+    iota(T.hrow[0:1, :], [[0, 8], [1, 20]], -10, 0, ["hrow"])
+    iota(T.pos[0:1, 0:256], [[1, 256]], 0, 0, ["pos"])
+    iota(T.pos[0:1, 256:512], [[256, 2], [0, 128]], 256, 0, ["pos"])
+    iota(T.rst8[:, :], [[0, max(P_CH) * 2], [-512, 8]], 512, 0, ["rst8"])
     iota(T.rst[:, :], [[0, max(N_CH)], [-512, 16]], 512, 0, ["rst"])
-    iota(T.iot[:, :], [[1, 4096]], -int(OFF), 0, ["iot"])
+    iota(T.iot[:, :], [[1, PADC]], -int(OFF), 0, ["iot"])
     C = T.colf
-    ID = AF.Identity
     ms(T.Z[:, 4096:PADC], 0.0, ["Zpad"])
     ts(T.pj[:, :], T.pi[:, :], 15, A.bitwise_and, ["pi"], ["pj"])
     ts(T.pg[:, :], T.pi[:, :], 4, A.arith_shift_right, ["pi"], ["pg"])
     ts(T.uint[:, 0:1], T.pi[:, :], 7, A.bitwise_and, ["pi"], ["uI"])
     cp(C[:, 0:1], T.pi[:, :], ["pi"], ["c0"])
+    ts(T.cjl[:, :], T.pi[:, :], 1, A.arith_shift_right, ["pi"], ["cjl"], 7, A.bitwise_and)
     cp(C[:, 1:2], T.pj[:, :], ["pj"], ["c1"])
     cp(C[:, 2:3], T.pg[:, :], ["pg"], ["c2"])
     cp(C[:, 10:11], T.uint[:, 0:1], ["uI"], ["c10"])
-    for t in range(VI - 1):
-        ms(T["ko%d" % t][:, 60:64], 0, ["koz%d" % t])
-    ms(T.srst[:, :], 1.0, ["srst"])
-    ms(T.sumr[:, :], 1.0, ["sumr"])
-    ms(T.crow[:, :], -17.0 * 2 ** 24, ["crow"])
+    ms(T.crow[0:1, :], -272.0, ["crow"])
+    cp(C[:, 3:4], T.cjl[:, :], ["cjl"], ["c3"])
     ms(T.onb[:, :], 1.0, ["onb"])
-    ms(T.S[:, 4096:PADC], 0.0, ["Spad"])
-    ms(T.fn[:, :], BIG, ["fnO", "fnA", "fnB"])
-    ms(T.srst[:, 0:256:16], -1048576.0, ["srst"], ["srst"])
-    ms(T.sumr[:, 0:126:21], 0.0, ["sumr"], ["sumr"])
-    ms(T.crow[:, 0:160:20], 2.0 ** 26, ["crow"], ["crow"])
-    act(C[:, 3:4], C[:, 1:2], ["c1"], ["c3"], scale=16.0)
-    act(C[:, 4:5], C[:, 1:2], ["c1"], ["c4"], scale=2.0)
-    for jb in range(3):
-        act(C[:, 5 + jb:6 + jb], C[:, 0:1], ["c0"], ["c5"], bias=-16.0 * jb)
-    for t in range(VI):
-        act(T["so%d" % t][:, 186:SW], T.iof[:, 0:SW - 186], ["iof"], ["soz%d" % t], scale=0.0)
-    act(T.msk[:, 0:64], T.iof[:, 0:64], ["iof"], ["msk"], scale=0.0)
-    act(T.msk2[:, 0:32], T.iof[:, 0:32], ["iof"], ["msk2"], scale=0.0)
-    act(T.pado[:, :], T.padf[:, :], ["padf", "c4"], ["pado"], func=ID, bias=C[:, 4:5])
-    act(T.tmp[:, 128:176], T.iob[:, :], ["iob", "c3"], ["tmpC"], func=ID, bias=C[:, 3:4])
-    act(T.hrow[:, :], T.hrf[:, :], ["hrf"], ["hrow"], scale=2.0 ** 20)
+    ms(T.on2[0:1, :], 2.0 ** 20, ["on2"])
+    ts(T.idh[:, :], T.iof[:, :], C[:, 0:1], A.is_equal, ["iof", "c0"], ["idh"])
+    ms(T.fn[:, :], BIG, ["fnO", "fnP", "fnA", "fnB"])
+    ms(T.crow[0:1, 0:160:20], 64.0, ["crow"], ["crow"])
+    act(C[:, 4:5], C[:, 1:2], ["c1"], ["c4"], bias=0.5)
+    act(T.sumr[:, :], T.iof[:, 0:126], ["iof"], ["sumr"], scale=0.0, bias=1.0)
+    for i in range(3):
+        act(T.S[:, 4096 + 128 * i:4224 + 128 * i], T.iof[:, 0:128], ["iof"], ["Spad"], scale=0.0)
+    act(T.so0[:, 186:198], T.iof[:, 0:12], ["iof"], ["of2"], scale=0.0)
     ts(C[:, 11:12], C[:, 1:2], 7.5, A.is_lt, ["c1"], ["c11"])
     ts(C[:, 12:13], C[:, 1:2], 7.5, A.is_gt, ["c1"], ["c11"])
     ts(T.bof[:, :], T.iog[:, :], C[:, 2:3], A.is_equal, ["iog", "c2"], ["bof"])
     for h in range(2):
         ts(T["f" + "ab"[h]][:, :], T.ioj[:, :], -8.0 * h, A.add, ["ioj", "c10"], ["f" + "ab"[h]], C[:, 10:11], A.is_equal)
-    ts(T.sel8[:, :], T.iof[:, 0:8], C[:, 2:3], A.is_equal, ["iof", "c2"], ["sel8"])
+    ms(T.sumr[:, 0:126:21], 0.0, ["sumr"], ["sumr"])
     for h in range(2):
         tt(T["f" + "ab"[h]][:, :], T["f" + "ab"[h]][:, :], T.bof[:, :], A.mult, ["f" + "ab"[h], "bof"], ["f" + "ab"[h]])
+    ts(T.sgh[:, :], T.sgi[:, :], -OFF, A.add, ["sgi"], ["sgh"])
+    act(T.sgl[:, :], T.sgi[:, :], ["sgi"], ["sgl"])
     for h in range(2):
         for o in range(2):
             c = 256 * o + 128 * h
             act(T.hsel[:, c:c + 128], T["f" + "ab"[h]][:, :], ["f" + "ab"[h], "c11"], ["hsel"], scale=C[:, 11 + o:12 + o])
-    ts(T.tmp[:, 0:48], T.io8[:, :], C[:, 2:3], A.is_gt, ["io8", "c2"], ["tmpA"], BIG, A.mult)
-    ts(T.tmp[:, 64:128], T.ioj[:, 0:64], C[:, 1:2], A.is_gt, ["ioj", "c1"], ["tmpB"], BIG, A.mult)
 
-    def later_constants():
-        cp(T.boh[:, :], T.bof[:, :], ["bof"], ["boh"])
-        ts(T.idb[:, :], T.iof[:, :], C[:, 0:1], A.is_equal, ["iof", "c0"], ["idb"])
-        ts(T.idh[:, :], T.iof[:, :], C[:, 0:1], A.is_equal, ["iof", "c0"], ["idh"])
-        ts(T.dm[:, :], T.ioj[:, 0:16], C[:, 1:2], A.is_equal, ["ioj", "c1"], ["dm"])
-        for jb in range(3):
-            ts(T.selj[0:48, 128 * jb:128 * jb + 128], T.ioj[0:48, 0:128], C[0:48, 5 + jb:6 + jb], A.is_equal, ["ioj", "c5"], ["selj"])
-        tt(T.mk6[:, :], T.tmp[:, 0:48], T.tmp[:, 128:176], A.add, ["tmpA", "tmpC"], ["mk6"])
-        for i in range(6):
-            ts(T.mk5[:, 8 * i:8 * i + 8], T.tmp[:, 8 * i:8 * i + 8], -1536.0 * (i % 2), A.add, ["tmpA"], ["mk5"])
-        cp(T.offs[:, 0:12], T.padf[:, :], ["padu"], ["offs0", "offs1", "offs2"])
-        ms(T.pl[:, 0:12], 4096, ["pl0"])
-        for a in range(2):
-            for jb in range(3):
-                c = 63 * a + 21 * jb
-                act(T.cur[:, c:c + 21], T.iof[:, 0:21], ["iof", "pado"], ["cur"], func=ID, scale=0.0, bias=T.pado[:, 4 * jb + a:4 * jb + a + 1])
-        act(T.cntw[:, :], T.sel8[:, :], ["sel8"], ["cntw"], scale=2.0 ** 25)
-        act(T.scw[:, 0:8], T.sel8[:, :], ["sel8"], ["scw"], scale=32.0)
-        act(T.scw[:, 8:16], T.sel8[:, :], ["sel8"], ["scw"], scale=-32.0)
-        act(T.pst[:, :], T.tmp[:, 0:48], ["tmpA"], ["pst"], scale=-4.0, bias=2 * BIG)
-        act(T.pns[:, :], T.tmp[:, 64:128], ["tmpB"], ["pns"], scale=-4.0, bias=2 * BIG)
-        act(T.msk[:, 64:96], T.tmp[:, 64:96], ["tmpB"], ["msk"])
-        act(T.msk2[:, 32:64], T.tmp[:, 64:96], ["tmpB"], ["msk2"])
+    def s_turn(r, bank):
+        mm(T["ps%d" % bank][:, 256 * (r % 2):256 * (r % 2) + 256], T.idh[:, r:r + 128], T.sgh[:, :], ["idh", "sgh"], ["B%d" % bank])
 
-    act(T.padf[:, :], T.pado[:, :], ["pado"], ["padu", "padf"], bias=OFF)
+    def s_lay(r, bank, q):
+        src = T["ps%d" % bank][:, 256 * (r % 2):256 * (r % 2) + 256]
+        if q == "v":
+            ts(T.S[:, r:4096:16], src, OFF, A.add, ["B%d" % bank], ["Sa"])
+        else:
+            act(T.S[:, r:4096:16], src, ["B%d" % bank], ["Sb"], bias=OFF)
 
-    cp(T.kl0[:, 0:60], T.kmi[:, 0:60], ["kmi"], ["kl0"])
-    ts(T.blo[:, 0:1024], T.booki[:, 0:1024], 63, A.bitwise_and, ["bookA"], ["blo"])
-    deps("y", ["blo"], [])
-    for i in (1, 2):
-        g.sync.dma_start(out=T.blo[:, 1024 * i:1024 * i + 1024], in_=T.blo[:, 0:1024]).then_inc(T.sem.lrp, 16)
-    note("y", [], ["brep"], ("lrp", 32, "dma"))
-    cp(T.sgl[:, :], T.sgi[:, :], ["sgi"], ["sgl"])
+    for r in range(10):
+        s_turn(r, r // 2)
+    for r in range(6):
+        s_lay(r, r // 2, "s")
+    ts(T.tmp[:, 0:72], T.io8[:, :], C[:, 2:3], A.not_equal, ["io8", "c2"], ["tmpA"], BIG, A.mult)
+    ts(T.tmp[:, 80:144], T.ioj[:, 0:64], C[:, 1:2], A.is_gt, ["ioj", "c1"], ["tmpB"], BIG, A.mult)
+    ts(T.mkn[:, :], T.ion[:, :], C[:, 1:2], A.is_gt, ["ion", "c1"], ["mkn"], BIG, A.mult)
+    ts(T.id2[:, :], T.iof[:, 0:128], C[:, 0:1], A.is_equal, ["iof", "c0"], ["id2"], 256.0, A.mult)
+    ts(T.mk7[:, :], T.iog[:, :], C[:, 3:4], A.not_equal, ["iog", "c3"], ["mk7"], 49152.0, A.mult)
+    ts(T.pst[:, :], T.io8[:, :], C[:, 2:3], A.is_le, ["io8", "c2"], ["pst"], 2 * BIG, A.mult)
+    ts(T.pns[:, :], T.ioj[:, 0:32], C[:, 4:5], A.subtract, ["ioj", "c4"], ["pns"], -4 * BIG, A.mult)
+    ts(T.msk[:, :], T.iom[:, :], C[:, 1:2], A.is_gt, ["iom", "c1"], ["msk"], BIG, A.mult)
+    ts(T.idb[:, :], T.iof[:, 0:128], C[:, 0:1], A.is_equal, ["iof", "c0"], ["idb"])
+    cp(T.kl0[:, :], T.kmi[:, 0:60], ["kmi"], ["kl0"])
+    cp(T.kc[:, 0:60], T.kmi[:, 0:60], ["kmi"], ["kc"])
+    for jb in range(3):
+        ts(T.selj[0:48, 128 * jb:128 * jb + 128], T.ioj[0:48, 0:128], 16.0 * jb, A.add, ["ioj", "c0"], ["selj"], C[0:48, 0:1], A.is_equal)
+    tt(T.scw[:, :], T.bof[:, :], T.sgn[:, :], A.mult, ["bof", "sgn"], ["scw"])
+    for jb in range(3):
+        ts(T.mk5[:, 24 * jb:24 * jb + 8], T.tmp[:, 0:8], 1024.0, A.add, ["tmpA"], ["mk5"])
+        ts(T.mk5[:, 24 * jb + 8:24 * jb + 24], T.tmp[:, 0:16], -1536.0, A.add, ["tmpA"], ["mk5"])
+    ts(T.padf[:, :], T.padh[:, :], C[:, 1:2], A.add, ["padh", "c1"], ["padu"], 2.0, A.mult)
+    ts(T.cur[:, :], T.curh[:, :], C[:, 1:2], A.add, ["curh", "c1"], ["cur"], 2.0, A.mult)
+    ts(T.cntw[:, :], T.iof[:, 0:8], C[:, 2:3], A.is_equal, ["iof", "c2"], ["cntw"], 2.0 ** 25, A.mult)
+    for r in range(6, 10):
+        s_lay(r, r // 2, "v")
+
     Zk = ["ZA", "ZB", "Zpad"]
     Zall = T.Z[:, :]
-    Sk = ["S0", "Spad"]
+    Sk = ["Sa", "Sb", "Spad"]
     bwin = T.booki[:, :]
     twin = T.tf[:, :]
+    BLOCKS = [(0, B0, 4), (B0, PH, 5)]
+    SB = (6, 7, 4)
 
-    BLOCKS = [(0, 96, (4, 7)), (96, PH, (0, 5))]
+    def names_of(t):
+        return 4 if t > 0 else 2
 
-    def bwide(t):
-        return 1024 if t == 0 else 3072
+    def book_at(t, a, b):
+        return T.booki[:, 0:1024 if t == 0 else 3072].indirect(T["kl%d" % t][:, a:b]), ["bookA", "kl%d" % t] + (["bookB"] if t > 0 else [])
 
-    def halves(t, between=None):
-        kl, keys = T["kl%d" % t], ["kl%d" % t] + (["brep"] if t > 0 else [])
-        act(T.thi[:, :], T.booki[:, 0:bwide(t)].indirect(kl[:, 0:KN]), ["bookA", "kl%d" % t] + (["bookB"] if t > 0 else []), ["thi"], bias=HI - 31.5)
-        if between:
-            between()
-        for (a, b, banks) in BLOCKS:
-            act(T.tlo[:, 2 * a:2 * b], T.blo[:, 0:bwide(t)].indirect(kl[:, a // 8:b // 8]), ["blo"] + keys, ["tlo%d" % a])
-            for (src, key, c0) in ((T.thi, "thi", 512), (T.tlo, "tlo%d" % a, 0)):
-                for o in (1, 0):
-                    for h in range(2):
-                        c = 256 * o + 128 * h
-                        mm(T["ps%d" % banks[o]][:, 0:b - a], T.hsel[:, c:c + 128], src[:, 2 * a + h:2 * b:2], ["hsel", key], ["B%d" % banks[o]], c0 > 0 and h == 0, c0 == 0 and h == 1)
-
-    def wholes(t, a, b, key):
-        cp(T.nat[:, a:b], T.booki[:, 0:bwide(t)].indirect(T["kl%d" % t][:, KN + a // 16:KN + b // 16]), ["bookA", "kl%d" % t] + (["bookB"] if t > 0 else []), [key])
+    def terms(t, i):
+        a, b, bank = BLOCKS[i]
+        src, keys = book_at(t, a // 8, b // 8)
+        act(T.thi[:, 2 * a:2 * b], src, keys, ["thi%d" % i], bias=-OFF)
+        for o in range(2):
+            for h in range(2):
+                c = 256 * o + 128 * h
+                mm(T["ps%d" % bank][:, o * (b - a):(o + 1) * (b - a)], T.hsel[:, c:c + 128], T.thi[:, 2 * a + h:2 * b:2], ["hsel", "thi%d" % i], ["B%d" % bank], h == 0, h == 1)
 
     def turned(i):
-        a, b, banks = BLOCKS[i]
-        ts(T.lb[:, a:b], T["ps%d" % banks[1]][:, 0:b - a], -HI, A.add, ["B%d" % banks[1]], ["lb%d" % i])
-        ts(T.la[:, a:b], T["ps%d" % banks[0]][:, 0:b - a], -HI, A.add, ["B%d" % banks[0]], ["la%d" % i])
+        a, b, bank = BLOCKS[i]
+        act(T.ll[:, 2 * a:2 * b], T["ps%d" % bank][:, 0:2 * (b - a)], ["B%d" % bank], ["ll%d" % i], bias=OFF)
 
-    def sinit(a, b):
-        act(T.S[:, a:b], T.iot[:, :].indirect(T.sgl[:, a // 16:b // 16]), ["iot", "sgl"], ["S0"], bias=OFF)
+    def half(o, c, n):
+        i = 0 if c < B0 else 1
+        a, b, bank = BLOCKS[i]
+        return T.ll[:, a + o * (b - a) + c:a + o * (b - a) + c + n], "ll%d" % i
+
+    def wholes(t):
+        src, keys = book_at(t, KN, 60)
+        act(T.nat[:, :], src, keys, ["nat"])
 
     def sread(v):
-        act(T.sp[:, :], T.S[:, :].indirect(T.pl[:, 12 * v:12 * v + 12]), Sk + ["pl%d" % v], ["sp"])
+        m = 3 * names_of(v)
+        act(T.sp[:, 0:16 * m], T.S[:, :].indirect(T.pl[:, 12 * v:12 * v + m]), Sk + ["plN%d" % v, "plO%d" % v], ["sp"])
 
-    def swrite(v, a=0, b=12):
-        cp(T.S[:, :].indirect(T.offs[:, 12 * v + a:12 * v + b]), T.sp[:, 16 * a:16 * b], ["offs0", "offs1", "offs2", "sp"] + Sk, Sk)
+    def swrite(v, a, b):
+        if a < 3 * names_of(v):
+            cp(T.S[:, :].indirect(T.offs[:, 12 * v + a:12 * v + b]), T.sp[:, 16 * a:16 * b], ["offs%d" % v, "sp"] + Sk, Sk)
 
     def yslot(k, n=1):
         if k < NP:
             return T.ysc[:, 384 * k + 7:384 * (k + n):8]
         return T.ysc[:, YN + 768 * (k - NP) + 15:YN + 768 * (k - NP + n):16]
 
-    def answers(t, head=None):
-        kl = T["kl%d" % t]
+    def answers(t, head):
         pits, nits = [], []
-        for (chs, its) in ((P0_CH if t == 0 else P_CH, pits), (N_CH, nits)):
+        for (chs, its) in ((P_CH, pits), (N_CH, nits)):
             c = 0
             for n in chs:
                 its.append((c, n))
@@ -314,96 +317,94 @@ def rank_program(g, core, T, topo):
 
         def ngather(i):
             c, n = nits[i]
-            act(T.G[:, YN + 16 * c:YN + 16 * (c + n)], Zall.indirect(T.nat[:, c:c + n]), Zk + ["natA" if i == 0 else "natB"], ["J%d" % i])
+            act(T.G[:, YN + 16 * c:YN + 16 * (c + n)], Zall.indirect(T.nat[:, c:c + n]), Zk + ["nat"], ["J%d" % i])
 
         def nscan(i):
             c, n = nits[i]
             scan(T.ysc[:, YN + 16 * c:YN + 16 * (c + n)], T.rst[:, 0:16 * n], T.G[:, YN + 16 * c:YN + 16 * (c + n)], A.max, A.min, ["rst", "J%d" % i], ["YN%d" % i])
 
-        def pgather(i, f):
+        def pgather(i, f=act):
             c, n = pits[i]
-            f(T.G[:, 16 * c:16 * (c + n)], Zall.indirect(T.lb[:, c:c + n]), Zk + ["lb0"] + (["lb1"] if c + n > BLOCKS[0][1] else []), ["G%d" % i])
+            lst, key = half(0, c, n)
+            f(T.G[:, 16 * c:16 * (c + n)], Zall.indirect(lst), Zk + [key], ["G%d" % i])
 
         def pfold(i):
             c, n = pits[i]
-            tt(T.H[:, 16 * c:16 * (c + n)], Zall.indirect(T.la[:, c:c + n]), T.G[:, 16 * c:16 * (c + n)], A.min, Zk + ["la0", "G%d" % i] + (["la1"] if c + n > BLOCKS[0][1] else []), ["H%d" % i])
+            lst, key = half(1, c, n)
+            tt(T.H[:, 16 * c:16 * (c + n)], Zall.indirect(lst), T.G[:, 16 * c:16 * (c + n)], A.min, Zk + [key, "G%d" % i], ["H%d" % i])
 
         def pscan(i):
             c, n = pits[i]
             scan(T.ysc[:, 16 * c:16 * (c + n)], T.rst8[:, 0:16 * n], T.H[:, 16 * c:16 * (c + n)], A.max, A.min, ["rst8", "H%d" % i], ["YP%d" % i])
 
-        late = t == 0
-        if not late:
-            ngather(0)
-            turned(0)
-            head()
         pgather(0, cp)
-        if not late:
-            turned(1)
-        statics()
-        pgather(1, act)
-        for i in range(2, len(pits)):
-            pgather(i, act)
-        if t > 0:
-            cp(T.kc[:, 60:120], kl[:, 0:60], ["kl%d" % t], ["kraw"])
-        else:
-            cp(C[:, 9:10], T.kmi[:, 60:61], ["wti"], ["c9"])
-        pfold(0)
-        if t > 0:
-            wholes(t, N_CH[0], NN, "natB")
-            ts(T.kc[:, 0:60], T.kc[:, 60:120], 1023, A.bitwise_and, ["kraw"], ["kc"])
-            nscan(0)
-        else:
-            ts(T.usel[:, :], T.sel8[:, :], C[:, 9:10], A.mult, ["sel8", "c9"], ["usel"])
-        for i in range(0 if late else 1, len(nits)):
+        pgather(1)
+        head()
+        turned(1)
+        statics(t)
+        pgather(2)
+        if t == 0:
+            wholes(t)
+        for i in range(3, len(pits)):
+            pgather(i)
+        for i in range(len(nits)):
             ngather(i)
-        pscan(0)
-        for i in range(6):
-            mm(T.ps0[:, 48 * i:48 * i + 48], T.idb[:, :], yslot(0), ["idb", "YP0"], ["B0"])
-        for i in range(1, len(pits)):
+        for i in (1, 0, 2):
             pfold(i)
-            if i == 1 and not late:
-                sums(1, NP - 1 + N_CH[0] // 48, "YN0")
-            if i > 2:
-                sums(0, sum(pits[i - 2]) // 24 - 1, "YP%d" % (i - 2))
-            if i > 1:
-                pscan(i - 1)
+        pscan(0)
+        pscan(1)
+        for k in range(4):
+            mm(T.ps0[:, 48 * k:48 * k + 48], T.idb[:, :], yslot(0), ["idb", "YP0"], ["B0"])
+        for i in range(3, len(pits)):
+            pfold(i)
+            sums(0, sum(pits[i - 2]) // 24 - 1, "YP%d" % (i - 2))
+            pscan(i - 1)
         pscan(len(pits) - 1)
         sums(0, sum(pits[-2]) // 24 - 1, "YP%d" % (len(pits) - 2))
-        first = 0 if late else 1
-        for i in range(first, len(nits)):
+        for i in range(len(nits)):
             nscan(i)
-            if i == first:
+            if i == 0:
                 sums(0, NP - 1, "YP%d" % (len(pits) - 1))
             else:
                 sums(1, NP - 1 + sum(nits[i - 1]) // 48, "YN%d" % (i - 1))
         sums(1, 19, "YN%d" % (len(nits) - 1))
 
-    def statics():
-        mm(T.ps2[0:48, 0:160], T.onb[0:1, 0:48], T.hrow[0:1, :], ["onb", "hrow"], ["B2"], True, False)
-        mm(T.ps3[0:48, 0:160], T.onb[0:1, 0:48], T.crow[0:1, :], ["onb", "crow"], ["B3"], True, False)
-        mm(T.ps5[:, 0:48], T.idh[:, :], T.mk5[:, :], ["idh", "mk5"], ["B5"], True, False)
-        mm(T.ps6[:, 0:48], T.idh[:, :], T.mk6[:, :], ["idh", "mk6"], ["B6"], True, False)
+    def places_of_terms(i):
+        b = SB[i]
+        mm(T["ps%d" % b][:, 0:256], T.onb[0:1, 0:128], T.pos[0:1, 0:256], ["onb", "pos"], ["B%d" % b], True, False)
+        if i:
+            mm(T["ps%d" % b][:, 0:256], T.pos[0:1, 128 + 128 * i:256 + 128 * i], T.onb[0:1, :], ["onb", "pos"], ["B%d" % b], False, False)
+        for c in range(2):
+            mm(T["ps%d" % b][:, 128 * c:128 * c + 128], T.id2[:, :], T.mk7[:, :], ["id2", "mk7"], ["B%d" % b], False, False)
 
-    halves(0)
-    wholes(0, 0, N_CH[0], "natA")
-    wholes(0, N_CH[0], NN, "natB")
-    cp(T.kc[:, 0:60], T.kmi[:, 0:60], ["kmi"], ["kc"])
-    later_constants()
-    turned(0)
+    def statics(t):
+        mm(T.ps2[0:48, 0:160], T.on2[0:1, :], T.hrow[0:1, :], ["on2", "hrow"], ["B2"], True, False)
+        mm(T.ps3[0:48, 0:160], T.on2[0:1, :], T.crow[0:1, :], ["on2", "crow"], ["B3"], True, False)
+        mm(T.ps5[:, 0:72], T.idh[:, 0:128], T.mk5[:, :], ["idh", "mk5"], ["B5"], True, False)
+        for i in range(3 if t > 0 else 2):
+            places_of_terms(i)
+
     act(T.Z[:, 0:16 * ZS], T.truv[:, :].indirect(T.sgl[:, 0:ZS]), ["truv", "sgl"], ["ZA"])
     cp(T.Z[:, 16 * ZS:4096], T.truv[:, :].indirect(T.sgl[:, ZS:256]), ["truv", "sgl"], ["ZB"])
-    turned(1)
-    answers(0)
-    SPIECE = [(0, 1280, 1792), (1792, 2816, 3328), (3328, 4096, 4096)]
-    SWAPS = [[], [], [0, 1], [2, 3], [4]]
+    terms(0, 0)
+    terms(0, 1)
+    turned(0)
+    cp(C[:, 9:10], T.kmi[:, 60:61], ["wti"], ["c9"])
+
+    def weights():
+        ts(T.usel[:, :], T.iof[:, 0:8], C[:, 2:3], A.is_equal, ["iof", "c2", "c9"], ["usel"], C[:, 9:10], A.mult)
+        for r in range(10, 14):
+            s_turn(r, (1, 4)[r // 2 - 5])
+
+    answers(0, weights)
 
     for t in range(VI):
         st, stk = T["st%d" % t], "st%d" % t
-        so, soz = T["so%d" % t], "soz%d" % t
+        so = T["so%d" % t]
         last = t == VI - 1
         old = t > 0
-        plk = "pl%d" % t
+        M = names_of(t)
+        o = 12 * t
         dst, frm = (nxt, prv) if not last else (prv, nxt)
 
         def send(src_ap, keys, land, c=0):
@@ -416,211 +417,197 @@ def rank_program(g, core, T, topo):
             wr[land] = ("a_" + land, len(topo.engines(frm, core)[:8]), "remote")
 
         if old:
-            act(T.sm[:, 28:31], T.ps1[:, 0:3], ["B1"], ["cc"], accum_out=T.cc[:, :])
-        act(T.hi[0:48, :], T.ps2[0:48, 0:160], ["B2"], ["hi"])
-        if old:
+            act(T.sm[:, 0:3], T.ps1[:, 0:3], ["B1"], ["cc"], accum_out=T.cc[:, :])
+            sread(t - 1)
             for a in range(2):
                 for jb in range(3):
                     c = 64 + 63 * a + 21 * jb
-                    act(T.ps1[:, c:c + 21], st[:, 198 + 21 * jb:219 + 21 * jb], [stk], ["B1"], scale=st[:, 186 + 4 * jb + a:187 + 4 * jb + a])
-        if t < 3:
-            sinit(SPIECE[t][0], SPIECE[t][1])
-        swap = SWAPS[t - 1] if old else []
-        for v in swap[:1]:
-            swrite(v, 0, 6)
+                    e = 186 + (4 * jb + 3 - a if t > 1 else 2 * jb + 1 - a)
+                    act(T.ps1[:, c:c + 21], st[:, 198 + 21 * jb:219 + 21 * jb], [stk], ["B1"], scale=st[:, e:e + 1])
+            cp(T.kc[:, 60:120], T["kl%d" % t][:, :], ["kl%d" % t], ["kraw"])
+        else:
+            for r in range(10, 14):
+                s_lay(r, (1, 4)[r // 2 - 5], "s")
+        cp(T.hi[0:48, :], T.ps2[0:48, 0:160], ["B2"], ["hi"])
+        if old:
+            ts(T.kc[:, 0:60], T.kc[:, 60:120], 1023, A.bitwise_and, ["kraw"], ["kc"])
         scan(T.su[0:48, :], T.ps3[0:48, 0:160], T.hi[0:48, :], A.max, A.min, ["B3", "hi"], ["su"])
         x = T.su[0:48, 19:160:20]
-        uI, uU, uQ, uA, uF, uB = [T.uint[0:48, 8 * i:8 * i + 8] for i in range(6)]
-        cp(uI, x, ["su"], ["uI"])
+        uU, uQ, uA, uF, uB = [T.uint[0:48, 8 * i:8 * i + 8] for i in range(5)]
+        ts(uU, x, 4095, A.bitwise_and, ["su"], ["uU"])
         ts(T.nk[0:48, 8:16], x, -2.0 ** -20, A.mult, ["su"], ["nkk"], 1546.49609375, A.add)
-        ts(uU, uI, 4095, A.bitwise_and, ["uI"], ["uU"])
-        if old:
-            tt(T.cur[:, :], st[:, 60:186], T.ps1[:, 64:190], A.add, [stk, "B1"], ["cur"])
         tt(uQ, uU, uU, A.mult, ["uU"], ["uQ"])
         ts(uA, uU, 37.0, A.mult, ["uU"] + (["cc"] if old else []), ["uA"], T.cc[0:48, 0:1] if old else 0.0, A.add)
+        ts(T.kz[0:48, :], T.nk[0:48, 8:16], 1556.0, A.is_equal, ["nkk"], ["kz"], float(t + 1 - 20), A.mult)
         ts(uF, uQ, 5, A.arith_shift_right, ["uQ"], ["uF"], 1023, A.bitwise_and)
         ts(uB, uA, 1023, A.bitwise_and, ["uA"], ["uB"])
+        tt(T.nk[0:48, 16:24], T.nk[0:48, 8:16], T.kz[0:48, :], A.add, ["nkk", "kz"], ["nks"])
         tt(T.nk[0:48, 0:8], uF, uB, A.add, ["uF", "uB"], ["nkn"])
         for jb in range(3):
-            mm(T.ps5[:, 16 * jb:16 * jb + 16], T.selj[0:48, 128 * jb:128 * jb + 128], T.nk[0:48, :], ["selj", "nkn", "nkk"], ["B5"], False, jb == 2)
-        for v in swap[:1]:
-            swrite(v, 6, 12)
-        for v in swap[1:]:
-            sread(v)
-        scan(T.pk[:, :], T.pst[:, :], T.ps5[:, 0:48], A.max, A.min, ["pst", "B5"], ["pk"])
-        n0 = T.pk[:, 7:48:16]
-        nw, nK, kz, kst = [T.sm[:, 4 * i:4 * i + 3] for i in range(4)]
+            mm(T.ps5[:, 24 * jb:24 * jb + 24], T.selj[0:48, 128 * jb:128 * jb + 128], T.nk[0:48, :], ["selj", "nkn", "nkk", "nks"], ["B5"], False, jb == 2)
+        if old:
+            swrite(t - 1, 0, 6)
+            tt(T.cur[:, :], st[:, 60:186], T.ps1[:, 64:190], A.add, [stk, "B1"], ["cur"])
+        else:
+            places_of_terms(2)
+            for r in (14, 15):
+                s_turn(r, 0)
+        scan(T.pk[:, :], T.pst[:, :], T.ps5[:, 0:72], A.max, A.min, ["pst", "B5"], ["pk"])
+        for jb in range(3):
+            red(T.nl[:, jb:jb + 1], T.ps5[:, 24 * jb:24 * jb + 8], A.min, ["B5"], ["nl"])
         eqo, neq = T.ps0[:, 0:63], T.ps3[:, 0:63]
-        cp(T.nl[:, 0:3], n0, ["pk"], ["nl"])
-        ts(kz, T.pk[:, 15:48:16], 20.0, A.is_equal, ["pk"], ["kz"], float(t + 1 - 20), A.mult)
         for jb in range(3):
-            act(T.ab[:, 21 * jb:21 * jb + 21], T.iof[:, 0:21], ["iof", "pk"], ["ab"], func=AF.Abs, scale=-1.0, bias=T.pk[:, 15 + 16 * jb:16 + 16 * jb])
+            ts(T.ps2[:, jb:60:3], T.iof[:, 0:20], T.pk[:, 23 + 24 * jb:24 + 24 * jb], A.is_equal, ["iof", "pk"], ["B2"], T.pk[:, 7 + 24 * jb:8 + 24 * jb], A.mult)
         cp(T.bkl[:, :], bwin.indirect(T.nl[:, 0:3]), ["bookA", "bookB", "nl"], ["bkl"])
-        if old:
-            act(eqo, T.ab[:, :], ["ab"], ["B0"], func=AF.Relu, scale=-1.0, bias=1.0)
-        ts(nK, n0, 1024.0, A.add, ["pk"], ["nK"])
-        tt(kst, kz, T.pk[:, 15:48:16], A.add, ["pk", "kz"], ["kst"])
-        act(T.zc[:, 384:768], Zall.indirect(T.bkl[:, 24:48]), Zk + ["bkl"], ["zcS"])
-        cp(T.zc[:, 0:384], Zall.indirect(T.bkl[:, 0:24]), Zk + ["bkl"], ["zcV"])
-        for p in range(16):
-            mm(T.ps4[0:48, p:256:16], T.zc[:, p:768:16], T.scw[:, :], ["zcS", "zcV", "scw"], ["B4"])
-        act(T.tf[:, :], T.iot[:, :].indirect(T.bkl[:, :]), ["iot", "bkl"], ["tf"])
-        if not last:
-            act(T.hitb[:, 0:3], T.ab[:, 20:63:21], ["ab"], ["hitb"], func=AF.Sign)
-        for jb in range(3):
-            act(T.ab[:, 21 * jb:21 * jb + 21], T.iof[:, 0:21], ["iof", "kst"], ["ab"], func=AF.Abs, scale=-1.0, bias=T.sm[:, 12 + jb:13 + jb])
-        act(so[:, 198:261], T.ab[:, :], ["ab", soz], ["eqk"], func=AF.Relu, scale=-1.0, bias=1.0)
-        act(neq, T.ab[:, :], ["ab"], ["B3"], func=AF.Sign)
-        if t < 2:
-            sinit(SPIECE[t][1], SPIECE[t][2])
-        for jb in range(3):
-            ts(T.ps2[:, jb:60:3], T.iof[:, 0:20], T.sm[:, 12 + jb:13 + jb], A.is_equal, ["iof", "kst", "nK"], ["B2"], T.sm[:, 4 + jb:5 + jb], A.mult)
-        if old:
-            for a in range(2):
-                tt(T.pr[:, 63 * a:63 * a + 63], T.cur[:, 63 * a:63 * a + 63], eqo, A.mult, ["cur", "B0"], ["pr"])
-        tt(T.kc[:, 60:120], T.kc[:, 0:60], T.ps2[:, 0:60], A.max, ["kc", "B2"], ["kraw"])
-        if old:
-            scan(T.osm[:, :], T.sumr[:, :], T.pr[:, :], A.mult, A.add, ["sumr", "pr"], ["osm"])
-
-        def spread(jb):
-            for o in range(2 if old else 0):
-                e = 63 * o + 21 * jb + 20
-                ts(T.dd[:, 32 * jb + 16 * o:32 * jb + 16 * o + 16], T.dm[:, :], T.osm[:, e:e + 1], A.mult, ["dm", "osm"], ["dd"])
-
+        for i in (1, 2):
+            act(T.zc[:, 256 * i:256 * i + 256], Zall.indirect(T.bkl[:, 16 * i:16 * i + 16]), Zk + ["bkl"], ["zc%d" % i])
         if not last:
             kok = "ko%d" % t
-            cp(T[kok][:, 0:60], T.kc[:, 60:120], ["kraw"], [kok])
-            send(T[kok][:, :], [kok, "koz%d" % t], "kl%d" % (t + 1))
+            tt(T[kok][:, :], T.kc[:, 0:60], T.ps2[:, 0:60], A.max, ["kc", "B2"], [kok])
+            send(T[kok][:, :], [kok], "kl%d" % (t + 1))
+        cp(T.zc[:, 0:256], Zall.indirect(T.bkl[:, 0:16]), Zk + ["bkl"], ["zc0"])
+        for i in (1, 0, 2):
+            mm(T["ps%d" % SB[i]][:, 0:256], T.scw[:, :], T.zc[:, 256 * i:256 * i + 256], ["zc%d" % i, "scw"], ["B%d" % SB[i]], False, True)
+        if not last:
+            act(T.tf[:, :], T.iot[:, :].indirect(T.bkl[:, :]), ["iot", "bkl"], ["tf"])
+            act(T.hitb[:, 0:3], T.pk[:, 15:72:24], ["pk"], ["hitb"], func=AF.Sign, scale=-1.0, bias=20.0)
+        for jb in range(3):
+            act(T.ab[:, 21 * jb:21 * jb + 21], T.iof[:, 0:21], ["iof", "pk"], ["ab"], func=AF.Abs, scale=-1.0, bias=T.pk[:, 23 + 24 * jb:24 + 24 * jb])
+        act(neq, T.ab[:, :], ["ab"], ["B3"], func=AF.Sign)
+        if last:
+            act(T.tf[:, :], T.iot[:, :].indirect(T.bkl[:, :]), ["iot", "bkl"], ["tf"])
         else:
+            act(so[:, 198:261], T.ab[:, :], ["ab"], ["eqk"], func=AF.Relu, scale=-1.0, bias=1.0)
+        if not old:
+            for r in (14, 15):
+                s_lay(r, 0, "v")
+        else:
+            for jb in range(3):
+                ts(T.ps0[:, 21 * jb:21 * jb + 21], T.iof[:, 0:21], T.pk[:, 15 + 24 * jb:16 + 24 * jb], A.is_equal, ["iof", "pk"], ["B0"])
+            if last:
+                tt(T.kc[:, 60:120], T.kc[:, 0:60], T.ps2[:, 0:60], A.max, ["kc", "B2"], ["kraw"])
+                ts(T.fa[:, 0:126], T.cur[:, :], OFF - 0.5, A.is_ge, ["cur"], ["fa"], -8192.0, A.mult)
+        for i in (1, 0, 2):
+            for c in range(2):
+                red(T.sk[:, 2 * i + c:2 * i + c + 1], T["ps%d" % SB[i]][:, 128 * c:128 * c + 128], A.min, ["B%d" % SB[i]], ["sk"])
+            if old and i == 1:
+                tt(T.pr[:, 0:63], T.cur[:, 0:63], eqo, A.mult, ["cur", "B0"], ["prA"])
+                tt(T.pr[:, 63:126], T.cur[:, 63:126], eqo, A.mult, ["cur", "B0"], ["prB"])
+        if old:
+            scan(T.osm[:, :], T.sumr[:, :], T.pr[:, :], A.mult, A.add, ["sumr", "prA", "prB"], ["osm"])
+        if last:
+            tt(T.fb[:, 0:126], T.cur[:, :], T.fa[:, 0:126], A.add, ["cur", "fa"], ["fb"])
+        elif old:
+            swrite(t - 1, 6, 8)
+        ts(T.sk[:, 6:12], T.sk[:, 0:6], 1023, A.bitwise_and, ["sk"], ["sq"])
+        if not last:
+            mm(T.ps1[:, 0:3], T.onb[:, 0:128], T.hitb[:, 0:3], ["onb", "hitb"], ["B1"])
+        if old:
+            for m in range(2):
+                ts(T.fo[:, m:6:2], T.osm[:, 63 * m + 20:63 * m + 63:21], OFF, A.add, ["osm"], ["fo"])
+            for m in range(2):
+                act(T.pl[:, o + m:o + 12:4], T.osm[:, 63 * m + 20:63 * m + 63:21], ["osm"], ["plO%d" % t], bias=OFF)
+        if last:
+            ts(T.fa[:, 0:126], T.fb[:, 0:126], OFF + 1.0, A.add, ["fb"], ["fa"], 0.0, A.max)
+        cp(T.fl[:, 0:6], T.sk[:, 6:12], ["sq"], ["fl"])
+        if old:
+            tt(T.fn[:, 129:320:2], T.iot[:, :].indirect(T.fo[:, 0:6]), T.msk[:, :], A.add, ["iot", "fo", "msk"], ["fnP"])
+            tt(T.fn[:, 1:128:2], T.iot[:, :].indirect(T.fo[:, 0:4]), T.tmp[:, 80:144], A.add, ["iot", "fo", "tmpB"], ["fnO"])
+        tt(T.fn[:, 128:320:2], twin.indirect(T.fl[:, 0:6]), T.mkn[:, 64:160], A.add, ["tf", "fl", "mkn"], ["fnB"])
+        tt(T.fn[:, 0:128:2], twin.indirect(T.fl[:, 0:4]), T.mkn[:, 0:64], A.add, ["tf", "fl", "mkn"], ["fnA"])
+        if last:
             ts(T.kc[:, 0:60], T.kc[:, 60:120], 1023, A.bitwise_and, ["kraw"], ["kc"])
-        for v in swap[1:]:
-            swrite(v, 0, 6)
-        scan(T.sk[0:48, :], T.srst[0:48, :], T.ps4[0:48, 0:256], A.add, A.max, ["srst", "B4"], ["sk"])
+            for jb in range(3):
+                for a in range(2):
+                    c = 63 * a + 21 * jb
+                    tt(T.ts3[:, 60 * a + jb:60 + 60 * a:3], T.fa[:, c:c + 20], T.ps3[:, 21 * jb:21 * jb + 20], A.mult, ["fa", "B3"], ["ts3"])
+        elif old:
+            swrite(t - 1, 8, 12)
+        for m in range(2):
+            scan(T.ns[:, 65 - m:96:2], T.pns[:, 0:16], T.fn[:, 256 + 2 * m:320:4], A.max, A.min, ["pns", "fnB"], ["nsB", "nsO"])
+        for m in range(2):
+            scan(T.ns[:, 1 - m:64:2], T.pns[:, 0:32], T.fn[:, 2 * m:128:4], A.max, A.min, ["pns", "fnA"], ["nsA", "nsO"])
         if last:
             cp(T.sf[:, 120:180], T.kc[:, 0:60], ["kc"], ["sfk"])
             send(T.sf[:, 120:180], ["sfk"], "homek")
-            ts(T.fa[:, 0:126], T.cur[:, :], OFF - 0.5, A.is_ge, ["cur"], ["fa"], -8192.0, A.mult)
-        key = T.sk[0:48, 15:256:16]
-        MG = 1.5 * 2 ** 28
-        ts(T.kr[0:48, :], key, MG, A.add, ["sk"], ["kr"], MG, A.subtract)
-        spread(0)
-        tt(T.qh[0:48, :], T.kr[0:48, :], key, A.subtract, ["kr", "sk"], ["qh"])
-        for jb in range(3):
-            mm(T.ps6[:, 16 * jb:16 * jb + 16], T.selj[0:48, 128 * jb:128 * jb + 128], T.qh[0:48, :], ["selj", "qh"], ["B6"], False, jb == 2)
-        spread(1)
-        spread(2)
-        if old:
-            mm(T.ps7[:, 0:96], T.boh[:, :], T.dd[:, :], ["boh", "dd"], ["B7"])
-            for m in range(2):
-                ts(T.pl[:, 12 * t + 2 + m:12 * t + 12:4], T.osm[:, 83 - 63 * m:126 - 63 * m:21], OFF, A.add, ["osm"], [plk])
-        if not last:
-            mm(T.ps1[:, 0:3], T.onb[:, :], T.hitb[:, 0:3], ["onb", "hitb"], ["B1"])
-        else:
-            tt(T.pr[:, :], T.cur[:, :], T.fa[:, 0:126], A.add, ["cur", "fa"], ["pr"])
-        for v in swap[1:]:
-            swrite(v, 6, 12)
-        scan(T.pk2[:, :], T.pst[:, :], T.ps6[:, 0:48], A.max, A.min, ["pst", "B6"], ["pk2"])
-        if last:
-            ts(T.fa[:, 0:126], T.pr[:, :], OFF, A.add, ["pr"], ["fa"], -1.0, A.max)
-        if old:
-            tt(T.fn[:, 0:32], T.ps7[:, 0:32], T.msk2[:, 32:64], A.add, ["B7", "msk2"], ["fnO"])
-            tt(T.fn[:, 96:128], T.ps7[:, 32:64], T.msk2[:, 32:64], A.add, ["B7", "msk2"], ["fnO"])
-            cp(T.fn[:, 128:160], T.ps7[:, 0:32], ["B7"], ["fnO"])
-        cp(T.fl[:, 0:4], T.pk2[:, 7:32:8], ["pk2"], ["flA"])
-        cp(T.fl[:, 4:10], T.pk2[:, 7:48:8], ["pk2"], ["flB"])
-        if old:
-            tt(T.fn[:, 256:320], T.ps7[:, 32:96], T.msk2[:, :], A.add, ["B7", "msk2"], ["fnO"])
-        tt(T.fn[:, 32:96], twin.indirect(T.fl[:, 0:4]), T.tmp[:, 64:128], A.add, ["tf", "flA", "tmpB"], ["fnA"])
-        tt(T.fn[:, 160:256], twin.indirect(T.fl[:, 4:10]), T.msk[:, :], A.add, ["tf", "flB", "msk"], ["fnB"])
-        scan(T.ns[:, 0:64], T.pns[:, :], T.fn[:, 32:96], A.max, A.min, ["pns", "fnA"], ["nsA"])
+            act(T.ps2[:, 0:120], T.ts3[:, :], ["ts3"], ["B2"], bias=-1.0)
         reg = [(0, 64), (64, 192), (128, 320)]
         eo = [0, 256, 768]
         nsk = ["nsA", "nsB"]
-        M = 4 if old else 2
 
         def name(jb, m):
-            return T.ns[:, 32 * jb + 16 * m + 15:32 * jb + 16 * m + 16] if m < 2 else T.osm[:, 63 * (m - 2) + 21 * jb + 20:63 * (m - 2) + 21 * jb + 21]
+            return T.ns[:, 32 * jb + 31 - m:32 * jb + 32 - m] if m < 2 else T.osm[:, 63 * (m - 2) + 21 * jb + 20:63 * (m - 2) + 21 * jb + 21]
 
         def eq(jb, m):
             a, b = reg[jb]
             w = b - a
-            col = name(jb, m)
             pos = eo[jb] + w * m
-            ts(T.eqb[:, pos:pos + w], T.fn[:, a:b], col, A.is_equal, ["fnO", "fnA"] + (["fnB"] if jb > 0 else []) + [("nsB" if jb == 2 else "nsA") if m < 2 else "osm"], ["e%d" % jb], 8192.0, A.mult)
+            ts(T.eqb[:, pos:pos + w], T.fn[:, a:b], name(jb, m), A.is_equal,
+               ["fnO", "fnA"] + (["fnP", "fnB"] if jb > 0 else []) + [("nsB" if jb == 2 else "nsA") if m < 2 else "osm"], ["e%d" % jb], 8192.0, A.mult)
 
         def count(jb):
             w = (reg[jb][1] - reg[jb][0]) * M // 2
-            o = eo[jb] // 2
-            scan(T.cn[:, o:o + w], T.eqb[:, eo[jb]:eo[jb] + w], T.eqb[:, eo[jb] + w:eo[jb] + 2 * w], A.add, A.add, ["e%d" % jb], ["cn%d" % jb], OFF - 8192.0 * M)
-            return T.cn[:, o + w - 1:o + w]
+            c = eo[jb] // 2
+            scan(T.cn[:, c:c + w], T.eqb[:, eo[jb]:eo[jb] + w], T.eqb[:, eo[jb] + w:eo[jb] + 2 * w], A.add, A.add, ["e%d" % jb], ["cn%d" % jb], OFF - 8192.0 * M)
+            return T.cn[:, c + w - 1:c + w]
 
-        def place(jb, col, ms_=range(4)):
-            for m in ms_:
-                if m < M:
-                    e = 4 * jb + m
-                    ts(T.offs[:, 12 * t + e:12 * t + e + 1], col, name(jb, m), A.add, nsk + ["osm", "padu", "cn%d" % jb], ["offs%d" % jb], T.padf[:, e:e + 1], A.min)
+        def place(jb, col):
+            ts(T.xo[:, M * jb:M * jb + M], T.ns[:, 32 * jb + 32 - M:32 * jb + 32], col, A.add, nsk + ["nsO", "cn%d" % jb], ["xo%d" % jb])
 
-        for m in range(2, M):
-            eq(0, m)
-        scan(T.ns[:, 64:96], T.pns[:, 0:32], T.fn[:, 224:256], A.max, A.min, ["pns", "fnB"], ["nsB"])
-        for m in list(range(2, M)) + [0, 1]:
-            eq(2, m)
-        for m in range(2, M):
-            eq(1, m)
-        for m in range(2):
-            ts(T.pl[:, 12 * t + m:12 * t + 12:4], T.ns[:, 31 - 16 * m:96:32], OFF, A.add, nsk, [plk])
+        def places():
+            tt(T.offs[:, o:o + 3 * M], T.xo[:, 0:3 * M], T.padf[:, 0:12] if old else T.padf[:, 12:18], A.min, ["xo0", "xo1", "xo2", "padu"], ["offs%d" % t])
+
+        def partners():
+            for m in range(2):
+                act(T.pl[:, o + M - 2 + m:o + 3 * M:M], T.ns[:, 31 - m:96:32], nsk, ["plN%d" % t], bias=OFF)
+
+        def beside():
+            for m in range(M - 2):
+                act(T.ns[:, 29 - m:96:32], T.osm[:, 63 * m + 20:63 * m + 63:21], ["osm"], ["nsO"])
+
         if not last:
-            halves(t + 1, lambda: act(T.zp[:, :], Zall.indirect(T.pl[:, 12 * t:12 * t + 12]), Zk + [plk], ["zp"]))
-            if SWAPS[t]:
-                sread(SWAPS[t][0])
+            partners()
+            beside()
+            act(T.zp[:, 0:48 * M], Zall.indirect(T.pl[:, o:o + 3 * M]), Zk + ["plN%d" % t, "plO%d" % t], ["zp"])
+            terms(t + 1, 0)
+            terms(t + 1, 1)
+            turned(0)
+            wholes(t + 1)
         else:
-            sread(t)
-
-        def named(jb, col):
-            ts(T.v6[:, 2 * jb:2 * jb + 2], T.v6[:, 2 * jb:2 * jb + 2], col, A.subtract, ["v6a", "cn%d" % jb], ["v6%d" % jb], -1.0, A.max)
-            for a in range(2):
-                act(T.ps2[:, 60 * a + jb:60 + 60 * a:3], so[:, 198 + 21 * jb:218 + 21 * jb], ["eqk", "v6%d" % jb], ["B2"], scale=T.v6[:, 2 * jb + a:2 * jb + a + 1])
-                c = 63 * a + 21 * jb
-                tt(T.ts3[:, 60 * a + jb:60 + 60 * a:3], T.fa[:, c:c + 20], T.ps3[:, 21 * jb:21 * jb + 20], A.mult, ["fa", "B3"], ["ts3N"])
-
+            for jb in (2, 1, 0):
+                for a in range(2):
+                    act(T.q1[:, 60 * a + jb:60 + 60 * a:3], T.ab[:, 21 * jb:21 * jb + 20], ["ab", nsk[jb // 2]], ["q1%d" % jb], func=AF.Identity, scale=-8192.0, bias=name(jb, a))
+        for jb in (2, 1, 0):
+            for m in list(range(2, M)) + [0, 1]:
+                eq(jb, m)
         c2 = count(2)
-        if last:
-            ts(T.v6[:, 0:6], T.ns[:, 15:96:16], 2 * OFF, A.add, nsk, ["v6a"])
-        for m in range(2):
-            eq(1, m)
-        for m in range(2):
-            eq(0, m)
-        if last:
-            named(2, c2)
-            c1 = count(1)
-            c0 = count(0)
-            place(2, c2)
-            named(1, c1)
-            named(0, c0)
-            break
-        o = 12 * t
-        place(2, c2, range(2))
         c1 = count(1)
         c0 = count(0)
-        place(2, c2, range(2, 4))
+        if last:
+            break
+        place(2, c2)
         place(1, c1)
         place(0, c0)
-        wholes(t + 1, 0, N_CH[0], "natA")
-        cp(Zall.indirect(T.offs[:, o:o + 12]), T.zp[:, :], ["offs0", "offs1", "offs2", "zp"], Zk)
+        tt(so[:, 123:186], T.cur[:, 63:126], neq, A.mult, ["cur", "B3"], ["soB"])
+        places()
+        tt(so[:, 60:123], T.cur[:, 0:63], neq, A.mult, ["cur", "B3"], ["soA"])
+        cp(Zall.indirect(T.offs[:, o:o + 3 * M]), T.zp[:, 0:48 * M], ["offs%d" % t, "zp"], Zk)
+        ts(so[:, 186:186 + 3 * M], T.offs[:, o:o + 3 * M], -OFF, A.add, ["offs%d" % t, "of2"], ["of2"])
+        answers(t + 1, lambda: send(so[:, 60:SW], ["soA", "soB", "of2", "eqk"], "st%d" % (t + 1), 60))
 
-        def names_go():
-            tt(so[:, 123:186], T.cur[:, 63:126], neq, A.mult, ["cur", "B3"], ["soB"])
-            tt(so[:, 60:123], T.cur[:, 0:63], neq, A.mult, ["cur", "B3"], ["soA"])
-            ts(so[:, 186:198], T.offs[:, o:o + 12], -OFF, A.add, ["offs0", "offs1", "offs2", soz], ["of2"])
-            send(so[:, 60:SW], ["soA", "soB", "of2", "eqk", soz], "st%d" % (t + 1), 60)
-
-        answers(t + 1, names_go)
-
+    beside()
+    partners()
+    for (jb, col) in ((2, c2), (1, c1), (0, c0)):
+        ts(T.x1[:, jb:120:3], T.q1[:, jb:120:3], col, A.subtract, ["q1%d" % jb, "cn%d" % jb], ["x1%d" % jb], 2 * OFF, A.add)
+    tt(T.sf[:, 0:120], T.x1[:, :], T.ps2[:, 0:120], A.max, ["x10", "x11", "x12", "B2"], ["sf"])
+    send(T.sf[:, 0:120], ["sf"], "home")
+    swrite(t - 1, 6, 12)
+    sread(t)
+    place(2, c2)
     place(1, c1)
     place(0, c0)
-    tt(T.sf[:, 0:120], T.ts3[:, 0:120], T.ps2[:, 0:120], A.add, ["ts3N", "B2"], ["sf"])
-    send(T.sf[:, 0:120], ["sf"], "home")
-    swrite(t)
+    places()
+    swrite(t, 0, 12)
     dma("y", T.yk[:, :], T.homek[:, :], "dout", ["homek"], [])
     dma("y", T.ys[:, :], T.S[0:128:16, 0:4096], "dout", Sk, [])
     dma("s", T.ya[:, :], T.home[:, 0:60], "dout", ["home"], [])

@@ -3,69 +3,68 @@ from concourse.mybir import dt, AluOpType, AxisListType, ActivationFunctionType
 
 VI = 6
 PADC = 4480
-P_CH = [64, 32, 48, 96, 96]
+P_CH = [24, 38, 42, 64, 72, 96]
+OWN = 2
 PH = sum(P_CH)
 NP = PH // 24
-N_CH = [144, 96, 32, 16]
+N_CH = [16, 80, 96, 48, 32, 16]
 NN = sum(N_CH)
-KN = 3 * NP
-B0 = 96
+KN = 3 * (NP - 1)
+B1 = 104
 ZS = 96
 YN, YW = 16 * PH, 16 * (PH + NN)
 OFF = 2048.0
+SO = 4096.0
 BIG = 30000.0
-SW = 261
+COL = (1, 0, 2)
+SW = 141
 
 _sb = {
     "truv": (4096, "bfloat16"), "Z": (PADC, "bfloat16"), "S": (PADC, "float32"), "iot": (PADC, "float32"),
-    "booki": (3072, "int32"), "kc": (120, "int32"), "sgi": (256, "int32"), "sgl": (256, "uint16"), "sgh": (256, "float16"), "kmi": (64, "int32"),
-    "G": (YW, "bfloat16"), "nat": (NN, "uint16"), "H": (16 * PH, "bfloat16"), "ysc": (YW, "bfloat16"),
+    "booki": (2048, "int32"), "kc": (120, "int32"), "sgi": (256, "int32"), "sgl": (256, "uint16"), "sgh": (256, "float16"), "kmi": (64, "int32"),
+    "G": (YW, "bfloat16"), "nat": (NN + 16, "uint16"), "H": (16 * PH, "bfloat16"), "ysc": (YW, "bfloat16"),
+    "kl": (72 * VI, "uint16"), "ko": (72 * VI, "uint16"), "kz": (32, "uint16"),
     "rst": (16 * max(N_CH), "bfloat16"), "rst8": (16 * max(P_CH), "bfloat16"), "thi": (2 * PH, "float16"),
-    "hsel": (512, "float16"), "ll": (2 * PH, "uint16"), "ab": (63, "float32"),
-    "pi": (1, "int32"), "pj": (1, "int32"), "pg": (1, "int32"), "cjl": (1, "int32"), "colf": (16, "float32"),
-    "iof": (144, "float32"), "iog": (128, "float32"), "ioj": (128, "float32"), "io8": (72, "float32"), "iom": (96, "float32"), "ion": (160, "float32"),
-    "sgn": (128, "float32"), "scw": (128, "bfloat16"), "id2": (128, "float16"), "mk7": (128, "float16"),
-    "pos": (512, "bfloat16"), "mkn": (160, "float32"),
-    "idb": (128, "bfloat16"), "idh": (144, "float16"), "bof": (128, "float32"), "onb": (256, "bfloat16"), "on2": (48, "bfloat16"),
-    "cntw": (8, "bfloat16"), "usel": (8, "bfloat16"),
-    "selj": (384, "float16"), "mk5": (72, "float16"), "pst": (72, "float32"), "tmp": (144, "float32"),
-    "msk": (96, "float32"), "pns": (32, "float32"), "hrow": (160, "bfloat16"), "crow": (160, "bfloat16"),
-    "padf": (18, "float32"), "padh": (18, "float32"), "curh": (126, "float32"), "sumr": (126, "float32"),
-    "lt": (912, "bfloat16"),
-    "hi": (160, "float32"), "su": (160, "int32"), "uint": (64, "int32"), "nk": (24, "float16"), "kz": (8, "float16"), "pk": (72, "float32"),
-    "nl": (4, "uint16"), "bkl": (48, "uint16"), "zc": (768, "bfloat16"), "tf": (768, "float32"),
-    "sm": (4, "float32"), "hitb": (4, "bfloat16"), "pr": (126, "float32"), "osm": (126, "float32"), "sk": (12, "int32"),
-    "fl": (6, "uint16"), "fo": (6, "uint16"), "fn": (320, "float16"), "ns": (96, "float32"),
+    "hsel": (512, "float16"), "ll": (2 * PH, "uint16"), "ki": (252, "int32"),
+    "pi": (1, "int32"), "pj": (1, "int32"), "pg": (1, "int32"), "colf": (16, "float32"),
+    "iof": (160, "float32"), "iog": (128, "float32"), "ioj": (128, "float32"), "ion": (96, "float32"), "io2": (42, "float32"),
+    "scw": (144, "bfloat16"), "pos": (336, "bfloat16"), "mkn": (96, "float32"), "rs17": (102, "bfloat16"), "inc": (102, "float32"),
+    "idb": (128, "bfloat16"), "idh": (144, "float16"), "bof": (128, "float32"), "onb": (128, "bfloat16"), "on2": (96, "bfloat16"),
+    "wts": (640, "bfloat16"), "msk": (96, "float32"), "pns": (48, "float32"), "hrow": (128, "bfloat16"), "crow": (128, "bfloat16"),
+    "padf": (18, "float32"), "padh": (18, "float32"), "curh": (126, "float32"), "sumr": (42, "float32"),
+    "lt": (960, "bfloat16"), "hi": (96, "float32"), "lo": (96, "float32"), "su": (96, "int32"), "uint": (24, "int32"),
+    "kb": (4, "bfloat16"), "kd": (8, "float32"), "nl": (4, "uint16"), "bkl": (48, "uint16"), "tf": (768, "float32"),
+    "hitb": (4, "bfloat16"), "pr": (126, "float32"), "osm": (132, "int32"), "sk": (204, "float32"),
+    "fl": (6, "uint16"), "fo": (6, "uint16"), "fn": (384, "float16"), "ns": (192, "float32"),
     "eqb": (1536, "bfloat16"), "cn": (768, "bfloat16"), "xo": (12, "float32"),
     "offs": (12 * VI, "uint16"), "pl": (12 * VI, "uint16"), "zp": (192, "bfloat16"), "sp": (192, "float32"),
-    "ts3": (120, "float32"), "q1": (120, "float32"), "x1": (120, "float32"), "cc": (1, "float32"), "sf": (180, "float32"), "cur": (126, "float32"),
-    "fa": (128, "float32"), "fb": (128, "float32"), "home": (120, "float32"), "homek": (60, "float32"),
+    "q1": (126, "float32"), "x1": (126, "float32"), "sf": (188, "float32"),
+    "fa": (128, "float32"), "fb": (128, "float32"), "home": (126, "float32"), "homek": (64, "float32"),
+    "ra": (256, "float32"), "ri": (256, "int32"), "rb": (256, "float32"),
 }
-SCRATCH = {}
+SCRATCH = {"zc": ("sbuf", [128, 6, 136], "bfloat16")}
 for _k in _sb:
     SCRATCH[_k] = ("sbuf", [128, _sb[_k][0]], _sb[_k][1])
 for _t in range(VI):
-    SCRATCH["st%d" % _t] = ("sbuf", [128, SW], "float32")
     SCRATCH["so%d" % _t] = ("sbuf", [128, SW], "float32")
-    SCRATCH["kl%d" % _t] = ("sbuf", [128, 60], "uint16")
-    SCRATCH["ko%d" % _t] = ("sbuf", [128, 60], "uint16")
+for _t in range(1, VI):
+    SCRATCH["st%d" % _t] = ("sbuf", [128, SW], "float32")
 for _t in range(8):
-    SCRATCH["ps%d" % _t] = ("psum", [128, 512], "float32")
-SEMAPHORES = (["sv", "ss", "sp_", "sg_", "lsg", "ltr", "lbk", "lbw", "lkm", "lwt", "dout", "lsem"]
-              + ["a_st%d" % _t for _t in range(1, VI)] + ["a_kl%d" % _t for _t in range(1, VI)] + ["a_home", "a_homek"])
+    SCRATCH["ps%d" % _t] = ("psum", [128, 16, 32] if _t in (3, 7) else [128, 512], "float32")
+SEMAPHORES = (["sv", "ss", "sp_", "sg_", "lsg", "ltr", "lbk", "lbw", "lkm", "lwt", "dout", "lsem", "dra", "drb", "a_home", "a_homek"]
+              + ["a_%s%d" % (_k, _t) for _k in ("st", "kl") for _t in range(1, VI)] + ["a_kz%d" % _t for _t in range(1, 4)])
 
 
 def rank_program(g, core, T, topo):
     rank = T.rank_of(core)
     if rank is None:
         return
-    A, AX, AF = AluOpType, AxisListType, ActivationFunctionType
+    A, AF = AluOpType, ActivationFunctionType
     cores = T.cores
-    nxt, prv = cores[(rank + 1) % 4], cores[(rank + 3) % 4]
 
     eng = {"v": g.vector, "s": g.scalar, "p": g.tensor, "g": g, "y": g.sync}
     semn = {"v": "sv", "s": "ss", "p": "sp_", "g": "sg_"}
-    cnt = {"v": 0, "s": 0, "p": 0, "g": 0}
+    cnt = {"v": 0, "s": 0, "p": 0, "g": 0, "sent": 0}
     waited = {}
     wr, rd = {}, {}
 
@@ -128,8 +127,8 @@ def rank_program(g, core, T, topo):
     def scan(out, d0, d1, op0, op1, r, w, init=0.0):
         E("v", lambda e: e.tensor_tensor_scan(out=out, data0=d0, data1=d1, initial=init, op0=op0, op1=op1), r, w)
 
-    def red(out, a, op, r, w):
-        E("v", lambda e: e.tensor_reduce(out=out, in_=a, axis=AX.X, op=op), r, w)
+    def flip(out, a, r, w):
+        E("v", lambda e: e.transpose(out=out, in_=a), r, w)
 
     def ms(ap, c, w, r=()):
         E("v", lambda e: e.memset(ap, c), r, w)
@@ -143,125 +142,146 @@ def rank_program(g, core, T, topo):
     def iota(out, pattern, base, cm, w):
         E("g", lambda e: e.iota(out, pattern, base, cm, allow_small_or_imprecise_dtypes=True), [], w)
 
+    def send(src_ap, keys, land, out_ap, step=1):
+        dst, frm = cores[(rank + step) % 4], cores[(rank - step) % 4]
+        deps("g", keys, [])
+        rid, pid = topo.addr(dst, core)
+        en = topo.engines(core, dst)
+        g.remote_dma(out_ap=out_ap, in_ap=src_ap, remote_sem=T.sem["a_" + land], local_sem=T.sem.lsem,
+                     pid=pid, routing_id=rid, dma_engine_mask=sum(1 << e for e in en))
+        cnt["sent"] += len(en)
+        wr[land] = ("a_" + land, len(topo.engines(frm, core)), "remote")
+
     dma("y", T.sgi[:, :], T.sg0[:, :], "lsg", [], ["sgi"])
     dma("s", T.kmi[:, 0:60], T.km0[:, :], "lkm", [], ["kmi"])
     dma("y", T.truv[:, :], T.tru[:, :], "ltr", [], ["truv"])
     dma("y", T.booki[:, 0:1024], T.book[:, :], "lbk", [], ["bookA"])
     dma("y", T.kmi[:, 60:61], T.wt[:, :], "lwt", [], ["wti"])
-    deps("y", ["bookA"], [])
-    for i in (1, 2):
-        g.sync.dma_start(out=T.booki[:, 1024 * i:1024 * i + 1024], in_=T.book[:, :]).then_inc(T.sem.lbw, 16)
-    note("y", [], ["bookB"], ("lbw", 32, "dma"))
+    dma("y", T.booki[:, 1024:2048], T.book[:, :], "lbw", ["bookA"], ["bookB"])
 
     iota(T.pi[:, :], [[0, 1]], 0, 1, ["pi"])
-    iota(T.iof[:, :], [[1, 144]], 0, 0, ["iof"])
+    iota(T.iof[:, :], [[1, 160]], 0, 0, ["iof"])
     iota(T.iog[:, :], [[1, 8], [0, 16]], 0, 0, ["iog"])
     iota(T.ioj[:, :], [[0, 8], [1, 16]], 0, 0, ["ioj"])
-    iota(T.io8[:, :], [[0, 9], [1, 8]], 0, 0, ["io8"])
-    iota(T.sgn[:, :], [[0, 64], [2048, 2]], -1024, 0, ["sgn"])
-    iota(T.ion[:, 0:64], [[0, 2], [1, 16], [0, 2]], 0, 0, ["ion"])
-    iota(T.ion[:, 64:160], [[50, 3], [1, 16], [0, 2]], -100, 0, ["ion"])
-    iota(T.iom[:, :], [[50, 3], [0, 2], [1, 16]], -100, 0, ["iom"])
-    iota(T.padh[:, 0:12], [[64, 3], [-16, 4]], 2048 + 48, 0, ["padh"])
-    iota(T.padh[:, 12:18], [[64, 3], [-16, 2]], 2048 + 16, 0, ["padh"])
-    iota(T.curh[:, :], [[16, 2], [64, 3], [0, 21]], 2048 - int(OFF) // 2, 0, ["curh"])
-    iota(T.hrow[0:1, :], [[0, 8], [1, 20]], -10, 0, ["hrow"])
-    iota(T.pos[0:1, 0:256], [[1, 256]], 0, 0, ["pos"])
-    iota(T.pos[0:1, 256:512], [[256, 2], [0, 128]], 256, 0, ["pos"])
-    iota(T.rst8[:, :], [[0, max(P_CH) * 2], [-512, 8]], 512, 0, ["rst8"])
-    iota(T.rst[:, :], [[0, max(N_CH)], [-512, 16]], 512, 0, ["rst"])
-    iota(T.iot[:, :], [[1, PADC]], -int(OFF), 0, ["iot"])
+    iota(T.ion[:, :], [[0, 3], [1, 16], [0, 2]], 0, 0, ["ion"])
+    iota(T.padh[:, 0:12], [[16, 2], [-32, 2], [64, 3]], 2048 + 32, 0, ["padh"])
+    iota(T.padh[:, 12:18], [[16, 2], [64, 3]], 2048, 0, ["padh"])
+    for jb in range(3):
+        iota(T.curh[:, jb:126:3], [[16, 2], [0, 21]], 2048 + 64 * COL[jb], 0, ["curh"])
+    iota(T.hrow[0:1, :], [[0, 4], [1, 32]], -10, 0, ["hrow"])
     C = T.colf
     ms(T.Z[:, 4096:PADC], 0.0, ["Zpad"])
+    act(T.S[:, 4096:PADC], T.Z[:, 4096:PADC], ["Zpad"], ["Spad"], func=AF.Silu)
     ts(T.pj[:, :], T.pi[:, :], 15, A.bitwise_and, ["pi"], ["pj"])
     ts(T.pg[:, :], T.pi[:, :], 4, A.arith_shift_right, ["pi"], ["pg"])
     ts(T.uint[:, 0:1], T.pi[:, :], 7, A.bitwise_and, ["pi"], ["uI"])
     cp(C[:, 0:1], T.pi[:, :], ["pi"], ["c0"])
-    ts(T.cjl[:, :], T.pi[:, :], 1, A.arith_shift_right, ["pi"], ["cjl"], 7, A.bitwise_and)
+    ms(T.scw[:, :], 0.0, ["scw"])
+    ms(T.wts[:, :], 0.0, ["wts"])
     cp(C[:, 1:2], T.pj[:, :], ["pj"], ["c1"])
     cp(C[:, 2:3], T.pg[:, :], ["pg"], ["c2"])
     cp(C[:, 10:11], T.uint[:, 0:1], ["uI"], ["c10"])
     ms(T.crow[0:1, :], -272.0, ["crow"])
-    cp(C[:, 3:4], T.cjl[:, :], ["cjl"], ["c3"])
+    ms(T.rs17[:, :], -2.0 ** 23, ["rs17"])
+    ms(T.inc[:, :], 1.0, ["inc"])
+    ts(T.uint[:, 1:2], T.pi[:, :], 14, A.bitwise_and, ["pi"], ["uJ"])
     ms(T.onb[:, :], 1.0, ["onb"])
     ms(T.on2[0:1, :], 2.0 ** 20, ["on2"])
-    ts(T.idh[:, :], T.iof[:, :], C[:, 0:1], A.is_equal, ["iof", "c0"], ["idh"])
-    ms(T.fn[:, :], BIG, ["fnO", "fnP", "fnA", "fnB"])
-    ms(T.crow[0:1, 0:160:20], 64.0, ["crow"], ["crow"])
-    act(C[:, 4:5], C[:, 1:2], ["c1"], ["c4"], bias=0.5)
-    act(T.sumr[:, :], T.iof[:, 0:126], ["iof"], ["sumr"], scale=0.0, bias=1.0)
-    for i in range(3):
-        act(T.S[:, 4096 + 128 * i:4224 + 128 * i], T.iof[:, 0:128], ["iof"], ["Spad"], scale=0.0)
-    act(T.so0[:, 186:198], T.iof[:, 0:12], ["iof"], ["of2"], scale=0.0)
+    ts(T.idh[:, :], T.iof[:, 0:144], C[:, 0:1], A.is_equal, ["iof", "c0"], ["idh"])
+    ms(T.fn[:, :], BIG, ["fnM", "fnN", "fnF1", "fnF2", "fnG1", "fnG2"])
+    ms(T.crow[0:1, 0:128:32], 64.0, ["crow"], ["crow"])
+    ms(T.rs17[:, 0:102:17], 2.0 ** 23, ["rs17"], ["rs17"])
+    ms(T.inc[:, 0:102:17], 2.0 ** 23, ["inc"], ["inc"])
+    ts(C[:, 3:4], T.uint[:, 1:2], 8.0, A.mult, ["uJ"], ["c3"], 15.0, A.add)
     ts(C[:, 11:12], C[:, 1:2], 7.5, A.is_lt, ["c1"], ["c11"])
     ts(C[:, 12:13], C[:, 1:2], 7.5, A.is_gt, ["c1"], ["c11"])
     ts(T.bof[:, :], T.iog[:, :], C[:, 2:3], A.is_equal, ["iog", "c2"], ["bof"])
     for h in range(2):
         ts(T["f" + "ab"[h]][:, :], T.ioj[:, :], -8.0 * h, A.add, ["ioj", "c10"], ["f" + "ab"[h]], C[:, 10:11], A.is_equal)
-    ms(T.sumr[:, 0:126:21], 0.0, ["sumr"], ["sumr"])
+    ts(C[:, 4:5], C[:, 1:2], 0.5, A.add, ["c1"], ["c4"])
+    ms(T.sumr[:, :], 1.0, ["sumr"])
+    ms(T.so0[:, 129:141], 0.0, ["of2"])
     for h in range(2):
         tt(T["f" + "ab"[h]][:, :], T["f" + "ab"[h]][:, :], T.bof[:, :], A.mult, ["f" + "ab"[h], "bof"], ["f" + "ab"[h]])
+    cp(T.kz[:, 0:3], T.kmi[:, 0:3], ["kmi"], ["kz0"])
     ts(T.sgh[:, :], T.sgi[:, :], -OFF, A.add, ["sgi"], ["sgh"])
-    act(T.sgl[:, :], T.sgi[:, :], ["sgi"], ["sgl"])
     for h in range(2):
         for o in range(2):
             c = 256 * o + 128 * h
             act(T.hsel[:, c:c + 128], T["f" + "ab"[h]][:, :], ["f" + "ab"[h], "c11"], ["hsel"], scale=C[:, 11 + o:12 + o])
+    act(T.sgl[:, :], T.sgi[:, :], ["sgi"], ["sgl"])
+    iota(T.rst8[:, :], [[0, max(P_CH) * 2], [-512, 8]], 512, 0, ["rst8"])
+    iota(T.rst[:, :], [[0, max(N_CH)], [-512, 16]], 512, 0, ["rst"])
+    for step in (1, 2, 3):
+        send(T.kz[:, 0:3], ["kz0"], "kz%d" % step, T.kz[:, 8 * step:8 * step + 3], step)
+    iota(T.io2[:, :], [[0, 2], [1, 21]], 128, 0, ["io2"])
+    iota(T.pos[0:1, 0:68], [[-256, 2], [128, 2], [0, 17]], 256, 0, ["pos"])
+    iota(T.pos[0:1, 68:102], [[128, 2], [0, 17]], 512, 0, ["pos"])
+    iota(T.pos[0:1, 102:204], [[0, 6], [1, 17]], 0, 0, ["pos"])
+    iota(T.pos[0:1, 204:332], [[0, 8], [16, 8], [0, 2]], 0, 0, ["pos"])
+    iota(T.iot[:, :], [[1, PADC]], -int(OFF), 0, ["iot"])
 
-    def s_turn(r, bank):
-        mm(T["ps%d" % bank][:, 256 * (r % 2):256 * (r % 2) + 256], T.idh[:, r:r + 128], T.sgh[:, :], ["idh", "sgh"], ["B%d" % bank])
+    S_BANK = (0, 3, 7, 4, 5, 2, 1, 6)
 
-    def s_lay(r, bank, q):
-        src = T["ps%d" % bank][:, 256 * (r % 2):256 * (r % 2) + 256]
+    def s_at(r):
+        b, h = S_BANK[r // 2], r % 2
+        return (T["ps%d" % b][:, 8 * h:8 * h + 8, :] if b in (3, 7) else T["ps%d" % b][:, 256 * h:256 * h + 256]), "B%d" % b
+
+    def s_lay(r, q):
+        src, key = s_at(r)
         if q == "v":
-            ts(T.S[:, r:4096:16], src, OFF, A.add, ["B%d" % bank], ["Sa"])
+            ts(T.S[:, r:4096:16], src, OFF + SO, A.add, [key], ["Sa"])
         else:
-            act(T.S[:, r:4096:16], src, ["B%d" % bank], ["Sb"], bias=OFF)
+            act(T.S[:, r:4096:16], src, [key], ["Sb"], bias=OFF + SO)
 
-    for r in range(10):
-        s_turn(r, r // 2)
-    for r in range(6):
-        s_lay(r, r // 2, "s")
-    ts(T.tmp[:, 0:72], T.io8[:, :], C[:, 2:3], A.not_equal, ["io8", "c2"], ["tmpA"], BIG, A.mult)
-    ts(T.tmp[:, 80:144], T.ioj[:, 0:64], C[:, 1:2], A.is_gt, ["ioj", "c1"], ["tmpB"], BIG, A.mult)
+    for r in range(16):
+        mm(s_at(r)[0], T.idh[:, r:r + 128], T.sgh[:, :], ["idh", "sgh"], [s_at(r)[1]])
+    for r in range(4):
+        s_lay(r, "s")
     ts(T.mkn[:, :], T.ion[:, :], C[:, 1:2], A.is_gt, ["ion", "c1"], ["mkn"], BIG, A.mult)
-    ts(T.id2[:, :], T.iof[:, 0:128], C[:, 0:1], A.is_equal, ["iof", "c0"], ["id2"], 256.0, A.mult)
-    ts(T.mk7[:, :], T.iog[:, :], C[:, 3:4], A.not_equal, ["iog", "c3"], ["mk7"], 49152.0, A.mult)
-    ts(T.pst[:, :], T.io8[:, :], C[:, 2:3], A.is_le, ["io8", "c2"], ["pst"], 2 * BIG, A.mult)
-    ts(T.pns[:, :], T.ioj[:, 0:32], C[:, 4:5], A.subtract, ["ioj", "c4"], ["pns"], -4 * BIG, A.mult)
-    ts(T.msk[:, :], T.iom[:, :], C[:, 1:2], A.is_gt, ["iom", "c1"], ["msk"], BIG, A.mult)
+    ts(T.pns[:, :], T.ioj[:, 0:48], C[:, 4:5], A.subtract, ["ioj", "c4"], ["pns"], -4 * BIG, A.mult)
+    ts(T.msk[:, :], T.ioj[:, 0:96], C[:, 1:2], A.is_gt, ["ioj", "c1"], ["msk"], BIG, A.mult)
     ts(T.idb[:, :], T.iof[:, 0:128], C[:, 0:1], A.is_equal, ["iof", "c0"], ["idb"])
-    cp(T.kl0[:, :], T.kmi[:, 0:60], ["kmi"], ["kl0"])
-    cp(T.kc[:, 0:60], T.kmi[:, 0:60], ["kmi"], ["kc"])
-    for jb in range(3):
-        ts(T.selj[0:48, 128 * jb:128 * jb + 128], T.ioj[0:48, 0:128], 16.0 * jb, A.add, ["ioj", "c0"], ["selj"], C[0:48, 0:1], A.is_equal)
-    tt(T.scw[:, :], T.bof[:, :], T.sgn[:, :], A.mult, ["bof", "sgn"], ["scw"])
-    for jb in range(3):
-        ts(T.mk5[:, 24 * jb:24 * jb + 8], T.tmp[:, 0:8], 1024.0, A.add, ["tmpA"], ["mk5"])
-        ts(T.mk5[:, 24 * jb + 8:24 * jb + 24], T.tmp[:, 0:16], -1536.0, A.add, ["tmpA"], ["mk5"])
+    cp(T.kl[:, 0:57], T.kmi[:, 3:60], ["kmi"], ["kl0"])
+    cp(T.kc[:, 0:57], T.kmi[:, 3:60], ["kmi"], ["kc"])
+    cp(T.homek[:, 1:4], T.kmi[:, 0:3], ["kmi"], ["homez"])
+    for s in range(2):
+        ts(T.scw[:, 14 + s:142:16], T.iof[:, 0:8], C[:, 2:3], A.is_equal, ["iof", "c2"], ["scw"], 2048.0 * s - 1024.0, A.mult)
+
+    def weights(i, v, keys):
+        for h in range(2):
+            c = 320 * i + 160 * h
+            ts(T.wts[:, c + 31:c + 159:32], T.iof[:, h:8:2], C[:, 2:3], A.is_equal, ["iof", "c2"] + keys, ["wts"], v, A.mult)
+
+    weights(1, 2.0 ** 25, [])
+    for i in range(3):
+        ts(T.inc[:, 34 * COL[i] + 16:34 * COL[i] + 34:17], T.iof[:, 2 * i:2 * i + 2], -128.0, A.mult, ["iof", "c3"], ["inc"], C[:, 3:4], A.subtract)
+    ms(T.sumr[:, 0:42:21], 0.0, ["sumr"], ["sumr"])
     ts(T.padf[:, :], T.padh[:, :], C[:, 1:2], A.add, ["padh", "c1"], ["padu"], 2.0, A.mult)
-    ts(T.cur[:, :], T.curh[:, :], C[:, 1:2], A.add, ["curh", "c1"], ["cur"], 2.0, A.mult)
-    ts(T.cntw[:, :], T.iof[:, 0:8], C[:, 2:3], A.is_equal, ["iof", "c2"], ["cntw"], 2.0 ** 25, A.mult)
-    for r in range(6, 10):
-        s_lay(r, r // 2, "v")
+    ts(T.so0[:, 0:126], T.curh[:, :], C[:, 4:5], A.add, ["curh", "c4"], ["cur"], 2.0, A.mult)
+    ts(T.hrow[0:1, :], T.hrow[0:1, :], 10.0, A.min, ["hrow"], ["hrow"])
+    for r in range(4, 10):
+        s_lay(r, "v")
 
     Zk = ["ZA", "ZB", "Zpad"]
     Zall = T.Z[:, :]
     Sk = ["Sa", "Sb", "Spad"]
     bwin = T.booki[:, :]
     twin = T.tf[:, :]
-    BLOCKS = [(0, B0, 4), (B0, PH, 5)]
-    SB = (6, 7, 4)
+    BLOCKS = [(0, 24, 4), (24, B1, 4), (B1, PH, 5)]
 
     def names_of(t):
         return 4 if t > 0 else 2
 
     def book_at(t, a, b):
-        return T.booki[:, 0:1024 if t == 0 else 3072].indirect(T["kl%d" % t][:, a:b]), ["bookA", "kl%d" % t] + (["bookB"] if t > 0 else [])
+        return T.booki[:, 0:1024 if t == 0 else 2048].indirect(T.kl[:, 72 * t + a:72 * t + b]), ["bookA", "kl%d" % t] + (["bookB"] if t > 0 else [])
 
     def terms(t, i):
         a, b, bank = BLOCKS[i]
-        src, keys = book_at(t, a // 8, b // 8)
+        if i:
+            src, keys = book_at(t, a // 8 - 3, b // 8 - 3)
+        else:
+            src, keys = T.booki[:, 0:1024].indirect(T.kz[:, 8 * (t % 4):8 * (t % 4) + 3]), ["bookA", "kz%d" % (t % 4)]
         act(T.thi[:, 2 * a:2 * b], src, keys, ["thi%d" % i], bias=-OFF)
         for o in range(2):
             for h in range(2):
@@ -273,55 +293,69 @@ def rank_program(g, core, T, topo):
         act(T.ll[:, 2 * a:2 * b], T["ps%d" % bank][:, 0:2 * (b - a)], ["B%d" % bank], ["ll%d" % i], bias=OFF)
 
     def half(o, c, n):
-        i = 0 if c < B0 else 1
+        i = 0 if c < 24 else 1 if c < B1 else 2
         a, b, bank = BLOCKS[i]
         return T.ll[:, a + o * (b - a) + c:a + o * (b - a) + c + n], "ll%d" % i
 
     def wholes(t):
-        src, keys = book_at(t, KN, 60)
-        act(T.nat[:, :], src, keys, ["nat"])
+        src, keys = book_at(t, KN - KN % 2, 57)
+        act(T.nat[:, 0:NN + 16 * (KN % 2)], src, keys, ["nat"])
 
     def sread(v):
         m = 3 * names_of(v)
-        act(T.sp[:, 0:16 * m], T.S[:, :].indirect(T.pl[:, 12 * v:12 * v + m]), Sk + ["plN%d" % v, "plO%d" % v], ["sp"])
+        act(T.sp[:, 0:16 * m], T.S[:, :].indirect(T.pl[:, 12 * v:12 * v + m]), Sk + ["pl%d" % v], ["sp"])
 
-    def swrite(v, a, b):
-        if a < 3 * names_of(v):
-            cp(T.S[:, :].indirect(T.offs[:, 12 * v + a:12 * v + b]), T.sp[:, 16 * a:16 * b], ["offs%d" % v, "sp"] + Sk, Sk)
+    def swrite(v, q):
+        m = 3 * names_of(v)
+        dst = T.S[:, :].indirect(T.offs[:, 12 * v:12 * v + m])
+        if q == "v":
+            cp(dst, T.sp[:, 0:16 * m], ["offs%d" % v, "sp"] + Sk, Sk)
+        else:
+            act(dst, T.sp[:, 0:16 * m], ["offs%d" % v, "sp"] + Sk, Sk, func=AF.Silu)
 
     def yslot(k, n=1):
         if k < NP:
             return T.ysc[:, 384 * k + 7:384 * (k + n):8]
         return T.ysc[:, YN + 768 * (k - NP) + 15:YN + 768 * (k - NP + n):16]
 
-    def answers(t, head):
+    def answers(t, filler, head):
         pits, nits = [], []
         for (chs, its) in ((P_CH, pits), (N_CH, nits)):
             c = 0
             for n in chs:
                 its.append((c, n))
                 c += n
-        done = [0, NP - 1]
+        done = [0, NP - 1, 0, NP - 1]
+        np_ = len(pits)
+
+        def rows(bank, i, x, src, key, end):
+            for h in range(2):
+                c = 320 * i + 160 * h + 31 - x
+                mm(T["ps%d" % bank][:, 0:3, 16 * h:16 * h + 16], T.wts[:, c:c + 128], src, [key, "wts"], ["B%d" % bank], False, end and h == 1)
 
         def sums(cls, upto, key):
             k0, k1 = done[cls] + 1, upto
             done[cls] = max(done[cls], upto)
             if k1 < k0:
                 return
-            tt(T.lt[:, 48 * (k0 - 1):48 * k1], yslot(k0, k1 - k0 + 1), T.ps0[:, 0:48 * (k1 - k0 + 1)], A.is_lt, [key, "B0"], ["lt" + key])
+            tt(T.lt[:, 48 * k0:48 * (k1 + 1)], yslot(k0, k1 - k0 + 1), T.ps0[:, 0:48 * (k1 - k0 + 1)], A.is_lt, [key, "B0"], ["lt" + key])
             for k in range(k0, k1 + 1):
-                for p in ([0] if k == 1 + t else []) + [20 - k]:
-                    mm(T.ps2[0:48, p:160:20], yslot(k), T.usel[:, :], [key, "usel"], ["B2"], False, k == 19)
-            for k in range(k0, k1 + 1):
-                mm(T.ps3[0:48, 20 - k:160:20], T.lt[:, 48 * (k - 1):48 * k], T.cntw[:, :], ["lt" + key, "cntw"], ["B3"], False, k == 19)
+                rows(3, 1, 20 - k, T.lt[:, 48 * k:48 * k + 48], "lt" + key, k == 19)
+
+        def weigh(cls, upto, key):
+            for k in range(done[2 + cls] + 1, upto + 1):
+                for x in ([0] if k == 1 + t else []) + [20 - k]:
+                    rows(7, 0, x, yslot(k), key, k == 19)
+            done[2 + cls] = max(done[2 + cls], upto)
 
         def ngather(i):
             c, n = nits[i]
-            act(T.G[:, YN + 16 * c:YN + 16 * (c + n)], Zall.indirect(T.nat[:, c:c + n]), Zk + ["nat"], ["J%d" % i])
+            act(T.G[:, YN + 16 * c:YN + 16 * (c + n)], Zall.indirect(T.nat[:, 16 * (KN % 2) + c:16 * (KN % 2) + c + n]), Zk + ["nat"], ["J%d" % i])
 
         def nscan(i):
             c, n = nits[i]
             scan(T.ysc[:, YN + 16 * c:YN + 16 * (c + n)], T.rst[:, 0:16 * n], T.G[:, YN + 16 * c:YN + 16 * (c + n)], A.max, A.min, ["rst", "J%d" % i], ["YN%d" % i])
+            weigh(1, NP - 1 + (c + n) // 48, "YN%d" % i)
 
         def pgather(i, f=act):
             c, n = pits[i]
@@ -336,214 +370,217 @@ def rank_program(g, core, T, topo):
         def pscan(i):
             c, n = pits[i]
             scan(T.ysc[:, 16 * c:16 * (c + n)], T.rst8[:, 0:16 * n], T.H[:, 16 * c:16 * (c + n)], A.max, A.min, ["rst8", "H%d" % i], ["YP%d" % i])
+            if i == 0:
+                for k in range(4):
+                    mm(T.ps0[:, 48 * k:48 * k + 48], T.idb[:, :], yslot(0), ["idb", "YP0"], ["B0"])
+            weigh(0, (c + n) // 24 - 1, "YP%d" % i)
 
-        pgather(0, cp)
-        pgather(1)
+        filler()
+        for i in range(OWN):
+            pgather(i, cp)
+        first = OWN
+        while pits[first][0] < B1:
+            pgather(first)
+            first += 1
         head()
-        turned(1)
-        statics(t)
-        pgather(2)
-        if t == 0:
-            wholes(t)
-        for i in range(3, len(pits)):
+        ngather(0)
+        for i in range(first, np_):
             pgather(i)
-        for i in range(len(nits)):
+        for i in range(1, len(nits)):
             ngather(i)
-        for i in (1, 0, 2):
-            pfold(i)
+        pfold(0)
+        pfold(1)
         pscan(0)
-        pscan(1)
-        for k in range(4):
-            mm(T.ps0[:, 48 * k:48 * k + 48], T.idb[:, :], yslot(0), ["idb", "YP0"], ["B0"])
-        for i in range(3, len(pits)):
+        for i in range(2, np_):
             pfold(i)
             sums(0, sum(pits[i - 2]) // 24 - 1, "YP%d" % (i - 2))
             pscan(i - 1)
-        pscan(len(pits) - 1)
-        sums(0, sum(pits[-2]) // 24 - 1, "YP%d" % (len(pits) - 2))
+        pscan(np_ - 1)
+        sums(0, sum(pits[-2]) // 24 - 1, "YP%d" % (np_ - 2))
         for i in range(len(nits)):
             nscan(i)
             if i == 0:
-                sums(0, NP - 1, "YP%d" % (len(pits) - 1))
-            else:
-                sums(1, NP - 1 + sum(nits[i - 1]) // 48, "YN%d" % (i - 1))
+                sums(0, NP - 1, "YP%d" % (np_ - 1))
+            elif i != len(nits) - 2:
+                j = min(i - 1, len(nits) - 3)
+                sums(1, NP - 1 + sum(nits[j]) // 48, "YN%d" % j)
         sums(1, 19, "YN%d" % (len(nits) - 1))
 
-    def places_of_terms(i):
-        b = SB[i]
-        mm(T["ps%d" % b][:, 0:256], T.onb[0:1, 0:128], T.pos[0:1, 0:256], ["onb", "pos"], ["B%d" % b], True, False)
-        if i:
-            mm(T["ps%d" % b][:, 0:256], T.pos[0:1, 128 + 128 * i:256 + 128 * i], T.onb[0:1, :], ["onb", "pos"], ["B%d" % b], False, False)
-        for c in range(2):
-            mm(T["ps%d" % b][:, 128 * c:128 * c + 128], T.id2[:, :], T.mk7[:, :], ["id2", "mk7"], ["B%d" % b], False, False)
-
-    def statics(t):
-        mm(T.ps2[0:48, 0:160], T.on2[0:1, :], T.hrow[0:1, :], ["on2", "hrow"], ["B2"], True, False)
-        mm(T.ps3[0:48, 0:160], T.on2[0:1, :], T.crow[0:1, :], ["on2", "crow"], ["B3"], True, False)
-        mm(T.ps5[:, 0:72], T.idh[:, 0:128], T.mk5[:, :], ["idh", "mk5"], ["B5"], True, False)
-        for i in range(3 if t > 0 else 2):
-            places_of_terms(i)
+    def head():
+        turned(2)
+        mm(T.ps7[:, 0:3, :], T.hrow[0:1, :], T.on2[0:1, :], ["on2", "hrow"], ["B7"], True, False)
+        mm(T.ps3[:, 0:3, :], T.crow[0:1, :], T.on2[0:1, :], ["on2", "crow"], ["B3"], True, False)
 
     act(T.Z[:, 0:16 * ZS], T.truv[:, :].indirect(T.sgl[:, 0:ZS]), ["truv", "sgl"], ["ZA"])
     cp(T.Z[:, 16 * ZS:4096], T.truv[:, :].indirect(T.sgl[:, ZS:256]), ["truv", "sgl"], ["ZB"])
-    terms(0, 0)
-    terms(0, 1)
+    BLOCKS[1] = (24, B1, 0)
+    for i in range(3):
+        terms(0, i)
     turned(0)
+    turned(1)
+    BLOCKS[1] = (24, B1, 4)
     cp(C[:, 9:10], T.kmi[:, 60:61], ["wti"], ["c9"])
 
-    def weights():
-        ts(T.usel[:, :], T.iof[:, 0:8], C[:, 2:3], A.is_equal, ["iof", "c2", "c9"], ["usel"], C[:, 9:10], A.mult)
-        for r in range(10, 14):
-            s_turn(r, (1, 4)[r // 2 - 5])
+    def first_head():
+        wholes(0)
+        head()
 
-    answers(0, weights)
+    answers(0, lambda: weights(0, C[:, 9:10], ["c9"]), first_head)
 
     for t in range(VI):
-        st, stk = T["st%d" % t], "st%d" % t
+        st, stk = T["st%d" % max(t, 1)], "st%d" % t
         so = T["so%d" % t]
         last = t == VI - 1
+        cur = so[:, 0:126] if not last else T.ki[:, 0:126]
         old = t > 0
         M = names_of(t)
         o = 12 * t
-        dst, frm = (nxt, prv) if not last else (prv, nxt)
-
-        def send(src_ap, keys, land, c=0):
-            deps("g", keys, [])
-            rid, pid = topo.addr(dst, core)
-            en = topo.engines(core, dst)[:8]
-            g.remote_dma(out_ap=T[land][:, c:], in_ap=src_ap, remote_sem=T.sem["a_" + land], local_sem=T.sem.lsem,
-                         pid=pid, routing_id=rid, dma_engine_mask=sum(1 << e for e in en))
-            cnt["sent"] = cnt.get("sent", 0) + len(en)
-            wr[land] = ("a_" + land, len(topo.engines(frm, core)[:8]), "remote")
-
-        if old:
-            act(T.sm[:, 0:3], T.ps1[:, 0:3], ["B1"], ["cc"], accum_out=T.cc[:, :])
+        if not old:
+            for r in (14, 15, 10, 11):
+                s_lay(r, "s")
+        if not last:
+            terms(t + 1, 0)
+        if last:
+            act(T.rb[:, :], T.ri[:, :], ["ri"], ["rb"], bias=-SO)
+            dma("y", T.S[0:128:16, 0:4096], T.rb[:, :], "drb", ["rb"], Sk)
+        elif old:
             sread(t - 1)
+            swrite(t - 1, "s")
+        if not old:
+            ms(T.pos[0:1, 118:204:17], 1.5 * 2.0 ** 23, ["pos"], ["pos"])
+            ms(T.zc[:, :, 128], 0.0, ["zcV"])
+        if not last:
+            turned(0)
+        if t == VI - 2:
+            dma("y", T.ra[:, :], T.S[0:128:16, 0:4096], "dra", Sk, ["ra"])
+        for i in range(2):
+            mm(T.ps6[:, 0:102], T.onb[0:1, :], T.pos[0:1, 102 * i:102 * i + 102], ["onb", "pos"], ["B6"], i == 0, False)
+        mm(T.ps6[:, 0:102], T.pos[0:1, 204:332], T.onb[0:1, 0:102], ["onb", "pos"], ["B6"], False, False)
+        if old:
+            cp(T.kc[:, 60:117], T.kl[:, 72 * t:72 * t + 57], ["kl%d" % t], ["kraw"])
             for a in range(2):
                 for jb in range(3):
-                    c = 64 + 63 * a + 21 * jb
-                    e = 186 + (4 * jb + 3 - a if t > 1 else 2 * jb + 1 - a)
-                    act(T.ps1[:, c:c + 21], st[:, 198 + 21 * jb:219 + 21 * jb], [stk], ["B1"], scale=st[:, e:e + 1])
-            cp(T.kc[:, 60:120], T["kl%d" % t][:, :], ["kl%d" % t], ["kraw"])
-        else:
-            for r in range(10, 14):
-                s_lay(r, (1, 4)[r // 2 - 5], "s")
-        cp(T.hi[0:48, :], T.ps2[0:48, 0:160], ["B2"], ["hi"])
+                    e = 129 + COL[jb] + (6 * a + 3 if t > 1 else 3 * a)
+                    ts(T.ps1[:, 64 + 63 * a + jb:127 + 63 * a:3], T.iof[:, 128:149], st[:, 126 + jb:127 + jb], A.is_equal, ["iof", stk], ["B1"], st[:, e:e + 1], A.mult)
+            ts(T.kc[:, 0:57], T.kc[:, 60:117], 1023, A.bitwise_and, ["kraw"], ["kc"])
+        flip(T.hi[:, :], T.ps7[:, 0:3, :], ["B7"], ["hi"])
+        flip(T.lo[:, :], T.ps3[:, 0:3, :], ["B3"], ["lo"])
         if old:
-            ts(T.kc[:, 0:60], T.kc[:, 60:120], 1023, A.bitwise_and, ["kraw"], ["kc"])
-        scan(T.su[0:48, :], T.ps3[0:48, 0:160], T.hi[0:48, :], A.max, A.min, ["B3", "hi"], ["su"])
-        x = T.su[0:48, 19:160:20]
-        uU, uQ, uA, uF, uB = [T.uint[0:48, 8 * i:8 * i + 8] for i in range(5)]
-        ts(uU, x, 4095, A.bitwise_and, ["su"], ["uU"])
-        ts(T.nk[0:48, 8:16], x, -2.0 ** -20, A.mult, ["su"], ["nkk"], 1546.49609375, A.add)
-        tt(uQ, uU, uU, A.mult, ["uU"], ["uQ"])
-        ts(uA, uU, 37.0, A.mult, ["uU"] + (["cc"] if old else []), ["uA"], T.cc[0:48, 0:1] if old else 0.0, A.add)
-        ts(T.kz[0:48, :], T.nk[0:48, 8:16], 1556.0, A.is_equal, ["nkk"], ["kz"], float(t + 1 - 20), A.mult)
-        ts(uF, uQ, 5, A.arith_shift_right, ["uQ"], ["uF"], 1023, A.bitwise_and)
-        ts(uB, uA, 1023, A.bitwise_and, ["uA"], ["uB"])
-        tt(T.nk[0:48, 16:24], T.nk[0:48, 8:16], T.kz[0:48, :], A.add, ["nkk", "kz"], ["nks"])
-        tt(T.nk[0:48, 0:8], uF, uB, A.add, ["uF", "uB"], ["nkn"])
-        for jb in range(3):
-            mm(T.ps5[:, 24 * jb:24 * jb + 24], T.selj[0:48, 128 * jb:128 * jb + 128], T.nk[0:48, :], ["selj", "nkn", "nkk", "nks"], ["B5"], False, jb == 2)
-        if old:
-            swrite(t - 1, 0, 6)
-            tt(T.cur[:, :], st[:, 60:186], T.ps1[:, 64:190], A.add, [stk, "B1"], ["cur"])
+            tt(cur, st[:, 0:126], T.ps1[:, 64:190], A.max, [stk, "B1"], ["cur"])
         else:
-            places_of_terms(2)
-            for r in (14, 15):
-                s_turn(r, 0)
-        scan(T.pk[:, :], T.pst[:, :], T.ps5[:, 0:72], A.max, A.min, ["pst", "B5"], ["pk"])
-        for jb in range(3):
-            red(T.nl[:, jb:jb + 1], T.ps5[:, 24 * jb:24 * jb + 8], A.min, ["B5"], ["nl"])
-        eqo, neq = T.ps0[:, 0:63], T.ps3[:, 0:63]
-        for jb in range(3):
-            ts(T.ps2[:, jb:60:3], T.iof[:, 0:20], T.pk[:, 23 + 24 * jb:24 + 24 * jb], A.is_equal, ["iof", "pk"], ["B2"], T.pk[:, 7 + 24 * jb:8 + 24 * jb], A.mult)
-        cp(T.bkl[:, :], bwin.indirect(T.nl[:, 0:3]), ["bookA", "bookB", "nl"], ["bkl"])
-        for i in (1, 2):
-            act(T.zc[:, 256 * i:256 * i + 256], Zall.indirect(T.bkl[:, 16 * i:16 * i + 16]), Zk + ["bkl"], ["zc%d" % i])
-        if not last:
-            kok = "ko%d" % t
-            tt(T[kok][:, :], T.kc[:, 0:60], T.ps2[:, 0:60], A.max, ["kc", "B2"], [kok])
-            send(T[kok][:, :], [kok], "kl%d" % (t + 1))
-        cp(T.zc[:, 0:256], Zall.indirect(T.bkl[:, 0:16]), Zk + ["bkl"], ["zc0"])
-        for i in (1, 0, 2):
-            mm(T["ps%d" % SB[i]][:, 0:256], T.scw[:, :], T.zc[:, 256 * i:256 * i + 256], ["zc%d" % i, "scw"], ["B%d" % SB[i]], False, True)
-        if not last:
-            act(T.tf[:, :], T.iot[:, :].indirect(T.bkl[:, :]), ["iot", "bkl"], ["tf"])
-            act(T.hitb[:, 0:3], T.pk[:, 15:72:24], ["pk"], ["hitb"], func=AF.Sign, scale=-1.0, bias=20.0)
-        for jb in range(3):
-            act(T.ab[:, 21 * jb:21 * jb + 21], T.iof[:, 0:21], ["iof", "pk"], ["ab"], func=AF.Abs, scale=-1.0, bias=T.pk[:, 23 + 24 * jb:24 + 24 * jb])
-        act(neq, T.ab[:, :], ["ab"], ["B3"], func=AF.Sign)
-        if last:
-            act(T.tf[:, :], T.iot[:, :].indirect(T.bkl[:, :]), ["iot", "bkl"], ["tf"])
-        else:
-            act(so[:, 198:261], T.ab[:, :], ["ab"], ["eqk"], func=AF.Relu, scale=-1.0, bias=1.0)
+            s_lay(12, "v")
+        scan(T.su[:, :], T.lo[:, :], T.hi[:, :], A.max, A.min, ["lo", "hi"], ["su"])
         if not old:
-            for r in (14, 15):
-                s_lay(r, 0, "v")
-        else:
-            for jb in range(3):
-                ts(T.ps0[:, 21 * jb:21 * jb + 21], T.iof[:, 0:21], T.pk[:, 15 + 24 * jb:16 + 24 * jb], A.is_equal, ["iof", "pk"], ["B0"])
-            if last:
-                tt(T.kc[:, 60:120], T.kc[:, 0:60], T.ps2[:, 0:60], A.max, ["kc", "B2"], ["kraw"])
-                ts(T.fa[:, 0:126], T.cur[:, :], OFF - 0.5, A.is_ge, ["cur"], ["fa"], -8192.0, A.mult)
-        for i in (1, 0, 2):
-            for c in range(2):
-                red(T.sk[:, 2 * i + c:2 * i + c + 1], T["ps%d" % SB[i]][:, 128 * c:128 * c + 128], A.min, ["B%d" % SB[i]], ["sk"])
-            if old and i == 1:
-                tt(T.pr[:, 0:63], T.cur[:, 0:63], eqo, A.mult, ["cur", "B0"], ["prA"])
-                tt(T.pr[:, 63:126], T.cur[:, 63:126], eqo, A.mult, ["cur", "B0"], ["prB"])
-        if old:
-            scan(T.osm[:, :], T.sumr[:, :], T.pr[:, :], A.mult, A.add, ["sumr", "prA", "prB"], ["osm"])
+            s_lay(13, "v")
         if last:
-            tt(T.fb[:, 0:126], T.cur[:, :], T.fa[:, 0:126], A.add, ["cur", "fa"], ["fb"])
-        elif old:
-            swrite(t - 1, 6, 8)
-        ts(T.sk[:, 6:12], T.sk[:, 0:6], 1023, A.bitwise_and, ["sk"], ["sq"])
+            ts(T.ki[:, 126:252], cur, 8191, A.bitwise_and, ["cur"], ["kand"])
+        x = T.su[:, 31:96:32]
+        uU, uQ, uA, uF, uB = [T.uint[:, 4 * i:4 * i + 3] for i in range(5)]
+
+        def olds(step, blocks=()):
+            if not old:
+                return
+            if step == 0:
+                for jb in blocks:
+                    ts(T.ps2[:, 128 + jb:254:3], T.io2[:, :], T.kb[:, jb:jb + 1], A.is_equal, ["io2", "kb"], ["xe"])
+            elif step == 1:
+                tt(T.pr[:, :], cur, T.ps2[:, 128:254], A.mult, ["cur", "xe"], ["pr"])
+            elif step == 2:
+                for jb in range(3):
+                    scan(T.osm[:, 42 * COL[jb]:42 * COL[jb] + 42], T.sumr[:, :], T.pr[:, jb:126:3], A.mult, A.add, ["sumr", "pr"], ["osm"])
+            elif step == 3:
+                ts(T.osm[:, 126:132], T.osm[:, 20:126:21], 8191, A.bitwise_and, ["osm"], ["om"])
+            elif step == 4:
+                ts(T.fo[:, :], T.osm[:, 126:132], -1.0, A.add, ["om"], ["fo"])
+                for m in range(2):
+                    ts(T.ns[:, 96 * m + 15:96 * m + 48:16], T.osm[:, 126 + m:132:2], -OFF - 1.0, A.add, ["om"], ["nsO"])
+            else:
+                tt(T.fn[:, 65:256:2], T.iot[:, :].indirect(T.fo[:, 0:6]), T.msk[:, :], A.add, ["iot", "fo", "msk"], ["fnN"])
+
+        ts(uU, x, 4095, A.bitwise_and, ["su"], ["uU"])
+        ts(T.kb[:, 0:3], x, -2.0 ** -20, A.mult, ["su"], ["kb"], 138.49609375, A.add)
+        ts(uA, uU, 37.0, A.mult, ["uU"] + (["B0"] if old else []), ["uA"], T.ps0[:, 400:401] if old else 0.0, A.add)
+        tt(uQ, uU, uU, A.mult, ["uU"], ["uQ"])
+        ts(T.kd[:, 0:3], T.kb[:, 0:3], 148.0, A.is_equal, ["kb"], ["kd"], float(t + 1 - 20), A.mult)
+        olds(0, (0, 1))
+        ts(uB, uA, 1023, A.bitwise_and, ["uA"], ["uB"])
+        ts(uF, uQ, 5, A.arith_shift_right, ["uQ"], ["uF"], 1023, A.bitwise_and)
+        tt(so[:, 126:129], T.kb[:, 0:3], T.kd[:, 0:3], A.add, ["kb", "kd"], ["ks"])
+        olds(0, (2,))
+        tt(T.nl[:, 0:3], uF, uB, A.add, ["uF", "uB"], ["nl"])
+        tt(T.kd[:, 4:7], uF, uB, A.add, ["uF", "uB"], ["nr"])
+        for jb in range(3):
+            ts(T.ps2[:, 256 + jb:313:3], T.iof[:, 129:148], so[:, 126 + jb:127 + jb], A.is_equal, ["iof", "ks"], ["xk"] + ([] if old else ["B2"]), -2048.0, A.mult)
+        cp(T.bkl[:, :], bwin.indirect(T.nl[:, 0:3]), ["bookA", "bookB", "nl"], ["bkl"])
+        for jb in range(3):
+            ts(T.ps2[:, jb:57:3], T.iof[:, 129:148], so[:, 126 + jb:127 + jb], A.is_equal, ["iof", "ks", "nr"], ["xn"], T.kd[:, 4 + jb:5 + jb], A.mult)
+        tt(T.kc[:, 60:117], T.kc[:, 0:57], T.ps2[:, 256:313], A.add, ["kc", "xk"], ["kraw"])
+        for c in range(3, 6):
+            act(T.zc[:, 2 * COL[c // 2] + c % 2, 0:128], Zall.indirect(T.bkl[:, 8 * c:8 * c + 8]), Zk + ["bkl"], ["zcS"])
+        act(T.tf[:, :], T.iot[:, :].indirect(T.bkl[:, :]), ["iot", "bkl"], ["tf"])
+        cp(T.zc[:, 2 * COL[0], 0:128], Zall.indirect(T.bkl[:, 0:8]), Zk + ["bkl"], ["zcV"])
         if not last:
-            mm(T.ps1[:, 0:3], T.onb[:, 0:128], T.hitb[:, 0:3], ["onb", "hitb"], ["B1"])
-        if old:
-            for m in range(2):
-                ts(T.fo[:, m:6:2], T.osm[:, 63 * m + 20:63 * m + 63:21], OFF, A.add, ["osm"], ["fo"])
-            for m in range(2):
-                act(T.pl[:, o + m:o + 12:4], T.osm[:, 63 * m + 20:63 * m + 63:21], ["osm"], ["plO%d" % t], bias=OFF)
-        if last:
-            ts(T.fa[:, 0:126], T.fb[:, 0:126], OFF + 1.0, A.add, ["fb"], ["fa"], 0.0, A.max)
-        cp(T.fl[:, 0:6], T.sk[:, 6:12], ["sq"], ["fl"])
-        if old:
-            tt(T.fn[:, 129:320:2], T.iot[:, :].indirect(T.fo[:, 0:6]), T.msk[:, :], A.add, ["iot", "fo", "msk"], ["fnP"])
-            tt(T.fn[:, 1:128:2], T.iot[:, :].indirect(T.fo[:, 0:4]), T.tmp[:, 80:144], A.add, ["iot", "fo", "tmpB"], ["fnO"])
-        tt(T.fn[:, 128:320:2], twin.indirect(T.fl[:, 0:6]), T.mkn[:, 64:160], A.add, ["tf", "fl", "mkn"], ["fnB"])
-        tt(T.fn[:, 0:128:2], twin.indirect(T.fl[:, 0:4]), T.mkn[:, 0:64], A.add, ["tf", "fl", "mkn"], ["fnA"])
-        if last:
-            ts(T.kc[:, 0:60], T.kc[:, 60:120], 1023, A.bitwise_and, ["kraw"], ["kc"])
+            kok, c = "ko%d" % t, 72 * t
+            tt(T.ko[:, c:c + 57], T.kc[:, 60:117], T.ps2[:, 0:57], A.max, ["kraw", "xn"], [kok])
+            send(T.ko[:, c:c + 57], [kok], "kl%d" % (t + 1), T.kl[:, c + 72:c + 129])
+        for c in range(1, 3):
+            cp(T.zc[:, 2 * COL[c // 2] + c % 2, 0:128], Zall.indirect(T.bkl[:, 8 * c:8 * c + 8]), Zk + ["bkl"], ["zcV"])
+        olds(1)
+        for r in range(8):
+            mm(T.ps6[:, 0:102], T.scw[:, 14 - 2 * r:142 - 2 * r], T.zc[:, :, 16 * r:16 * r + 17], ["zcV", "zcS", "scw"], ["B6"], False, r == 7)
+        if not last:
+            ts(T.hitb[:, 0:3], T.kb[:, 0:3], 147.5, A.is_lt, ["kb"], ["hitb"])
             for jb in range(3):
-                for a in range(2):
-                    c = 63 * a + 21 * jb
-                    tt(T.ts3[:, 60 * a + jb:60 + 60 * a:3], T.fa[:, c:c + 20], T.ps3[:, 21 * jb:21 * jb + 20], A.mult, ["fa", "B3"], ["ts3"])
-        elif old:
-            swrite(t - 1, 8, 12)
-        for m in range(2):
-            scan(T.ns[:, 65 - m:96:2], T.pns[:, 0:16], T.fn[:, 256 + 2 * m:320:4], A.max, A.min, ["pns", "fnB"], ["nsB", "nsO"])
-        for m in range(2):
-            scan(T.ns[:, 1 - m:64:2], T.pns[:, 0:32], T.fn[:, 2 * m:128:4], A.max, A.min, ["pns", "fnA"], ["nsA", "nsO"])
+                mm(T.ps0[:, 400:401], T.onb[:, :], T.hitb[:, jb:jb + 1], ["onb", "hitb"], ["B0"], jb == 0, jb == 2)
+        else:
+            tt(T.kc[:, 0:57], T.kc[:, 60:117], T.ps2[:, 0:57], A.max, ["kraw", "xn"], ["kc"])
+            for jb in range(3):
+                ts(T.ps0[:, jb:126:3], T.io2[:, :], so[:, 126 + jb:127 + jb], A.is_equal, ["io2", "ks"], ["B0"], 8192.0, A.mult)
+        olds(2)
         if last:
-            cp(T.sf[:, 120:180], T.kc[:, 0:60], ["kc"], ["sfk"])
-            send(T.sf[:, 120:180], ["sfk"], "homek")
-            act(T.ps2[:, 0:120], T.ts3[:, :], ["ts3"], ["B2"], bias=-1.0)
-        reg = [(0, 64), (64, 192), (128, 320)]
+            ts(T.kc[:, 60:117], T.kc[:, 0:57], 1023, A.bitwise_and, ["kc"], ["kraw"])
+            tt(T.fb[:, 0:126], T.ki[:, 126:252], T.ps0[:, 0:126], A.add, ["kand", "B0"], ["fb"])
+        olds(3)
+        if last:
+            ts(T.ps4[:, 0:126], T.fb[:, 0:126], 4096.5, A.is_lt, ["fb"], ["B4"])
+            cp(T.sf[:, 128:185], T.kc[:, 60:117], ["kraw"], ["sfk"])
+            send(T.sf[:, 128:185], ["sfk"], "homek", T.homek[:, 4:61], -1)
+        olds(4)
+        if last:
+            tt(T.fa[:, 0:126], T.fb[:, 0:126], T.ps4[:, 0:126], A.mult, ["fb", "B4"], ["fa"])
+        scan(T.sk[:, 0:102], T.rs17[:, :], T.ps6[:, 0:102], A.max, A.min, ["rs17", "B6"], ["sk"])
+        scan(T.sk[:, 102:204], T.inc[:, :], T.ps6[:, 0:102], A.add, A.min, ["inc", "B6"], ["sk"])
+        olds(5)
+        tt(T.fl[:, 0:6], T.sk[:, 16:102:17], T.sk[:, 118:204:17], A.subtract, ["sk"], ["fl"])
+        lower = ((2, 256, 384, 0), (1, 0, 64, 2))
+        for (i, a, b, c) in lower if old else ():
+            act(T.fn[:, a + 1:b:2], T.iot[:, :].indirect(T.fo[:, c:4]), ["iot", "fo"], ["fnG%d" % i])
+        if last:
+            act(T.ps2[:, 0:126], T.fa[:, 0:126], ["fa"], ["B2", "xe", "xk", "xn"], bias=-1.0)
+        for (i, a, b, c) in lower:
+            act(T.fn[:, a:b:2], twin.indirect(T.fl[:, c:4]), ["tf", "fl"], ["fnF%d" % i])
+        tt(T.fn[:, 64:256:2], twin.indirect(T.fl[:, 0:6]), T.mkn[:, :], A.add, ["tf", "fl", "mkn"], ["fnM"])
+        for m in range(2, M):
+            c = (15, 111)[m - 2] + 16 * COL[2]
+            ts(T.eqb[:, 864 + 192 * m:960 + 192 * m], T.fn[:, 193:384:2], T.ns[:, c:c + 1], A.is_equal, ["fnN", "fnG2", "nsO"], ["e2"], 8192.0, A.mult)
+        for m in range(2):
+            scan(T.ns[:, 96 * m + 48:96 * m + 96], T.pns[:, :], T.fn[:, 64 + 2 * m:256:4], A.max, A.min, ["pns", "fnM"], ["nsN"])
+        reg = [(128, 192), (0, 128), (192, 384)]
         eo = [0, 256, 768]
-        nsk = ["nsA", "nsB"]
 
         def name(jb, m):
-            return T.ns[:, 32 * jb + 31 - m:32 * jb + 32 - m] if m < 2 else T.osm[:, 63 * (m - 2) + 21 * jb + 20:63 * (m - 2) + 21 * jb + 21]
+            c = (63, 159, 15, 111)[m] + 16 * COL[jb]
+            return T.ns[:, c:c + 1]
 
         def eq(jb, m):
             a, b = reg[jb]
             w = b - a
             pos = eo[jb] + w * m
+            if jb == 2 and m > 1:
+                ts(T.eqb[:, pos:pos + 96], T.fn[:, a:b:2], name(jb, m), A.is_equal, ["fnM", "fnF2", "nsO"], ["e2"], 8192.0, A.mult)
+                return
             ts(T.eqb[:, pos:pos + w], T.fn[:, a:b], name(jb, m), A.is_equal,
-               ["fnO", "fnA"] + (["fnP", "fnB"] if jb > 0 else []) + [("nsB" if jb == 2 else "nsA") if m < 2 else "osm"], ["e%d" % jb], 8192.0, A.mult)
+               ["fnM", "fnN", "fnF%d" % jb, "fnG%d" % jb, "nsN" if m < 2 else "nsO"], ["e%d" % jb], 8192.0, A.mult)
 
         def count(jb):
             w = (reg[jb][1] - reg[jb][0]) * M // 2
@@ -552,34 +589,31 @@ def rank_program(g, core, T, topo):
             return T.cn[:, c + w - 1:c + w]
 
         def place(jb, col):
-            ts(T.xo[:, M * jb:M * jb + M], T.ns[:, 32 * jb + 32 - M:32 * jb + 32], col, A.add, nsk + ["nsO", "cn%d" % jb], ["xo%d" % jb])
+            ts(T.xo[:, COL[jb]:3 * M:3], T.ns[:, (15 if old else 63) + 16 * COL[jb]:192:192 // M], col, A.add, ["nsN", "nsO", "cn%d" % jb], ["xo%d" % jb])
 
         def places():
             tt(T.offs[:, o:o + 3 * M], T.xo[:, 0:3 * M], T.padf[:, 0:12] if old else T.padf[:, 12:18], A.min, ["xo0", "xo1", "xo2", "padu"], ["offs%d" % t])
 
         def partners():
+            h = 3 * M // 2
             for m in range(2):
-                act(T.pl[:, o + M - 2 + m:o + 3 * M:M], T.ns[:, 31 - m:96:32], nsk, ["plN%d" % t], bias=OFF)
-
-        def beside():
-            for m in range(M - 2):
-                act(T.ns[:, 29 - m:96:32], T.osm[:, 63 * m + 20:63 * m + 63:21], ["osm"], ["nsO"])
+                act(T.pl[:, o + h * m:o + h * m + h], T.ns[:, 96 * (1 - m) + (15 if old else 63):96 * (2 - m):16], ["nsN", "nsO"], ["pl%d" % t], bias=OFF)
 
         if not last:
             partners()
-            beside()
-            act(T.zp[:, 0:48 * M], Zall.indirect(T.pl[:, o:o + 3 * M]), Zk + ["plN%d" % t, "plO%d" % t], ["zp"])
-            terms(t + 1, 0)
             terms(t + 1, 1)
-            turned(0)
+            act(T.zp[:, 0:48 * M], Zall.indirect(T.pl[:, o:o + 3 * M]), Zk + ["pl%d" % t], ["zp"])
+            terms(t + 1, 2)
+            turned(1)
             wholes(t + 1)
         else:
             for jb in (2, 1, 0):
                 for a in range(2):
-                    act(T.q1[:, 60 * a + jb:60 + 60 * a:3], T.ab[:, 21 * jb:21 * jb + 20], ["ab", nsk[jb // 2]], ["q1%d" % jb], func=AF.Identity, scale=-8192.0, bias=name(jb, a))
-        for jb in (2, 1, 0):
-            for m in list(range(2, M)) + [0, 1]:
-                eq(jb, m)
+                    act(T.q1[:, 63 * a + jb:63 * a + 63:3], T.ps0[:, 63 * a + jb:63 * a + 63:3], ["B0", "nsN"], ["q1%d" % jb], func=AF.Identity, bias=name(jb, a))
+        for ms_ in (range(2, M), range(2)):
+            for jb in (2, 1, 0):
+                for m in ms_:
+                    eq(jb, m)
         c2 = count(2)
         c1 = count(1)
         c0 = count(0)
@@ -588,30 +622,34 @@ def rank_program(g, core, T, topo):
         place(2, c2)
         place(1, c1)
         place(0, c0)
-        tt(so[:, 123:186], T.cur[:, 63:126], neq, A.mult, ["cur", "B3"], ["soB"])
         places()
-        tt(so[:, 60:123], T.cur[:, 0:63], neq, A.mult, ["cur", "B3"], ["soA"])
+        if t == VI - 2:
+            cp(T.ri[:, :], T.ra[:, :], ["ra"], ["ri"])
         cp(Zall.indirect(T.offs[:, o:o + 3 * M]), T.zp[:, 0:48 * M], ["offs%d" % t, "zp"], Zk)
-        ts(so[:, 186:186 + 3 * M], T.offs[:, o:o + 3 * M], -OFF, A.add, ["offs%d" % t, "of2"], ["of2"])
-        answers(t + 1, lambda: send(so[:, 60:SW], ["soA", "soB", "of2", "eqk"], "st%d" % (t + 1), 60))
 
-    beside()
+        def state():
+            ts(so[:, 129:129 + 3 * M], T.offs[:, o:o + 3 * M], 8192.0 * (t + 1) + 1.0, A.add, ["offs%d" % t, "of2"], ["of2"])
+            send(so[:, :], ["cur", "ks", "of2"], "st%d" % (t + 1), T["st%d" % (t + 1)][:, :])
+
+        answers(t + 1, state, head)
+
     partners()
+    sread(t - 1)
     for (jb, col) in ((2, c2), (1, c1), (0, c0)):
-        ts(T.x1[:, jb:120:3], T.q1[:, jb:120:3], col, A.subtract, ["q1%d" % jb, "cn%d" % jb], ["x1%d" % jb], 2 * OFF, A.add)
-    tt(T.sf[:, 0:120], T.x1[:, :], T.ps2[:, 0:120], A.max, ["x10", "x11", "x12", "B2"], ["sf"])
-    send(T.sf[:, 0:120], ["sf"], "home")
-    swrite(t - 1, 6, 12)
-    sread(t)
+        ts(T.x1[:, jb:126:3], T.q1[:, jb:126:3], col, A.subtract, ["q1%d" % jb, "cn%d" % jb], ["x1%d" % jb], -2 * OFF, A.add)
     place(2, c2)
     place(1, c1)
     place(0, c0)
+    tt(T.sf[:, 0:126], T.x1[:, :], T.ps2[:, 0:126], A.max, ["x10", "x11", "x12", "B2"], ["sf"])
+    send(T.sf[:, 0:123], ["sf"], "home", T.home[:, 0:123], -1)
     places()
-    swrite(t, 0, 12)
-    dma("y", T.yk[:, :], T.homek[:, :], "dout", ["homek"], [])
+    swrite(t - 1, "v")
+    sread(t)
+    swrite(t, "v")
+    dma("s", T.yk[:, :], T.homek[:, 1:61], "dout", ["homek", "homez"], [])
     dma("y", T.ys[:, :], T.S[0:128:16, 0:4096], "dout", Sk, [])
     dma("s", T.ya[:, :], T.home[:, 0:60], "dout", ["home"], [])
-    dma("y", T.yb[:, :], T.home[:, 60:120], "dout", ["home"], [])
+    dma("y", T.yb[:, :], T.home[:, 63:123], "dout", ["home"], [])
     need("y", "dout", 64)
     need("g", "lsem", cnt["sent"])
     for q in ("v", "s", "p", "g"):

@@ -7,7 +7,7 @@ P_CH = [24, 38, 42, 64, 72, 96]
 OWN = 2
 PH = sum(P_CH)
 NP = PH // 24
-N_CH = [16, 80, 96, 48, 32, 16]
+N_CH = [32, 112, 96, 32, 16]
 NN = sum(N_CH)
 KN = 3 * (NP - 1)
 B1 = 104
@@ -16,42 +16,49 @@ YN, YW = 16 * PH, 16 * (PH + NN)
 OFF = 2048.0
 SO = 4096.0
 BIG = 30000.0
-COL = (1, 0, 2)
-SW = 141
+TFV = 2
+SW = 180
 
 _sb = {
     "truv": (4096, "bfloat16"), "Z": (PADC, "bfloat16"), "S": (PADC, "float32"), "iot": (PADC, "float32"),
-    "booki": (2048, "int32"), "kc": (120, "int32"), "sgi": (256, "int32"), "sgl": (256, "uint16"), "sgh": (256, "float16"), "kmi": (64, "int32"),
-    "G": (YW, "bfloat16"), "nat": (NN + 16, "uint16"), "H": (16 * PH, "bfloat16"), "ysc": (YW, "bfloat16"),
+    "booki": (4096, "int32"), "kc": (128, "int32"), "k2": (57, "float32"), "kw": (64, "float32"), "nw": (8, "float32"), "rep": (4, "uint16"), "sgi": (256, "int32"), "sgl": (256, "uint16"), "sgh": (256, "float16"), "kmi": (64, "int32"),
+    "G": (YW, "bfloat16"), "H": (YN, "bfloat16"), "ysc": (YW, "bfloat16"), "nat": (NN + 16, "uint16"), "nz": (48, "uint16"),
     "kl": (72 * VI, "uint16"), "ko": (72 * VI, "uint16"), "kz": (32, "uint16"),
-    "rst": (16 * max(N_CH), "bfloat16"), "rst8": (16 * max(P_CH), "bfloat16"), "thi": (2 * PH, "float16"),
-    "hsel": (512, "float16"), "ll": (2 * PH, "uint16"), "ki": (252, "int32"),
+    "thi": (2 * PH, "float16"), "hsel": (288, "float16"), "ll": (2 * PH, "uint16"), "kj": (SW, "int32"),
     "pi": (1, "int32"), "pj": (1, "int32"), "pg": (1, "int32"), "colf": (16, "float32"),
-    "iof": (160, "float32"), "iog": (128, "float32"), "ioj": (128, "float32"), "ion": (96, "float32"), "io2": (42, "float32"),
+    "iof": (160, "float32"), "ioj": (48, "float32"), "ion": (96, "float32"), "io2": (40, "float32"), "iox": (32, "float32"),
+    "rst": (16 * max(N_CH), "bfloat16"), "rst8": (16 * max(P_CH), "bfloat16"), "idb": (128, "bfloat16"), "lt": (960, "bfloat16"),
     "scw": (144, "bfloat16"), "pos": (336, "bfloat16"), "mkn": (96, "float32"), "rs17": (102, "bfloat16"), "inc": (102, "float32"),
-    "idb": (128, "bfloat16"), "idh": (144, "float16"), "bof": (128, "float32"), "onb": (128, "bfloat16"), "on2": (96, "bfloat16"),
-    "wts": (640, "bfloat16"), "msk": (96, "float32"), "pns": (48, "float32"), "hrow": (128, "bfloat16"), "crow": (128, "bfloat16"),
-    "padf": (18, "float32"), "padh": (18, "float32"), "curh": (126, "float32"), "sumr": (42, "float32"),
-    "lt": (960, "bfloat16"), "hi": (96, "float32"), "lo": (96, "float32"), "su": (96, "int32"), "uint": (24, "int32"),
-    "kb": (4, "bfloat16"), "kd": (8, "float32"), "nl": (4, "uint16"), "bkl": (48, "uint16"), "tf": (768, "float32"),
-    "hitb": (4, "bfloat16"), "pr": (126, "float32"), "osm": (132, "int32"), "sk": (204, "float32"),
-    "fl": (6, "uint16"), "fo": (6, "uint16"), "fn": (384, "float16"), "ns": (192, "float32"),
-    "eqb": (1536, "bfloat16"), "cn": (768, "bfloat16"), "xo": (12, "float32"),
-    "offs": (12 * VI, "uint16"), "pl": (12 * VI, "uint16"), "zp": (192, "bfloat16"), "sp": (192, "float32"),
-    "q1": (126, "float32"), "x1": (126, "float32"), "sf": (188, "float32"),
-    "fa": (128, "float32"), "fb": (128, "float32"), "home": (126, "float32"), "homek": (64, "float32"),
+    "idh": (144, "float16"), "onb": (128, "bfloat16"), "on2": (96, "bfloat16"),
+    "wts": (640, "bfloat16"), "msk": (48, "float32"), "pns": (48, "float32"), "hrow": (128, "bfloat16"), "crow": (128, "bfloat16"),
+    "padh": (12, "float32"), "curh": (192, "float32"),
+    "hi": (96, "float32"), "lo": (96, "float32"), "su": (84, "int32"), "osm": (SW, "int32"), "ki": (SW, "int32"), "uint": (24, "int32"),
+    "kb": (8, "bfloat16"), "kd": (12, "float32"), "nl": (4, "uint16"), "bkl": (48, "uint16"), "tf": (768, "float32"), "zw": (768, "bfloat16"),
+    "hitb": (4, "bfloat16"), "om": (6, "int32"), "sk": (204, "float32"),
+    "fl": (6, "uint16"), "of0": (6, "uint16"),
+    "eqb": (1536, "bfloat16"), "cn": (768, "bfloat16"),
+    "offs": (12 * VI, "uint16"), "pl": (12, "uint16"), "zp": (192, "bfloat16"), "zq": (96, "bfloat16"), "sp": (192, "float32"),
+    "q1": (120, "float32"), "mk0": (20, "float32"), "x1": (120, "float32"), "sf": (188, "float32"), "fg": (128, "float32"),
+    "fa": (128, "float32"), "fb": (128, "float32"), "home": (120, "float32"), "homek": (64, "float32"),
+    "pw": (64, "float32"), "pk": (8, "int32"), "prm": (8, "uint16"),
     "ra": (256, "float32"), "ri": (256, "int32"), "rb": (256, "float32"),
 }
-SCRATCH = {"zc": ("sbuf", [128, 6, 136], "bfloat16")}
+_sb3 = {
+    "zc": (6, 136, "bfloat16"), "fn": (6, 96, "float16"), "ns": (2, 96, "float32"),
+    "fo": (2, 4, "uint16"), "xo": (2, 6, "float32"), "padf": (2, 6, "float32"),
+}
+SCRATCH = {}
 for _k in _sb:
     SCRATCH[_k] = ("sbuf", [128, _sb[_k][0]], _sb[_k][1])
+for _k in _sb3:
+    SCRATCH[_k] = ("sbuf", [128, _sb3[_k][0], _sb3[_k][1]], _sb3[_k][2])
 for _t in range(VI):
     SCRATCH["so%d" % _t] = ("sbuf", [128, SW], "float32")
 for _t in range(1, VI):
     SCRATCH["st%d" % _t] = ("sbuf", [128, SW], "float32")
 for _t in range(8):
     SCRATCH["ps%d" % _t] = ("psum", [128, 16, 32] if _t in (3, 7) else [128, 512], "float32")
-SEMAPHORES = (["sv", "ss", "sp_", "sg_", "lsg", "ltr", "lbk", "lbw", "lkm", "lwt", "dout", "lsem", "dra", "drb", "a_home", "a_homek"]
+SEMAPHORES = (["sv", "ss", "sp_", "sg_", "lsg", "ltr", "lbk", "lbw", "lbx", "lkm", "lwt", "dout", "lsem", "dra", "drb", "a_home", "a_homek"]
               + ["a_%s%d" % (_k, _t) for _k in ("st", "kl") for _t in range(1, VI)] + ["a_kz%d" % _t for _t in range(1, 4)])
 
 
@@ -139,8 +146,11 @@ def rank_program(g, core, T, topo):
     def mm(out, lhsT, rhs, r, w, start=True, stop=True):
         E("p", lambda e: e.matmul(out, lhsT, rhs, start, stop), r, w)
 
-    def iota(out, pattern, base, cm, w):
-        E("g", lambda e: e.iota(out, pattern, base, cm, allow_small_or_imprecise_dtypes=True), [], w)
+    def iota(out, pattern, base, cm, w, r=()):
+        E("g", lambda e: e.iota(out, pattern, base, cm, allow_small_or_imprecise_dtypes=True), r, w)
+
+    def gcp(out, a, n, r, w):
+        E("g", lambda e: e.affine_select(out, a, [[0, n]], A.is_ge, 0.0, 0, 0), r, w)
 
     def send(src_ap, keys, land, out_ap, step=1):
         dst, frm = cores[(rank + step) % 4], cores[(rank - step) % 4]
@@ -158,70 +168,74 @@ def rank_program(g, core, T, topo):
     dma("y", T.booki[:, 0:1024], T.book[:, :], "lbk", [], ["bookA"])
     dma("y", T.kmi[:, 60:61], T.wt[:, :], "lwt", [], ["wti"])
     dma("y", T.booki[:, 1024:2048], T.book[:, :], "lbw", ["bookA"], ["bookB"])
+    dma("y", T.booki[:, 2048:4096], T.booki[:, 0:2048], "lbx", ["bookA", "bookB"], ["bookC"])
 
     iota(T.pi[:, :], [[0, 1]], 0, 1, ["pi"])
     iota(T.iof[:, :], [[1, 160]], 0, 0, ["iof"])
-    iota(T.iog[:, :], [[1, 8], [0, 16]], 0, 0, ["iog"])
-    iota(T.ioj[:, :], [[0, 8], [1, 16]], 0, 0, ["ioj"])
+    iota(T.ioj[:, :], [[0, 3], [1, 16]], 0, 0, ["ioj"])
     iota(T.ion[:, :], [[0, 3], [1, 16], [0, 2]], 0, 0, ["ion"])
-    iota(T.padh[:, 0:12], [[16, 2], [-32, 2], [64, 3]], 2048 + 32, 0, ["padh"])
-    iota(T.padh[:, 12:18], [[16, 2], [64, 3]], 2048, 0, ["padh"])
-    for jb in range(3):
-        iota(T.curh[:, jb:126:3], [[16, 2], [0, 21]], 2048 + 64 * COL[jb], 0, ["curh"])
     iota(T.hrow[0:1, :], [[0, 4], [1, 32]], -10, 0, ["hrow"])
     C = T.colf
     ms(T.Z[:, 4096:PADC], 0.0, ["Zpad"])
     act(T.S[:, 4096:PADC], T.Z[:, 4096:PADC], ["Zpad"], ["Spad"], func=AF.Silu)
+    ms(T.crow[0:1, :], -272.0, ["crow"])
+    ms(T.on2[0:1, :], 2.0 ** 20, ["on2"])
+    cp(C[:, 0:1], T.pi[:, :], ["pi"], ["c0"])
     ts(T.pj[:, :], T.pi[:, :], 15, A.bitwise_and, ["pi"], ["pj"])
     ts(T.pg[:, :], T.pi[:, :], 4, A.arith_shift_right, ["pi"], ["pg"])
-    ts(T.uint[:, 0:1], T.pi[:, :], 7, A.bitwise_and, ["pi"], ["uI"])
-    cp(C[:, 0:1], T.pi[:, :], ["pi"], ["c0"])
-    ms(T.scw[:, :], 0.0, ["scw"])
+    ts(T.uint[:, 0:1], T.pi[:, :], 8, A.bitwise_and, ["pi"], ["uI"])
+    ts(T.uint[:, 1:2], T.pi[:, :], 14, A.bitwise_and, ["pi"], ["uJ"])
+    ts(C[:, 10:11], T.pi[:, :], 1008.0, A.add, ["pi"], ["c10"])
     ms(T.wts[:, :], 0.0, ["wts"])
+    ts(T.idh[:, :], T.iof[:, 0:144], C[:, 0:1], A.is_equal, ["iof", "c0"], ["idh"])
     cp(C[:, 1:2], T.pj[:, :], ["pj"], ["c1"])
     cp(C[:, 2:3], T.pg[:, :], ["pg"], ["c2"])
-    cp(C[:, 10:11], T.uint[:, 0:1], ["uI"], ["c10"])
-    ms(T.crow[0:1, :], -272.0, ["crow"])
-    ms(T.rs17[:, :], -2.0 ** 23, ["rs17"])
-    ms(T.inc[:, :], 1.0, ["inc"])
-    ts(T.uint[:, 1:2], T.pi[:, :], 14, A.bitwise_and, ["pi"], ["uJ"])
-    ms(T.onb[:, :], 1.0, ["onb"])
-    ms(T.on2[0:1, :], 2.0 ** 20, ["on2"])
-    ts(T.idh[:, :], T.iof[:, 0:144], C[:, 0:1], A.is_equal, ["iof", "c0"], ["idh"])
-    ms(T.fn[:, :], BIG, ["fnM", "fnN", "fnF1", "fnF2", "fnG1", "fnG2"])
-    ms(T.crow[0:1, 0:128:32], 64.0, ["crow"], ["crow"])
-    ms(T.rs17[:, 0:102:17], 2.0 ** 23, ["rs17"], ["rs17"])
-    ms(T.inc[:, 0:102:17], 2.0 ** 23, ["inc"], ["inc"])
+    ts(C[:, 11:12], T.uint[:, 0:1], 125.0, A.mult, ["uI", "c10"], ["c11"], C[:, 0:1], A.add)
+    ts(C[:, 12:13], T.uint[:, 0:1], -125.0, A.mult, ["uI", "c10"], ["c12"], C[:, 10:11], A.add)
     ts(C[:, 3:4], T.uint[:, 1:2], 8.0, A.mult, ["uJ"], ["c3"], 15.0, A.add)
-    ts(C[:, 11:12], C[:, 1:2], 7.5, A.is_lt, ["c1"], ["c11"])
-    ts(C[:, 12:13], C[:, 1:2], 7.5, A.is_gt, ["c1"], ["c11"])
-    ts(T.bof[:, :], T.iog[:, :], C[:, 2:3], A.is_equal, ["iog", "c2"], ["bof"])
-    for h in range(2):
-        ts(T["f" + "ab"[h]][:, :], T.ioj[:, :], -8.0 * h, A.add, ["ioj", "c10"], ["f" + "ab"[h]], C[:, 10:11], A.is_equal)
+    ms(T.crow[0:1, 0:128:32], 64.0, ["crow"], ["crow"])
+    W = [T.pw[:, 8 * i:8 * i + 8] for i in range(8)]
+    ts(W[0], T.iof[:, 0:128:16], C[:, 1:2], A.add, ["iof", "c1"], ["w0"], 119.0, A.min)
+    ts(T.idb[:, :], T.iof[:, 0:128], C[:, 0:1], A.is_equal, ["iof", "c0"], ["idb"])
+    ts(T.hsel[:, 0:144], T.iof[:, 0:144], -8.0, A.add, ["iof", "c11"], ["hsel"], C[:, 11:12], A.is_equal)
+    ts(W[1], W[0], 59.5, A.is_gt, ["w0"], ["w1"], -60.0, A.mult)
+    ts(T.hsel[:, 144:288], T.iof[:, 0:144], C[:, 12:13], A.is_equal, ["iof", "c12"], ["hsel"])
     ts(C[:, 4:5], C[:, 1:2], 0.5, A.add, ["c1"], ["c4"])
-    ms(T.sumr[:, :], 1.0, ["sumr"])
-    ms(T.so0[:, 129:141], 0.0, ["of2"])
-    for h in range(2):
-        tt(T["f" + "ab"[h]][:, :], T["f" + "ab"[h]][:, :], T.bof[:, :], A.mult, ["f" + "ab"[h], "bof"], ["f" + "ab"[h]])
-    cp(T.kz[:, 0:3], T.kmi[:, 0:3], ["kmi"], ["kz0"])
+    ts(C[:, 5:6], C[:, 1:2], 0.5, A.mult, ["c1"], ["c5"], 0.25, A.add)
+    tt(W[4], W[0], W[1], A.add, ["w0", "w1"], ["w4"])
+    ts(T.mkn[:, :], T.ion[:, :], C[:, 1:2], A.is_gt, ["ion", "c1"], ["mkn"], BIG, A.mult)
+    ts(T.msk[:, :], T.ioj[:, :], C[:, 1:2], A.is_gt, ["ioj", "c1"], ["msk"], BIG, A.mult)
+    ts(T.pns[:, :], T.ioj[:, :], C[:, 4:5], A.subtract, ["ioj", "c4"], ["pns"], -4 * BIG, A.mult)
+    ts(T.pk[:, :], W[4], -1.0, A.add, ["w4"], ["pk"], 1.0 / 3.0, A.mult)
     ts(T.sgh[:, :], T.sgi[:, :], -OFF, A.add, ["sgi"], ["sgh"])
-    for h in range(2):
-        for o in range(2):
-            c = 256 * o + 128 * h
-            act(T.hsel[:, c:c + 128], T["f" + "ab"[h]][:, :], ["f" + "ab"[h], "c11"], ["hsel"], scale=C[:, 11 + o:12 + o])
+    cp(T.kz[:, 0:3], T.kmi[:, 0:3], ["kmi"], ["kz0"])
+    ts(W[1], T.pk[:, :], -3.0, A.mult, ["pk"], ["w1"])
     act(T.sgl[:, :], T.sgi[:, :], ["sgi"], ["sgl"])
-    iota(T.rst8[:, :], [[0, max(P_CH) * 2], [-512, 8]], 512, 0, ["rst8"])
     iota(T.rst[:, :], [[0, max(N_CH)], [-512, 16]], 512, 0, ["rst"])
+    iota(T.rst8[:, :], [[0, max(P_CH) * 2], [-512, 8]], 512, 0, ["rst8"])
     for step in (1, 2, 3):
         send(T.kz[:, 0:3], ["kz0"], "kz%d" % step, T.kz[:, 8 * step:8 * step + 3], step)
-    iota(T.io2[:, :], [[0, 2], [1, 21]], 128, 0, ["io2"])
-    iota(T.pos[0:1, 0:68], [[-256, 2], [128, 2], [0, 17]], 256, 0, ["pos"])
-    iota(T.pos[0:1, 68:102], [[128, 2], [0, 17]], 512, 0, ["pos"])
+    for (ap, c, key) in ((T.onb[:, :], 1, "onb"), (T.rs17[:, :], -2 ** 23, "rs17"), (T.inc[:, :], 1, "inc"), (T.scw[:, :], 0, "scw"),
+                         (T.kw[:, :], 0, "kw"), (T.nw[:, :], 0, "nw"), (T.zc[:, :, 128], 0, "zc0"),
+                         (T.ns[:, :, 63:96:16], int(BIG), "nsO")):
+        n = 1
+        for d in ap.shape[1:]:
+            n *= d
+        iota(ap, [[0, n]], c, 0, [key])
+    iota(T.pos[0:1, 0:102], [[128, 6], [0, 17]], 0, 0, ["pos"])
     iota(T.pos[0:1, 102:204], [[0, 6], [1, 17]], 0, 0, ["pos"])
     iota(T.pos[0:1, 204:332], [[0, 8], [16, 8], [0, 2]], 0, 0, ["pos"])
+    iota(T.rs17[:, 0:102:17], [[0, 6]], 2 ** 23, 0, ["rs17"], ["rs17"])
+    iota(T.inc[:, 0:102:17], [[0, 6]], 2 ** 23, 0, ["inc"], ["inc"])
+    iota(T.pos[0:1, 118:204:17], [[0, 6]], 3 * 2 ** 22, 0, ["pos"], ["pos"])
+    iota(T.padh[:, :], [[16, 2], [32, 2], [64, 3]], 2048, 0, ["padh"])
+    for a in range(2):
+        iota(T.curh[:, 96 * a:96 * a + 96], [[32, 3], [16384, 32]], 1024 + 8 * a, 0, ["curh"])
+    iota(T.io2[:, :], [[0, 2], [1, 20]], 128, 0, ["io2"])
+    iota(T.iox[:, :], [[-1, 32]], 148, 0, ["iox"])
     iota(T.iot[:, :], [[1, PADC]], -int(OFF), 0, ["iot"])
 
-    S_BANK = (0, 3, 7, 4, 5, 2, 1, 6)
+    S_BANK = (6, 2, 5, 1, 7, 3, 1, 1)
 
     def s_at(r):
         b, h = S_BANK[r // 2], r % 2
@@ -234,19 +248,13 @@ def rank_program(g, core, T, topo):
         else:
             act(T.S[:, r:4096:16], src, [key], ["Sb"], bias=OFF + SO)
 
-    for r in range(16):
-        mm(s_at(r)[0], T.idh[:, r:r + 128], T.sgh[:, :], ["idh", "sgh"], [s_at(r)[1]])
-    for r in range(4):
-        s_lay(r, "s")
-    ts(T.mkn[:, :], T.ion[:, :], C[:, 1:2], A.is_gt, ["ion", "c1"], ["mkn"], BIG, A.mult)
-    ts(T.pns[:, :], T.ioj[:, 0:48], C[:, 4:5], A.subtract, ["ioj", "c4"], ["pns"], -4 * BIG, A.mult)
-    ts(T.msk[:, :], T.ioj[:, 0:96], C[:, 1:2], A.is_gt, ["ioj", "c1"], ["msk"], BIG, A.mult)
-    ts(T.idb[:, :], T.iof[:, 0:128], C[:, 0:1], A.is_equal, ["iof", "c0"], ["idb"])
+    def s_turn(rows):
+        for r in rows:
+            mm(s_at(r)[0], T.idh[:, r:r + 128], T.sgh[:, :], ["idh", "sgh"], [s_at(r)[1]])
+
+    s_turn(range(8))
     cp(T.kl[:, 0:57], T.kmi[:, 3:60], ["kmi"], ["kl0"])
-    cp(T.kc[:, 0:57], T.kmi[:, 3:60], ["kmi"], ["kc"])
     cp(T.homek[:, 1:4], T.kmi[:, 0:3], ["kmi"], ["homez"])
-    for s in range(2):
-        ts(T.scw[:, 14 + s:142:16], T.iof[:, 0:8], C[:, 2:3], A.is_equal, ["iof", "c2"], ["scw"], 2048.0 * s - 1024.0, A.mult)
 
     def weights(i, v, keys):
         for h in range(2):
@@ -254,19 +262,31 @@ def rank_program(g, core, T, topo):
             ts(T.wts[:, c + 31:c + 159:32], T.iof[:, h:8:2], C[:, 2:3], A.is_equal, ["iof", "c2"] + keys, ["wts"], v, A.mult)
 
     weights(1, 2.0 ** 25, [])
-    for i in range(3):
-        ts(T.inc[:, 34 * COL[i] + 16:34 * COL[i] + 34:17], T.iof[:, 2 * i:2 * i + 2], -128.0, A.mult, ["iof", "c3"], ["inc"], C[:, 3:4], A.subtract)
-    ms(T.sumr[:, 0:42:21], 0.0, ["sumr"], ["sumr"])
-    ts(T.padf[:, :], T.padh[:, :], C[:, 1:2], A.add, ["padh", "c1"], ["padu"], 2.0, A.mult)
-    ts(T.so0[:, 0:126], T.curh[:, :], C[:, 4:5], A.add, ["curh", "c4"], ["cur"], 2.0, A.mult)
-    ts(T.hrow[0:1, :], T.hrow[0:1, :], 10.0, A.min, ["hrow"], ["hrow"])
-    for r in range(4, 10):
-        s_lay(r, "v")
+    tt(T.rep[:, :], T.pw[:, 8:12], T.pw[:, 32:36], A.add, ["w1", "w4"], ["rep"])
+
+    def late(i):
+        if i == 0:
+            for s in range(2):
+                ts(T.scw[:, 14 + s:142:16], T.iof[:, 0:8], C[:, 2:3], A.is_equal, ["iof", "c2"], ["scw"], 2048.0 * s - 1024.0, A.mult)
+            ts(T.inc[:, 16:102:17], T.iof[:, 0:6], -128.0, A.mult, ["iof", "c3"], ["inc"], C[:, 3:4], A.subtract)
+            ts(T.padf[:, :, :], T.padh[:, :], C[:, 1:2], A.add, ["padh", "c1"], ["padu"], 2.0, A.mult)
+            ts(T.so0[:, :], T.curh[:, 0:SW], C[:, 5:6], A.add, ["curh", "c5"], ["cur"], 4.0, A.mult)
+        elif i == 1:
+            ts(W[2], W[0], 59.5, A.is_gt, ["w0"], ["w2"], -1824.0, A.mult)
+            ts(W[3], W[0], 32.0, A.mult, ["w0"], ["w3"])
+            ts(W[6], T.pk[:, :], -97.0, A.mult, ["pk"], ["w6"])
+        elif i == 2:
+            ts(W[7], T.pk[:, :], 0.5, A.is_gt, ["pk"], ["w7"], 20.0, A.mult)
+            tt(W[5], W[2], W[3], A.add, ["w2", "w3"], ["w5"])
+        elif i == 3:
+            tt(W[1], W[6], W[7], A.add, ["w6", "w7"], ["w1"])
+        else:
+            tt(T.prm[:, :], W[1], W[5], A.add, ["w1", "w5"], ["perm"])
 
     Zk = ["ZA", "ZB", "Zpad"]
     Zall = T.Z[:, :]
     Sk = ["Sa", "Sb", "Spad"]
-    bwin = T.booki[:, :]
+    bwin = T.booki[:, 0:2048]
     twin = T.tf[:, :]
     BLOCKS = [(0, 24, 4), (24, B1, 4), (B1, PH, 5)]
 
@@ -274,7 +294,7 @@ def rank_program(g, core, T, topo):
         return 4 if t > 0 else 2
 
     def book_at(t, a, b):
-        return T.booki[:, 0:1024 if t == 0 else 2048].indirect(T.kl[:, 72 * t + a:72 * t + b]), ["bookA", "kl%d" % t] + (["bookB"] if t > 0 else [])
+        return T.booki[:, 0:1024 if t == 0 else 4096].indirect(T.kl[:, 72 * t + a:72 * t + b]), ["bookA", "kl%d" % t] + (["bookB", "bookC"] if t > 0 else [])
 
     def terms(t, i):
         a, b, bank = BLOCKS[i]
@@ -285,7 +305,7 @@ def rank_program(g, core, T, topo):
         act(T.thi[:, 2 * a:2 * b], src, keys, ["thi%d" % i], bias=-OFF)
         for o in range(2):
             for h in range(2):
-                c = 256 * o + 128 * h
+                c = 144 * o + 8 - 8 * (h - o)
                 mm(T["ps%d" % bank][:, o * (b - a):(o + 1) * (b - a)], T.hsel[:, c:c + 128], T.thi[:, 2 * a + h:2 * b:2], ["hsel", "thi%d" % i], ["B%d" % bank], h == 0, h == 1)
 
     def turned(i):
@@ -302,21 +322,26 @@ def rank_program(g, core, T, topo):
         act(T.nat[:, 0:NN + 16 * (KN % 2)], src, keys, ["nat"])
 
     def sread(v):
-        m = 3 * names_of(v)
-        act(T.sp[:, 0:16 * m], T.S[:, :].indirect(T.pl[:, 12 * v:12 * v + m]), Sk + ["pl%d" % v], ["sp"])
+        for a in range(2):
+            act(T.sp[:, 96 * a:96 * a + 96], T.S[:, :].indirect(T.offs[:, 12 * v + 6 - 6 * a:12 * v + 12 - 6 * a]), Sk + ["offs%d" % v], ["sp"])
 
     def swrite(v, q):
-        m = 3 * names_of(v)
-        dst = T.S[:, :].indirect(T.offs[:, 12 * v:12 * v + m])
+        dst = T.S[:, :].indirect(T.offs[:, 12 * v:12 * v + 12])
         if q == "v":
-            cp(dst, T.sp[:, 0:16 * m], ["offs%d" % v, "sp"] + Sk, Sk)
+            cp(dst, T.sp[:, :], ["offs%d" % v, "sp"] + Sk, Sk)
         else:
-            act(dst, T.sp[:, 0:16 * m], ["offs%d" % v, "sp"] + Sk, Sk, func=AF.Silu)
+            act(dst, T.sp[:, :], ["offs%d" % v, "sp"] + Sk, Sk, func=AF.Silu)
 
     def yslot(k, n=1):
         if k < NP:
             return T.ysc[:, 384 * k + 7:384 * (k + n):8]
         return T.ysc[:, YN + 768 * (k - NP) + 15:YN + 768 * (k - NP + n):16]
+
+    def taken(t, a):
+        st = T["st%d" % t]
+        for jb in range(3):
+            c, e = 128 + 96 * a + 32 * jb, 32 * jb + 20
+            ts(T.ps2[:, c:c + 32], T.iox[:, :], st[:, e:e + 1], A.is_equal, ["iox", "st%d" % t], ["X"], st[:, e + 1 + a:e + 2 + a], A.mult)
 
     def answers(t, filler, head):
         pits, nits = [], []
@@ -348,6 +373,10 @@ def rank_program(g, core, T, topo):
                     rows(7, 0, x, yslot(k), key, k == 19)
             done[2 + cls] = max(done[2 + cls], upto)
 
+        def spread(y0, key):
+            for k in range(4):
+                mm(T.ps0[:, 48 * k:48 * k + 48], T.idb[:, :], y0, ["idb", key], ["B0"])
+
         def ngather(i):
             c, n = nits[i]
             act(T.G[:, YN + 16 * c:YN + 16 * (c + n)], Zall.indirect(T.nat[:, 16 * (KN % 2) + c:16 * (KN % 2) + c + n]), Zk + ["nat"], ["J%d" % i])
@@ -371,26 +400,37 @@ def rank_program(g, core, T, topo):
             c, n = pits[i]
             scan(T.ysc[:, 16 * c:16 * (c + n)], T.rst8[:, 0:16 * n], T.H[:, 16 * c:16 * (c + n)], A.max, A.min, ["rst8", "H%d" % i], ["YP%d" % i])
             if i == 0:
-                for k in range(4):
-                    mm(T.ps0[:, 48 * k:48 * k + 48], T.idb[:, :], yslot(0), ["idb", "YP0"], ["B0"])
+                spread(yslot(0), "YP0")
             weigh(0, (c + n) // 24 - 1, "YP%d" % i)
 
-        filler()
-        for i in range(OWN):
-            pgather(i, cp)
+        if t == 0:
+            cp(T.nz[:, :], T.booki[:, 0:1024].indirect(T.kz[:, 0:3]), ["bookA", "kz0"], ["nz"])
+            filler()
+            cp(T.eqb[:, 0:768], Zall.indirect(T.nz[:, :]), Zk + ["nz"], ["e0", "e1"])
+            pgather(1, cp)
+        else:
+            filler()
+            for i in range(OWN):
+                pgather(i, cp)
         first = OWN
         while pits[first][0] < B1:
             pgather(first)
             first += 1
         head()
-        ngather(0)
+        if t == 0:
+            ngather(0)
         for i in range(first, np_):
             pgather(i)
-        for i in range(1, len(nits)):
+        for i in range(t == 0, len(nits)):
             ngather(i)
-        pfold(0)
-        pfold(1)
-        pscan(0)
+        if t:
+            pfold(0)
+            pfold(1)
+            pscan(0)
+        else:
+            scan(T.eqb[:, 768:1536], T.rst[:, 0:768], T.eqb[:, 0:768], A.max, A.min, ["rst", "e0", "e1"], ["e2"])
+            spread(T.eqb[:, 783:1536:16], "e2")
+            pfold(1)
         for i in range(2, np_):
             pfold(i)
             sums(0, sum(pits[i - 2]) // 24 - 1, "YP%d" % (i - 2))
@@ -404,216 +444,242 @@ def rank_program(g, core, T, topo):
             elif i != len(nits) - 2:
                 j = min(i - 1, len(nits) - 3)
                 sums(1, NP - 1 + sum(nits[j]) // 48, "YN%d" % j)
+        if t:
+            taken(t, 0)
         sums(1, 19, "YN%d" % (len(nits) - 1))
 
     def head():
-        turned(2)
         mm(T.ps7[:, 0:3, :], T.hrow[0:1, :], T.on2[0:1, :], ["on2", "hrow"], ["B7"], True, False)
         mm(T.ps3[:, 0:3, :], T.crow[0:1, :], T.on2[0:1, :], ["on2", "crow"], ["B3"], True, False)
 
     act(T.Z[:, 0:16 * ZS], T.truv[:, :].indirect(T.sgl[:, 0:ZS]), ["truv", "sgl"], ["ZA"])
     cp(T.Z[:, 16 * ZS:4096], T.truv[:, :].indirect(T.sgl[:, ZS:256]), ["truv", "sgl"], ["ZB"])
-    BLOCKS[1] = (24, B1, 0)
-    for i in range(3):
-        terms(0, i)
-    turned(0)
+    BLOCKS[2] = (B1, PH, 4)
+    terms(0, 1)
+    wholes(0)
     turned(1)
-    BLOCKS[1] = (24, B1, 4)
-    cp(C[:, 9:10], T.kmi[:, 60:61], ["wti"], ["c9"])
+    terms(0, 2)
+
+    def first_filler():
+        cp(C[:, 9:10], T.kmi[:, 60:61], ["wti"], ["c9"])
 
     def first_head():
-        wholes(0)
+        weights(0, C[:, 9:10], ["c9"])
+        turned(2)
         head()
 
-    answers(0, lambda: weights(0, C[:, 9:10], ["c9"]), first_head)
+    answers(0, first_filler, first_head)
+    BLOCKS[2] = (B1, PH, 5)
 
     for t in range(VI):
         st, stk = T["st%d" % max(t, 1)], "st%d" % t
         so = T["so%d" % t]
         last = t == VI - 1
-        cur = so[:, 0:126] if not last else T.ki[:, 0:126]
+        cur = so if not last else T.ki
         old = t > 0
         M = names_of(t)
         o = 12 * t
         if not old:
-            for r in (14, 15, 10, 11):
+            for r in range(4):
                 s_lay(r, "s")
         if not last:
             terms(t + 1, 0)
-        if last:
-            act(T.rb[:, :], T.ri[:, :], ["ri"], ["rb"], bias=-SO)
-            dma("y", T.S[0:128:16, 0:4096], T.rb[:, :], "drb", ["rb"], Sk)
-        elif old:
+        if t == 1:
+            for r in (14, 15):
+                s_lay(r, "s")
+        if old:
             sread(t - 1)
             swrite(t - 1, "s")
         if not old:
-            ms(T.pos[0:1, 118:204:17], 1.5 * 2.0 ** 23, ["pos"], ["pos"])
-            ms(T.zc[:, :, 128], 0.0, ["zcV"])
+            late(0)
+            for r in (4, 5):
+                s_lay(r, "s")
         if not last:
             turned(0)
-        if t == VI - 2:
+        if last:
             dma("y", T.ra[:, :], T.S[0:128:16, 0:4096], "dra", Sk, ["ra"])
         for i in range(2):
             mm(T.ps6[:, 0:102], T.onb[0:1, :], T.pos[0:1, 102 * i:102 * i + 102], ["onb", "pos"], ["B6"], i == 0, False)
         mm(T.ps6[:, 0:102], T.pos[0:1, 204:332], T.onb[0:1, 0:102], ["onb", "pos"], ["B6"], False, False)
         if old:
-            cp(T.kc[:, 60:117], T.kl[:, 72 * t:72 * t + 57], ["kl%d" % t], ["kraw"])
-            for a in range(2):
-                for jb in range(3):
-                    e = 129 + COL[jb] + (6 * a + 3 if t > 1 else 3 * a)
-                    ts(T.ps1[:, 64 + 63 * a + jb:127 + 63 * a:3], T.iof[:, 128:149], st[:, 126 + jb:127 + jb], A.is_equal, ["iof", stk], ["B1"], st[:, e:e + 1], A.mult)
-            ts(T.kc[:, 0:57], T.kc[:, 60:117], 1023, A.bitwise_and, ["kraw"], ["kc"])
+            taken(t, 1)
+        kl = T.kl[:, 72 * t:72 * t + 57]
+        ts(T.kc[:, 64:121], kl, 2047.5, A.is_lt, ["kl%d" % t], ["kraw"], 2048.0, A.mult)
         flip(T.hi[:, :], T.ps7[:, 0:3, :], ["B7"], ["hi"])
-        flip(T.lo[:, :], T.ps3[:, 0:3, :], ["B3"], ["lo"])
         if old:
-            tt(cur, st[:, 0:126], T.ps1[:, 64:190], A.max, [stk, "B1"], ["cur"])
-        else:
-            s_lay(12, "v")
-        scan(T.su[:, :], T.lo[:, :], T.hi[:, :], A.max, A.min, ["lo", "hi"], ["su"])
+            tt(cur[:, :], st[:, :], T.ps2[:, 128:128 + SW], A.max, [stk, "X"], ["cur"])
+        flip(T.lo[:, :], T.ps3[:, 0:3, :], ["B3"], ["lo"])
+        tt(T.k2[:, :], kl, T.kc[:, 64:121], A.add, ["kl%d" % t, "kraw"], ["k2"])
         if not old:
-            s_lay(13, "v")
+            s_turn(range(8, 12))
+            s_lay(6, "v")
         if last:
-            ts(T.ki[:, 126:252], cur, 8191, A.bitwise_and, ["cur"], ["kand"])
-        x = T.su[:, 31:96:32]
+            ts(T.kj[:, :], T.ki[:, :], 8191, A.bitwise_and, ["cur"], ["kand"])
+        scan(T.su[:, :], T.lo[:, 0:84], T.hi[:, 0:84], A.max, A.min, ["lo", "hi"], ["su"])
+        if old:
+            for a in range(2):
+                scan(T.osm[:, 96 * a:96 * a + 84], T.lo[:, 0:84], cur[:, 96 * a:96 * a + 84], A.max, A.min, ["lo", "cur"], ["osm"])
+        else:
+            s_lay(7, "v")
+            s_turn((12, 13))
+            s_lay(12, "s")
+        x = T.su[:, 19:84:32]
         uU, uQ, uA, uF, uB = [T.uint[:, 4 * i:4 * i + 3] for i in range(5)]
-
-        def olds(step, blocks=()):
-            if not old:
-                return
-            if step == 0:
-                for jb in blocks:
-                    ts(T.ps2[:, 128 + jb:254:3], T.io2[:, :], T.kb[:, jb:jb + 1], A.is_equal, ["io2", "kb"], ["xe"])
-            elif step == 1:
-                tt(T.pr[:, :], cur, T.ps2[:, 128:254], A.mult, ["cur", "xe"], ["pr"])
-            elif step == 2:
-                for jb in range(3):
-                    scan(T.osm[:, 42 * COL[jb]:42 * COL[jb] + 42], T.sumr[:, :], T.pr[:, jb:126:3], A.mult, A.add, ["sumr", "pr"], ["osm"])
-            elif step == 3:
-                ts(T.osm[:, 126:132], T.osm[:, 20:126:21], 8191, A.bitwise_and, ["osm"], ["om"])
-            elif step == 4:
-                ts(T.fo[:, :], T.osm[:, 126:132], -1.0, A.add, ["om"], ["fo"])
-                for m in range(2):
-                    ts(T.ns[:, 96 * m + 15:96 * m + 48:16], T.osm[:, 126 + m:132:2], -OFF - 1.0, A.add, ["om"], ["nsO"])
-            else:
-                tt(T.fn[:, 65:256:2], T.iot[:, :].indirect(T.fo[:, 0:6]), T.msk[:, :], A.add, ["iot", "fo", "msk"], ["fnN"])
-
+        ks = so[:, 20:96:32]
+        ksj = [so[:, 32 * jb + 20:32 * jb + 21] for jb in range(3)]
         ts(uU, x, 4095, A.bitwise_and, ["su"], ["uU"])
         ts(T.kb[:, 0:3], x, -2.0 ** -20, A.mult, ["su"], ["kb"], 138.49609375, A.add)
-        ts(uA, uU, 37.0, A.mult, ["uU"] + (["B0"] if old else []), ["uA"], T.ps0[:, 400:401] if old else 0.0, A.add)
+        if old:
+            ts(T.om[:, :], T.osm[:, 19:SW:32], 8191, A.bitwise_and, ["osm"], ["om"])
         tt(uQ, uU, uU, A.mult, ["uU"], ["uQ"])
-        ts(T.kd[:, 0:3], T.kb[:, 0:3], 148.0, A.is_equal, ["kb"], ["kd"], float(t + 1 - 20), A.mult)
-        olds(0, (0, 1))
-        ts(uB, uA, 1023, A.bitwise_and, ["uA"], ["uB"])
+        ts(uA, uU, 37.0, A.mult, ["uU"] + (["B0"] if old else []), ["uA"], T.ps0[:, 400:401] if old else 0.0, A.add)
+        ts(T.kb[:, 4:7], T.kb[:, 0:3], 148.0, A.is_equal, ["kb"], ["kd"], float(t + 1 - 20), A.mult)
+        if old:
+            ts(T.fo[:, :, 0:3], T.om[:, :], -1.0, A.add, ["om"], ["fo"])
         ts(uF, uQ, 5, A.arith_shift_right, ["uQ"], ["uF"], 1023, A.bitwise_and)
-        tt(so[:, 126:129], T.kb[:, 0:3], T.kd[:, 0:3], A.add, ["kb", "kd"], ["ks"])
-        olds(0, (2,))
+        ts(uB, uA, 1023, A.bitwise_and, ["uA"], ["uB"])
+        for jb in range(3):
+            ts(T.ps2[:, jb:57:3], T.iof[:, 129:148], T.kb[:, 4 + jb:5 + jb], A.subtract, ["iof", "kb", "kd"], ["xk"] + ([] if old else ["B2"]), T.kb[:, jb:jb + 1], A.not_equal)
+        for a in range(2 * old):
+            for i in (1, 2):
+                act(T.fn[:, 2 * i + 1, 32 * i + a:96:2], T.iot[:, :].indirect(T.fo[:, a, 0:3 - i]), ["iot", "fo"], ["fnG"])
+            if not last:
+                act(T.zp[:, 144 - 96 * a:192 - 96 * a], Zall.indirect(T.fo[:, a, 0:3]), Zk + ["fo"], ["zpO"])
+        if last:
+            act(T.fg[:, :], T.kj[:, :].indirect(T.prm[:, :]), ["kand", "perm"], ["fg"])
+
+        def olds(a):
+            if old:
+                tt(T.fn[:, 1, a:96:2], T.iot[:, :].indirect(T.fo[:, a, 0:3]), T.msk[:, 0:48], A.add, ["iot", "fo", "msk"], ["fnN"])
+            else:
+                s_lay(10 + a, "v")
+
         tt(T.nl[:, 0:3], uF, uB, A.add, ["uF", "uB"], ["nl"])
-        tt(T.kd[:, 4:7], uF, uB, A.add, ["uF", "uB"], ["nr"])
-        for jb in range(3):
-            ts(T.ps2[:, 256 + jb:313:3], T.iof[:, 129:148], so[:, 126 + jb:127 + jb], A.is_equal, ["iof", "ks"], ["xk"] + ([] if old else ["B2"]), -2048.0, A.mult)
+        tt(T.nw[:, 0:3], uF, uB, A.add, ["uF", "uB"], ["nw"])
+        if last:
+            tt(ks, T.kb[:, 0:3], T.kb[:, 4:7], A.add, ["kb", "kd"], ["ks"])
+        tt(T.kw[:, 0:57], T.k2[:, :], T.ps2[:, 0:57], A.mult, ["k2", "xk"], ["kw"])
         cp(T.bkl[:, :], bwin.indirect(T.nl[:, 0:3]), ["bookA", "bookB", "nl"], ["bkl"])
-        for jb in range(3):
-            ts(T.ps2[:, jb:57:3], T.iof[:, 129:148], so[:, 126 + jb:127 + jb], A.is_equal, ["iof", "ks", "nr"], ["xn"], T.kd[:, 4 + jb:5 + jb], A.mult)
-        tt(T.kc[:, 60:117], T.kc[:, 0:57], T.ps2[:, 256:313], A.add, ["kc", "xk"], ["kraw"])
-        for c in range(3, 6):
-            act(T.zc[:, 2 * COL[c // 2] + c % 2, 0:128], Zall.indirect(T.bkl[:, 8 * c:8 * c + 8]), Zk + ["bkl"], ["zcS"])
-        act(T.tf[:, :], T.iot[:, :].indirect(T.bkl[:, :]), ["iot", "bkl"], ["tf"])
-        cp(T.zc[:, 2 * COL[0], 0:128], Zall.indirect(T.bkl[:, 0:8]), Zk + ["bkl"], ["zcV"])
+        nrep = T.nw[:, :].indirect(T.rep[:, :])
         if not last:
             kok, c = "ko%d" % t, 72 * t
-            tt(T.ko[:, c:c + 57], T.kc[:, 60:117], T.ps2[:, 0:57], A.max, ["kraw", "xn"], [kok])
+            tt(T.ko[:, c:c + 64], nrep, T.kw[:, :], A.max, ["kw", "nw", "rep"], [kok])
             send(T.ko[:, c:c + 57], [kok], "kl%d" % (t + 1), T.kl[:, c + 72:c + 129])
-        for c in range(1, 3):
-            cp(T.zc[:, 2 * COL[c // 2] + c % 2, 0:128], Zall.indirect(T.bkl[:, 8 * c:8 * c + 8]), Zk + ["bkl"], ["zcV"])
-        olds(1)
-        for r in range(8):
-            mm(T.ps6[:, 0:102], T.scw[:, 14 - 2 * r:142 - 2 * r], T.zc[:, :, 16 * r:16 * r + 17], ["zcV", "zcS", "scw"], ["B6"], False, r == 7)
+        else:
+            tt(T.kc[:, 0:64], nrep, T.kw[:, :], A.max, ["kw", "nw", "rep", "kraw"], ["kc"])
+            ts(T.mk0[:, :], T.io2[:, 0:20], ksj[0], A.is_equal, ["io2", "ks"], ["mk0"], 8192.0, A.mult)
+        for c in range(6):
+            (act if c % 2 else cp)(T.zc[:, c, 0:128], Zall.indirect(T.bkl[:, 8 * c:8 * c + 8]), Zk + ["bkl"], ["zc%d" % c])
+        tfv = TFV if old and not last else 0
+        act(T.tf[:, 128 * tfv:768], T.iot[:, :].indirect(T.bkl[:, 8 * tfv:48]), ["iot", "bkl"], ["tfS"] + ([] if tfv else ["tfV"]))
+        if not last:
+            tt(ks, T.kb[:, 0:3], T.kb[:, 4:7], A.add, ["kb", "kd"], ["ks", "cur"])
+        if old:
+            ts(T.ns[:, :, 63:96:16], T.om[:, :], -OFF - 1.0, A.add, ["om"], ["nsO"])
+        if tfv:
+            cp(T.tf[:, 0:128 * tfv], T.iot[:, :].indirect(T.bkl[:, 0:8 * tfv]), ["iot", "bkl"], ["tfV"])
+        if not old:
+            for r in (8, 9):
+                s_lay(r, "v")
+            s_lay(13, "s")
+        if not last:
+            gcp(T.zw[:, :], T.zc[:, :, 0:128], 768, ["zc%d" % c for c in range(6)], ["zw"])
+        for i in range(3):
+            for r in range(8):
+                mm(T.ps6[:, 34 * i:34 * i + 34], T.scw[:, 14 - 2 * r:142 - 2 * r], T.zc[:, 2 * i:2 * i + 2, 16 * r:16 * r + 17],
+                   ["zc%d" % (2 * i), "zc%d" % (2 * i + 1), "scw"], ["B6"], False, i == 2 and r == 7)
+        eo = [0, 256, 768]
+
+        def name(jb, m):
+            c = 48 * (m % 2) + 16 * jb + 15
+            return T.ns[:, m // 2, c:c + 1]
+
+        def eq(jb, m, part):
+            w = (64 if old else 32) * (jb + 1)
+            pos = eo[jb] + w * m * M // 4 + (w // 2 if part == 1 else 0)
+            a, b = ((0, 2), (1, 2), (0, 1 if old else 2))[part]
+            ts(T.eqb[:, pos:pos + 64 // b * (jb + 1)], T.fn[:, a:2 * jb + 2:b, 32 * jb:32 * jb + 32], name(jb, m), A.is_equal,
+               [k for k in (["fnM", "fnF"] if part != 1 else []) + (["fnN", "fnG"] if part and old else []) if jb or k in ("fnM", "fnN")]
+               + ["nsO" if m % 2 else "nsN"], ["e%d" % jb], 8192.0, A.mult)
+
         if not last:
             ts(T.hitb[:, 0:3], T.kb[:, 0:3], 147.5, A.is_lt, ["kb"], ["hitb"])
             for jb in range(3):
                 mm(T.ps0[:, 400:401], T.onb[:, :], T.hitb[:, jb:jb + 1], ["onb", "hitb"], ["B0"], jb == 0, jb == 2)
+            ts(T.kd[:, 8:11], ks, -65536.0, A.mult, ["ks"], ["kx"], 148.0 * 65536.0 + 8192.0 * (t + 1) + 1.0, A.add)
         else:
-            tt(T.kc[:, 0:57], T.kc[:, 60:117], T.ps2[:, 0:57], A.max, ["kraw", "xn"], ["kc"])
+            ts(T.kc[:, 64:121], T.kc[:, 0:57], 1023, A.bitwise_and, ["kc"], ["kraw"])
             for jb in range(3):
-                ts(T.ps0[:, jb:126:3], T.io2[:, :], so[:, 126 + jb:127 + jb], A.is_equal, ["io2", "ks"], ["B0"], 8192.0, A.mult)
-        olds(2)
-        if last:
-            ts(T.kc[:, 60:117], T.kc[:, 0:57], 1023, A.bitwise_and, ["kc"], ["kraw"])
-            tt(T.fb[:, 0:126], T.ki[:, 126:252], T.ps0[:, 0:126], A.add, ["kand", "B0"], ["fb"])
-        olds(3)
-        if last:
-            ts(T.ps4[:, 0:126], T.fb[:, 0:126], 4096.5, A.is_lt, ["fb"], ["B4"])
-            cp(T.sf[:, 128:185], T.kc[:, 60:117], ["kraw"], ["sfk"])
+                ts(T.ps0[:, jb:120:3], T.io2[:, :], ksj[jb], A.is_equal, ["io2", "ks"], ["B0"], 8192.0, A.mult)
+            ts(T.ri[:, :], T.ra[:, :], -SO, A.add, ["ra"], ["ri"])
+            cp(T.sf[:, 128:185], T.kc[:, 64:121], ["kraw"], ["sfk"])
             send(T.sf[:, 128:185], ["sfk"], "homek", T.homek[:, 4:61], -1)
-        olds(4)
-        if last:
-            tt(T.fa[:, 0:126], T.fb[:, 0:126], T.ps4[:, 0:126], A.mult, ["fb", "B4"], ["fa"])
+            tt(T.fb[:, 0:120], T.fg[:, 0:120], T.ps0[:, 0:120], A.add, ["fg", "B0"], ["fb"])
+            act(T.rb[:, :], T.ri[:, :], ["ri"], ["rb"])
+            dma("y", T.S[0:128:16, 0:4096], T.rb[:, :], "drb", ["rb"], Sk)
+        OLD = (1, 3) if old else ()
         scan(T.sk[:, 0:102], T.rs17[:, :], T.ps6[:, 0:102], A.max, A.min, ["rs17", "B6"], ["sk"])
         scan(T.sk[:, 102:204], T.inc[:, :], T.ps6[:, 0:102], A.add, A.min, ["inc", "B6"], ["sk"])
-        olds(5)
-        tt(T.fl[:, 0:6], T.sk[:, 16:102:17], T.sk[:, 118:204:17], A.subtract, ["sk"], ["fl"])
-        lower = ((2, 256, 384, 0), (1, 0, 64, 2))
-        for (i, a, b, c) in lower if old else ():
-            act(T.fn[:, a + 1:b:2], T.iot[:, :].indirect(T.fo[:, c:4]), ["iot", "fo"], ["fnG%d" % i])
         if last:
-            act(T.ps2[:, 0:126], T.fa[:, 0:126], ["fa"], ["B2", "xe", "xk", "xn"], bias=-1.0)
-        for (i, a, b, c) in lower:
-            act(T.fn[:, a:b:2], twin.indirect(T.fl[:, c:4]), ["tf", "fl"], ["fnF%d" % i])
-        tt(T.fn[:, 64:256:2], twin.indirect(T.fl[:, 0:6]), T.mkn[:, :], A.add, ["tf", "fl", "mkn"], ["fnM"])
-        for m in range(2, M):
-            c = (15, 111)[m - 2] + 16 * COL[2]
-            ts(T.eqb[:, 864 + 192 * m:960 + 192 * m], T.fn[:, 193:384:2], T.ns[:, c:c + 1], A.is_equal, ["fnN", "fnG2", "nsO"], ["e2"], 8192.0, A.mult)
+            ts(T.ps4[:, 0:120], T.fb[:, 0:120], 4096.5, A.is_lt, ["fb"], ["B4"])
+        olds(0)
+        tt(T.fl[:, 0:6], T.sk[:, 16:102:17], T.sk[:, 118:204:17], A.subtract, ["sk"], ["fl"])
+        olds(1)
+        if last:
+            tt(T.fa[:, 0:120], T.fb[:, 0:120], T.ps4[:, 0:120], A.mult, ["fb", "B4"], ["fa"])
+        for i in (1, 2):
+            act(T.fn[:, 2 * i, 32 * i:96], twin.indirect(T.fl[:, 0:6 - 2 * i]), ["tfV", "tfS", "fl"], ["fnF"])
+        if last:
+            act(T.ps2[:, 0:120], T.fa[:, 0:120], ["fa"], ["B2", "xk", "X"], bias=-1.0)
+        else:
+            act(T.zq[:, :], T.zw[:, :].indirect(T.fl[:, 0:6]), ["zw", "fl"], ["zq"])
+            for a in range(2):
+                c = 24 * M * (1 - a)
+                gcp(T.zp[:, c:c + 48], T.zq[:, a:96:2], 48, ["zq"], ["zpN"])
+        tt(T.fn[:, 0, :], twin.indirect(T.fl[:, 0:6]), T.mkn[:, :], A.add, ["tfV", "tfS", "fl", "mkn"], ["fnM"])
+        for m in OLD:
+            eq(2, m, 1)
+        if not old:
+            late(1)
+            s_turn((14, 15))
         for m in range(2):
-            scan(T.ns[:, 96 * m + 48:96 * m + 96], T.pns[:, :], T.fn[:, 64 + 2 * m:256:4], A.max, A.min, ["pns", "fnM"], ["nsN"])
-        reg = [(128, 192), (0, 128), (192, 384)]
-        eo = [0, 256, 768]
-
-        def name(jb, m):
-            c = (63, 159, 15, 111)[m] + 16 * COL[jb]
-            return T.ns[:, c:c + 1]
-
-        def eq(jb, m):
-            a, b = reg[jb]
-            w = b - a
-            pos = eo[jb] + w * m
-            if jb == 2 and m > 1:
-                ts(T.eqb[:, pos:pos + 96], T.fn[:, a:b:2], name(jb, m), A.is_equal, ["fnM", "fnF2", "nsO"], ["e2"], 8192.0, A.mult)
-                return
-            ts(T.eqb[:, pos:pos + w], T.fn[:, a:b], name(jb, m), A.is_equal,
-               ["fnM", "fnN", "fnF%d" % jb, "fnG%d" % jb, "nsN" if m < 2 else "nsO"], ["e%d" % jb], 8192.0, A.mult)
+            scan(T.ns[:, m, 0:48], T.pns[:, :], T.fn[:, 0, m:96:2], A.max, A.min, ["pns", "fnM"], ["nsN"])
+        if not old:
+            late(2)
 
         def count(jb):
-            w = (reg[jb][1] - reg[jb][0]) * M // 2
+            w = (64 if old else 32) * (jb + 1) * M // 2
             c = eo[jb] // 2
             scan(T.cn[:, c:c + w], T.eqb[:, eo[jb]:eo[jb] + w], T.eqb[:, eo[jb] + w:eo[jb] + 2 * w], A.add, A.add, ["e%d" % jb], ["cn%d" % jb], OFF - 8192.0 * M)
             return T.cn[:, c + w - 1:c + w]
 
         def place(jb, col):
-            ts(T.xo[:, COL[jb]:3 * M:3], T.ns[:, (15 if old else 63) + 16 * COL[jb]:192:192 // M], col, A.add, ["nsN", "nsO", "cn%d" % jb], ["xo%d" % jb])
+            ts(T.xo[:, :, jb:6:3], T.ns[:, :, 16 * jb + 15:96:48], col, A.add, ["nsN", "nsO", "cn%d" % jb], ["xo%d" % jb])
 
         def places():
-            tt(T.offs[:, o:o + 3 * M], T.xo[:, 0:3 * M], T.padf[:, 0:12] if old else T.padf[:, 12:18], A.min, ["xo0", "xo1", "xo2", "padu"], ["offs%d" % t])
-
-        def partners():
-            h = 3 * M // 2
-            for m in range(2):
-                act(T.pl[:, o + h * m:o + h * m + h], T.ns[:, 96 * (1 - m) + (15 if old else 63):96 * (2 - m):16], ["nsN", "nsO"], ["pl%d" % t], bias=OFF)
+            tt(T.offs[:, o:o + 12], T.xo[:, :, :], T.padf[:, :, :], A.min, ["xo0", "xo1", "xo2", "padu"], ["offs%d" % t])
 
         if not last:
-            partners()
             terms(t + 1, 1)
-            act(T.zp[:, 0:48 * M], Zall.indirect(T.pl[:, o:o + 3 * M]), Zk + ["pl%d" % t], ["zp"])
             terms(t + 1, 2)
             turned(1)
             wholes(t + 1)
+            turned(2)
         else:
-            for jb in (2, 1, 0):
+            for jb in (2, 1):
                 for a in range(2):
-                    act(T.q1[:, 63 * a + jb:63 * a + 63:3], T.ps0[:, 63 * a + jb:63 * a + 63:3], ["B0", "nsN"], ["q1%d" % jb], func=AF.Identity, bias=name(jb, a))
-        for ms_ in (range(2, M), range(2)):
-            for jb in (2, 1, 0):
-                for m in ms_:
-                    eq(jb, m)
+                    act(T.q1[:, 60 * a + jb:60 * a + 60:3], T.ps0[:, 60 * a + jb:60 * a + 60:3], ["B0", "nsN"], ["q1%d" % jb], func=AF.Identity, bias=name(jb, 2 * a))
+            for a in range(2):
+                act(T.pl[:, 6 - 6 * a:12 - 6 * a], T.ns[:, a, 15:96:16], ["nsN", "nsO"], ["pl"], bias=OFF)
+            act(T.sp[:, :], T.S[:, :].indirect(T.pl[:, :]), Sk + ["pl"], ["sp"])
+        for jb in (0, 1, 2):
+            for m in OLD:
+                eq(jb, m, 0 if jb == 2 else 2)
+        for jb in (2, 1, 0):
+            for m in (0, 2):
+                eq(jb, m, 2)
+        for a in range(2 * last):
+            ts(T.q1[:, 60 * a:60 * a + 60:3], T.mk0[:, :], name(0, 2 * a), A.add, ["mk0", "nsN"], ["q10"])
         c2 = count(2)
         c1 = count(1)
         c0 = count(0)
@@ -622,34 +688,37 @@ def rank_program(g, core, T, topo):
         place(2, c2)
         place(1, c1)
         place(0, c0)
-        places()
-        if t == VI - 2:
-            cp(T.ri[:, :], T.ra[:, :], ["ra"], ["ri"])
-        cp(Zall.indirect(T.offs[:, o:o + 3 * M]), T.zp[:, 0:48 * M], ["offs%d" % t, "zp"], Zk)
+        if not old:
+            late(3)
+        if old:
+            places()
+            cp(Zall.indirect(T.offs[:, o:o + 12]), T.zp[:, :], ["offs%d" % t, "zpN", "zpO"], Zk)
+        else:
+            tt(T.of0[:, :], T.xo[:, :, 0:3], T.padf[:, :, 0:3], A.min, ["xo0", "xo1", "xo2", "padu"], ["of0"])
+            places()
+            late(4)
+            cp(Zall.indirect(T.of0[:, :]), T.zp[:, 0:96], ["of0", "zpN"], Zk)
 
         def state():
-            ts(so[:, 129:129 + 3 * M], T.offs[:, o:o + 3 * M], 8192.0 * (t + 1) + 1.0, A.add, ["offs%d" % t, "of2"], ["of2"])
-            send(so[:, :], ["cur", "ks", "of2"], "st%d" % (t + 1), T["st%d" % (t + 1)][:, :])
+            for a in range(2):
+                tt(so[:, 21 + a:96:32], T.offs[:, o + 6 * a:o + 6 * a + 3], T.kd[:, 8:11], A.add, ["offs%d" % t, "kx", "ks"], ["of2%d" % a])
+            send(so[:, :], ["cur", "ks", "of20", "of21"], "st%d" % (t + 1), T["st%d" % (t + 1)][:, :])
 
         answers(t + 1, state, head)
 
-    partners()
-    sread(t - 1)
     for (jb, col) in ((2, c2), (1, c1), (0, c0)):
-        ts(T.x1[:, jb:126:3], T.q1[:, jb:126:3], col, A.subtract, ["q1%d" % jb, "cn%d" % jb], ["x1%d" % jb], -2 * OFF, A.add)
+        ts(T.x1[:, jb:120:3], T.q1[:, jb:120:3], col, A.subtract, ["q1%d" % jb, "cn%d" % jb], ["x1%d" % jb], -2 * OFF, A.add)
     place(2, c2)
     place(1, c1)
     place(0, c0)
-    tt(T.sf[:, 0:126], T.x1[:, :], T.ps2[:, 0:126], A.max, ["x10", "x11", "x12", "B2"], ["sf"])
-    send(T.sf[:, 0:123], ["sf"], "home", T.home[:, 0:123], -1)
+    tt(T.sf[:, 0:120], T.x1[:, :], T.ps2[:, 0:120], A.max, ["x10", "x11", "x12", "B2"], ["sf"])
+    send(T.sf[:, 0:120], ["sf"], "home", T.home[:, 0:120], -1)
     places()
-    swrite(t - 1, "v")
-    sread(t)
-    swrite(t, "v")
     dma("s", T.yk[:, :], T.homek[:, 1:61], "dout", ["homek", "homez"], [])
+    swrite(t, "v")
     dma("y", T.ys[:, :], T.S[0:128:16, 0:4096], "dout", Sk, [])
     dma("s", T.ya[:, :], T.home[:, 0:60], "dout", ["home"], [])
-    dma("y", T.yb[:, :], T.home[:, 63:123], "dout", ["home"], [])
+    dma("y", T.yb[:, :], T.home[:, 60:120], "dout", ["home"], [])
     need("y", "dout", 64)
     need("g", "lsem", cnt["sent"])
     for q in ("v", "s", "p", "g"):

from concourse.bass import DstId, RemoteDMATransfer
from concourse.mybir import dt, AluOpType, AxisListType, ActivationFunctionType

VI = 6
PADC = 4480
P_CH = [24, 38, 42, 64, 72, 96]
OWN = 2
PH = sum(P_CH)
NP = PH // 24
N_CH = [32, 112, 96, 32, 16]
NN = sum(N_CH)
KN = 3 * (NP - 1)
B1 = 104
ZS = 96
YN, YW = 16 * PH, 16 * (PH + NN)
OFF = 2048.0
SO = 4096.0
BIG = 30000.0
TFV = 2
SW = 180

_sb = {
    "truv": (4096, "bfloat16"), "Z": (PADC, "bfloat16"), "S": (PADC, "float32"), "iot": (PADC, "float32"),
    "booki": (4096, "int32"), "kc": (128, "int32"), "k2": (57, "float32"), "kw": (64, "float32"), "nw": (8, "float32"), "rep": (4, "uint16"), "sgi": (256, "int32"), "sgl": (256, "uint16"), "sgh": (256, "float16"), "kmi": (64, "int32"),
    "G": (YW, "bfloat16"), "H": (YN, "bfloat16"), "ysc": (YW, "bfloat16"), "nat": (NN + 16, "uint16"), "nz": (48, "uint16"),
    "kl": (72 * VI, "uint16"), "ko": (72 * VI, "uint16"), "kz": (32, "uint16"),
    "thi": (2 * PH, "float16"), "hsel": (288, "float16"), "ll": (2 * PH, "uint16"), "kj": (SW, "int32"),
    "pi": (1, "int32"), "pj": (1, "int32"), "pg": (1, "int32"), "colf": (16, "float32"),
    "iof": (160, "float32"), "ioj": (48, "float32"), "ion": (96, "float32"), "io2": (40, "float32"), "iox": (32, "float32"),
    "rst": (16 * max(N_CH), "bfloat16"), "rst8": (16 * max(P_CH), "bfloat16"), "idb": (128, "bfloat16"), "lt": (960, "bfloat16"),
    "scw": (144, "bfloat16"), "pos": (336, "bfloat16"), "mkn": (96, "float32"), "rs17": (102, "bfloat16"), "inc": (102, "float32"),
    "idh": (144, "float16"), "onb": (128, "bfloat16"), "on2": (96, "bfloat16"),
    "wts": (640, "bfloat16"), "msk": (48, "float32"), "pns": (48, "float32"), "hrow": (128, "bfloat16"), "crow": (128, "bfloat16"),
    "padh": (12, "float32"), "curh": (192, "float32"),
    "hi": (96, "float32"), "lo": (96, "float32"), "su": (84, "int32"), "osm": (SW, "int32"), "ki": (SW, "int32"), "uint": (24, "int32"),
    "kb": (8, "bfloat16"), "kd": (12, "float32"), "nl": (4, "uint16"), "bkl": (48, "uint16"), "tf": (768, "float32"), "zw": (768, "bfloat16"),
    "hitb": (4, "bfloat16"), "om": (6, "int32"), "sk": (204, "float32"),
    "fl": (6, "uint16"), "of0": (6, "uint16"),
    "eqb": (1536, "bfloat16"), "cn": (768, "bfloat16"),
    "offs": (12 * VI, "uint16"), "pl": (12, "uint16"), "zp": (192, "bfloat16"), "zq": (96, "bfloat16"), "sp": (192, "float32"),
    "q1": (120, "float32"), "mk0": (20, "float32"), "x1": (120, "float32"), "sf": (188, "float32"), "fg": (128, "float32"),
    "fa": (128, "float32"), "fb": (128, "float32"), "home": (120, "float32"), "homek": (64, "float32"),
    "pw": (64, "float32"), "pk": (8, "int32"), "prm": (8, "uint16"),
    "ra": (256, "float32"), "ri": (256, "int32"), "rb": (256, "float32"),
}
_sb3 = {
    "zc": (6, 136, "bfloat16"), "fn": (6, 96, "float16"), "ns": (2, 96, "float32"),
    "fo": (2, 4, "uint16"), "xo": (2, 6, "float32"), "padf": (2, 6, "float32"),
}
SCRATCH = {}
for _k in _sb:
    SCRATCH[_k] = ("sbuf", [128, _sb[_k][0]], _sb[_k][1])
for _k in _sb3:
    SCRATCH[_k] = ("sbuf", [128, _sb3[_k][0], _sb3[_k][1]], _sb3[_k][2])
for _t in range(VI):
    SCRATCH["so%d" % _t] = ("sbuf", [128, SW], "float32")
for _t in range(1, VI):
    SCRATCH["st%d" % _t] = ("sbuf", [128, SW], "float32")
for _t in range(8):
    SCRATCH["ps%d" % _t] = ("psum", [128, 16, 32] if _t in (3, 7) else [128, 512], "float32")
SEMAPHORES = (["sv", "ss", "sp_", "sg_", "lsg", "ltr", "lbk", "lbw", "lbx", "lkm", "lwt", "dout", "lsem", "dra", "drb", "a_home", "a_homek"]
              + ["a_%s%d" % (_k, _t) for _k in ("st", "kl") for _t in range(1, VI)] + ["a_kz%d" % _t for _t in range(1, 4)])


def rank_program(g, core, T, topo):
    rank = T.rank_of(core)
    if rank is None:
        return
    A, AF = AluOpType, ActivationFunctionType
    cores = T.cores

    eng = {"v": g.vector, "s": g.scalar, "p": g.tensor, "g": g, "y": g.sync}
    semn = {"v": "sv", "s": "ss", "p": "sp_", "g": "sg_"}
    cnt = {"v": 0, "s": 0, "p": 0, "g": 0, "sent": 0}
    waited = {}
    wr, rd = {}, {}

    def need(q, sem, n):
        if waited.get((q, sem), 0) < n:
            waited[(q, sem)] = n
            eng[q].wait_ge(T.sem[sem], n)

    def deps(q, r, w):
        lst = {}
        for k in r:
            if k in wr:
                sem, n, q2 = wr[k]
                if not (q == "p" and q2 == "p"):
                    lst[sem] = max(lst.get(sem, 0), n)
            if k[0] == "B":
                for (sem, n, q2) in rd.get(k, {}).values():
                    if q2 != q:
                        lst[sem] = max(lst.get(sem, 0), n)
        for k in w:
            if k in wr and wr[k][2] != q:
                lst[wr[k][0]] = max(lst.get(wr[k][0], 0), wr[k][1])
            for (sem, n, q2) in rd.get(k, {}).values():
                if q2 != q or q != "p":
                    lst[sem] = max(lst.get(sem, 0), n)
        for sem in lst:
            need(q, sem, lst[sem])

    def note(q, r, w, tag):
        for k in r:
            rd.setdefault(k, {})[q] = tag
        for k in w:
            wr[k] = tag
            rd[k] = {}

    def E(q, f, r, w):
        deps(q, r, w)
        i = f(eng[q])
        cnt[q] += 1
        i.then_inc(T.sem[semn[q]], 1)
        note(q, r, w, (semn[q], cnt[q], q))

    def dma(q, out, in_, sem, r, w):
        deps(q, r, w)
        eng[q].dma_start(out=out, in_=in_).then_inc(T.sem[sem], 16)
        note(q, r, w, (sem, 16, "dma"))

    def ts(out, in0, s1, op0, r, w, s2=None, op1=None):
        if op1 is None:
            E("v", lambda e: e.tensor_scalar(out=out, in0=in0, scalar1=s1, scalar2=None, op0=op0), r, w)
        else:
            E("v", lambda e: e.tensor_scalar(out=out, in0=in0, scalar1=s1, scalar2=s2, op0=op0, op1=op1), r, w)

    def tt(out, a, b, op, r, w):
        E("v", lambda e: e.tensor_tensor(out=out, in0=a, in1=b, op=op), r, w)

    def cp(out, a, r, w):
        E("v", lambda e: e.tensor_copy(out=out, in_=a), r, w)

    def scan(out, d0, d1, op0, op1, r, w, init=0.0):
        E("v", lambda e: e.tensor_tensor_scan(out=out, data0=d0, data1=d1, initial=init, op0=op0, op1=op1), r, w)

    def flip(out, a, r, w):
        E("v", lambda e: e.transpose(out=out, in_=a), r, w)

    def ms(ap, c, w, r=()):
        E("v", lambda e: e.memset(ap, c), r, w)

    def act(out, a, r, w, func=None, **kw):
        E("s", lambda e: e.activation(out=out, in_=a, func=AF.Copy if func is None else func, **kw), r, w)

    def mm(out, lhsT, rhs, r, w, start=True, stop=True):
        E("p", lambda e: e.matmul(out, lhsT, rhs, start, stop), r, w)

    def iota(out, pattern, base, cm, w, r=()):
        E("g", lambda e: e.iota(out, pattern, base, cm, allow_small_or_imprecise_dtypes=True), r, w)

    def gcp(out, a, n, r, w):
        E("g", lambda e: e.affine_select(out, a, [[0, n]], A.is_ge, 0.0, 0, 0), r, w)

    def send(src_ap, keys, land, out_ap, step=1):
        dst, frm = cores[(rank + step) % 4], cores[(rank - step) % 4]
        deps("g", keys, [])
        rid, pid = topo.addr(dst, core)
        en = topo.engines(core, dst)
        g.remote_dma(out_ap=out_ap, in_ap=src_ap, remote_sem=T.sem["a_" + land], local_sem=T.sem.lsem,
                     pid=pid, routing_id=rid, dma_engine_mask=sum(1 << e for e in en))
        cnt["sent"] += len(en)
        wr[land] = ("a_" + land, len(topo.engines(frm, core)), "remote")

    dma("y", T.sgi[:, :], T.sg0[:, :], "lsg", [], ["sgi"])
    dma("s", T.kmi[:, 0:60], T.km0[:, :], "lkm", [], ["kmi"])
    dma("y", T.truv[:, :], T.tru[:, :], "ltr", [], ["truv"])
    dma("y", T.booki[:, 0:1024], T.book[:, :], "lbk", [], ["bookA"])
    dma("y", T.kmi[:, 60:61], T.wt[:, :], "lwt", [], ["wti"])
    dma("y", T.booki[:, 1024:2048], T.book[:, :], "lbw", ["bookA"], ["bookB"])
    dma("y", T.booki[:, 2048:4096], T.booki[:, 0:2048], "lbx", ["bookA", "bookB"], ["bookC"])

    iota(T.pi[:, :], [[0, 1]], 0, 1, ["pi"])
    iota(T.iof[:, :], [[1, 160]], 0, 0, ["iof"])
    iota(T.ioj[:, :], [[0, 3], [1, 16]], 0, 0, ["ioj"])
    iota(T.ion[:, :], [[0, 3], [1, 16], [0, 2]], 0, 0, ["ion"])
    iota(T.hrow[0:1, :], [[0, 4], [1, 32]], -10, 0, ["hrow"])
    C = T.colf
    ms(T.Z[:, 4096:PADC], 0.0, ["Zpad"])
    act(T.S[:, 4096:PADC], T.Z[:, 4096:PADC], ["Zpad"], ["Spad"], func=AF.Silu)
    ms(T.crow[0:1, :], -272.0, ["crow"])
    ms(T.on2[0:1, :], 2.0 ** 20, ["on2"])
    cp(C[:, 0:1], T.pi[:, :], ["pi"], ["c0"])
    ts(T.pj[:, :], T.pi[:, :], 15, A.bitwise_and, ["pi"], ["pj"])
    ts(T.pg[:, :], T.pi[:, :], 4, A.arith_shift_right, ["pi"], ["pg"])
    ts(T.uint[:, 0:1], T.pi[:, :], 8, A.bitwise_and, ["pi"], ["uI"])
    ts(T.uint[:, 1:2], T.pi[:, :], 14, A.bitwise_and, ["pi"], ["uJ"])
    ts(C[:, 10:11], T.pi[:, :], 1008.0, A.add, ["pi"], ["c10"])
    ms(T.wts[:, :], 0.0, ["wts"])
    ts(T.idh[:, :], T.iof[:, 0:144], C[:, 0:1], A.is_equal, ["iof", "c0"], ["idh"])
    cp(C[:, 1:2], T.pj[:, :], ["pj"], ["c1"])
    cp(C[:, 2:3], T.pg[:, :], ["pg"], ["c2"])
    ts(C[:, 11:12], T.uint[:, 0:1], 125.0, A.mult, ["uI", "c10"], ["c11"], C[:, 0:1], A.add)
    ts(C[:, 12:13], T.uint[:, 0:1], -125.0, A.mult, ["uI", "c10"], ["c12"], C[:, 10:11], A.add)
    ts(C[:, 3:4], T.uint[:, 1:2], 8.0, A.mult, ["uJ"], ["c3"], 15.0, A.add)
    ms(T.crow[0:1, 0:128:32], 64.0, ["crow"], ["crow"])
    W = [T.pw[:, 8 * i:8 * i + 8] for i in range(8)]
    ts(W[0], T.iof[:, 0:128:16], C[:, 1:2], A.add, ["iof", "c1"], ["w0"], 119.0, A.min)
    ts(T.idb[:, :], T.iof[:, 0:128], C[:, 0:1], A.is_equal, ["iof", "c0"], ["idb"])
    ts(T.hsel[:, 0:144], T.iof[:, 0:144], -8.0, A.add, ["iof", "c11"], ["hsel"], C[:, 11:12], A.is_equal)
    ts(W[1], W[0], 59.5, A.is_gt, ["w0"], ["w1"], -60.0, A.mult)
    ts(T.hsel[:, 144:288], T.iof[:, 0:144], C[:, 12:13], A.is_equal, ["iof", "c12"], ["hsel"])
    ts(C[:, 4:5], C[:, 1:2], 0.5, A.add, ["c1"], ["c4"])
    ts(C[:, 5:6], C[:, 1:2], 0.5, A.mult, ["c1"], ["c5"], 0.25, A.add)
    tt(W[4], W[0], W[1], A.add, ["w0", "w1"], ["w4"])
    ts(T.mkn[:, :], T.ion[:, :], C[:, 1:2], A.is_gt, ["ion", "c1"], ["mkn"], BIG, A.mult)
    ts(T.msk[:, :], T.ioj[:, :], C[:, 1:2], A.is_gt, ["ioj", "c1"], ["msk"], BIG, A.mult)
    ts(T.pns[:, :], T.ioj[:, :], C[:, 4:5], A.subtract, ["ioj", "c4"], ["pns"], -4 * BIG, A.mult)
    ts(T.pk[:, :], W[4], -1.0, A.add, ["w4"], ["pk"], 1.0 / 3.0, A.mult)
    ts(T.sgh[:, :], T.sgi[:, :], -OFF, A.add, ["sgi"], ["sgh"])
    cp(T.kz[:, 0:3], T.kmi[:, 0:3], ["kmi"], ["kz0"])
    ts(W[1], T.pk[:, :], -3.0, A.mult, ["pk"], ["w1"])
    act(T.sgl[:, :], T.sgi[:, :], ["sgi"], ["sgl"])
    iota(T.rst[:, :], [[0, max(N_CH)], [-512, 16]], 512, 0, ["rst"])
    iota(T.rst8[:, :], [[0, max(P_CH) * 2], [-512, 8]], 512, 0, ["rst8"])
    for step in (1, 2, 3):
        send(T.kz[:, 0:3], ["kz0"], "kz%d" % step, T.kz[:, 8 * step:8 * step + 3], step)
    for (ap, c, key) in ((T.onb[:, :], 1, "onb"), (T.rs17[:, :], -2 ** 23, "rs17"), (T.inc[:, :], 1, "inc"), (T.scw[:, :], 0, "scw"),
                         (T.kw[:, :], 0, "kw"), (T.nw[:, :], 0, "nw"), (T.zc[:, :, 128], 0, "zc0"),
                         (T.ns[:, :, 63:96:16], int(BIG), "nsO")):
        n = 1
        for d in ap.shape[1:]:
            n *= d
        iota(ap, [[0, n]], c, 0, [key])
    iota(T.pos[0:1, 0:102], [[128, 6], [0, 17]], 0, 0, ["pos"])
    iota(T.pos[0:1, 102:204], [[0, 6], [1, 17]], 0, 0, ["pos"])
    iota(T.pos[0:1, 204:332], [[0, 8], [16, 8], [0, 2]], 0, 0, ["pos"])
    iota(T.rs17[:, 0:102:17], [[0, 6]], 2 ** 23, 0, ["rs17"], ["rs17"])
    iota(T.inc[:, 0:102:17], [[0, 6]], 2 ** 23, 0, ["inc"], ["inc"])
    iota(T.pos[0:1, 118:204:17], [[0, 6]], 3 * 2 ** 22, 0, ["pos"], ["pos"])
    iota(T.padh[:, :], [[16, 2], [32, 2], [64, 3]], 2048, 0, ["padh"])
    for a in range(2):
        iota(T.curh[:, 96 * a:96 * a + 96], [[32, 3], [16384, 32]], 1024 + 8 * a, 0, ["curh"])
    iota(T.io2[:, :], [[0, 2], [1, 20]], 128, 0, ["io2"])
    iota(T.iox[:, :], [[-1, 32]], 148, 0, ["iox"])
    iota(T.iot[:, :], [[1, PADC]], -int(OFF), 0, ["iot"])

    S_BANK = (6, 2, 5, 1, 7, 3, 1, 1)

    def s_at(r):
        b, h = S_BANK[r // 2], r % 2
        return (T["ps%d" % b][:, 8 * h:8 * h + 8, :] if b in (3, 7) else T["ps%d" % b][:, 256 * h:256 * h + 256]), "B%d" % b

    def s_lay(r, q):
        src, key = s_at(r)
        if q == "v":
            ts(T.S[:, r:4096:16], src, OFF + SO, A.add, [key], ["Sa"])
        else:
            act(T.S[:, r:4096:16], src, [key], ["Sb"], bias=OFF + SO)

    def s_turn(rows):
        for r in rows:
            mm(s_at(r)[0], T.idh[:, r:r + 128], T.sgh[:, :], ["idh", "sgh"], [s_at(r)[1]])

    s_turn(range(8))
    cp(T.kl[:, 0:57], T.kmi[:, 3:60], ["kmi"], ["kl0"])
    cp(T.homek[:, 1:4], T.kmi[:, 0:3], ["kmi"], ["homez"])

    def weights(i, v, keys):
        for h in range(2):
            c = 320 * i + 160 * h
            ts(T.wts[:, c + 31:c + 159:32], T.iof[:, h:8:2], C[:, 2:3], A.is_equal, ["iof", "c2"] + keys, ["wts"], v, A.mult)

    weights(1, 2.0 ** 25, [])
    tt(T.rep[:, :], T.pw[:, 8:12], T.pw[:, 32:36], A.add, ["w1", "w4"], ["rep"])

    def late(i):
        if i == 0:
            for s in range(2):
                ts(T.scw[:, 14 + s:142:16], T.iof[:, 0:8], C[:, 2:3], A.is_equal, ["iof", "c2"], ["scw"], 2048.0 * s - 1024.0, A.mult)
            ts(T.inc[:, 16:102:17], T.iof[:, 0:6], -128.0, A.mult, ["iof", "c3"], ["inc"], C[:, 3:4], A.subtract)
            ts(T.padf[:, :, :], T.padh[:, :], C[:, 1:2], A.add, ["padh", "c1"], ["padu"], 2.0, A.mult)
            ts(T.so0[:, :], T.curh[:, 0:SW], C[:, 5:6], A.add, ["curh", "c5"], ["cur"], 4.0, A.mult)
        elif i == 1:
            ts(W[2], W[0], 59.5, A.is_gt, ["w0"], ["w2"], -1824.0, A.mult)
            ts(W[3], W[0], 32.0, A.mult, ["w0"], ["w3"])
            ts(W[6], T.pk[:, :], -97.0, A.mult, ["pk"], ["w6"])
        elif i == 2:
            ts(W[7], T.pk[:, :], 0.5, A.is_gt, ["pk"], ["w7"], 20.0, A.mult)
            tt(W[5], W[2], W[3], A.add, ["w2", "w3"], ["w5"])
        elif i == 3:
            tt(W[1], W[6], W[7], A.add, ["w6", "w7"], ["w1"])
        else:
            tt(T.prm[:, :], W[1], W[5], A.add, ["w1", "w5"], ["perm"])

    Zk = ["ZA", "ZB", "Zpad"]
    Zall = T.Z[:, :]
    Sk = ["Sa", "Sb", "Spad"]
    bwin = T.booki[:, 0:2048]
    twin = T.tf[:, :]
    BLOCKS = [(0, 24, 4), (24, B1, 4), (B1, PH, 5)]

    def names_of(t):
        return 4 if t > 0 else 2

    def book_at(t, a, b):
        return T.booki[:, 0:1024 if t == 0 else 4096].indirect(T.kl[:, 72 * t + a:72 * t + b]), ["bookA", "kl%d" % t] + (["bookB", "bookC"] if t > 0 else [])

    def terms(t, i):
        a, b, bank = BLOCKS[i]
        if i:
            src, keys = book_at(t, a // 8 - 3, b // 8 - 3)
        else:
            src, keys = T.booki[:, 0:1024].indirect(T.kz[:, 8 * (t % 4):8 * (t % 4) + 3]), ["bookA", "kz%d" % (t % 4)]
        act(T.thi[:, 2 * a:2 * b], src, keys, ["thi%d" % i], bias=-OFF)
        for o in range(2):
            for h in range(2):
                c = 144 * o + 8 - 8 * (h - o)
                mm(T["ps%d" % bank][:, o * (b - a):(o + 1) * (b - a)], T.hsel[:, c:c + 128], T.thi[:, 2 * a + h:2 * b:2], ["hsel", "thi%d" % i], ["B%d" % bank], h == 0, h == 1)

    def turned(i):
        a, b, bank = BLOCKS[i]
        act(T.ll[:, 2 * a:2 * b], T["ps%d" % bank][:, 0:2 * (b - a)], ["B%d" % bank], ["ll%d" % i], bias=OFF)

    def half(o, c, n):
        i = 0 if c < 24 else 1 if c < B1 else 2
        a, b, bank = BLOCKS[i]
        return T.ll[:, a + o * (b - a) + c:a + o * (b - a) + c + n], "ll%d" % i

    def wholes(t):
        src, keys = book_at(t, KN - KN % 2, 57)
        act(T.nat[:, 0:NN + 16 * (KN % 2)], src, keys, ["nat"])

    def sread(v):
        for a in range(2):
            act(T.sp[:, 96 * a:96 * a + 96], T.S[:, :].indirect(T.offs[:, 12 * v + 6 - 6 * a:12 * v + 12 - 6 * a]), Sk + ["offs%d" % v], ["sp"])

    def swrite(v, q):
        dst = T.S[:, :].indirect(T.offs[:, 12 * v:12 * v + 12])
        if q == "v":
            cp(dst, T.sp[:, :], ["offs%d" % v, "sp"] + Sk, Sk)
        else:
            act(dst, T.sp[:, :], ["offs%d" % v, "sp"] + Sk, Sk, func=AF.Silu)

    def yslot(k, n=1):
        if k < NP:
            return T.ysc[:, 384 * k + 7:384 * (k + n):8]
        return T.ysc[:, YN + 768 * (k - NP) + 15:YN + 768 * (k - NP + n):16]

    def taken(t, a):
        st = T["st%d" % t]
        for jb in range(3):
            c, e = 128 + 96 * a + 32 * jb, 32 * jb + 20
            ts(T.ps2[:, c:c + 32], T.iox[:, :], st[:, e:e + 1], A.is_equal, ["iox", "st%d" % t], ["X"], st[:, e + 1 + a:e + 2 + a], A.mult)

    def answers(t, filler, head):
        pits, nits = [], []
        for (chs, its) in ((P_CH, pits), (N_CH, nits)):
            c = 0
            for n in chs:
                its.append((c, n))
                c += n
        done = [0, NP - 1, 0, NP - 1]
        np_ = len(pits)

        def rows(bank, i, x, src, key, end):
            for h in range(2):
                c = 320 * i + 160 * h + 31 - x
                mm(T["ps%d" % bank][:, 0:3, 16 * h:16 * h + 16], T.wts[:, c:c + 128], src, [key, "wts"], ["B%d" % bank], False, end and h == 1)

        def sums(cls, upto, key):
            k0, k1 = done[cls] + 1, upto
            done[cls] = max(done[cls], upto)
            if k1 < k0:
                return
            tt(T.lt[:, 48 * k0:48 * (k1 + 1)], yslot(k0, k1 - k0 + 1), T.ps0[:, 0:48 * (k1 - k0 + 1)], A.is_lt, [key, "B0"], ["lt" + key])
            for k in range(k0, k1 + 1):
                rows(3, 1, 20 - k, T.lt[:, 48 * k:48 * k + 48], "lt" + key, k == 19)

        def weigh(cls, upto, key):
            for k in range(done[2 + cls] + 1, upto + 1):
                for x in ([0] if k == 1 + t else []) + [20 - k]:
                    rows(7, 0, x, yslot(k), key, k == 19)
            done[2 + cls] = max(done[2 + cls], upto)

        def spread(y0, key):
            for k in range(4):
                mm(T.ps0[:, 48 * k:48 * k + 48], T.idb[:, :], y0, ["idb", key], ["B0"])

        def ngather(i):
            c, n = nits[i]
            act(T.G[:, YN + 16 * c:YN + 16 * (c + n)], Zall.indirect(T.nat[:, 16 * (KN % 2) + c:16 * (KN % 2) + c + n]), Zk + ["nat"], ["J%d" % i])

        def nscan(i):
            c, n = nits[i]
            scan(T.ysc[:, YN + 16 * c:YN + 16 * (c + n)], T.rst[:, 0:16 * n], T.G[:, YN + 16 * c:YN + 16 * (c + n)], A.max, A.min, ["rst", "J%d" % i], ["YN%d" % i])
            weigh(1, NP - 1 + (c + n) // 48, "YN%d" % i)

        def pgather(i, f=act):
            c, n = pits[i]
            lst, key = half(0, c, n)
            f(T.G[:, 16 * c:16 * (c + n)], Zall.indirect(lst), Zk + [key], ["G%d" % i])

        def pfold(i):
            c, n = pits[i]
            lst, key = half(1, c, n)
            tt(T.H[:, 16 * c:16 * (c + n)], Zall.indirect(lst), T.G[:, 16 * c:16 * (c + n)], A.min, Zk + [key, "G%d" % i], ["H%d" % i])

        def pscan(i):
            c, n = pits[i]
            scan(T.ysc[:, 16 * c:16 * (c + n)], T.rst8[:, 0:16 * n], T.H[:, 16 * c:16 * (c + n)], A.max, A.min, ["rst8", "H%d" % i], ["YP%d" % i])
            if i == 0:
                spread(yslot(0), "YP0")
            weigh(0, (c + n) // 24 - 1, "YP%d" % i)

        if t == 0:
            cp(T.nz[:, :], T.booki[:, 0:1024].indirect(T.kz[:, 0:3]), ["bookA", "kz0"], ["nz"])
            filler()
            cp(T.eqb[:, 0:768], Zall.indirect(T.nz[:, :]), Zk + ["nz"], ["e0", "e1"])
            pgather(1, cp)
        else:
            filler()
            for i in range(OWN):
                pgather(i, cp)
        first = OWN
        while pits[first][0] < B1:
            pgather(first)
            first += 1
        head()
        if t == 0:
            ngather(0)
        for i in range(first, np_):
            pgather(i)
        for i in range(t == 0, len(nits)):
            ngather(i)
        if t:
            pfold(0)
            pfold(1)
            pscan(0)
        else:
            scan(T.eqb[:, 768:1536], T.rst[:, 0:768], T.eqb[:, 0:768], A.max, A.min, ["rst", "e0", "e1"], ["e2"])
            spread(T.eqb[:, 783:1536:16], "e2")
            pfold(1)
        for i in range(2, np_):
            pfold(i)
            sums(0, sum(pits[i - 2]) // 24 - 1, "YP%d" % (i - 2))
            pscan(i - 1)
        pscan(np_ - 1)
        sums(0, sum(pits[-2]) // 24 - 1, "YP%d" % (np_ - 2))
        for i in range(len(nits)):
            nscan(i)
            if i == 0:
                sums(0, NP - 1, "YP%d" % (np_ - 1))
            elif i != len(nits) - 2:
                j = min(i - 1, len(nits) - 3)
                sums(1, NP - 1 + sum(nits[j]) // 48, "YN%d" % j)
        if t:
            taken(t, 0)
        sums(1, 19, "YN%d" % (len(nits) - 1))

    def head():
        mm(T.ps7[:, 0:3, :], T.hrow[0:1, :], T.on2[0:1, :], ["on2", "hrow"], ["B7"], True, False)
        mm(T.ps3[:, 0:3, :], T.crow[0:1, :], T.on2[0:1, :], ["on2", "crow"], ["B3"], True, False)

    act(T.Z[:, 0:16 * ZS], T.truv[:, :].indirect(T.sgl[:, 0:ZS]), ["truv", "sgl"], ["ZA"])
    cp(T.Z[:, 16 * ZS:4096], T.truv[:, :].indirect(T.sgl[:, ZS:256]), ["truv", "sgl"], ["ZB"])
    BLOCKS[2] = (B1, PH, 4)
    terms(0, 1)
    wholes(0)
    turned(1)
    terms(0, 2)

    def first_filler():
        cp(C[:, 9:10], T.kmi[:, 60:61], ["wti"], ["c9"])

    def first_head():
        weights(0, C[:, 9:10], ["c9"])
        turned(2)
        head()

    answers(0, first_filler, first_head)
    BLOCKS[2] = (B1, PH, 5)

    for t in range(VI):
        st, stk = T["st%d" % max(t, 1)], "st%d" % t
        so = T["so%d" % t]
        last = t == VI - 1
        cur = so if not last else T.ki
        old = t > 0
        M = names_of(t)
        o = 12 * t
        if not old:
            for r in range(4):
                s_lay(r, "s")
        if not last:
            terms(t + 1, 0)
        if t == 1:
            for r in (14, 15):
                s_lay(r, "s")
        if old:
            sread(t - 1)
            swrite(t - 1, "s")
        if not old:
            late(0)
            for r in (4, 5):
                s_lay(r, "s")
        if not last:
            turned(0)
        if last:
            dma("y", T.ra[:, :], T.S[0:128:16, 0:4096], "dra", Sk, ["ra"])
        for i in range(2):
            mm(T.ps6[:, 0:102], T.onb[0:1, :], T.pos[0:1, 102 * i:102 * i + 102], ["onb", "pos"], ["B6"], i == 0, False)
        mm(T.ps6[:, 0:102], T.pos[0:1, 204:332], T.onb[0:1, 0:102], ["onb", "pos"], ["B6"], False, False)
        if old:
            taken(t, 1)
        kl = T.kl[:, 72 * t:72 * t + 57]
        ts(T.kc[:, 64:121], kl, 2047.5, A.is_lt, ["kl%d" % t], ["kraw"], 2048.0, A.mult)
        flip(T.hi[:, :], T.ps7[:, 0:3, :], ["B7"], ["hi"])
        if old:
            tt(cur[:, :], st[:, :], T.ps2[:, 128:128 + SW], A.max, [stk, "X"], ["cur"])
        flip(T.lo[:, :], T.ps3[:, 0:3, :], ["B3"], ["lo"])
        tt(T.k2[:, :], kl, T.kc[:, 64:121], A.add, ["kl%d" % t, "kraw"], ["k2"])
        if not old:
            s_turn(range(8, 12))
            s_lay(6, "v")
        if last:
            ts(T.kj[:, :], T.ki[:, :], 8191, A.bitwise_and, ["cur"], ["kand"])
        scan(T.su[:, :], T.lo[:, 0:84], T.hi[:, 0:84], A.max, A.min, ["lo", "hi"], ["su"])
        if old:
            for a in range(2):
                scan(T.osm[:, 96 * a:96 * a + 84], T.lo[:, 0:84], cur[:, 96 * a:96 * a + 84], A.max, A.min, ["lo", "cur"], ["osm"])
        else:
            s_lay(7, "v")
            s_turn((12, 13))
            s_lay(12, "s")
        x = T.su[:, 19:84:32]
        uU, uQ, uA, uF, uB = [T.uint[:, 4 * i:4 * i + 3] for i in range(5)]
        ks = so[:, 20:96:32]
        ksj = [so[:, 32 * jb + 20:32 * jb + 21] for jb in range(3)]
        ts(uU, x, 4095, A.bitwise_and, ["su"], ["uU"])
        ts(T.kb[:, 0:3], x, -2.0 ** -20, A.mult, ["su"], ["kb"], 138.49609375, A.add)
        if old:
            ts(T.om[:, :], T.osm[:, 19:SW:32], 8191, A.bitwise_and, ["osm"], ["om"])
        tt(uQ, uU, uU, A.mult, ["uU"], ["uQ"])
        ts(uA, uU, 37.0, A.mult, ["uU"] + (["B0"] if old else []), ["uA"], T.ps0[:, 400:401] if old else 0.0, A.add)
        ts(T.kb[:, 4:7], T.kb[:, 0:3], 148.0, A.is_equal, ["kb"], ["kd"], float(t + 1 - 20), A.mult)
        if old:
            ts(T.fo[:, :, 0:3], T.om[:, :], -1.0, A.add, ["om"], ["fo"])
        ts(uF, uQ, 5, A.arith_shift_right, ["uQ"], ["uF"], 1023, A.bitwise_and)
        ts(uB, uA, 1023, A.bitwise_and, ["uA"], ["uB"])
        for jb in range(3):
            ts(T.ps2[:, jb:57:3], T.iof[:, 129:148], T.kb[:, 4 + jb:5 + jb], A.subtract, ["iof", "kb", "kd"], ["xk"] + ([] if old else ["B2"]), T.kb[:, jb:jb + 1], A.not_equal)
        for a in range(2 * old):
            for i in (1, 2):
                act(T.fn[:, 2 * i + 1, 32 * i + a:96:2], T.iot[:, :].indirect(T.fo[:, a, 0:3 - i]), ["iot", "fo"], ["fnG"])
            if not last:
                act(T.zp[:, 144 - 96 * a:192 - 96 * a], Zall.indirect(T.fo[:, a, 0:3]), Zk + ["fo"], ["zpO"])
        if last:
            act(T.fg[:, :], T.kj[:, :].indirect(T.prm[:, :]), ["kand", "perm"], ["fg"])

        def olds(a):
            if old:
                tt(T.fn[:, 1, a:96:2], T.iot[:, :].indirect(T.fo[:, a, 0:3]), T.msk[:, 0:48], A.add, ["iot", "fo", "msk"], ["fnN"])
            else:
                s_lay(10 + a, "v")

        tt(T.nl[:, 0:3], uF, uB, A.add, ["uF", "uB"], ["nl"])
        tt(T.nw[:, 0:3], uF, uB, A.add, ["uF", "uB"], ["nw"])
        if last:
            tt(ks, T.kb[:, 0:3], T.kb[:, 4:7], A.add, ["kb", "kd"], ["ks"])
        tt(T.kw[:, 0:57], T.k2[:, :], T.ps2[:, 0:57], A.mult, ["k2", "xk"], ["kw"])
        cp(T.bkl[:, :], bwin.indirect(T.nl[:, 0:3]), ["bookA", "bookB", "nl"], ["bkl"])
        nrep = T.nw[:, :].indirect(T.rep[:, :])
        if not last:
            kok, c = "ko%d" % t, 72 * t
            tt(T.ko[:, c:c + 64], nrep, T.kw[:, :], A.max, ["kw", "nw", "rep"], [kok])
            send(T.ko[:, c:c + 57], [kok], "kl%d" % (t + 1), T.kl[:, c + 72:c + 129])
        else:
            tt(T.kc[:, 0:64], nrep, T.kw[:, :], A.max, ["kw", "nw", "rep", "kraw"], ["kc"])
            ts(T.mk0[:, :], T.io2[:, 0:20], ksj[0], A.is_equal, ["io2", "ks"], ["mk0"], 8192.0, A.mult)
        for c in range(6):
            (act if c % 2 else cp)(T.zc[:, c, 0:128], Zall.indirect(T.bkl[:, 8 * c:8 * c + 8]), Zk + ["bkl"], ["zc%d" % c])
        tfv = TFV if old and not last else 0
        act(T.tf[:, 128 * tfv:768], T.iot[:, :].indirect(T.bkl[:, 8 * tfv:48]), ["iot", "bkl"], ["tfS"] + ([] if tfv else ["tfV"]))
        if not last:
            tt(ks, T.kb[:, 0:3], T.kb[:, 4:7], A.add, ["kb", "kd"], ["ks", "cur"])
        if old:
            ts(T.ns[:, :, 63:96:16], T.om[:, :], -OFF - 1.0, A.add, ["om"], ["nsO"])
        if tfv:
            cp(T.tf[:, 0:128 * tfv], T.iot[:, :].indirect(T.bkl[:, 0:8 * tfv]), ["iot", "bkl"], ["tfV"])
        if not old:
            for r in (8, 9):
                s_lay(r, "v")
            s_lay(13, "s")
        if not last:
            gcp(T.zw[:, :], T.zc[:, :, 0:128], 768, ["zc%d" % c for c in range(6)], ["zw"])
        for i in range(3):
            for r in range(8):
                mm(T.ps6[:, 34 * i:34 * i + 34], T.scw[:, 14 - 2 * r:142 - 2 * r], T.zc[:, 2 * i:2 * i + 2, 16 * r:16 * r + 17],
                   ["zc%d" % (2 * i), "zc%d" % (2 * i + 1), "scw"], ["B6"], False, i == 2 and r == 7)
        eo = [0, 256, 768]

        def name(jb, m):
            c = 48 * (m % 2) + 16 * jb + 15
            return T.ns[:, m // 2, c:c + 1]

        def eq(jb, m, part):
            w = (64 if old else 32) * (jb + 1)
            pos = eo[jb] + w * m * M // 4 + (w // 2 if part == 1 else 0)
            a, b = ((0, 2), (1, 2), (0, 1 if old else 2))[part]
            ts(T.eqb[:, pos:pos + 64 // b * (jb + 1)], T.fn[:, a:2 * jb + 2:b, 32 * jb:32 * jb + 32], name(jb, m), A.is_equal,
               [k for k in (["fnM", "fnF"] if part != 1 else []) + (["fnN", "fnG"] if part and old else []) if jb or k in ("fnM", "fnN")]
               + ["nsO" if m % 2 else "nsN"], ["e%d" % jb], 8192.0, A.mult)

        if not last:
            ts(T.hitb[:, 0:3], T.kb[:, 0:3], 147.5, A.is_lt, ["kb"], ["hitb"])
            for jb in range(3):
                mm(T.ps0[:, 400:401], T.onb[:, :], T.hitb[:, jb:jb + 1], ["onb", "hitb"], ["B0"], jb == 0, jb == 2)
            ts(T.kd[:, 8:11], ks, -65536.0, A.mult, ["ks"], ["kx"], 148.0 * 65536.0 + 8192.0 * (t + 1) + 1.0, A.add)
        else:
            ts(T.kc[:, 64:121], T.kc[:, 0:57], 1023, A.bitwise_and, ["kc"], ["kraw"])
            for jb in range(3):
                ts(T.ps0[:, jb:120:3], T.io2[:, :], ksj[jb], A.is_equal, ["io2", "ks"], ["B0"], 8192.0, A.mult)
            ts(T.ri[:, :], T.ra[:, :], -SO, A.add, ["ra"], ["ri"])
            cp(T.sf[:, 128:185], T.kc[:, 64:121], ["kraw"], ["sfk"])
            send(T.sf[:, 128:185], ["sfk"], "homek", T.homek[:, 4:61], -1)
            tt(T.fb[:, 0:120], T.fg[:, 0:120], T.ps0[:, 0:120], A.add, ["fg", "B0"], ["fb"])
            act(T.rb[:, :], T.ri[:, :], ["ri"], ["rb"])
            dma("y", T.S[0:128:16, 0:4096], T.rb[:, :], "drb", ["rb"], Sk)
        OLD = (1, 3) if old else ()
        scan(T.sk[:, 0:102], T.rs17[:, :], T.ps6[:, 0:102], A.max, A.min, ["rs17", "B6"], ["sk"])
        scan(T.sk[:, 102:204], T.inc[:, :], T.ps6[:, 0:102], A.add, A.min, ["inc", "B6"], ["sk"])
        if last:
            ts(T.ps4[:, 0:120], T.fb[:, 0:120], 4096.5, A.is_lt, ["fb"], ["B4"])
        olds(0)
        tt(T.fl[:, 0:6], T.sk[:, 16:102:17], T.sk[:, 118:204:17], A.subtract, ["sk"], ["fl"])
        olds(1)
        if last:
            tt(T.fa[:, 0:120], T.fb[:, 0:120], T.ps4[:, 0:120], A.mult, ["fb", "B4"], ["fa"])
        for i in (1, 2):
            act(T.fn[:, 2 * i, 32 * i:96], twin.indirect(T.fl[:, 0:6 - 2 * i]), ["tfV", "tfS", "fl"], ["fnF"])
        if last:
            act(T.ps2[:, 0:120], T.fa[:, 0:120], ["fa"], ["B2", "xk", "X"], bias=-1.0)
        else:
            act(T.zq[:, :], T.zw[:, :].indirect(T.fl[:, 0:6]), ["zw", "fl"], ["zq"])
            for a in range(2):
                c = 24 * M * (1 - a)
                gcp(T.zp[:, c:c + 48], T.zq[:, a:96:2], 48, ["zq"], ["zpN"])
        tt(T.fn[:, 0, :], twin.indirect(T.fl[:, 0:6]), T.mkn[:, :], A.add, ["tfV", "tfS", "fl", "mkn"], ["fnM"])
        for m in OLD:
            eq(2, m, 1)
        if not old:
            late(1)
            s_turn((14, 15))
        for m in range(2):
            scan(T.ns[:, m, 0:48], T.pns[:, :], T.fn[:, 0, m:96:2], A.max, A.min, ["pns", "fnM"], ["nsN"])
        if not old:
            late(2)

        def count(jb):
            w = (64 if old else 32) * (jb + 1) * M // 2
            c = eo[jb] // 2
            scan(T.cn[:, c:c + w], T.eqb[:, eo[jb]:eo[jb] + w], T.eqb[:, eo[jb] + w:eo[jb] + 2 * w], A.add, A.add, ["e%d" % jb], ["cn%d" % jb], OFF - 8192.0 * M)
            return T.cn[:, c + w - 1:c + w]

        def place(jb, col):
            ts(T.xo[:, :, jb:6:3], T.ns[:, :, 16 * jb + 15:96:48], col, A.add, ["nsN", "nsO", "cn%d" % jb], ["xo%d" % jb])

        def places():
            tt(T.offs[:, o:o + 12], T.xo[:, :, :], T.padf[:, :, :], A.min, ["xo0", "xo1", "xo2", "padu"], ["offs%d" % t])

        if not last:
            terms(t + 1, 1)
            terms(t + 1, 2)
            turned(1)
            wholes(t + 1)
            turned(2)
        else:
            for jb in (2, 1):
                for a in range(2):
                    act(T.q1[:, 60 * a + jb:60 * a + 60:3], T.ps0[:, 60 * a + jb:60 * a + 60:3], ["B0", "nsN"], ["q1%d" % jb], func=AF.Identity, bias=name(jb, 2 * a))
            for a in range(2):
                act(T.pl[:, 6 - 6 * a:12 - 6 * a], T.ns[:, a, 15:96:16], ["nsN", "nsO"], ["pl"], bias=OFF)
            act(T.sp[:, :], T.S[:, :].indirect(T.pl[:, :]), Sk + ["pl"], ["sp"])
        for jb in (0, 1, 2):
            for m in OLD:
                eq(jb, m, 0 if jb == 2 else 2)
        for jb in (2, 1, 0):
            for m in (0, 2):
                eq(jb, m, 2)
        for a in range(2 * last):
            ts(T.q1[:, 60 * a:60 * a + 60:3], T.mk0[:, :], name(0, 2 * a), A.add, ["mk0", "nsN"], ["q10"])
        c2 = count(2)
        c1 = count(1)
        c0 = count(0)
        if last:
            break
        place(2, c2)
        place(1, c1)
        place(0, c0)
        if not old:
            late(3)
        if old:
            places()
            cp(Zall.indirect(T.offs[:, o:o + 12]), T.zp[:, :], ["offs%d" % t, "zpN", "zpO"], Zk)
        else:
            tt(T.of0[:, :], T.xo[:, :, 0:3], T.padf[:, :, 0:3], A.min, ["xo0", "xo1", "xo2", "padu"], ["of0"])
            places()
            late(4)
            cp(Zall.indirect(T.of0[:, :]), T.zp[:, 0:96], ["of0", "zpN"], Zk)

        def state():
            for a in range(2):
                tt(so[:, 21 + a:96:32], T.offs[:, o + 6 * a:o + 6 * a + 3], T.kd[:, 8:11], A.add, ["offs%d" % t, "kx", "ks"], ["of2%d" % a])
            send(so[:, :], ["cur", "ks", "of20", "of21"], "st%d" % (t + 1), T["st%d" % (t + 1)][:, :])

        answers(t + 1, state, head)

    for (jb, col) in ((2, c2), (1, c1), (0, c0)):
        ts(T.x1[:, jb:120:3], T.q1[:, jb:120:3], col, A.subtract, ["q1%d" % jb, "cn%d" % jb], ["x1%d" % jb], -2 * OFF, A.add)
    place(2, c2)
    place(1, c1)
    place(0, c0)
    tt(T.sf[:, 0:120], T.x1[:, :], T.ps2[:, 0:120], A.max, ["x10", "x11", "x12", "B2"], ["sf"])
    send(T.sf[:, 0:120], ["sf"], "home", T.home[:, 0:120], -1)
    places()
    dma("s", T.yk[:, :], T.homek[:, 1:61], "dout", ["homek", "homez"], [])
    swrite(t, "v")
    dma("y", T.ys[:, :], T.S[0:128:16, 0:4096], "dout", Sk, [])
    dma("s", T.ya[:, :], T.home[:, 0:60], "dout", ["home"], [])
    dma("y", T.yb[:, :], T.home[:, 60:120], "dout", ["home"], [])
    need("y", "dout", 64)
    need("g", "lsem", cnt["sent"])
    for q in ("v", "s", "p", "g"):
        need("g", semn[q], cnt[q])
